import numpy as np, ml_dtypes
CORES = [3,11,19,27,35,43,51,59]
N = 8
import mx_ref
BF = ml_dtypes.bfloat16
def gentries(a):
    return np.ascontiguousarray(a.reshape(8, 16, -1).transpose(0, 2, 1)).reshape(8, -1)
def gtable(e):
    e = np.asarray(e); return np.ascontiguousarray(e.reshape(8, -1, 16).transpose(0, 2, 1)).reshape(128, -1).astype(np.int32)
def gcols(t, e):
    v = np.concatenate([t.reshape(8, 16, -1, 4), np.zeros((8, 16, 1, 4), BF)], axis=2)
    return np.ascontiguousarray(np.stack([v[g][:, e[g]] for g in range(8)])).reshape(128, -1)
def tile(rs):
    return np.stack(rs, axis=2).reshape(128, -1).astype(BF)
def pick(q, e):
    c = np.concatenate([q[0].reshape(128, -1, 4), np.zeros((128, 1, 4), np.uint8)], axis=1); s = np.concatenate([q[1], np.ones((16, 1), np.uint8)], axis=1)
    return (np.ascontiguousarray(c[:, e].reshape(128, -1)), np.ascontiguousarray(s[:, e]))
def join(*qs):
    return (np.concatenate([q[0] for q in qs], axis=1), np.concatenate([q[1] for q in qs], axis=1))
def put(q, e, v):
    c, s = q[0].reshape(128, -1, 4).copy(), q[1].copy(); c[:, e] = v[0].reshape(128, -1, 4); s[:, e] = v[1]
    return (c.reshape(128, -1), s)
def pk(c, s):
    return (np.ascontiguousarray(c), mx_ref.live(s))
def emit(q):
    return q[0], q[1]
def packed(v, rng):
    q = [mx_ref.quantize(np.ascontiguousarray(v[r])) for r in range(N)]
    return np.stack([a for a, b in q]), np.stack([mx_ref.plane(b, rng) for a, b in q])
def values_of_codes():
    e, c = np.zeros((128, 128, 4), np.float32), np.zeros((128, 2, 4), np.uint8)
    e[np.arange(128), np.arange(128), 0] = 1
    c[:127, :, 0] = np.arange(256).reshape(2, 128).T[:127]
    return mx_ref.matmul(mx_ref.quantize(e.reshape(128, 512).astype(BF)), (c.reshape(128, 8), np.full((16, 2), 127, np.uint8))).T.reshape(-1).astype(np.float64)
CODE_VALUE, SCALE_VALUE = values_of_codes(), 2.0 ** (np.arange(256) - 127.0)
def decode(q):
    return (CODE_VALUE[q[0]].reshape(16, 8, -1, 4) * SCALE_VALUE[q[1]][:, None, :, None] + 0.0).reshape(128, -1).astype(np.float32)
def f(rng, *shape):
    return mx_ref.flush((rng.standard_normal(shape, dtype=np.float32) * np.exp2(rng.integers(-2, 3, shape[:-1] + (1,)))).astype(BF))
def wide(rng, *shape, cols=0):
    v = rng.standard_normal(shape, dtype=np.float32) * np.exp2(rng.integers(-12, 13, shape)).astype(np.float32)
    if cols: v *= np.repeat(np.exp2(rng.integers(-cols, cols + 1, shape[:-2] + (1, shape[-1] // 4))) * (rng.random(shape[:-2] + (1, shape[-1] // 4)) > 0.0625), 4, axis=-1).astype(np.float32)
    return mx_ref.flush(v.astype(BF))
C, K, R, H = 256, 96, 3, 6
ROWS_USED = [(16 * g, 16 * g, 8) for g in range(8)] + [(16 * g + 1, 16 * g, 9) for g in range(8)] + [(8, 0, 10)]
def big(v):
    v = np.clip(v.astype(np.float32), -2.0 ** 21, 2.0 ** 21)
    v[np.abs(v) < np.float32(2.0 ** -16)] = 0
    return v.astype(BF)
def numbers_of(rng):
    return {"x": big(f(rng, N, 128, 4 * C)), "u": np.array(f(rng, N, 128, 512)), "v": np.array(f(rng, N, 128, 512))}
def links(rng):
    return np.stack([gtable(rng.integers(0, C, (8, C))) for r in range(N)])
def layers(rng):
    w = np.clip(big(f(rng, N, 128, 2048)).astype(np.float32) * np.float32(0.25), -1.0, 1.0)
    return w.astype(BF).reshape(N, 8, 16, 4, 8, 16, 4)
def weights(rng, w, still=[]):
    for i in still:
        w[:, :, i] = 0
        w[:, :, :, :, :, i] = 0
    c, p = packed(np.ascontiguousarray(w).reshape(N, 128, 2048), rng)
    return {"wc": c, "ws": p}
def setup_inputs(rng):
    return {**numbers_of(rng), "ol": links(rng), **weights(rng, layers(rng))}
def setup_inputs_ties(rng):
    d = numbers_of(rng)
    o = rng.permutation(N)
    x = d["x"].reshape(N, 8, 16, C, 4)
    x[:, :, :3] = 0
    x[:, :, :3, :, 0] = rng.integers(0, 3, (N, 8, 3, C)).astype(np.float32).astype(BF)
    k = np.ones(N, np.float32)
    k[o[0]] = 0
    k[o[1]] = -1
    u = d["u"].reshape(N, 128, 128, 4)
    for i, h, j in ROWS_USED:
        u[:, :, i] = 0
        u[:, h + j - 8, i, 0] = k.astype(BF)
    p = links(rng)
    e = np.stack([rng.permutation(C) for g in range(8)]).reshape(8, -1, 4)
    n = np.zeros((8, C), np.int64)
    np.put_along_axis(n, e.reshape(8, C), np.roll(e, -1, axis=2).reshape(8, C), axis=1)
    p[o[0]] = gtable(n)
    return {"x": x.reshape(N, 128, 4 * C), "u": u.reshape(N, 128, 512), "v": d["v"], "ol": p, **weights(rng, layers(rng), [0, 1, 2])}
def setup_inputs_near(rng):
    d = numbers_of(rng)
    o = rng.permutation(N) % 3
    x = d["x"].astype(np.float32).reshape(N, 8, 16, C, 4)
    x[:, :, 0] = 0
    x[:, :, 8:] = 0
    x[:, :, 0, :, 0] = rng.integers(0, 2, (N, 8, C)) * 2.0 - 1.0
    s = rng.integers(0, 16, (N, 8, 3, C))
    x[:, :, 8:11] = ((s[..., None] >> np.arange(4)) & 1) * np.exp2(np.arange(4) - 23.0)
    x[:, :, 11, :, 0] = 2.0 ** -10
    for r in range(N):
        for g in rng.permutation(8)[:4]: x[r, g, 0, rng.integers(C), 0] = 2.0 ** 20 * rng.choice([-1.0, 1.0])
    u = d["u"].reshape(N, 128, 128, 4)
    for i, h, j in ROWS_USED:
        u[:, :, i] = 0
        for r in range(N):
            k = 1.0 if o[r] == 0 else 2.0 ** -30
            u[r, h + j, i] = k
            if o[r] < 2:
                u[r, h, i, 0] = k
                u[r, h + 11, i, 0] = k
    return {"x": x.reshape(N, 128, 4 * C).astype(BF), "u": u.reshape(N, 128, 512), "v": d["v"], "ol": links(rng), **weights(rng, layers(rng), [0, 8, 9, 10, 11, 12, 13, 14, 15])}
def setup_inputs_chains(rng):
    d = numbers_of(rng)
    o = rng.permutation(N)
    p = []
    for r in range(N):
        e = np.zeros((8, C), np.int64)
        if o[r] == 0:
            n = rng.permutation(C)
            hub = np.sort(n[K - 1:])
            e[:, hub] = hub
            e[:, n[:K - 1]] = hub[rng.permutation(8 * (K - 1)) % (C - K + 1)].reshape(8, K - 1)
        elif o[r] % 2 == 0:
            for g in range(8):
                n = rng.permutation(C)
                e[g, n] = np.roll(n, -1)
        else:
            n = rng.permutation(C)
            low, hub, m = n[:K].reshape(-1, 8), n[K:], np.arange(K // 8)
            e[:, hub] = hub
            g = int(rng.integers(8))
            e[np.ix_([i for i in range(8) if i != g], n[:K])] = hub[rng.permutation(7 * K) % (C - K)].reshape(7, K)
            e[g, low[:, :7]] = low[:, 1:]
            e[g, low[:, 7]] = hub[:K // 8]
            e[g, hub[-(K // 8):]] = low[m, 7 - m % 8]
        p.append(gtable(e))
    x = d["x"].astype(np.float32).reshape(N, 8, 16, C, 4)
    k = rng.random((N, 1, 1, C, 1)) < 0.5
    k[:, :, :, 0] = True
    s = (1.125 + 0.25 * rng.integers(0, 4, x.shape)) * np.exp2(-rng.integers(8, 15, x.shape).astype(np.float64)) * rng.choice([-1.0, 1.0], x.shape)
    s[:, :, ::8, :, 0] = 1.96875 * rng.choice([-1.0, 1.0], (N, 8, 2, C))
    x = np.where(k, s, x).astype(np.float32).astype(BF)
    return {"x": x.reshape(N, 128, 4 * C), "u": d["u"], "v": d["v"], "ol": np.stack(p), **weights(rng, layers(rng))}
def setup_inputs_ends(rng):
    o = rng.permutation(N) % 4
    h = rng.permutation(8)
    a = np.full((N, 8, 16, C, 4), 2.0 ** 21)
    a[:, h[:4]] *= 1 - 0.1 * rng.random((N, 4, 16, C, 4))
    c = rng.integers(0, 2, (N, 1, 1, C, 1)) * 2.0 - 1.0
    c[o == 0] = 1
    c[o == 1] = -1
    a = a * c
    a[o == 3] = 2.0 ** -24
    u = np.full((N, 128, 128, 4), 2.0 ** 30)
    u[o == 3] = 2.0 ** -30
    for g in h[4:]: u[:, np.arange(128) // 16 != g, 16 * g:16 * g + 2] = 0
    k = rng.integers(0, 2, (N, 1, 128, 1)) * 2.0 - 1.0
    k[:, :, 1::16] = 1
    u = u * k + 0.0
    v = rng.choice([-1.0, 1.0], (N, 128, 512)) * np.where(o % 2 == 0, 2.0 ** 30, 2.0 ** -30)[:, None, None]
    w = np.ones((N, 128, 2048), np.float32)
    t = np.zeros((N, 8, C), np.int64)
    for r in range(N):
        if o[r] == 0: t[r] = C - 1
        if o[r] == 2:
            t[r] = np.arange(C)
            w[r] = rng.choice([-1.0, 1.0], (128, 2048))
        if o[r] == 3: t[r] = rng.integers(0, 2, (8, C)) * (C - 1)
    x, u, v = [b.astype(np.float32).astype(BF) for b in (a.reshape(N, 128, 4 * C), u.reshape(N, 128, 512), v)]
    return {"x": x, "u": u, "v": v, "ol": np.stack([gtable(t[r]) for r in range(N)]), **weights(rng, w.astype(BF))}
def setup_inputs_spread(rng):
    d = setup_inputs(rng)
    d["x"] = big(wide(rng, N, 128, 4 * C, cols=6))
    return d
def check_inputs(d):
    b = []
    for k, lo, hi in (("x", -24, 21), ("u", -30, 30), ("v", -30, 30)):
        a = np.abs(d[k].astype(np.float32))
        if not (np.isfinite(a).all() and ((a == 0) | (a >= 2.0 ** lo) & (a <= 2.0 ** hi)).all()): b.append("a value of " + k)
    if not ((d["ol"] >= 0) & (d["ol"] < C)).all(): b.append("an entry of ol")
    none, least, most = [emit(mx_ref.quantize(np.full((128, 16), k, np.float32).astype(BF)))[1][0, 0] for k in (0.0, 2.0 ** -30, 1.0)]
    for r in range(N):
        if ((d["wc"][r] == 0x7F) | (d["wc"][r] == 0xFF)).any(): b.append("wc: a code that is no number")
        s = mx_ref.live(d["ws"][r])
        if ((s != none) & ((s < least) | (s > most))).any(): b.append("ws: a scale out of range")
        elif not (np.abs(decode(pk(d["wc"][r], d["ws"][r]))) <= 1).all(): b.append("W: a number beyond 1")
    return b
def places(s):
    return np.argsort(np.argsort(s, axis=-1, kind="stable"), axis=-1, kind="stable")
def reference(x, u, v, ol, wc, ws):
    qu = [mx_ref.quantize(u[r]) for r in range(N)]
    lay = [pk(wc[r], ws[r]) for r in range(N)]
    now = [x[r] for r in range(N)]
    link = [gentries(ol[r]).astype(np.int64) for r in range(N)]
    for t in range(R):
        means, sent, given, freed, spliced = [], [], [], [], []
        for r in range(N):
            q = mx_ref.quantize(now[r])
            s = mx_ref.matmul(qu[r], q) + np.float32(0.0)
            own = decode(q)
            birth, snap = places(s[8]), places(s[::16])
            hops = [link[r]]
            for i in range(H - 1): hops.append(np.take_along_axis(link[r], hops[-1], axis=1))
            read = hops[-1]
            for p in hops[::-1]: read = np.where(birth[p] <= snap, p, read)
            z = ((own + gcols(own.astype(BF), read).astype(np.float32)) * np.float32(0.5)).astype(BF)
            e = np.argsort(-s[1::16], axis=1, kind="stable")[:, :K]
            count = np.bincount(read.reshape(-1), minlength=C)
            d = np.sort(np.argsort(count, kind="stable")[:K])
            gone = np.zeros(C, bool)
            gone[d] = True
            l = np.tile(np.arange(C), (8, 1))
            for p in hops[::-1]: l = np.where(gone[p], l, p)
            means.append(z)
            sent.append(mx_ref.quantize(gcols(z, e)))
            given.append(e)
            freed.append(d)
            spliced.append(l)
        for r in range(N):
            b4 = (r + N - 1) % N
            a = sent[b4]
            da = decode(a)
            m = tile([mx_ref.matmul(pick(lay[r], np.arange(128 * b, 128 * b + 128)), a) * np.float32(0.0078125) + da[:, b::4] for b in range(4)])
            z = means[r].reshape(128, C, 4).copy()
            z[:, freed[r]] = m.reshape(128, K, 4)
            now[r] = z.reshape(128, 4 * C)
            link[r] = spliced[r]
            link[r][:, freed[r]] = given[b4]
    y, lk = np.zeros((N, 128, C), np.float32), np.zeros((N, 8, C), np.float32)
    oc, osc = np.zeros((N, 128, 4 * C), np.uint8), np.zeros((N, 16, C), np.uint8)
    for r in range(N):
        q = mx_ref.quantize(now[r])
        y[r] = mx_ref.matmul(mx_ref.quantize(v[r]), q)
        lk[r] = link[r]
        oc[r], osc[r] = emit(q)
    return {"y": y, "lk": lk, "oc": oc, "osc": osc}

@@ -1,0 +1,628 @@
+import numpy as np
+from concourse.bass import DstId, RemoteDMATransfer
+from concourse.mybir import dt, AluOpType, AxisListType, ActivationFunctionType
+
+OP = AluOpType
+AF = ActivationFunctionType
+ROUNDS, KEEP = 3, 96
+F, B, I, U, X4, U8 = "float32", "bfloat16", "int32", "uint16", "float8_e4m3fn_x4", "uint8"
+
+SCRATCH = {}
+
+
+def _sb(dtype, **widths):
+    for name in widths:
+        SCRATCH[name] = ("sbuf", [128, widths[name]], dtype)
+
+
+def _q(**widths):
+    for name in widths:
+        SCRATCH["c" + name] = ("sbuf", [128, widths[name]], X4)
+        SCRATCH["s" + name] = ("sbuf", [128, widths[name]], U8)
+
+
+_sb(B, XT=1024, UT=512, VTL=512)
+_sb(I, OL=16, PC=1, PI=4, OI=72, RI=32, CI=24, LI=144)
+_q(W=512, U=128, UP=384, V=128, X=1024, L=320, P=384, E=384)
+_q(K=1024)
+_q(C=1664)
+_sb(B, TK=5120)
+_sb(F, IR=256, ID=256, TI=128, BK=512, PF=16, RQ=256, BS=256, BE=256, TR=128, CY=368, CB=368, CW=16, CX=16, CT=16)
+_sb(U, OU=72)
+_sb(B, ME=256, KP=256, ON=288, EX=256)
+_sb(F, MS=512, SWS=256, SG=256, SWE=256, EG=256, SB2=2, DL=4, TH0=128, TH1=128)
+_sb(B, BT=1024, CT2=8192, AJ=1024)
+_sb(F, VH=1792, VT=1792, T6=80, CM=96, XX=192, MN=80, T1=32)
+_sb(B, FT=1024, FU=1024, Z=1024, ET=512, RT=512)
+_sb(F, AR=32, RW=32, EC=256, EP=48, EF=256, PK=96)
+_sb(U, EP16=16, EO=32, LS=144, LL=144, R16=16, NI16=16, M16=32, L16=16)
+_sb(B, RD=512, XR=512, RX=512)
+_sb(F, XE=256, ES=96, RS=256)
+_sb(F, CA=8, CJ=512, CF=16, QQ=176, W3=32)
+_sb(B, RP=256, TO=256, FB=128, EQM=256, CU=256, OV=256, Z2=256, GN=256)
+_sb(F, SC=16, GS=256, M1=256, Y0=256, NS=256, SM=208, YA=256, YB=256, YX=352, NR=256, CL=64, YO=256)
+for _i in range(8):
+    SCRATCH["P%d" % _i] = ("psum", [128, 512], F)
+PS = ["P%d" % i for i in range(8)]
+PLACE = {"B": ("C", 0)}
+TILE_N = (128, 128, 192, 256)
+for _i in range(4):
+    PLACE["X%d" % _i] = ("X", 256 * _i)
+    PLACE["KR%d" % _i] = ("K", 128 * _i)
+    PLACE["C%d" % _i] = ("C", 256 + sum(TILE_N[:_i]))
+    PLACE["D%d" % _i] = ("C", 960 + sum(TILE_N[:_i]))
+for _i in range(3):
+    PLACE["E%d" % _i] = ("E", 128 * _i)
+for _i, _k in enumerate(("KS", "KB", "KT", "KU")):
+    PLACE[_k] = ("K", 512 + 128 * _i)
+WAKE, SLACK, FLIGHT = 0.3, 0.25, 4.5
+LONG = {"MS": .25, "MSE": .25, "SWS": .25, "SWE": .25, "SG": .25, "EG": .25, "V0": .25, "TT": .25, "VT": .25, "XE": .25,
+        "EC": .25, "RS": .25, "NSx": .25, "GS": .25, "NRx": .25, "BTe": .37, "BTf": .37, "Z": .37, "BTa": .13, "BTb": .13,
+        "BTc": .13, "BTd": .13, "EF": .8, "XS": .13, "RY": .13, "TO": .13, "EQM": .13, "CU": .13, "OV": .13, "GN": .13,
+        "Zx": .45, "Y0": .45, "RD": .13, "FU": .45, "X": .36, "Xs": .36, "VH": .37, "CJ": .39, "CA": .39, "FT": .23,
+        "XR": .36, "RX": .36, "ET": .2, "RP": .36, "YA": .36, "YB": .36, "YX": .36, "M": .3, "TH": .13, "AC": .25,
+        "P": .24, "Pb": .13, "B": .24, "C": .17, "D": .17, "E": .13, "RT": .1, "TKS": .45, "TKB": 1.2, "TKT": 1.2, "TK": 1.2,
+        "IR": .6, "ID": .6, "BK": 1.0, "CY": .8, "RQ": .23, "ME": .23, "KP": .23, "BS": .23, "BE": .23, "EX": .3, "CB": .3}
+
+
+def duration(q, key):
+    if q == "P":
+        return 0.2
+    if q == "G" and key[:3] == "snd":
+        return 0.7
+    if key[:2] == "ct" or key[:2] == "AR" and "." in key:
+        return 0.02 + 0.00083 * max(64, 16 * int(key.split(".")[1]))
+    return LONG.get(key.rstrip("0123456789s") or key, LONG.get(key.rstrip("0123456789"), 0.075))
+
+SEMAPHORES = ["sV", "sA", "sP", "sG", "dX", "dU", "dO", "dW", "dVV", "dPad", "dY", "dLk", "dOc", "ls",
+              "aC0", "aC1", "aC2", "aL0", "aL1", "aL2"]
+
+
+def rank_program(g, core, T, topo):
+    rank = T.rank_of(core)
+    if rank is None:
+        return
+    cores = T.cores
+    n_ranks = len(cores)
+    nxt, prv = cores[(rank + 1) % n_ranks], cores[(rank - 1) % n_ranks]
+    eng = {"V": g.vector, "A": g.scalar, "P": g.tensor, "G": g, "S": g.sync}
+    own = {"V": "sV", "A": "sA", "P": "sP", "G": "sG"}
+    cnt, known, lastw, readers = {}, {q: {} for q in eng}, {}, {}
+
+    def sync(q, toks):
+        for s, n, clk in sorted(toks, key=lambda t: -sum(t[2].values())):
+            if known[q].get(s, 0) < n:
+                eng[q].wait_ge(T.sem[s], n)
+                for k in clk:
+                    known[q][k] = max(known[q].get(k, 0), clk[k])
+                known[q][s] = max(known[q].get(s, 0), n)
+
+    def deps(q, r, w):
+        toks, me = [], own.get(q)
+        for k in r:
+            if k in lastw and not (q == "P" and lastw[k][0] == "sP"):
+                toks.append(lastw[k])
+            if k in PS:
+                toks += [t for s, t in readers.get(k, {}).items() if s != me]
+        for k in w:
+            if k in lastw and not (q == "P" and lastw[k][0] == "sP"):
+                toks.append(lastw[k])
+            toks += [t for s, t in readers.get(k, {}).items()]
+        sync(q, toks)
+
+    def done(tok, r, w):
+        for k in r:
+            readers.setdefault(k, {})[tok[0]] = tok
+        for k in w:
+            lastw[k] = tok
+            readers[k] = {}
+
+    nodes = []
+
+    def emit(q, r, w, fn):
+        def issue():
+            deps(q, r, w)
+            s = own[q]
+            fn(eng[q]).then_inc(T.sem[s], 1)
+            cnt[s] = cnt.get(s, 0) + 1
+            clk = dict(known[q])
+            clk[s] = cnt[s]
+            done((s, cnt[s], clk), r, w)
+        nodes.append((q, r, w, issue, duration(q, w[0]), 0.0))
+
+    def dma(q, s, r, w, pairs):
+        def issue():
+            deps(q, r, w)
+            for o, i in pairs:
+                eng[q].dma_start(o, i).then_inc(T.sem[s], 16)
+                cnt[s] = cnt.get(s, 0) + 16
+            done((s, cnt[s], dict(known[q])), r, w)
+        nodes.append((q, r, w, issue, 0.1, 2.0))
+
+    def arrival(key, r, tok):
+        nodes.append(("R", r, [key], lambda: done(tok, [], [key]), 0.0, FLIGHT))
+
+    def schedule():
+        n = len(nodes)
+        succ, left = [[] for _ in range(n)], [0] * n
+        wr, rd = {}, {}
+
+        def edge(a, b, lag):
+            if a != b:
+                succ[a].append((b, lag))
+                left[b] += 1
+        for i, (q, r, w, fn, c, late) in enumerate(nodes):
+            for k in r:
+                if k in wr:
+                    edge(wr[k], i, 0.0 if q == "P" and nodes[wr[k]][0] == "P" else WAKE)
+                if k in PS:
+                    for j in rd.get(k, []):
+                        if nodes[j][0] != q:
+                            edge(j, i, WAKE)
+            for k in w:
+                if k in wr:
+                    edge(wr[k], i, 0.0 if q == "P" and nodes[wr[k]][0] == "P" else WAKE)
+                for j in rd.get(k, []):
+                    edge(j, i, WAKE)
+            for k in r:
+                rd.setdefault(k, []).append(i)
+            for k in w:
+                wr[k], rd[k] = i, []
+        rest = [0.0] * n
+        for i in range(n - 1, -1, -1):
+            rest[i] = nodes[i][4] + nodes[i][5] + max([lag + rest[j] for j, lag in succ[i]] + [0.0])
+        ready, free, todo = [0.0] * n, {}, [i for i in range(n) if not left[i]]
+        while todo:
+            best = None
+            for i in todo:
+                at = max(ready[i], free.get(nodes[i][0], 0.0))
+                if best is None or (at, -rest[i]) < best[:2]:
+                    best = (at, -rest[i], i)
+            at, i = best[0], best[2]
+            for j in todo:
+                if nodes[j][0] == nodes[i][0] and max(ready[j], free.get(nodes[j][0], 0.0)) <= at + SLACK and rest[j] > rest[i]:
+                    i = j
+            at = max(ready[i], free.get(nodes[i][0], 0.0))
+            todo.remove(i)
+            nodes[i][3]()
+            end = at + nodes[i][4]
+            free[nodes[i][0]] = end
+            for j, lag in succ[i]:
+                ready[j] = max(ready[j], (at if lag == 0.0 and nodes[j][0] == nodes[i][0] else end + nodes[i][5]) + lag)
+                left[j] -= 1
+                if not left[j]:
+                    todo.append(j)
+
+    def tt(r, w, out, a, b, op):
+        emit("V", r, w, lambda e: e.tensor_tensor(out, a, b, op))
+
+    def ts(r, w, out, a, s1, o1, s2=None, o2=None):
+        if o2 is None:
+            emit("V", r, w, lambda e: e.tensor_scalar(out, a, s1, None, o1))
+        else:
+            emit("V", r, w, lambda e: e.tensor_scalar(out, a, s1, s2, o1, o2))
+
+    def cp(r, w, out, a):
+        emit("V", r, w, lambda e: e.tensor_copy(out, a))
+
+    def scan(r, w, out, d0, d1, init=0.0, o0=OP.mult, o1=OP.add):
+        emit("V", r, w, lambda e: e.tensor_tensor_scan(out, d0, d1, init, o0, o1))
+
+    def turn(r, w, out, a):
+        emit("V", r, w, lambda e: e.transpose(out, a))
+
+    def fill(w, ap, x):
+        emit("V", [], w, lambda e: e.memset(ap, x))
+
+    def quant(r, name, c0, c1, tile):
+        k, o = PLACE.get(name, (name, 0))
+        emit("V", r, [name if c0 == 0 else name + "b"],
+             lambda e: e.quantize_mx(T["c" + k][:, o + c0:o + c1], T["s" + k][:, o + c0:o + c1], tile))
+
+    def act(r, w, out, a, fn=AF.Copy, bias=0.0, scale=1.0, acc=None):
+        if acc is None:
+            emit("A", r, w, lambda e: e.activation(out, a, fn, bias, scale))
+        else:
+            emit("A", r, w, lambda e: e.activation(out, a, fn, bias, scale, accum_out=acc))
+
+    def mm(r, bank, n, L, l0, R, r0, start=True, stop=True):
+        L, lo_ = PLACE.get(L, (L, 0))
+        R, ro_ = PLACE.get(R, (R, 0))
+        l0, r0 = l0 + lo_, r0 + ro_
+        emit("P", r, [bank], lambda e: e.matmul_mx(
+            T[bank][:, 0:n], T["c" + L][:, l0:l0 + 128], T["s" + L][:, l0:l0 + 128],
+            T["c" + R][:, r0:r0 + n], T["s" + R][:, r0:r0 + n], start, stop))
+
+    def iota(w, out, pattern, base, cm):
+        emit("G", [], w, lambda e: e.iota(out, pattern, base, cm, allow_small_or_imprecise_dtypes=True))
+
+    def iotai(w, out, pattern, base, cm):
+        emit("G", [], w, lambda e: e.iota(out, pattern, base, cm))
+
+    dma("S", "dX", [], ["XT"], [(T.XT[:], T.x[:])])
+    dma("A", "dU", [], ["UT"], [(T.UT[:], T.u[:])])
+    dma("S", "dO", [], ["OL"], [(T.OL[:], T.ol[:])])
+    dma("A", "dW", [], ["W"], [(T.cW[:].bitcast(dt.uint8), T.wc[:]), (T.sW[:], T.ws[:])])
+    dma("S", "dVV", [], ["VTL"], [(T.VTL[:], T.v[:])])
+
+    iotai(["PC"], T.PC[:], [[0, 1]], 0, 1)
+    iotai(["OI"], T.OI[:, 0:8], [[16, 8]], 0, 0)
+    iotai(["OI"], T.OI[:, 8:16], [[16, 8]], 1, 0)
+    iotai(["OI"], T.OI[:, 16:24], [[0, 8]], 8, 0)
+    iotai(["OI"], T.OI[:, 24:40], [[1, 16]], 0, 0)
+    iotai(["OI"], T.OI[:, 40:56], [[16, 16]], 15, 0)
+    iotai(["OI2"], T.OI[:, 56:72], [[2, 8], [0, 2]], 0, 0)
+    iota(["IR"], T.IR[:], [[0, 16], [1, 16]], 0, 0)
+    iota(["TI"], T.TI[:], [[1, 128]], 0, -1)
+    iota(["ID"], T.ID[:], [[1, 256]], 0, 0)
+    iota(["BK"], T.BK[:], [[1, 8], [0, 64]], 0, 0)
+    iota(["CW"], T.CW[:], [[16, 16]], 0, 0)
+    iota(["CT0"], T.CT[:], [[32, 8], [0, 2]], 0, 0)
+    iota(["CY"], T.CY[:], [[1, 368]], -112, 0)
+    iota(["T128"], T.TK[:, 4096:4608], [[0, 512]], 128, 0)
+    fill(["T256"], T.TK[:, 4608:5120], 256.0)
+    cp(["OI"], ["OU"], T.OU[:, 0:56], T.OI[:, 0:56])
+    ts(["PC"], ["PI"], T.PI[:, 0:1], T.PC[:], 15, OP.bitwise_and)
+    ts(["PC"], ["PI1"], T.PI[:, 1:2], T.PC[:], 4, OP.arith_shift_right)
+    ts(["PI1"], ["PI2"], T.PI[:, 2:3], T.PI[:, 1:2], 1, OP.bitwise_and)
+    cp(["PI"], ["q"], T.PF[:, 0:1], T.PI[:, 0:1])
+    cp(["PI1"], ["g"], T.PF[:, 1:2], T.PI[:, 1:2])
+    cp(["PI2"], ["m1"], T.PF[:, 2:3], T.PI[:, 2:3])
+    ts(["OI2", "m1"], ["OU2"], T.OU[:, 56:72], T.OI[:, 56:72], T.PF[:, 2:3], OP.add)
+    ts(["q"], ["qn"], T.PF[:, 4:5], T.PF[:, 0:1], -1.0, OP.mult, -0.5, OP.add)
+    ts(["BK", "g"], ["TKS"], T.TK[:, 2048:2560], T.BK[:], T.PF[:, 1:2], OP.is_equal)
+    emit("G", ["T256"], ["TKB"], lambda e: e.affine_select(
+        T.TK[:, 2560:3072], T.TK[:, 4608:5120], [[0, 128], [-1, 4]], OP.is_gt, 0.0, 2, 0))
+    for i in (2, 3):
+        emit("G", ["TKS"], ["TKT%d" % i], lambda e, i=i: e.affine_select(
+            T.TK[:, 2048 + 512 * i:2560 + 512 * i], T.TK[:, 2048:2560], [[0, 128], [1, 4]], OP.is_equal, 0.0, -i, 0))
+    for b in range(4):
+        emit("G", ["T128"], ["TK%d" % b], lambda e, b=b: e.affine_select(
+            T.TK[:, 512 * b:512 * b + 512], T.TK[:, 4096:4608], [[-1, 128], [1000, 4]], OP.is_equal, 0.0, -1000 * b, 1))
+    ts(["q"], ["nq"], T.PF[:, 12:13], T.PF[:, 0:1], -1.0, OP.mult)
+    act(["IR", "nq"], ["RQ"], T.RQ[:], T.IR[:], AF.Identity, T.PF[:, 12:13])
+    act(["RQ"], ["BS"], T.BS[:], T.RQ[:], AF.Abs)
+    act(["BS"], ["ME"], T.ME[:], T.BS[:], AF.Relu, 1.0, -1.0)
+    act(["IR"], ["KP"], T.KP[:], T.IR[:], AF.Sign)
+    act(["RQ"], ["BE"], T.BE[:], T.RQ[:], AF.Sign, 0.5)
+    act(["BE"], ["BE"], T.BE[:], T.BE[:], AF.Relu)
+    act(["BE"], ["BS"], T.BS[:], T.BE[:], AF.Copy, 0.0, -2.0 ** 90)
+    act(["BE"], ["RQ"], T.RQ[:], T.BE[:], AF.Copy, 0.0, 512.0)
+    act(["ME"], ["EX"], T.EX[:], T.ME[:], AF.Copy, 0.0, -2.0 ** 20)
+    tt(["RQ", "EX"], ["EX"], T.EX[:], T.RQ[:], T.EX[:], OP.add)
+    act(["BE"], ["BE"], T.BE[:], T.BE[:], AF.Copy, 0.0, 2.0 ** 90)
+    act(["TI"], ["TR"], T.TR[:], T.TI[:], AF.Sign, 0.5, -1.0)
+    act(["TR"], ["TR"], T.TR[:], T.TR[:], AF.Relu)
+    ts(["q"], ["xq"], T.PF[:, 5:6], T.PF[:, 0:1], -512.0, OP.mult, 7680.0, OP.add)
+    ts(["xq"], ["nxq"], T.PF[:, 14:15], T.PF[:, 5:6], -1.0, OP.mult)
+    for i in range(4):
+        ts(["xq"], ["xq4"], T.PF[:, 8 + i:9 + i], T.PF[:, 5:6], -4.0, OP.mult, float(i), OP.add)
+    quant(["UT"], "U", 0, 128, T.UT[:, 0:512])
+    emit("V", ["U", "OU"], ["UPc"], lambda e: e.tensor_copy(
+        T.cUP[:, 0:384].bitcast(dt.uint32), T.cU[:, 0:128].bitcast(dt.uint32).indirect(T.OU[:, 0:24])))
+    emit("A", ["U", "OU"], ["UPs"], lambda e: e.activation(
+        T.sUP[:, 0:384], T.sU[:, 0:128].indirect(T.OU[:, 0:24]), AF.Copy))
+    UPK = ["UPc", "UPs"]
+    quant(["XT"], "X0", 0, 256, T.XT[:])
+    for a in range(4):
+        o, e = 1024 * a + 256 * a, 1024 * a + 4 * TILE_N[a]
+        fill(["CT2%d" % a], T.CT2[:, o:e], 0.0)
+        act(["CT2%d" % a], ["CT3%d" % a], T.CT2[:, 4096 + o:4096 + e], T.CT2[:, o:e])
+    fill(["AR"], T.AR[:], 0.0)
+    dma("S", "dPad", ["X0"], ["pad"], [(T.cL[:, 288:320].bitcast(dt.uint8), T.cX[:, 0:32].bitcast(dt.uint8)),
+                                       (T.sL[:, 288:320], T.sX[:, 0:32])])
+
+    ZC = ["CT%d%d" % (i, a) for i in (2, 3) for a in range(4)]
+
+    def late_constants():
+        for b in range(4):
+            quant(["TK%d" % b], "KR%d" % b, 0, 128, T.TK[:, 512 * b:512 * b + 512])
+
+    def birth_constants():
+        for i, k in enumerate(("KS", "KB", "KT", "KU")):
+            quant(["TKS", "TKB", "TKT2", "TKT3"], k, 0, 128, T.TK[:, 2048 + 512 * i:2560 + 512 * i])
+        ts(["CW", "xq"], ["CX"], T.CX[:], T.CW[:], T.PF[:, 5:6], OP.subtract)
+        ts(["CW", "xq"], ["CP"], T.W3[:, 16:32], T.CW[:], T.PF[:, 5:6], OP.add)
+        ts(["PC"], ["PI3"], T.PI[:, 3:4], T.PC[:], 31, OP.bitwise_and)
+        cp(["PI3"], ["x32"], T.PF[:, 6:7], T.PI[:, 3:4])
+        ts(["x32", "xq"], ["x32q"], T.PF[:, 7:8], T.PF[:, 6:7], T.PF[:, 5:6], OP.add)
+        ts(["CT0", "x32q"], ["CT"], T.CT[:], T.CT[:], T.PF[:, 7:8], OP.add)
+
+    def count_constants():
+        ts(["nq"], ["nq128"], T.PF[:, 13:14], T.PF[:, 12:13], -128.0, OP.add)
+        act(["CY", "nq128"], ["CB"], T.CB[:], T.CY[:], AF.Abs, T.PF[:, 13:14])
+        act(["CB"], ["CB"], T.CB[:], T.CB[:], AF.Relu, 512.0, -512.0)
+        act(["CY", "nq"], ["CY"], T.CY[:], T.CY[:], AF.Abs, T.PF[:, 12:13])
+        act(["CY"], ["CY"], T.CY[:], T.CY[:], AF.Relu, 1.0, -1.0)
+        tt(["CY", "CB"], ["CB"], T.CB[:], T.CB[:], T.CY[:], OP.add)
+        fill(["ON"], T.ON[:, 0:32], 1.0)
+        fill(["ZR"], T.ON[:, 32:288], 0.0)
+        fill(["CM6"], T.CM[:], 0.0)
+        fill(["Q4z"], T.QQ[:, 48:80], 0.0)
+        fill(["ETz"], T.ET[:, 384:512], 0.0)
+        fill(["RTz"], T.RT[:, 384:512], 0.0)
+        quant(["VTL"], "V", 0, 128, T.VTL[:])
+
+    ts(["CW", "q"], ["CW"], T.CW[:], T.CW[:], T.PF[:, 0:1], OP.add)
+    cp(["CW"], ["CL"], T.CL[:, 0:16], T.CW[:])
+    cp(["OL"], ["LW"], T.CL[:, 16:32], T.OL[:])
+    cp(["OL"], ["L16"], T.L16[:], T.OL[:])
+
+    BC, BC15, BC32 = T.OU[:, 24:40], T.OU[:, 40:56], T.OU[:, 56:72]
+    E15 = slice(15, 256, 16)
+    rid, pid = topo.addr(nxt)[0], topo.addr(nxt)[1]
+    mask = topo.mask(core, nxt)
+    n_eng = len(topo.engines(core, nxt))
+    n_arr = len(topo.engines(prv, core))
+    sent = [0]
+
+    def send(r, out, src, rsem):
+        def issue():
+            deps("G", r, [])
+            g.remote_dma(out, src, T.sem[rsem], T.sem.ls, pid, rid, mask)
+            sent[0] += n_eng
+        nodes.append(("G", r, ["snd" + rsem], issue, 0.7, 0.0))
+
+    pending = []
+
+    for t in range(ROUNDS):
+        X = "X%d" % t
+        XK = [X, X + "s"]
+        mm(XK + UPK, "P7", 256, "UP", 0, X, 0)
+        mm(XK + UPK, "P5", 128, X, 0, "UP", 256)
+        mm(XK + UPK, "P6", 128, X, 128, "UP", 256)
+        mm(XK + UPK, "P4", 256, "UP", 256, X, 0)
+        mm(XK + UPK, "P3", 256, "UP", 128, X, 0)
+        act(["P5"], ["SB0"], T.SB2[:, 0:1], T.P5[:, 0:1])
+        act(["P6"], ["SB1"], T.SB2[:, 1:2], T.P6[:, 0:1])
+        act(["SB0", "SB1"], ["DL"], T.DL[:, 0:2], T.SB2[:, 0:2], AF.Abs, 0.0, 1.25 * 2.0 ** -24)
+        tt(["P7", "ME"], ["MS"], T.MS[:, 0:256], T.P7[:, 0:256], T.ME[:], OP.mult)
+        if t == 0:
+            birth_constants()
+        act(["DL"], ["DL2"], T.DL[:, 2:4], T.DL[:, 0:2], AF.Identity, 2.0 ** -120)
+        for h in range(2):
+            act(["TR", "DL2", "SB0", "SB1"], ["TH%d" % h], T["TH%d" % h][:], T.TR[:], AF.Identity,
+                T.SB2[:, h:h + 1], T.DL[:, 2 + h:3 + h])
+        for f in pending[:2]:
+            f()
+        scan(["KP", "MS"], ["SWS"], T.SWS[:], T.KP[:], T.MS[:, 0:256])
+        tt(["P7", "BS"], ["SG"], T.SG[:], T.P7[:, 0:256], T.BS[:], OP.add)
+        ts(["P4", "SB0"], ["BTa"], T.BT[:, 512:1024:4], T.P4[:, 128:256], T.SB2[:, 0:1], OP.is_ge)
+        ts(["P4", "SB1"], ["BTb"], T.BT[:, 1:512:4], T.P4[:, 0:128], T.SB2[:, 1:2], OP.is_gt)
+        tt(["P3", "ME"], ["MSE"], T.MS[:, 256:512], T.P3[:, 0:256], T.ME[:], OP.mult)
+        tt(["SWS", "SG", "OU"], ["BTe"], T.BT[:, 2:1024:4], T.SWS[:].indirect(BC15), T.SG[:], OP.is_lt)
+        scan(["KP", "MSE"], ["SWE"], T.SWE[:], T.KP[:], T.MS[:, 256:512])
+        tt(["P3", "BE"], ["EG"], T.EG[:], T.P3[:, 0:256], T.BE[:], OP.add)
+        tt(["P4", "TH0"], ["BTc"], T.BT[:, 0:512:4], T.P4[:, 0:128], T.TH0[:], OP.is_ge)
+        tt(["P4", "TH1"], ["BTd"], T.BT[:, 513:1024:4], T.P4[:, 128:256], T.TH1[:], OP.is_ge)
+
+        tt(["SWE", "EG", "OU"], ["BTf"], T.BT[:, 3:1024:4], T.SWE[:].indirect(BC15), T.EG[:], OP.is_gt)
+
+        def pair(s, m):
+            bank, w, k, op = (("P7", T.SWS, "SWS", OP.is_gt), ("P3", T.SWE, "SWE", OP.is_lt))[s]
+            if m:
+                o, n = 4096 * s + 1024 * (m // 4), 64 * m
+                v = T.CT2[:, o + m % 4:o + n:4]
+                ts([bank, k] + ZC, ["ct%d.%d" % (s, m)], v, T[bank][:, 0:16 * m], w[:, 16 * m + 15:16 * m + 16], op)
+                j = m % 4
+                act(["ct%d.%d" % (s, m), "AR"], ["AR%d.%d" % (s, m), "AJ%d" % j], T.AJ[:, 256 * j:256 * j + 16 * m], v,
+                    AF.Copy, 0.0, 1.0, T.AR[:, 16 * s + m:16 * s + m + 1])
+
+        def pair_sum(s, a):
+            o, n, k, bank = 4096 * s + 1024 * a, TILE_N[a], "CD"[s] + str(a), ("P4", "P5")[s]
+            quant(["ct%d.%d" % (s, m) for m in range(4 * a, 4 * a + 4) if m] + ZC, k, 0, n, T.CT2[:, o:o + 4 * n])
+            mm([k, "KS"], bank, n, "KS", 0, k, 0, False, a == 3)
+
+        def row_sum(s):
+            scan(["KP", ("BTe", "BTf")[s]], ["RD%d" % s], T.RD[:, 256 * s:256 * s + 256], T.KP[:], T.BT[:, 2 + s:1024:4])
+            tt(["RD%d" % s, "AR"] + ["AR%d.%d" % (s, m) for m in range(1, 16)], ["RW%d" % s], T.RW[:, 16 * s:16 * s + 16],
+               T.RD[:, 256 * s + 15:256 * s + 256:16], T.AR[:, 16 * s:16 * s + 16], OP.add)
+
+        pair(0, 15)
+        quant(["BTa", "BTb", "BTc", "BTd", "BTe", "BTf"], "B", 0, 256, T.BT[:])
+        mm(["B", "KB"], "P6", 256, "KB", 0, "B", 0)
+        mm(["B", "KT"], "P4", 256, "KT", 0, "B", 0, True, False)
+        if t == 0:
+            late_constants()
+        for b in range(4):
+            mm(XK + ["KR%d" % b], ("P0", "P1", "P2", "P5")[b], 256, "KR%d" % b, 0, X, 0)
+        pair(0, 14)
+        tt(["P6", "ID"], ["V0"], T.VH[:, 1536:1792], T.P6[:, 0:256], T.ID[:], OP.add)
+        pair(0, 13)
+        pair(0, 12)
+        for m in range(11, 3, -1):
+            pair(0, m)
+        for f in pending[2:]:
+            f()
+        for m in range(3, 0, -1):
+            pair(0, m)
+        for a in range(4):
+            pair_sum(0, a)
+        if t == 0:
+            count_constants()
+        for i in range(6):
+            src, k = (T.VH[:, 1536:1792], "V0") if i == 0 else (T.VH[:, 256 * i - 256:256 * i], "VH%d" % (i - 1))
+            act([k, "L16"], ["VH%d" % i], T.VH[:, 256 * i:256 * i + 256], src.indirect(T.L16[:]),
+                AF.Identity, 65536.0)
+            if i == 0:
+                row_sum(0)
+                act(["RW0", "OU"], ["XR"], T.XR[:, 0:256], T.RW[:, 0:16].indirect(BC))
+        def half(b):
+            k = ("P0", "P1", "P2", "P5")[b]
+            act([k], ["FT%d" % b], T.FT[:, 256 * b:256 * b + 256], T[k][:, 0:256], AF.Copy, 0.0, 2.0 ** -8)
+            act([k], ["FU%d" % b], T.FU[:, 256 * b:256 * b + 256], T[k][:, 0:256], AF.Copy, 0.0, 2.0 ** -8)
+        half(3)
+        mm(["B", "KU"], "P5", 256, "KU", 0, "B", 0, True, False)
+        for m in range(15, 7, -1):
+            pair(1, m)
+        turn(["XR"], ["XS"], T.XR[:, 256:512], T.XR[:, 0:256])
+        turn(["P4"], ["TT"], T.VT[:, 1536:1792], T.P4[:, 0:256])
+        scan(["EX", "XS"], ["XE"], T.XE[:], T.EX[:], T.XR[:, 256:512], 0.0, OP.add, OP.max)
+        for m in range(7, 0, -1):
+            pair(1, m)
+            if m == 6:
+                tt(["TT", "CT"], ["T1a"], T.T1[:, 0:16], T.VT[:, 1536:1792:16], T.CT[:], OP.add)
+            if m == 4:
+                tt(["T1a", "XE"], ["T1b"], T.T1[:, 16:32], T.T1[:, 0:16], T.XE[:, E15], OP.subtract)
+                for i in range(5):
+                    act(["T1b"], ["T6%d" % i], T.T6[:, 16 * i:16 * i + 16], T.T1[:, 16:32], AF.Identity,
+                        255.5 + 65536.0 * (i + 1), 256.0)
+        for b in range(3):
+            half(b)
+        for a in range(4):
+            pair_sum(1, a)
+        for i in range(6):
+            turn(["VH%d" % i], ["VT%d" % i], T.VT[:, 256 * i:256 * i + 256], T.VH[:, 256 * i:256 * i + 256])
+        VTK = ["VT%d" % i for i in range(6)]
+        tt(VTK[:5] + ["T6%d" % i for i in range(5)] + ["CM6"], ["CM"], T.CM[:, 0:80], T.VT[:, 0:1280:16], T.T6[:], OP.is_gt)
+        act(["CM", "CM6"], ["XXa"], T.XX[:, 0:96], T.CM[:], AF.Copy, 0.0, 2.0 ** 20)
+        tt(["XXa"] + VTK, ["XXb"], T.XX[:, 96:192], T.XX[:, 0:96], T.VT[:, 0:1536:16], OP.add)
+        tt(["XXb"], ["MNa"], T.MN[:, 0:48], T.XX[:, 96:144], T.XX[:, 144:192], OP.min)
+        tt(["MNa"], ["MNb"], T.MN[:, 48:64], T.MN[:, 0:16], T.MN[:, 16:32], OP.min)
+        tt(["MNa", "MNb"], ["RI0"], T.RI[:, 0:16], T.MN[:, 48:64], T.MN[:, 32:48], OP.min)
+        ts(["RI0"], ["RI1"], T.RI[:, 16:32], T.RI[:, 0:16], 255, OP.bitwise_and)
+        cp(["RI1"], ["RI2"], T.EP[:, 32:48], T.RI[:, 16:32])
+        act(["RI2", "OU"], ["RX"], T.RX[:, 0:256], T.EP[:, 32:48].indirect(BC))
+        row_sum(1)
+        turn(["RX"], ["RY"], T.RX[:, 256:512], T.RX[:, 0:256])
+        scan(["EX", "RY"], ["RS"], T.RS[:], T.EX[:], T.RX[:, 256:512], 0.0, OP.add, OP.max)
+        ts(["RS", "xq"], ["R16"], T.R16[:], T.RS[:, E15], T.PF[:, 5:6], OP.subtract)
+        for z in range(8):
+            act(["CB", "R16"], ["CJ%d" % (z % 2), "CA%d" % z], T.CJ[:, 256 * (z % 2):256 * (z % 2) + 256], T.CB[:, 112 - 16 * z:368 - 16 * z].indirect(T.R16[:]),
+                AF.Copy, 0.0, 1.0, T.CA[:, z:z + 1])
+        scan(["EX", "P5"], ["EC"], T.EC[:], T.EX[:], T.P5[:, 0:256], 0.0, OP.add, OP.max)
+        tt(["CX", "RW1"], ["EPa"], T.EP[:, 0:16], T.CX[:], T.RW[:, 16:32], OP.subtract)
+        tt(["EPa", "EC"], ["EP"], T.EP[:, 16:32], T.EP[:, 0:16], T.EC[:, E15], OP.add)
+        cp(["EP"], ["EP16"], T.EP16[:], T.EP[:, 16:32])
+        cp(["ID", "EP16"], ["EF"], T.EF[:, 0:256].indirect(T.EP16[:]), T.ID[:])
+        for b in range(4):
+            f = T.FT[:, 256 * b:256 * b + 256]
+            tt(["FT%d" % b, "FU%d" % b, "R16"], ["Z%d" % b], T.Z[:, b:1024:4], f.indirect(T.R16[:]),
+               T.FU[:, 256 * b:256 * b + 256], OP.add)
+            if b == 1:
+                scan(["EX", "EF"], ["ES"], T.ES[:], T.EX[:, 0:96], T.EF[:, 0:96], 0.0, OP.add, OP.max)
+            if b == 2:
+                for i in range(4):
+                    ts(["ES", "xq4"], ["EO%d" % i], T.EO[:, 8 * i:8 * i + 6], T.ES[:, 15:96:16], 4.0, OP.mult,
+                       T.PF[:, 8 + i:9 + i], OP.add)
+        ZK = ["Z0", "Z1", "Z2", "Z3"]
+        for b in range(4):
+            (cp, cp, act, act)[b](ZK + ["EO%d" % b], ["ET%d" % b], T.ET[:, b:384:4], T.Z[:].indirect(T.EO[:, 8 * b:8 * b + 6]))
+        act(["EF"], ["PKa"], T.PK[:, 0:48], T.EF[:, 48:96], AF.Copy, 0.0, 256.0)
+        lo = KEEP * (ROUNDS - 1 - t)
+
+        def send_columns():
+            quant(["ET0", "ET1", "ET2", "ET3", "ETz"], "E%d" % t, 0, 128, T.ET[:])
+            send(["E%d" % t], T.cL[:, lo:lo + KEEP].bitcast(dt.uint8),
+                 T.cE[:, 128 * t:128 * t + KEEP].bitcast(dt.uint8), "aC%d" % t)
+            send(["E%d" % t], T.sL[:, lo:lo + KEEP], T.sE[:, 128 * t:128 * t + KEEP], "aC%d" % t)
+            send(["LS%d" % t], T.LL[:, 48 * t:48 * t + 48], T.LS[:, 48 * t:48 * t + 48], "aL%d" % t)
+            arrival("L%d" % t, ["sndaC%d" % t], ("aC%d" % t, 2 * n_arr, {}))
+            arrival("LL%d" % t, ["sndaL%d" % t], ("aL%d" % t, n_arr, {}))
+        tt(["PKa", "EF"], ["PKb"], T.PK[:, 48:96], T.PK[:, 0:48], T.EF[:, 0:48], OP.add)
+        quant(ZK, "P", 0, 256, T.Z[:])
+        cp(["PKb"], ["LS%d" % t], T.LS[:, 48 * t:48 * t + 48], T.PK[:, 48:96])
+        cp(["CA%d" % z for z in range(8)], ["CI0"], T.CI[:, 0:8], T.CA[:])
+        ts(["CI0"], ["CI1"], T.CI[:, 8:16], T.CI[:, 0:8], 511, OP.bitwise_and)
+        ts(["CI0"], ["CI2"], T.CI[:, 16:24], T.CI[:, 0:8], 9, OP.arith_shift_right)
+        Q1, Q2, Q3, Q4, Q5, Q6, Q7 = [(a, a + 32) for a in (0, 16, 32, 48, 80, 112, 144)]
+
+        def qq(q, a=0, b=32, step=1, p=0, np_=128):
+            return T.QQ[p:p + np_, q[0] + a:q[0] + b:step]
+        cp(["CI1", "CI2"], ["Q1"], qq(Q1, 0, 16, 1, 0, 64), T.CI[64:128, 8:24])
+        cp(["CI1", "CI2"], ["Q1b"], qq(Q1, 0, 16, 1, 64, 64), T.CI[0:64, 8:24])
+        tt(["CI1", "CI2", "Q1", "Q1b"], ["Q2"], qq(Q2, 0, 16), T.CI[:, 8:24], qq(Q1, 0, 16), OP.add)
+        for a in range(4):
+            b = a ^ 1
+            (cp, cp, act, act)[a](["Q2"], ["Q3%d" % a], qq(Q3, 0, 16, 1, 32 * a, 32), qq(Q2, 0, 16, 1, 32 * b, 32))
+        tt(["Q2", "Q30", "Q31", "Q32", "Q33", "Q4z"], ["Q4"], qq(Q4, 0, 16), qq(Q2, 0, 16), qq(Q3, 0, 16), OP.add)
+        turn(["Q4", "Q4z"], ["Q5"], qq(Q5), qq(Q4))
+        tt(["Q5"], ["Q6"], qq(Q6, 0, 16), qq(Q5, 0, 16), qq(Q5, 16, 32), OP.add)
+        tt(["Q5"], ["Q6b"], qq(Q6, 16, 32), qq(Q5, 0, 16), qq(Q5, 16, 32), OP.add)
+        turn(["Q6", "Q6b"], ["Q7"], qq(Q7), qq(Q6))
+        send_columns()
+        act(["Q7", "OU2"], ["RP"], T.RP[:], qq(Q7).indirect(BC32))
+        turn(["RP"], ["TO"], T.TO[:], T.RP[:])
+        act(["TO", "qn"], ["AJ0", "AC"], T.AJ[:, 0:256], T.TO[:], AF.Sign, T.PF[:, 4:5], 1.0, T.SC[:, 0:1])
+        ts(["AC"], ["F1"], T.SC[:, 2:3], T.SC[:, 0:1], 64.0, OP.is_le)
+        ts(["ON", "F1"], ["FB"], T.FB[:, 0:32], T.ON[:, 0:32], T.SC[:, 2:3], OP.mult, -15.5 / 16, OP.add)
+        turn(["FB"], ["FX"], T.FB[:, 64:96], T.FB[:, 0:32])
+        emit("V", ["FX"], ["SF"], lambda e: e.tensor_reduce(T.SC[:, 4:5], T.FB[:, 64:80], AxisListType.X, OP.add))
+        act(["TO", "SF"], ["AJ1", "NP"], T.AJ[:, 256:512], T.TO[:], AF.Sign, T.SC[:, 4:5], 1.0, T.SC[:, 5:6])
+        ts(["TO", "SF"], ["EQM"], T.EQM[:], T.TO[:], T.SC[:, 4:5], OP.add, 0.5, OP.is_equal)
+        scan(["EQM", "ZR"], ["CU"], T.CU[:], T.EQM[:], T.ON[:, 32:288], 32.0, OP.add, OP.max)
+        ts(["CU", "NP"], ["OV"], T.OV[:], T.CU[:], 2.0, OP.mult, T.SC[:, 5:6], OP.is_gt)
+        tt(["TO", "OV"], ["Zx"], T.Z2[:], T.TO[:], T.OV[:], OP.add)
+        ts(["Zx", "SF"], ["GN"], T.GN[:], T.Z2[:], T.SC[:, 4:5], OP.add, 0.5, OP.is_le)
+        scan(["GN", "ZR"], ["GS"], T.GS[:], T.GN[:], T.ON[:, 32:288], 255.0, OP.add, OP.max)
+        scan(["GS", "GN"], ["M1"], T.M1[:], T.GS[:], T.GN[:], 0.0, OP.max, OP.mult)
+        tt(["M1", "ID"], ["Y0"], T.Y0[:], T.M1[:], T.ID[:], OP.max)
+        scan(["EX", "M1"], ["NSx"], T.NS[:], T.EX[:], T.M1[:], 0.0, OP.add, OP.max)
+        tt(["NSx", "CP"], ["NSw"], T.W3[:, 0:16], T.NS[:, E15], T.W3[:, 16:32], OP.max)
+        ts(["NSw", "xq"], ["NI16"], T.NI16[:], T.W3[:, 0:16], T.PF[:, 5:6], OP.subtract)
+        act(["NSw", "nxq"], ["NS"], T.CL[:, 32:48], T.W3[:, 0:16], AF.Identity, T.PF[:, 14:15])
+        for b in range(4):
+            k = PS[b]
+            mm(["L%d" % t, "pad", "W"], k, 128, "W", 128 * b, "L", lo, True, False)
+            mm(["L%d" % t, "pad", "KR%d" % b], k, 128, "KR%d" % b, 0, "L", lo, False, True)
+        for b in range(2):
+            act([PS[b], "RTz"], ["RT%d" % b], T.RT[:, b:384:4], T[PS[b]][:, 0:96], AF.Copy, 0.0, 2.0 ** -7)
+        for b in range(2, 4):
+            ts([PS[b], "RTz"], ["RT%d" % b], T.RT[:, b:384:4], T[PS[b]][:, 0:96], 2.0 ** -7, OP.mult)
+        quant(["RT0", "RT1", "RT2", "RT3", "RTz"], "P", 256, 384, T.RT[:])
+        XN = "X%d" % (t + 1)
+        emit("V", ["P", "Pb", "NI16"], [XN], lambda e, t=t: e.tensor_copy(
+            T.cX[:, 256 * t + 256:256 * t + 512].bitcast(dt.uint32), T.cP[:, :].bitcast(dt.uint32).indirect(T.NI16[:])))
+        emit("A", ["P", "Pb", "NI16"], [XN + "s"], lambda e, t=t: e.activation(
+            T.sX[:, 256 * t + 256:256 * t + 512], T.sP[:, :].indirect(T.NI16[:]), AF.Copy))
+        act(["NSw", "nxq"], ["NS2"], T.CL[:, 48:64], T.W3[:, 0:16], AF.Identity, T.PF[:, 14:15])
+        ts(["NS", "NS2"], ["GW"], T.SM[:, 0:32], T.CL[:, 32:64], 256.0, OP.is_ge)
+        tt(["NS", "LW", "CL"], ["D1"], T.SM[:, 32:64], T.CL[:, 16:48], T.CL[:, 0:32], OP.subtract)
+        tt(["GW", "D1"], ["D2"], T.SM[:, 64:96], T.SM[:, 0:32], T.SM[:, 32:64], OP.mult)
+        tt(["D2", "LW", "CL"], ["D3"], T.SM[:, 96:128], T.SM[:, 64:96], T.CL[:, 0:32], OP.add)
+        cp(["D3"], ["M16"], T.M16[:], T.SM[:, 96:128])
+
+        def chain(t=t):
+            src, k = T.Y0, "Y0"
+            for i in range(5):
+                dst, kd = ((T.YA, "YA"), (T.YB, "YB"))[i % 2] if i < 4 else (T.YX, "YX")
+                act([k, "M16"], [kd], dst[:, 0:256], src[:, 0:256].indirect(T.M16[:, 0:16]))
+                src, k = dst, kd
+            act(["YX", "YXe", "M16"], ["M1"], T.M1[:], T.YX[:].indirect(T.M16[:, 16:32]))
+
+        def unpack(t=t):
+            LL = "LL%d" % t
+            cp([LL], ["LI0"], T.LI[:, 0:48], T.LL[:, 48 * t:48 * t + 48])
+            ts(["LI0"], ["LI1"], T.LI[:, 48:96], T.LI[:, 0:48], 255, OP.bitwise_and)
+            ts(["LI0"], ["LI2"], T.LI[:, 96:144], T.LI[:, 0:48], 8, OP.arith_shift_right)
+            cp(["LI1", "LI2"], ["YXe"], T.YX[:, 256:352], T.LI[:, 48:144])
+
+        def relink():
+            scan(["EX", "M1"], ["NRx"], T.NR[:], T.EX[:], T.M1[:], 0.0, OP.add, OP.max)
+            r = T.SM[:, 144:160]
+            sm = [T.SM[:, 160 + 16 * i:176 + 16 * i] for i in range(3)]
+            act(["NRx", "nxq"], ["NR"], r, T.NR[:, E15], AF.Identity, T.PF[:, 14:15])
+            ts(["NR"], ["FL"], sm[0], r, 256.0, OP.is_ge)
+            tt(["CW", "NR"], ["G1"], sm[1], T.CW[:], r, OP.subtract)
+            tt(["FL", "G1"], ["G2"], sm[2], sm[0], sm[1], OP.mult)
+            tt(["G2", "NR"], ["LW"], T.CL[:, 16:32], sm[2], r, OP.add)
+            cp(["LW"], ["L16"], T.L16[:], T.CL[:, 16:32])
+        pending = [unpack, chain, relink]
+
+    mm(["V", "X3", "X3s"], "P7", 256, "V", 0, "X3", 0)
+    dma("S", "dOc", ["X3", "X3s"], ["oc"], [(T.oc[:, :], T.cX[:, 768:1024].bitcast(dt.uint8))] + [
+        (T.osc[4 * k:4 * k + 4, :], T.sX[32 * k:32 * k + 4, 768:1024]) for k in range(4)])
+    pending[0]()
+    pending[1]()
+    cp(["P7"], ["YO"], T.YO[:], T.P7[:, 0:256])
+    dma("S", "dY", ["YO"], ["y"], [(T.y[:, :], T.YO[:])])
+    ts(["M1"], ["GS"], T.GS[:], T.M1[:], 256.0, OP.is_ge)
+    tt(["ID", "M1"], ["NRx"], T.NR[:], T.ID[:], T.M1[:], OP.subtract)
+    tt(["GS", "NRx"], ["Y0"], T.Y0[:], T.GS[:], T.NR[:], OP.mult)
+    tt(["Y0", "M1"], ["NSx", "NS"], T.NS[:], T.Y0[:], T.M1[:], OP.add)
+    dma("S", "dLk", ["NS"], ["lk"], [(T.lk[:, :], T.NS[0:128:16, :])])
+    schedule()
+    for s in cnt:
+        if known["S"].get(s, 0) < cnt[s]:
+            g.sync.wait_ge(T.sem[s], cnt[s])
+    g.wait_ge(T.sem.ls, sent[0])

@@ -1,5 +1,3 @@
-import numpy as np
-from concourse.bass import DstId, RemoteDMATransfer
 from concourse.mybir import dt, AluOpType, AxisListType, ActivationFunctionType
 
 OP = AluOpType
@@ -21,60 +19,40 @@ def _q(**widths):
         SCRATCH["s" + name] = ("sbuf", [128, widths[name]], U8)
 
 
+TILE_N = (256, 192, 128, 128)
+TILE_O = [sum(TILE_N[:a]) for a in range(5)]
 _sb(B, XT=1024, UT=512, VTL=512)
-_sb(I, OL=16, PC=1, PI=4, OI=72, RI=32, CI=24, LI=144)
+_sb(I, OL=16, PC=1, PI=8, OI=48, CI=24, LI=144, I0=112, I1=120)
 _q(W=512, U=128, UP=384, V=128, X=1024, L=320, P=384, E=384)
-_q(K=1024)
-_q(C=1664)
-_sb(B, TK=5120)
-_sb(F, IR=256, ID=256, TI=128, BK=512, PF=16, RQ=256, BS=256, BE=256, TR=128, CY=368, CB=368, CW=16, CX=16, CT=16)
+_q(K=768)
+_q(C=256 + 2 * TILE_O[4])
+_sb(B, TK=3584, IR=256, I4=96, TI=128, BK=512, NB=256, RS=512, RC=256, EX=256, EB=256, E4=96, ET0=512, TR=128)
+_sb(B, C64=32, ZR=256, PD2=96)
+_sb(F, ID=256, PF=24, CY=368, CB=368, CW=32, NN=8, CP=16, C8=128, TMP=8)
 _sb(U, OU=72)
-_sb(B, ME=256, KP=256, ON=288, EX=256)
-_sb(F, MS=512, SWS=256, SG=256, SWE=256, EG=256, SB2=2, DL=4, TH0=128, TH1=128)
-_sb(B, BT=1024, CT2=8192, AJ=1024)
-_sb(F, VH=1792, VT=1792, T6=80, CM=96, XX=192, MN=80, T1=32)
+_sb(F, SG=512, SW=512, SB2=2, DL=2, TH0=128, TH1=128, AR=32, RW=32, EC=512, TE=16, EP=16)
+_sb(B, BT=1024, CT=8 * TILE_O[4], AJ=1024, RD=512)
+_sb(F, LF=256, VH=1536, VT=1888, D7=112, CM=112, HR=112, D8=128, G8=128, HL=128)
 _sb(B, FT=1024, FU=1024, Z=1024, ET=512, RT=512)
-_sb(F, AR=32, RW=32, EC=256, EP=48, EF=256, PK=96)
-_sb(U, EP16=16, EO=32, LS=144, LL=144, R16=16, NI16=16, M16=32, L16=16)
-_sb(B, RD=512, XR=512, RX=512)
-_sb(F, XE=256, ES=96, RS=256)
-_sb(F, CA=8, CJ=512, CF=16, QQ=176, W3=32)
-_sb(B, RP=256, TO=256, FB=128, EQM=256, CU=256, OV=256, Z2=256, GN=256)
-_sb(F, SC=16, GS=256, M1=256, Y0=256, NS=256, SM=208, YA=256, YB=256, YX=352, NR=256, CL=64, YO=256)
-for _i in range(8):
-    SCRATCH["P%d" % _i] = ("psum", [128, 512], F)
-PS = ["P%d" % i for i in range(8)]
-PLACE = {"B": ("C", 0)}
-TILE_N = (128, 128, 192, 256)
+_sb(F, EF=256, ES=96, PK=96)
+_sb(U, EP16=16, EO=24, LS=144, LL=144, R16=16, NI16=16, L16=16, H16=96)
+_sb(F, CA=8, CJ=512, QQ=128, SC=8, XS=16, HD=64, HO=32, EW=256, EQ=256, YO=256, LO=256)
+_sb(B, RP=256, TO=256, FB=128, LT=256, LE=256, AA=256, GS=272, GN=256, P1=256, P0=256, FL=1536, FP=2048, YX=352)
+for _k in ("PA", "PB", "PC_", "Q0", "Q1", "Q2"):
+    SCRATCH[_k] = ("psum", [128, 512], F)
+SCRATCH["PD"] = ("psum", [128, 1024], F)
+BANK = {"PA": ("PA", 0), "PB": ("PB", 0), "PC_": ("PC_", 0), "Q0": ("Q0", 0), "Q1": ("Q1", 0), "Q2": ("Q2", 0),
+        "PD0": ("PD", 0), "PD1": ("PD", 512)}
+PLACE = {"B": ("C", 0), "KS": ("K", 512), "KB": ("K", 640), "Pb": ("P", 256)}
 for _i in range(4):
     PLACE["X%d" % _i] = ("X", 256 * _i)
     PLACE["KR%d" % _i] = ("K", 128 * _i)
-    PLACE["C%d" % _i] = ("C", 256 + sum(TILE_N[:_i]))
-    PLACE["D%d" % _i] = ("C", 960 + sum(TILE_N[:_i]))
-for _i in range(3):
+    PLACE["C0%d" % _i] = ("C", 256 + TILE_O[_i])
+    PLACE["C1%d" % _i] = ("C", 256 + TILE_O[4] + TILE_O[_i])
     PLACE["E%d" % _i] = ("E", 128 * _i)
-for _i, _k in enumerate(("KS", "KB", "KT", "KU")):
-    PLACE[_k] = ("K", 512 + 128 * _i)
-WAKE, SLACK, FLIGHT = 0.3, 0.25, 4.5
-LONG = {"MS": .25, "MSE": .25, "SWS": .25, "SWE": .25, "SG": .25, "EG": .25, "V0": .25, "TT": .25, "VT": .25, "XE": .25,
-        "EC": .25, "RS": .25, "NSx": .25, "GS": .25, "NRx": .25, "BTe": .37, "BTf": .37, "Z": .37, "BTa": .13, "BTb": .13,
-        "BTc": .13, "BTd": .13, "EF": .8, "XS": .13, "RY": .13, "TO": .13, "EQM": .13, "CU": .13, "OV": .13, "GN": .13,
-        "Zx": .45, "Y0": .45, "RD": .13, "FU": .45, "X": .36, "Xs": .36, "VH": .37, "CJ": .39, "CA": .39, "FT": .23,
-        "XR": .36, "RX": .36, "ET": .2, "RP": .36, "YA": .36, "YB": .36, "YX": .36, "M": .3, "TH": .13, "AC": .25,
-        "P": .24, "Pb": .13, "B": .24, "C": .17, "D": .17, "E": .13, "RT": .1, "TKS": .45, "TKB": 1.2, "TKT": 1.2, "TK": 1.2,
-        "IR": .6, "ID": .6, "BK": 1.0, "CY": .8, "RQ": .23, "ME": .23, "KP": .23, "BS": .23, "BE": .23, "EX": .3, "CB": .3}
+CYCLE, WAKE, SLACK, FLIGHT, JUMP, STREW, SEND = 0.00088, 0.2, 0.15, 3.5, 1.5, 3.5, 0.7
 
-
-def duration(q, key):
-    if q == "P":
-        return 0.2
-    if q == "G" and key[:3] == "snd":
-        return 0.7
-    if key[:2] == "ct" or key[:2] == "AR" and "." in key:
-        return 0.02 + 0.00083 * max(64, 16 * int(key.split(".")[1]))
-    return LONG.get(key.rstrip("0123456789s") or key, LONG.get(key.rstrip("0123456789"), 0.075))
-
-SEMAPHORES = ["sV", "sA", "sP", "sG", "dX", "dU", "dO", "dW", "dVV", "dPad", "dY", "dLk", "dOc", "ls",
+SEMAPHORES = ["sV", "sA", "sP", "sG", "dX", "dU", "dO", "dW", "dVV", "dPad", "dF", "dY", "dLk", "dOc", "ls",
               "aC0", "aC1", "aC2", "aL0", "aL1", "aL2"]
 
 
@@ -102,7 +80,7 @@ def rank_program(g, core, T, topo):
         for k in r:
             if k in lastw and not (q == "P" and lastw[k][0] == "sP"):
                 toks.append(lastw[k])
-            if k in PS:
+            if k in BANK:
                 toks += [t for s, t in readers.get(k, {}).items() if s != me]
         for k in w:
             if k in lastw and not (q == "P" and lastw[k][0] == "sP"):
@@ -119,7 +97,7 @@ def rank_program(g, core, T, topo):
 
     nodes = []
 
-    def emit(q, r, w, fn):
+    def emit(q, r, w, fn, time, alone=False):
         def issue():
             deps(q, r, w)
             s = own[q]
@@ -128,7 +106,9 @@ def rank_program(g, core, T, topo):
             clk = dict(known[q])
             clk[s] = cnt[s]
             done((s, cnt[s], clk), r, w)
-        nodes.append((q, r, w, issue, duration(q, w[0]), 0.0))
+            if alone:
+                sync(q, [(s, cnt[s], clk)])
+        nodes.append((q, r, w, issue, time, -WAKE if alone else 0.0))
 
     def dma(q, s, r, w, pairs):
         def issue():
@@ -137,7 +117,7 @@ def rank_program(g, core, T, topo):
                 eng[q].dma_start(o, i).then_inc(T.sem[s], 16)
                 cnt[s] = cnt.get(s, 0) + 16
             done((s, cnt[s], dict(known[q])), r, w)
-        nodes.append((q, r, w, issue, 0.1, 2.0))
+        nodes.append((q, r, w, issue, 0.1, 2.5))
 
     def arrival(key, r, tok):
         nodes.append(("R", r, [key], lambda: done(tok, [], [key]), 0.0, FLIGHT))
@@ -155,7 +135,7 @@ def rank_program(g, core, T, topo):
             for k in r:
                 if k in wr:
                     edge(wr[k], i, 0.0 if q == "P" and nodes[wr[k]][0] == "P" else WAKE)
-                if k in PS:
+                if k in BANK:
                     for j in rd.get(k, []):
                         if nodes[j][0] != q:
                             edge(j, i, WAKE)
@@ -188,56 +168,74 @@ def rank_program(g, core, T, topo):
             end = at + nodes[i][4]
             free[nodes[i][0]] = end
             for j, lag in succ[i]:
-                ready[j] = max(ready[j], (at if lag == 0.0 and nodes[j][0] == nodes[i][0] else end + nodes[i][5]) + lag)
+                ready[j] = max(ready[j], end + nodes[i][5] + lag)
                 left[j] -= 1
                 if not left[j]:
                     todo.append(j)
 
-    def tt(r, w, out, a, b, op):
-        emit("V", r, w, lambda e: e.tensor_tensor(out, a, b, op))
+    def cyc(n):
+        return CYCLE * max(64, n)
 
-    def ts(r, w, out, a, s1, o1, s2=None, o2=None):
+    def tt(r, w, out, a, b, op, n=64):
+        emit("V", r, w, lambda e: e.tensor_tensor(out, a, b, op), cyc(n))
+
+    def across(r, w, out, a, b):
+        emit("V", r, w, lambda e: e.tensor_tensor(out, a, b, OP.add), cyc(64) + WAKE, True)
+
+    def ts(r, w, out, a, s1, o1, s2=None, o2=None, n=64):
         if o2 is None:
-            emit("V", r, w, lambda e: e.tensor_scalar(out, a, s1, None, o1))
+            emit("V", r, w, lambda e: e.tensor_scalar(out, a, s1, None, o1), cyc(n))
         else:
-            emit("V", r, w, lambda e: e.tensor_scalar(out, a, s1, s2, o1, o2))
+            emit("V", r, w, lambda e: e.tensor_scalar(out, a, s1, s2, o1, o2), cyc(n))
 
-    def cp(r, w, out, a):
-        emit("V", r, w, lambda e: e.tensor_copy(out, a))
+    def cp(r, w, out, a, n=64):
+        emit("V", r, w, lambda e: e.tensor_copy(out, a), cyc(n))
 
-    def scan(r, w, out, d0, d1, init=0.0, o0=OP.mult, o1=OP.add):
-        emit("V", r, w, lambda e: e.tensor_tensor_scan(out, d0, d1, init, o0, o1))
+    def scan(r, w, out, d0, d1, init, o0, o1, n=64):
+        emit("V", r, w, lambda e: e.tensor_tensor_scan(out, d0, d1, init, o0, o1), cyc(n))
 
-    def turn(r, w, out, a):
-        emit("V", r, w, lambda e: e.transpose(out, a))
+    def turn(r, w, out, a, n=64):
+        emit("V", r, w, lambda e: e.transpose(out, a), cyc(n))
 
-    def fill(w, ap, x):
-        emit("V", [], w, lambda e: e.memset(ap, x))
+    def fill(w, ap, x, n=64):
+        emit("V", [], w, lambda e: e.memset(ap, x), cyc(n))
 
-    def quant(r, name, c0, c1, tile):
+    def quant(r, name, n, tile):
         k, o = PLACE.get(name, (name, 0))
-        emit("V", r, [name if c0 == 0 else name + "b"],
-             lambda e: e.quantize_mx(T["c" + k][:, o + c0:o + c1], T["s" + k][:, o + c0:o + c1], tile))
+        emit("V", r, [name], lambda e: e.quantize_mx(T["c" + k][:, o:o + n], T["s" + k][:, o:o + n], tile), CYCLE * (16 + 1.06 * n))
 
-    def act(r, w, out, a, fn=AF.Copy, bias=0.0, scale=1.0, acc=None):
+    def act(r, w, out, a, fn=AF.Copy, bias=0.0, scale=1.0, acc=None, n=64):
         if acc is None:
-            emit("A", r, w, lambda e: e.activation(out, a, fn, bias, scale))
+            emit("A", r, w, lambda e: e.activation(out, a, fn, bias, scale), cyc(n))
         else:
-            emit("A", r, w, lambda e: e.activation(out, a, fn, bias, scale, accum_out=acc))
+            emit("A", r, w, lambda e: e.activation(out, a, fn, bias, scale, accum_out=acc), cyc(n) + 0.02)
+
+    def far(n):
+        return 70 + JUMP * n
+
+    def ps(bank, a, b, step=1):
+        return T[BANK[bank][0]][:, BANK[bank][1] + a:BANK[bank][1] + b:step]
 
     def mm(r, bank, n, L, l0, R, r0, start=True, stop=True):
         L, lo_ = PLACE.get(L, (L, 0))
         R, ro_ = PLACE.get(R, (R, 0))
         l0, r0 = l0 + lo_, r0 + ro_
+        o = BANK[bank][1]
         emit("P", r, [bank], lambda e: e.matmul_mx(
-            T[bank][:, 0:n], T["c" + L][:, l0:l0 + 128], T["s" + L][:, l0:l0 + 128],
-            T["c" + R][:, r0:r0 + n], T["s" + R][:, r0:r0 + n], start, stop))
+            T[BANK[bank][0]][:, o:o + n], T["c" + L][:, l0:l0 + 128], T["s" + L][:, l0:l0 + 128],
+            T["c" + R][:, r0:r0 + n], T["s" + R][:, r0:r0 + n], start, stop), 0.00125 * (n + 16))
 
-    def iota(w, out, pattern, base, cm):
-        emit("G", [], w, lambda e: e.iota(out, pattern, base, cm, allow_small_or_imprecise_dtypes=True))
+    def iota(w, out, pattern, base, cm, n, whole=False):
+        if whole:
+            emit("G", [], w, lambda e: e.iota(out, pattern, base, cm), 0.13 + 2 * n * CYCLE)
+        else:
+            emit("G", [], w, lambda e: e.iota(out, pattern, base, cm, allow_small_or_imprecise_dtypes=True), 0.13 + 2 * n * CYCLE)
 
-    def iotai(w, out, pattern, base, cm):
-        emit("G", [], w, lambda e: e.iota(out, pattern, base, cm))
+    def pick(r, w, out, row, n=256):
+        scan(r + ["EX"], w, out, T.EX[:], row, 0.0, OP.add, OP.max, n)
+
+    def pick2(r, w, out, row):
+        scan(r + ["EB"], w, out, T.EB[:], row, 0.0, OP.add, OP.max, 128)
 
     dma("S", "dX", [], ["XT"], [(T.XT[:], T.x[:])])
     dma("A", "dU", [], ["UT"], [(T.UT[:], T.u[:])])
@@ -245,110 +243,131 @@ def rank_program(g, core, T, topo):
     dma("A", "dW", [], ["W"], [(T.cW[:].bitcast(dt.uint8), T.wc[:]), (T.sW[:], T.ws[:])])
     dma("S", "dVV", [], ["VTL"], [(T.VTL[:], T.v[:])])
 
-    iotai(["PC"], T.PC[:], [[0, 1]], 0, 1)
-    iotai(["OI"], T.OI[:, 0:8], [[16, 8]], 0, 0)
-    iotai(["OI"], T.OI[:, 8:16], [[16, 8]], 1, 0)
-    iotai(["OI"], T.OI[:, 16:24], [[0, 8]], 8, 0)
-    iotai(["OI"], T.OI[:, 24:40], [[1, 16]], 0, 0)
-    iotai(["OI"], T.OI[:, 40:56], [[16, 16]], 15, 0)
-    iotai(["OI2"], T.OI[:, 56:72], [[2, 8], [0, 2]], 0, 0)
-    iota(["IR"], T.IR[:], [[0, 16], [1, 16]], 0, 0)
-    iota(["TI"], T.TI[:], [[1, 128]], 0, -1)
-    iota(["ID"], T.ID[:], [[1, 256]], 0, 0)
-    iota(["BK"], T.BK[:], [[1, 8], [0, 64]], 0, 0)
-    iota(["CW"], T.CW[:], [[16, 16]], 0, 0)
-    iota(["CT0"], T.CT[:], [[32, 8], [0, 2]], 0, 0)
-    iota(["CY"], T.CY[:], [[1, 368]], -112, 0)
-    iota(["T128"], T.TK[:, 4096:4608], [[0, 512]], 128, 0)
-    fill(["T256"], T.TK[:, 4608:5120], 256.0)
-    cp(["OI"], ["OU"], T.OU[:, 0:56], T.OI[:, 0:56])
-    ts(["PC"], ["PI"], T.PI[:, 0:1], T.PC[:], 15, OP.bitwise_and)
-    ts(["PC"], ["PI1"], T.PI[:, 1:2], T.PC[:], 4, OP.arith_shift_right)
-    ts(["PI1"], ["PI2"], T.PI[:, 2:3], T.PI[:, 1:2], 1, OP.bitwise_and)
-    cp(["PI"], ["q"], T.PF[:, 0:1], T.PI[:, 0:1])
-    cp(["PI1"], ["g"], T.PF[:, 1:2], T.PI[:, 1:2])
-    cp(["PI2"], ["m1"], T.PF[:, 2:3], T.PI[:, 2:3])
-    ts(["OI2", "m1"], ["OU2"], T.OU[:, 56:72], T.OI[:, 56:72], T.PF[:, 2:3], OP.add)
-    ts(["q"], ["qn"], T.PF[:, 4:5], T.PF[:, 0:1], -1.0, OP.mult, -0.5, OP.add)
-    ts(["BK", "g"], ["TKS"], T.TK[:, 2048:2560], T.BK[:], T.PF[:, 1:2], OP.is_equal)
-    emit("G", ["T256"], ["TKB"], lambda e: e.affine_select(
-        T.TK[:, 2560:3072], T.TK[:, 4608:5120], [[0, 128], [-1, 4]], OP.is_gt, 0.0, 2, 0))
-    for i in (2, 3):
-        emit("G", ["TKS"], ["TKT%d" % i], lambda e, i=i: e.affine_select(
-            T.TK[:, 2048 + 512 * i:2560 + 512 * i], T.TK[:, 2048:2560], [[0, 128], [1, 4]], OP.is_equal, 0.0, -i, 0))
+    iota(["PC"], T.PC[:], [[0, 1]], 0, 1, 1, True)
+    iota(["OI"], T.OI[:, 0:16], [[1, 2], [16, 8]], 0, 0, 16, True)
+    iota(["OIb"], T.OI[:, 16:24], [[0, 8]], 8, 0, 8, True)
+    iota(["OI2"], T.OI[:, 24:40], [[2, 8], [0, 2]], 0, 0, 16, True)
+    iota(["IR"], T.IR[:], [[0, 16], [1, 16]], 0, 0, 256)
+    iota(["TI"], T.TI[:], [[1, 128]], 0, -1, 128)
+    iota(["ID"], T.ID[:], [[1, 256]], 0, 0, 256)
+    iota(["BK"], T.BK[:], [[1, 8], [0, 64]], 0, 0, 512)
+    iota(["C16"], T.CW[:, 16:32], [[16, 16]], 0, 0, 16)
+    iota(["NN"], T.NN[:], [[1, 8]], 0, 0, 8)
+    iota(["I4"], T.I4[:], [[0, 24], [1, 4]], 0, 0, 96)
+    iota(["CY"], T.CY[:], [[1, 368]], -112, 0, 368)
+    cp(["OI", "OIb"], ["OU"], T.OU[:, 0:24], T.OI[:, 0:24])
+    PF = {}
+    names = ("q", "g", "m1", "q8", "r8", "q4", "r4")
+    for i, (sh, bits) in enumerate(((0, 15), (4, 7), (4, 1), (3, 1), (0, 7), (2, 3), (0, 3))):
+        ts(["PC"], ["PI%d" % i], T.PI[:, i:i + 1], T.PC[:], sh, OP.arith_shift_right, bits, OP.bitwise_and)
+        PF[names[i]] = T.PF[:, i:i + 1]
+    cp(["PI0", "PI1"], ["q", "g"], T.PF[:, 0:2], T.PI[:, 0:2])
+    cp(["PI%d" % i for i in range(2, 7)], list(names[2:]), T.PF[:, 2:7], T.PI[:, 2:7])
+
+    def number(name, src, s1, o1, s2, o2, more=[]):
+        PF[name] = T.PF[:, len(PF):len(PF) + 1]
+        ts([src] + more, [name], PF[name], PF[src], s1, o1, s2, o2)
+
+    def affine(name, src, scale, bias):
+        PF[name] = T.PF[:, len(PF):len(PF) + 1]
+        act([src], [name], PF[name], PF[src], AF.Identity, bias, scale)
+    affine("q1", "q", 1.0, 1.0)
+    affine("qn", "q", -1.0, -0.5)
+    number("xq", "q", 15.0, OP.is_lt, 512.0, OP.mult)
+    affine("lb", "xq", 0.25, 0.0)
+    affine("lb1", "xq", 0.25, 1.0)
+    affine("lbc", "xq", 0.25, -223.0)
+    affine("xq1", "xq", 1.0, 1.0)
+    affine("q7", "q", 7.0, 1.0)
+    affine("nq", "q", -1.0, 0.0)
+    affine("nq128", "q", -1.0, -128.0)
+    affine("q3", "q", 1.0, -3.0)
+    affine("q16", "q", 1.0, -16.0)
+    affine("q41", "q4", 1.0, 1.0)
+    number("eo", "q4", 3.0, OP.is_lt, -2048.0, OP.mult)
+    tt(["eo", "r4"], ["eo"], PF["eo"], PF["eo"], PF["r4"], OP.add)
+    affine("t8", "q8", 16.0, 15.0)
+    number("g8", "r8", 256.0, OP.mult, PF["t8"], OP.add, ["t8"])
+    affine("t7", "q8", 7.0, 0.0)
+    ts(["OI2", "m1"], ["BC32"], T.OU[:, 24:40], T.OI[:, 24:40], PF["m1"], OP.add)
+    ts(["C16", "q3"], ["r7a"], T.TMP[:], T.CW[:, 16:24], PF["q3"], OP.add, 1.0 / 7, OP.mult)
+    cp(["r7a"], ["r7b"], T.OI[:, 40:48], T.TMP[:])
+    cp(["r7b"], ["REP7"], T.OU[:, 40:48], T.OI[:, 40:48])
+    ts(["NN", "q7"], ["HOPS"], T.OU[:, 48:54], T.NN[:, 0:6], PF["q7"], OP.add)
+    ts(["NN", "g8"], ["G8L"], T.OU[:, 56:64], T.NN[:], 32.0, OP.mult, PF["g8"], OP.add)
+    ts(["r8", "t7"], ["d8"], T.SC[:, 7:8], PF["r8"], 6.0, OP.min, PF["t7"], OP.add)
+    ts(["NN", "d8"], ["D8L"], T.OU[:, 64:72], T.NN[:], 14.0, OP.mult, T.SC[:, 7:8], OP.add)
+    BC32, REP7, HOPS, G8L, D8L = T.OU[:, 24:40], T.OU[:, 40:47], T.OU[:, 48:54], T.OU[:, 56:64], T.OU[:, 64:72]
+    ts(["IR", "q"], ["NB"], T.NB[:], T.IR[:], PF["q"], OP.not_equal, 2.0 ** 90, OP.mult, 128)
+    fill(["RS"], T.RS[:], 0.0, 256)
+    fill(["RS"], T.RS[:, 0:256:16], 2.0 ** 95)
+    fill(["RS"], T.RS[:, 256:512:16], -2.0 ** 95)
+    fill(["RC"], T.RC[:], 512.0, 128)
+    ts(["C16", "q16"], ["RC"], T.RC[:, 0:256:16], T.CW[:, 16:32], -1.0, OP.mult, PF["q16"], OP.add)
+    ts(["IR", "q"], ["e0"], T.ET0[:, 0:256], T.IR[:], PF["q"], OP.is_equal, -2.0 ** 20, OP.mult, 128)
+    ts(["IR", "q1"], ["e1"], T.ET0[:, 256:512], T.IR[:], PF["q1"], OP.is_equal, 512.0, OP.mult, 128)
+    tt(["e0", "e1"], ["EX"], T.EX[:], T.ET0[:, 0:256], T.ET0[:, 256:512], OP.add, 512)
+    act(["EX"], ["EB"], T.EB[:], T.EX[:], AF.Copy, 0.0, 0.25, n=256)
+    ts(["I4", "q4", "EX"], ["e0"], T.ET0[:, 0:96], T.I4[:], PF["q4"], OP.is_equal, -2.0 ** 20, OP.mult)
+    ts(["I4", "q41", "EX"], ["e1"], T.ET0[:, 256:352], T.I4[:], PF["q41"], OP.is_equal, 512.0, OP.mult)
+    tt(["e0", "e1"], ["E4"], T.E4[:], T.ET0[:, 0:96], T.ET0[:, 256:352], OP.add, 192)
+    ts(["TI"], ["TR"], T.TR[:], T.TI[:], 0.0, OP.is_le)
+    fill(["T128"], T.TK[:, 3072:3584], 128.0, 256)
+    fill(["TKB"], T.TK[:, 2560:3072], 1.0, 256)
+    ts(["BK", "g"], ["TKS"], T.TK[:, 2048:2560], T.BK[:], PF["g"], OP.is_equal, n=256)
+    quant(["TKB"], "KB", 128, T.TK[:, 2560:3072])
+    quant(["TKS"], "KS", 128, T.TK[:, 2048:2560])
     for b in range(4):
         emit("G", ["T128"], ["TK%d" % b], lambda e, b=b: e.affine_select(
-            T.TK[:, 512 * b:512 * b + 512], T.TK[:, 4096:4608], [[-1, 128], [1000, 4]], OP.is_equal, 0.0, -1000 * b, 1))
-    ts(["q"], ["nq"], T.PF[:, 12:13], T.PF[:, 0:1], -1.0, OP.mult)
-    act(["IR", "nq"], ["RQ"], T.RQ[:], T.IR[:], AF.Identity, T.PF[:, 12:13])
-    act(["RQ"], ["BS"], T.BS[:], T.RQ[:], AF.Abs)
-    act(["BS"], ["ME"], T.ME[:], T.BS[:], AF.Relu, 1.0, -1.0)
-    act(["IR"], ["KP"], T.KP[:], T.IR[:], AF.Sign)
-    act(["RQ"], ["BE"], T.BE[:], T.RQ[:], AF.Sign, 0.5)
-    act(["BE"], ["BE"], T.BE[:], T.BE[:], AF.Relu)
-    act(["BE"], ["BS"], T.BS[:], T.BE[:], AF.Copy, 0.0, -2.0 ** 90)
-    act(["BE"], ["RQ"], T.RQ[:], T.BE[:], AF.Copy, 0.0, 512.0)
-    act(["ME"], ["EX"], T.EX[:], T.ME[:], AF.Copy, 0.0, -2.0 ** 20)
-    tt(["RQ", "EX"], ["EX"], T.EX[:], T.RQ[:], T.EX[:], OP.add)
-    act(["BE"], ["BE"], T.BE[:], T.BE[:], AF.Copy, 0.0, 2.0 ** 90)
-    act(["TI"], ["TR"], T.TR[:], T.TI[:], AF.Sign, 0.5, -1.0)
-    act(["TR"], ["TR"], T.TR[:], T.TR[:], AF.Relu)
-    ts(["q"], ["xq"], T.PF[:, 5:6], T.PF[:, 0:1], -512.0, OP.mult, 7680.0, OP.add)
-    ts(["xq"], ["nxq"], T.PF[:, 14:15], T.PF[:, 5:6], -1.0, OP.mult)
-    for i in range(4):
-        ts(["xq"], ["xq4"], T.PF[:, 8 + i:9 + i], T.PF[:, 5:6], -4.0, OP.mult, float(i), OP.add)
-    quant(["UT"], "U", 0, 128, T.UT[:, 0:512])
-    emit("V", ["U", "OU"], ["UPc"], lambda e: e.tensor_copy(
-        T.cUP[:, 0:384].bitcast(dt.uint32), T.cU[:, 0:128].bitcast(dt.uint32).indirect(T.OU[:, 0:24])))
-    emit("A", ["U", "OU"], ["UPs"], lambda e: e.activation(
-        T.sUP[:, 0:384], T.sU[:, 0:128].indirect(T.OU[:, 0:24]), AF.Copy))
-    UPK = ["UPc", "UPs"]
-    quant(["XT"], "X0", 0, 256, T.XT[:])
-    for a in range(4):
-        o, e = 1024 * a + 256 * a, 1024 * a + 4 * TILE_N[a]
-        fill(["CT2%d" % a], T.CT2[:, o:e], 0.0)
-        act(["CT2%d" % a], ["CT3%d" % a], T.CT2[:, 4096 + o:4096 + e], T.CT2[:, o:e])
+            T.TK[:, 512 * b:512 * b + 512], T.TK[:, 3072:3584], [[-1, 128], [1000, 4]], OP.is_equal, 0.0, -1000 * b, 1), 1.1)
+        quant(["TK%d" % b], "KR%d" % b, 128, T.TK[:, 512 * b:512 * b + 512])
+    quant(["UT"], "U", 128, T.UT[:])
+    for i in (0, 2, 1):
+        c = slice(128 * i, 128 * i + 128)
+        emit("V", ["U", "OU"], ["UPc%d" % i], lambda e, i=i, c=c: e.tensor_copy(
+            T.cUP[:, c].bitcast(dt.uint32), T.cU[:, 0:128].bitcast(dt.uint32).indirect(T.OU[:, 8 * i:8 * i + 8])), cyc(far(128)))
+        emit("A", ["U", "OU"], ["UPs%d" % i], lambda e, i=i, c=c: e.activation(
+            T.sUP[:, c], T.sU[:, 0:128].indirect(T.OU[:, 8 * i:8 * i + 8]), AF.Copy), cyc(far(128)))
+    quant(["XT"], "X0", 256, T.XT[:])
+    for s in range(2):
+        for a in range(4):
+            o = 4 * (TILE_O[4] * s + TILE_O[a])
+            lo = 64 * (13 - 4 * a)
+            fill(["z%d%d" % (s, a)], T.CT[:, o + lo:o + 4 * TILE_N[a]], 0.0, 2 * TILE_N[a] - lo // 2)
+    fill(["zB"], T.BT[:], 0.0, 512)
     fill(["AR"], T.AR[:], 0.0)
     dma("S", "dPad", ["X0"], ["pad"], [(T.cL[:, 288:320].bitcast(dt.uint8), T.cX[:, 0:32].bitcast(dt.uint8)),
                                        (T.sL[:, 288:320], T.sX[:, 0:32])])
-
-    ZC = ["CT%d%d" % (i, a) for i in (2, 3) for a in range(4)]
-
-    def late_constants():
-        for b in range(4):
-            quant(["TK%d" % b], "KR%d" % b, 0, 128, T.TK[:, 512 * b:512 * b + 512])
-
-    def birth_constants():
-        for i, k in enumerate(("KS", "KB", "KT", "KU")):
-            quant(["TKS", "TKB", "TKT2", "TKT3"], k, 0, 128, T.TK[:, 2048 + 512 * i:2560 + 512 * i])
-        ts(["CW", "xq"], ["CX"], T.CX[:], T.CW[:], T.PF[:, 5:6], OP.subtract)
-        ts(["CW", "xq"], ["CP"], T.W3[:, 16:32], T.CW[:], T.PF[:, 5:6], OP.add)
-        ts(["PC"], ["PI3"], T.PI[:, 3:4], T.PC[:], 31, OP.bitwise_and)
-        cp(["PI3"], ["x32"], T.PF[:, 6:7], T.PI[:, 3:4])
-        ts(["x32", "xq"], ["x32q"], T.PF[:, 7:8], T.PF[:, 6:7], T.PF[:, 5:6], OP.add)
-        ts(["CT0", "x32q"], ["CT"], T.CT[:], T.CT[:], T.PF[:, 7:8], OP.add)
-
-    def count_constants():
-        ts(["nq"], ["nq128"], T.PF[:, 13:14], T.PF[:, 12:13], -128.0, OP.add)
-        act(["CY", "nq128"], ["CB"], T.CB[:], T.CY[:], AF.Abs, T.PF[:, 13:14])
-        act(["CB"], ["CB"], T.CB[:], T.CB[:], AF.Relu, 512.0, -512.0)
-        act(["CY", "nq"], ["CY"], T.CY[:], T.CY[:], AF.Abs, T.PF[:, 12:13])
-        act(["CY"], ["CY"], T.CY[:], T.CY[:], AF.Relu, 1.0, -1.0)
-        tt(["CY", "CB"], ["CB"], T.CB[:], T.CB[:], T.CY[:], OP.add)
-        fill(["ON"], T.ON[:, 0:32], 1.0)
-        fill(["ZR"], T.ON[:, 32:288], 0.0)
-        fill(["CM6"], T.CM[:], 0.0)
-        fill(["Q4z"], T.QQ[:, 48:80], 0.0)
-        fill(["ETz"], T.ET[:, 384:512], 0.0)
-        fill(["RTz"], T.RT[:, 384:512], 0.0)
-        quant(["VTL"], "V", 0, 128, T.VTL[:])
-
-    ts(["CW", "q"], ["CW"], T.CW[:], T.CW[:], T.PF[:, 0:1], OP.add)
-    cp(["CW"], ["CL"], T.CL[:, 0:16], T.CW[:])
-    cp(["OL"], ["LW"], T.CL[:, 16:32], T.OL[:])
+    act(["CY", "nq128"], ["CB"], T.CB[:], T.CY[:], AF.Abs, PF["nq128"], n=368)
+    act(["CB"], ["CB"], T.CB[:], T.CB[:], AF.Relu, 1024.0, -1024.0, n=368)
+    act(["CY", "nq"], ["CY"], T.CY[:], T.CY[:], AF.Abs, PF["nq"], n=368)
+    act(["CY"], ["CY"], T.CY[:], T.CY[:], AF.Relu, 1.0, -1.0, n=368)
+    tt(["CY", "CB"], ["CB"], T.CB[:], T.CB[:], T.CY[:], OP.add, 736)
+    fill(["C64"], T.C64[:], 64.0)
+    fill(["ZR"], T.ZR[:], 0.0, 128)
+    fill(["PD2"], T.PD2[:], 0.0)
+    fill(["PD2"], T.PD2[:, 1:96:2], 256.0)
+    fill(["Q4z"], T.QQ[:, 0:32], 0.0)
+    fill(["ETz"], T.ET[:, 384:512], 0.0)
+    fill(["RTz"], T.RT[:, 384:512], 0.0)
+    fill(["GS0"], T.GS[:, 0:16], 32.0)
+    fill(["I1z"], T.I1[:, 112:120], 0)
+    fill(["YXz"], T.YX[:, 0:256], 0.0, 128)
+    fill(["C8"], T.C8[:], 0.0, 128)
+    fill(["HD"], T.HD[:], 0.0)
+    quant(["VTL"], "V", 128, T.VTL[:])
+    CW = T.CW[:, 0:16]
+    ts(["C16", "q"], ["CW"], CW, T.CW[:, 16:32], PF["q"], OP.add)
+    ts(["CW", "lbc"], ["CP"], T.CP[:], CW, PF["lbc"], OP.add)
+    cp(["CW"], ["C8"], T.C8[:, 0:128:8], CW)
+    cp(["CW"], ["HD"], T.HD[:, 33:64:2], CW)
+    for s in (0, 7):
+        act(["ZR", "lb"], ["FP%d" % s], T.FP[:, 256 * s:256 * s + 256], T.ZR[:], AF.Identity, PF["lb"], n=256)
+    VV, VT0, VT6 = T.VT[:, 105:1888:16], T.VT[:, 105:1888:112], T.VT[:, 201:1888:112]
+    act(["ZR", "xq"], ["VT0"], VT0, T.ZR[:, 0:16], AF.Identity, PF["xq"])
     cp(["OL"], ["L16"], T.L16[:], T.OL[:])
+    ts(["OL", "xq"], ["VT6"], VT6, T.OL[:], 2.0 ** -8, OP.mult, PF["xq"], OP.add)
 
-    BC, BC15, BC32 = T.OU[:, 24:40], T.OU[:, 40:56], T.OU[:, 56:72]
     E15 = slice(15, 256, 16)
     rid, pid = topo.addr(nxt)[0], topo.addr(nxt)[1]
     mask = topo.mask(core, nxt)
@@ -361,266 +380,168 @@ def rank_program(g, core, T, topo):
             deps("G", r, [])
             g.remote_dma(out, src, T.sem[rsem], T.sem.ls, pid, rid, mask)
             sent[0] += n_eng
-        nodes.append(("G", r, ["snd" + rsem], issue, 0.7, 0.0))
-
-    pending = []
+        nodes.append(("G", r, ["snd" + rsem], issue, SEND, 0.0))
 
     for t in range(ROUNDS):
         X = "X%d" % t
         XK = [X, X + "s"]
-        mm(XK + UPK, "P7", 256, "UP", 0, X, 0)
-        mm(XK + UPK, "P5", 128, X, 0, "UP", 256)
-        mm(XK + UPK, "P6", 128, X, 128, "UP", 256)
-        mm(XK + UPK, "P4", 256, "UP", 256, X, 0)
-        mm(XK + UPK, "P3", 256, "UP", 128, X, 0)
-        act(["P5"], ["SB0"], T.SB2[:, 0:1], T.P5[:, 0:1])
-        act(["P6"], ["SB1"], T.SB2[:, 1:2], T.P6[:, 0:1])
-        act(["SB0", "SB1"], ["DL"], T.DL[:, 0:2], T.SB2[:, 0:2], AF.Abs, 0.0, 1.25 * 2.0 ** -24)
-        tt(["P7", "ME"], ["MS"], T.MS[:, 0:256], T.P7[:, 0:256], T.ME[:], OP.mult)
-        if t == 0:
-            birth_constants()
-        act(["DL"], ["DL2"], T.DL[:, 2:4], T.DL[:, 0:2], AF.Identity, 2.0 ** -120)
+        last = t == ROUNDS - 1
+        mm(XK + ["UPc0", "UPs0"], "PA", 256, "UP", 0, X, 0)
+        mm(XK + ["U"], "PD0", 128, X, 0, "U", 0)
+        mm(XK + ["U"], "PD1", 128, X, 128, "U", 0)
+        mm(XK + ["UPc2", "UPs2"], "PC_", 256, "UP", 256, X, 0)
+        mm(XK + ["UPc1", "UPs1"], "PB", 256, "UP", 128, X, 0)
+        act(["PD0", "PD1"], ["SB"], T.SB2[:], T.PD[:, 8:1024:512])
+        act(["PD0", "PD1"], ["DL"], T.DL[:], T.PD[:, 8:1024:512], AF.Abs, 2.0 ** -124, 1.25 * 2.0 ** -24)
         for h in range(2):
-            act(["TR", "DL2", "SB0", "SB1"], ["TH%d" % h], T["TH%d" % h][:], T.TR[:], AF.Identity,
-                T.SB2[:, h:h + 1], T.DL[:, 2 + h:3 + h])
-        for f in pending[:2]:
-            f()
-        scan(["KP", "MS"], ["SWS"], T.SWS[:], T.KP[:], T.MS[:, 0:256])
-        tt(["P7", "BS"], ["SG"], T.SG[:], T.P7[:, 0:256], T.BS[:], OP.add)
-        ts(["P4", "SB0"], ["BTa"], T.BT[:, 512:1024:4], T.P4[:, 128:256], T.SB2[:, 0:1], OP.is_ge)
-        ts(["P4", "SB1"], ["BTb"], T.BT[:, 1:512:4], T.P4[:, 0:128], T.SB2[:, 1:2], OP.is_gt)
-        tt(["P3", "ME"], ["MSE"], T.MS[:, 256:512], T.P3[:, 0:256], T.ME[:], OP.mult)
-        tt(["SWS", "SG", "OU"], ["BTe"], T.BT[:, 2:1024:4], T.SWS[:].indirect(BC15), T.SG[:], OP.is_lt)
-        scan(["KP", "MSE"], ["SWE"], T.SWE[:], T.KP[:], T.MS[:, 256:512])
-        tt(["P3", "BE"], ["EG"], T.EG[:], T.P3[:, 0:256], T.BE[:], OP.add)
-        tt(["P4", "TH0"], ["BTc"], T.BT[:, 0:512:4], T.P4[:, 0:128], T.TH0[:], OP.is_ge)
-        tt(["P4", "TH1"], ["BTd"], T.BT[:, 513:1024:4], T.P4[:, 128:256], T.TH1[:], OP.is_ge)
+            act(["TR", "DL", "SB"], ["TH%d" % h], T["TH%d" % h][:], T.TR[:], AF.Identity,
+                T.SB2[:, h:h + 1], T.DL[:, h:h + 1], n=128)
+        ts(["PC_", "SB", "zB"], ["BTa"], T.BT[:, 512:1024:4], ps("PC_", 128, 256), T.SB2[:, 0:1], OP.is_ge, n=128)
+        ts(["PC_", "SB", "zB"], ["BTb"], T.BT[:, 1:512:4], ps("PC_", 0, 128), T.SB2[:, 1:2], OP.is_gt, n=128)
+        tt(["PC_", "TH0", "zB"], ["BTc"], T.BT[:, 0:512:4], ps("PC_", 0, 128), T.TH0[:], OP.is_ge, 128)
+        tt(["PC_", "TH1", "zB"], ["BTd"], T.BT[:, 513:1024:4], ps("PC_", 128, 256), T.TH1[:], OP.is_ge, 128)
+        quant(["BTa", "BTb", "BTc", "BTd"], "B", 256, T.BT[:])
+        mm(["B", "KB"], "PC_", 256, "KB", 0, "B", 0)
 
-        tt(["SWE", "EG", "OU"], ["BTf"], T.BT[:, 3:1024:4], T.SWE[:].indirect(BC15), T.EG[:], OP.is_gt)
-
-        def pair(s, m):
-            bank, w, k, op = (("P7", T.SWS, "SWS", OP.is_gt), ("P3", T.SWE, "SWE", OP.is_lt))[s]
-            if m:
-                o, n = 4096 * s + 1024 * (m // 4), 64 * m
-                v = T.CT2[:, o + m % 4:o + n:4]
-                ts([bank, k] + ZC, ["ct%d.%d" % (s, m)], v, T[bank][:, 0:16 * m], w[:, 16 * m + 15:16 * m + 16], op)
-                j = m % 4
-                act(["ct%d.%d" % (s, m), "AR"], ["AR%d.%d" % (s, m), "AJ%d" % j], T.AJ[:, 256 * j:256 * j + 16 * m], v,
-                    AF.Copy, 0.0, 1.0, T.AR[:, 16 * s + m:16 * s + m + 1])
-
-        def pair_sum(s, a):
-            o, n, k, bank = 4096 * s + 1024 * a, TILE_N[a], "CD"[s] + str(a), ("P4", "P5")[s]
-            quant(["ct%d.%d" % (s, m) for m in range(4 * a, 4 * a + 4) if m] + ZC, k, 0, n, T.CT2[:, o:o + 4 * n])
-            mm([k, "KS"], bank, n, "KS", 0, k, 0, False, a == 3)
-
-        def row_sum(s):
-            scan(["KP", ("BTe", "BTf")[s]], ["RD%d" % s], T.RD[:, 256 * s:256 * s + 256], T.KP[:], T.BT[:, 2 + s:1024:4])
+        def places(s):
+            bank, sums = (("PA", "PD0"), ("PB", "PD1"))[s]
+            c = slice(256 * s, 256 * s + 256)
+            o = 4 * TILE_O[4] * s
+            tt([bank, "NB"], ["SG%d" % s], T.SG[:, c], ps(bank, 0, 256), T.NB[:], (OP.add, OP.subtract)[s], 256)
+            scan(["RS", "SG%d" % s], ["SW%d" % s], T.SW[:, c], T.RS[:, c], T.SG[:, c], 0.0, OP.add, (OP.min, OP.max)[s], 256)
+            run = T.CT[:, o:o + 1024:4]
+            tt([bank, "SW%d" % s, "z%d0" % s], ["ct%d.16" % s], run, ps(bank, 0, 256), T.SW[:, c], (OP.is_ge, OP.is_le)[s], 256)
+            scan(["RC", "ct%d.16" % s], ["RD%d" % s], T.RD[:, c], T.RC[:], run, 0.0, OP.min, OP.add, 128)
+            for a in range(4):
+                ms = [m for m in range(16 - 4 * a, 12 - 4 * a, -1)]
+                for j, m in enumerate(ms):
+                    if m < 16:
+                        v = T.CT[:, o + 4 * TILE_O[a] + j:o + 4 * TILE_O[a] + 64 * m:4]
+                        ts([bank, "SW%d" % s, "z%d%d" % (s, a)], ["ct%d.%d" % (s, m)], v, ps(bank, 0, 16 * m),
+                           T.SW[:, 256 * s + 16 * m + 15:256 * s + 16 * m + 16], (OP.is_gt, OP.is_lt)[s], n=16 * m)
+                        act(["ct%d.%d" % (s, m), "AR"], ["AR%d.%d" % (s, m), "AJ%d" % j], T.AJ[:, 256 * j:256 * j + 16 * m], v,
+                            AF.Copy, 0.0, 1.0, T.AR[:, 16 * s + m:16 * s + m + 1], n=16 * m)
+                k = "C%d%d" % (s, a)
+                quant(["ct%d.%d" % (s, m) for m in ms], k, TILE_N[a], T.CT[:, o + 4 * TILE_O[a]:o + 4 * TILE_O[a + 1]])
+                mm([k, "KS"], sums, TILE_N[a], "KS", 0, k, 0, a == 0, a == 3)
             tt(["RD%d" % s, "AR"] + ["AR%d.%d" % (s, m) for m in range(1, 16)], ["RW%d" % s], T.RW[:, 16 * s:16 * s + 16],
                T.RD[:, 256 * s + 15:256 * s + 256:16], T.AR[:, 16 * s:16 * s + 16], OP.add)
-
-        pair(0, 15)
-        quant(["BTa", "BTb", "BTc", "BTd", "BTe", "BTf"], "B", 0, 256, T.BT[:])
-        mm(["B", "KB"], "P6", 256, "KB", 0, "B", 0)
-        mm(["B", "KT"], "P4", 256, "KT", 0, "B", 0, True, False)
-        if t == 0:
-            late_constants()
+            pick([sums], ["EC%d" % s], T.EC[:, c], ps(sums, 0, 256))
+            tt(["EC%d" % s, "RW%d" % s], ["PL%d" % s], (T.TE, T.EP)[s][:], T.EC[:, 256 * s + 15:256 * s + 256:16],
+               T.RW[:, 16 * s:16 * s + 16], OP.subtract)
+        places(0)
+        places(1)
         for b in range(4):
-            mm(XK + ["KR%d" % b], ("P0", "P1", "P2", "P5")[b], 256, "KR%d" % b, 0, X, 0)
-        pair(0, 14)
-        tt(["P6", "ID"], ["V0"], T.VH[:, 1536:1792], T.P6[:, 0:256], T.ID[:], OP.add)
-        pair(0, 13)
-        pair(0, 12)
-        for m in range(11, 3, -1):
-            pair(0, m)
-        for f in pending[2:]:
-            f()
-        for m in range(3, 0, -1):
-            pair(0, m)
-        for a in range(4):
-            pair_sum(0, a)
-        if t == 0:
-            count_constants()
-        for i in range(6):
-            src, k = (T.VH[:, 1536:1792], "V0") if i == 0 else (T.VH[:, 256 * i - 256:256 * i], "VH%d" % (i - 1))
-            act([k, "L16"], ["VH%d" % i], T.VH[:, 256 * i:256 * i + 256], src.indirect(T.L16[:]),
-                AF.Identity, 65536.0)
-            if i == 0:
-                row_sum(0)
-                act(["RW0", "OU"], ["XR"], T.XR[:, 0:256], T.RW[:, 0:16].indirect(BC))
-        def half(b):
-            k = ("P0", "P1", "P2", "P5")[b]
-            act([k], ["FT%d" % b], T.FT[:, 256 * b:256 * b + 256], T[k][:, 0:256], AF.Copy, 0.0, 2.0 ** -8)
-            act([k], ["FU%d" % b], T.FU[:, 256 * b:256 * b + 256], T[k][:, 0:256], AF.Copy, 0.0, 2.0 ** -8)
-        half(3)
-        mm(["B", "KU"], "P5", 256, "KU", 0, "B", 0, True, False)
-        for m in range(15, 7, -1):
-            pair(1, m)
-        turn(["XR"], ["XS"], T.XR[:, 256:512], T.XR[:, 0:256])
-        turn(["P4"], ["TT"], T.VT[:, 1536:1792], T.P4[:, 0:256])
-        scan(["EX", "XS"], ["XE"], T.XE[:], T.EX[:], T.XR[:, 256:512], 0.0, OP.add, OP.max)
-        for m in range(7, 0, -1):
-            pair(1, m)
-            if m == 6:
-                tt(["TT", "CT"], ["T1a"], T.T1[:, 0:16], T.VT[:, 1536:1792:16], T.CT[:], OP.add)
-            if m == 4:
-                tt(["T1a", "XE"], ["T1b"], T.T1[:, 16:32], T.T1[:, 0:16], T.XE[:, E15], OP.subtract)
-                for i in range(5):
-                    act(["T1b"], ["T6%d" % i], T.T6[:, 16 * i:16 * i + 16], T.T1[:, 16:32], AF.Identity,
-                        255.5 + 65536.0 * (i + 1), 256.0)
-        for b in range(3):
-            half(b)
-        for a in range(4):
-            pair_sum(1, a)
-        for i in range(6):
-            turn(["VH%d" % i], ["VT%d" % i], T.VT[:, 256 * i:256 * i + 256], T.VH[:, 256 * i:256 * i + 256])
-        VTK = ["VT%d" % i for i in range(6)]
-        tt(VTK[:5] + ["T6%d" % i for i in range(5)] + ["CM6"], ["CM"], T.CM[:, 0:80], T.VT[:, 0:1280:16], T.T6[:], OP.is_gt)
-        act(["CM", "CM6"], ["XXa"], T.XX[:, 0:96], T.CM[:], AF.Copy, 0.0, 2.0 ** 20)
-        tt(["XXa"] + VTK, ["XXb"], T.XX[:, 96:192], T.XX[:, 0:96], T.VT[:, 0:1536:16], OP.add)
-        tt(["XXb"], ["MNa"], T.MN[:, 0:48], T.XX[:, 96:144], T.XX[:, 144:192], OP.min)
-        tt(["MNa"], ["MNb"], T.MN[:, 48:64], T.MN[:, 0:16], T.MN[:, 16:32], OP.min)
-        tt(["MNa", "MNb"], ["RI0"], T.RI[:, 0:16], T.MN[:, 48:64], T.MN[:, 32:48], OP.min)
-        ts(["RI0"], ["RI1"], T.RI[:, 16:32], T.RI[:, 0:16], 255, OP.bitwise_and)
-        cp(["RI1"], ["RI2"], T.EP[:, 32:48], T.RI[:, 16:32])
-        act(["RI2", "OU"], ["RX"], T.RX[:, 0:256], T.EP[:, 32:48].indirect(BC))
-        row_sum(1)
-        turn(["RX"], ["RY"], T.RX[:, 256:512], T.RX[:, 0:256])
-        scan(["EX", "RY"], ["RS"], T.RS[:], T.EX[:], T.RX[:, 256:512], 0.0, OP.add, OP.max)
-        ts(["RS", "xq"], ["R16"], T.R16[:], T.RS[:, E15], T.PF[:, 5:6], OP.subtract)
+            k = ("Q0", "Q1", "Q2", "Q0")[b]
+            mm(XK + ["KR%d" % b], k, 256, "KR%d" % b, 0, X, 0)
+            act([k], ["FT%d" % b], T.FT[:, 256 * b:256 * b + 256], ps(k, 0, 256), AF.Copy, 0.0, 2.0 ** -8, n=256)
+        dma("S", "dF", ["FT0", "FT1", "FT2", "FT3"], ["FU"], [(T.FU[:], T.FT[:])])
+        act(["ID", "L16"], ["LF"], T.LF[:], T.ID[:].indirect(T.L16[:]), AF.Copy, 0.0, 2.0 ** -8, n=far(256))
+        tt(["PC_", "LF"], ["VH0"], T.VH[:, 0:256], ps("PC_", 0, 256), T.LF[:], OP.add, 256)
+        for i in range(1, 6):
+            act(["VH%d" % (i - 1), "L16"], ["VH%d" % i], T.VH[:, 256 * i:256 * i + 256],
+                T.VH[:, 256 * i - 256:256 * i].indirect(T.L16[:]), n=far(256))
+            pick(["VH%d" % i], ["VT%d" % (6 - i)], T.VT[:, 96 - 16 * i:96 - 16 * i + 1786:7], T.VH[:, 256 * i:256 * i + 256])
+        VK = ["VT%d" % k for k in range(7)]
+        ts(VK + ["xq"], ["I0"], T.I0[:], VV, PF["xq"], OP.subtract, 256.0, OP.mult, 112)
+        ts(["I0"], ["I1"], T.I1[:, 0:112], T.I0[:], 255, OP.bitwise_and, n=112)
+        tt(["I1", "I1z"], ["D7"], T.D7[:], T.I1[:, 0:112], T.I1[:, 1:113], OP.subtract, 224)
+        tt(VK + ["PL0", "REP7"], ["CM"], T.CM[:], T.TE[:].indirect(REP7), VV, OP.is_le, far(112))
+        scan(["CM", "D7"], ["HR"], T.HR[:, 0:111], T.CM[:, 0:111], T.D7[:, 1:112], 0.0, OP.mult, OP.add, 111)
+        cp(["HR"], ["R16"], T.R16[:], T.HR[:, 5:111:7])
         for z in range(8):
-            act(["CB", "R16"], ["CJ%d" % (z % 2), "CA%d" % z], T.CJ[:, 256 * (z % 2):256 * (z % 2) + 256], T.CB[:, 112 - 16 * z:368 - 16 * z].indirect(T.R16[:]),
-                AF.Copy, 0.0, 1.0, T.CA[:, z:z + 1])
-        scan(["EX", "P5"], ["EC"], T.EC[:], T.EX[:], T.P5[:, 0:256], 0.0, OP.add, OP.max)
-        tt(["CX", "RW1"], ["EPa"], T.EP[:, 0:16], T.CX[:], T.RW[:, 16:32], OP.subtract)
-        tt(["EPa", "EC"], ["EP"], T.EP[:, 16:32], T.EP[:, 0:16], T.EC[:, E15], OP.add)
-        cp(["EP"], ["EP16"], T.EP16[:], T.EP[:, 16:32])
-        cp(["ID", "EP16"], ["EF"], T.EF[:, 0:256].indirect(T.EP16[:]), T.ID[:])
+            act(["CB", "R16"], ["CJ%d" % (z % 2), "CA%d" % z], T.CJ[:, 256 * (z % 2):256 * (z % 2) + 256],
+                T.CB[:, 112 - 16 * z:368 - 16 * z].indirect(T.R16[:]), AF.Copy, 0.0, 1.0, T.CA[:, z:z + 1], n=far(256))
         for b in range(4):
-            f = T.FT[:, 256 * b:256 * b + 256]
-            tt(["FT%d" % b, "FU%d" % b, "R16"], ["Z%d" % b], T.Z[:, b:1024:4], f.indirect(T.R16[:]),
-               T.FU[:, 256 * b:256 * b + 256], OP.add)
-            if b == 1:
-                scan(["EX", "EF"], ["ES"], T.ES[:], T.EX[:, 0:96], T.EF[:, 0:96], 0.0, OP.add, OP.max)
-            if b == 2:
-                for i in range(4):
-                    ts(["ES", "xq4"], ["EO%d" % i], T.EO[:, 8 * i:8 * i + 6], T.ES[:, 15:96:16], 4.0, OP.mult,
-                       T.PF[:, 8 + i:9 + i], OP.add)
+            tt(["FT%d" % b, "FU", "R16"], ["Z%d" % b], T.Z[:, b:1024:4], T.FT[:, 256 * b:256 * b + 256].indirect(T.R16[:]),
+               T.FU[:, 256 * b:256 * b + 256], OP.add, far(256))
         ZK = ["Z0", "Z1", "Z2", "Z3"]
-        for b in range(4):
-            (cp, cp, act, act)[b](ZK + ["EO%d" % b], ["ET%d" % b], T.ET[:, b:384:4], T.Z[:].indirect(T.EO[:, 8 * b:8 * b + 6]))
-        act(["EF"], ["PKa"], T.PK[:, 0:48], T.EF[:, 48:96], AF.Copy, 0.0, 256.0)
+        quant(ZK, "P", 256, T.Z[:])
+        ts(["PL1", "xq1"], ["EP16"], T.EP16[:], T.EP[:], PF["xq1"], OP.subtract)
+        cp(["ID", "EP16"], ["EF"], T.EF[:].indirect(T.EP16[:]), T.ID[:], 60 + STREW * 256)
+        scan(["E4", "EF"], ["ES"], T.ES[:], T.E4[:], T.EF[:, 0:96], 0.0, OP.add, OP.max, 96)
+        ts(["ES", "eo"], ["EO"], T.EO[:], T.ES[:, 3:96:4], 4.0, OP.mult, PF["eo"], OP.add)
+        cp(ZK + ["EO"], ["ETa"], T.ET[:, 0:192], T.Z[:].indirect(T.EO[:, 0:12]), far(192))
+        cp(ZK + ["EO"], ["ETb"], T.ET[:, 192:384], T.Z[:].indirect(T.EO[:, 12:24]), far(192))
+        scan(["PD2", "EF"], ["PK"], T.PK[:], T.PD2[:], T.EF[:, 0:96], 0.0, OP.mult, OP.add, 96)
+        cp(["PK"], ["LS%d" % t], T.LS[:, 48 * t:48 * t + 48], T.PK[:, 1:96:2])
         lo = KEEP * (ROUNDS - 1 - t)
-
-        def send_columns():
-            quant(["ET0", "ET1", "ET2", "ET3", "ETz"], "E%d" % t, 0, 128, T.ET[:])
-            send(["E%d" % t], T.cL[:, lo:lo + KEEP].bitcast(dt.uint8),
-                 T.cE[:, 128 * t:128 * t + KEEP].bitcast(dt.uint8), "aC%d" % t)
-            send(["E%d" % t], T.sL[:, lo:lo + KEEP], T.sE[:, 128 * t:128 * t + KEEP], "aC%d" % t)
-            send(["LS%d" % t], T.LL[:, 48 * t:48 * t + 48], T.LS[:, 48 * t:48 * t + 48], "aL%d" % t)
-            arrival("L%d" % t, ["sndaC%d" % t], ("aC%d" % t, 2 * n_arr, {}))
-            arrival("LL%d" % t, ["sndaL%d" % t], ("aL%d" % t, n_arr, {}))
-        tt(["PKa", "EF"], ["PKb"], T.PK[:, 48:96], T.PK[:, 0:48], T.EF[:, 0:48], OP.add)
-        quant(ZK, "P", 0, 256, T.Z[:])
-        cp(["PKb"], ["LS%d" % t], T.LS[:, 48 * t:48 * t + 48], T.PK[:, 48:96])
-        cp(["CA%d" % z for z in range(8)], ["CI0"], T.CI[:, 0:8], T.CA[:])
-        ts(["CI0"], ["CI1"], T.CI[:, 8:16], T.CI[:, 0:8], 511, OP.bitwise_and)
-        ts(["CI0"], ["CI2"], T.CI[:, 16:24], T.CI[:, 0:8], 9, OP.arith_shift_right)
-        Q1, Q2, Q3, Q4, Q5, Q6, Q7 = [(a, a + 32) for a in (0, 16, 32, 48, 80, 112, 144)]
-
-        def qq(q, a=0, b=32, step=1, p=0, np_=128):
-            return T.QQ[p:p + np_, q[0] + a:q[0] + b:step]
-        cp(["CI1", "CI2"], ["Q1"], qq(Q1, 0, 16, 1, 0, 64), T.CI[64:128, 8:24])
-        cp(["CI1", "CI2"], ["Q1b"], qq(Q1, 0, 16, 1, 64, 64), T.CI[0:64, 8:24])
-        tt(["CI1", "CI2", "Q1", "Q1b"], ["Q2"], qq(Q2, 0, 16), T.CI[:, 8:24], qq(Q1, 0, 16), OP.add)
+        quant(["ETa", "ETb", "ETz"], "E%d" % t, 128, T.ET[:])
+        send(["LS%d" % t], T.LL[:, 48 * t:48 * t + 48], T.LS[:, 48 * t:48 * t + 48], "aL%d" % t)
+        send(["E%d" % t], T.cL[:, lo:lo + KEEP].bitcast(dt.uint8), T.cE[:, 128 * t:128 * t + KEEP].bitcast(dt.uint8), "aC%d" % t)
+        send(["E%d" % t], T.sL[:, lo:lo + KEEP], T.sE[:, 128 * t:128 * t + KEEP], "aC%d" % t)
+        arrival("L%d" % t, ["sndaC%d" % t], ("aC%d" % t, 2 * n_arr, {}))
+        arrival("LL%d" % t, ["sndaL%d" % t], ("aL%d" % t, n_arr, {}))
+        cp(["I1", "I1z", "HOPS"], ["H16"], T.H16[:], T.I1[:].indirect(HOPS), far(96))
+        tt(["D7", "D8L", "C8"], ["D8", "D8e"], T.D8[:], T.D7[:].indirect(D8L), T.C8[:], OP.add, far(128))
+        across(["CA%d" % z for z in range(8)], ["CI0"], T.CI[0:64, 0:8], T.CA[0:64, :], T.CA[64:128, :])
+        ts(["CI0"], ["CI1"], T.CI[0:64, 8:16], T.CI[0:64, 0:8], 1023, OP.bitwise_and)
+        ts(["CI0"], ["CI2"], T.CI[0:64, 16:24], T.CI[0:64, 0:8], 10, OP.arith_shift_right)
+        across(["CI1", "CI2", "Q4z"], ["Q4"], T.QQ[0:32, 0:16], T.CI[0:32, 8:24], T.CI[32:64, 8:24])
+        turn(["Q4"], ["Q5"], T.QQ[0:32, 32:64], T.QQ[0:32, 0:32])
+        tt(["Q5"], ["Q6"], T.QQ[0:32, 64:80], T.QQ[0:32, 32:48], T.QQ[0:32, 48:64], OP.add)
+        tt(["Q5"], ["Q6b"], T.QQ[0:32, 80:96], T.QQ[0:32, 32:48], T.QQ[0:32, 48:64], OP.add)
         for a in range(4):
-            b = a ^ 1
-            (cp, cp, act, act)[a](["Q2"], ["Q3%d" % a], qq(Q3, 0, 16, 1, 32 * a, 32), qq(Q2, 0, 16, 1, 32 * b, 32))
-        tt(["Q2", "Q30", "Q31", "Q32", "Q33", "Q4z"], ["Q4"], qq(Q4, 0, 16), qq(Q2, 0, 16), qq(Q3, 0, 16), OP.add)
-        turn(["Q4", "Q4z"], ["Q5"], qq(Q5), qq(Q4))
-        tt(["Q5"], ["Q6"], qq(Q6, 0, 16), qq(Q5, 0, 16), qq(Q5, 16, 32), OP.add)
-        tt(["Q5"], ["Q6b"], qq(Q6, 16, 32), qq(Q5, 0, 16), qq(Q5, 16, 32), OP.add)
-        turn(["Q6", "Q6b"], ["Q7"], qq(Q7), qq(Q6))
-        send_columns()
-        act(["Q7", "OU2"], ["RP"], T.RP[:], qq(Q7).indirect(BC32))
-        turn(["RP"], ["TO"], T.TO[:], T.RP[:])
-        act(["TO", "qn"], ["AJ0", "AC"], T.AJ[:, 0:256], T.TO[:], AF.Sign, T.PF[:, 4:5], 1.0, T.SC[:, 0:1])
-        ts(["AC"], ["F1"], T.SC[:, 2:3], T.SC[:, 0:1], 64.0, OP.is_le)
-        ts(["ON", "F1"], ["FB"], T.FB[:, 0:32], T.ON[:, 0:32], T.SC[:, 2:3], OP.mult, -15.5 / 16, OP.add)
-        turn(["FB"], ["FX"], T.FB[:, 64:96], T.FB[:, 0:32])
-        emit("V", ["FX"], ["SF"], lambda e: e.tensor_reduce(T.SC[:, 4:5], T.FB[:, 64:80], AxisListType.X, OP.add))
-        act(["TO", "SF"], ["AJ1", "NP"], T.AJ[:, 256:512], T.TO[:], AF.Sign, T.SC[:, 4:5], 1.0, T.SC[:, 5:6])
-        ts(["TO", "SF"], ["EQM"], T.EQM[:], T.TO[:], T.SC[:, 4:5], OP.add, 0.5, OP.is_equal)
-        scan(["EQM", "ZR"], ["CU"], T.CU[:], T.EQM[:], T.ON[:, 32:288], 32.0, OP.add, OP.max)
-        ts(["CU", "NP"], ["OV"], T.OV[:], T.CU[:], 2.0, OP.mult, T.SC[:, 5:6], OP.is_gt)
-        tt(["TO", "OV"], ["Zx"], T.Z2[:], T.TO[:], T.OV[:], OP.add)
-        ts(["Zx", "SF"], ["GN"], T.GN[:], T.Z2[:], T.SC[:, 4:5], OP.add, 0.5, OP.is_le)
-        scan(["GN", "ZR"], ["GS"], T.GS[:], T.GN[:], T.ON[:, 32:288], 255.0, OP.add, OP.max)
-        scan(["GS", "GN"], ["M1"], T.M1[:], T.GS[:], T.GN[:], 0.0, OP.max, OP.mult)
-        tt(["M1", "ID"], ["Y0"], T.Y0[:], T.M1[:], T.ID[:], OP.max)
-        scan(["EX", "M1"], ["NSx"], T.NS[:], T.EX[:], T.M1[:], 0.0, OP.add, OP.max)
-        tt(["NSx", "CP"], ["NSw"], T.W3[:, 0:16], T.NS[:, E15], T.W3[:, 16:32], OP.max)
-        ts(["NSw", "xq"], ["NI16"], T.NI16[:], T.W3[:, 0:16], T.PF[:, 5:6], OP.subtract)
-        act(["NSw", "nxq"], ["NS"], T.CL[:, 32:48], T.W3[:, 0:16], AF.Identity, T.PF[:, 14:15])
+            turn(["Q6", "Q6b"], ["Q7%d" % a], T.QQ[32 * a:32 * a + 32, 96:128], T.QQ[0:32, 64:96])
+        act(["Q70", "Q71", "Q72", "Q73", "BC32"], ["RP"], T.RP[:], T.QQ[:, 96:128].indirect(BC32), n=far(256))
+        turn(["RP"], ["TO"], T.TO[:], T.RP[:], 128)
+        act(["TO", "qn"], ["AJ0", "AC"], T.AJ[:, 0:256], T.TO[:], AF.Sign, PF["qn"], 1.0, T.SC[:, 0:1], n=256)
+        ts(["C64", "AC"], ["FBa"], T.FB[:, 0:32], T.C64[:], T.SC[:, 0:1], OP.is_ge)
+        ts(["C64", "AC"], ["FBb"], T.FB[:, 32:64], T.C64[:], T.SC[:, 0:1], OP.mult, 2.0 ** -7, OP.mult)
+        turn(["FBa", "FBb"], ["FX"], T.FB[:, 64:128], T.FB[:, 0:64])
+        emit("V", ["FX"], ["SF"], lambda e: e.tensor_reduce(T.SC[:, 1:2], T.FB[:, 64:80], AxisListType.X, OP.add), cyc(64))
+        scan(["FX"], ["XS"], T.XS[:], T.FB[:, 64:80], T.FB[:, 96:112], 128.0, OP.mult, OP.max)
+        ts(["TO", "SF"], ["LT"], T.LT[:], T.TO[:], T.SC[:, 1:2], OP.add, 16.0, OP.is_lt, 128)
+        ts(["TO", "SF"], ["LE"], T.LE[:], T.TO[:], T.SC[:, 1:2], OP.add, 16.0, OP.is_le, 128)
+        scan(["LT", "ZR", "XS"], ["AA"], T.AA[:], T.LT[:], T.ZR[:], T.XS[:, 15:16], OP.add, OP.max, 128)
+        scan(["LE", "AA", "GS0"], ["GS"], T.GS[:, 1:257], T.LE[:], T.AA[:], 32.0, OP.add, OP.min, 128)
+        pick2(["GS"], ["P1"], T.P1[:], T.GS[:, 1:257])
+        pick2(["GS"], ["P0"], T.P0[:], T.GS[:, 0:256])
+        scan(["GS"], ["GN"], T.GN[:], T.GS[:, 1:257], T.GS[:, 0:256], 0.0, OP.max, OP.subtract, 128)
+        tt(["P1", "P0", "HD"], ["HDa"], T.HD[:, 1:32:2], T.P1[:, E15], T.P0[:, E15], OP.subtract)
+        tt(["P1", "CP", "HD"], ["HDb"], T.HD[:, 32:64:2], T.P1[:, E15], T.CP[:], OP.subtract)
+        scan(["HDa", "HDb"], ["HO"], T.HO[:], T.HD[:, 0:32], T.HD[:, 32:64], 0.0, OP.mult, OP.add)
+        cp(["HO"], ["NI16"], T.NI16[:], T.HO[:, 1:32:2])
         for b in range(4):
-            k = PS[b]
+            k = ("Q0", "Q1", "Q2", "PC_")[b]
             mm(["L%d" % t, "pad", "W"], k, 128, "W", 128 * b, "L", lo, True, False)
             mm(["L%d" % t, "pad", "KR%d" % b], k, 128, "KR%d" % b, 0, "L", lo, False, True)
-        for b in range(2):
-            act([PS[b], "RTz"], ["RT%d" % b], T.RT[:, b:384:4], T[PS[b]][:, 0:96], AF.Copy, 0.0, 2.0 ** -7)
-        for b in range(2, 4):
-            ts([PS[b], "RTz"], ["RT%d" % b], T.RT[:, b:384:4], T[PS[b]][:, 0:96], 2.0 ** -7, OP.mult)
-        quant(["RT0", "RT1", "RT2", "RT3", "RTz"], "P", 256, 384, T.RT[:])
+            if b < 3:
+                act([k, "RTz"], ["RT%d" % b], T.RT[:, b:384:4], ps(k, 0, 96), AF.Copy, 0.0, 2.0 ** -7, n=96)
+            else:
+                ts([k, "RTz"], ["RT%d" % b], T.RT[:, b:384:4], ps(k, 0, 96), 2.0 ** -7, OP.mult, n=96)
+        quant(["RT0", "RT1", "RT2", "RT3"], "Pb", 128, T.RT[:])
         XN = "X%d" % (t + 1)
         emit("V", ["P", "Pb", "NI16"], [XN], lambda e, t=t: e.tensor_copy(
-            T.cX[:, 256 * t + 256:256 * t + 512].bitcast(dt.uint32), T.cP[:, :].bitcast(dt.uint32).indirect(T.NI16[:])))
+            T.cX[:, 256 * t + 256:256 * t + 512].bitcast(dt.uint32), T.cP[:, :].bitcast(dt.uint32).indirect(T.NI16[:])), cyc(far(256)))
         emit("A", ["P", "Pb", "NI16"], [XN + "s"], lambda e, t=t: e.activation(
-            T.sX[:, 256 * t + 256:256 * t + 512], T.sP[:, :].indirect(T.NI16[:]), AF.Copy))
-        act(["NSw", "nxq"], ["NS2"], T.CL[:, 48:64], T.W3[:, 0:16], AF.Identity, T.PF[:, 14:15])
-        ts(["NS", "NS2"], ["GW"], T.SM[:, 0:32], T.CL[:, 32:64], 256.0, OP.is_ge)
-        tt(["NS", "LW", "CL"], ["D1"], T.SM[:, 32:64], T.CL[:, 16:48], T.CL[:, 0:32], OP.subtract)
-        tt(["GW", "D1"], ["D2"], T.SM[:, 64:96], T.SM[:, 0:32], T.SM[:, 32:64], OP.mult)
-        tt(["D2", "LW", "CL"], ["D3"], T.SM[:, 96:128], T.SM[:, 64:96], T.CL[:, 0:32], OP.add)
-        cp(["D3"], ["M16"], T.M16[:], T.SM[:, 96:128])
+            T.sX[:, 256 * t + 256:256 * t + 512], T.sP[:, :].indirect(T.NI16[:]), AF.Copy), cyc(far(256)))
+        for i in range(3):
+            c = slice(512 * i, 512 * i + 512)
+            (cp if last and i == 1 else act)(["GN", "H16"], ["FL%d" % i], T.FL[:, c], T.GN[:].indirect(T.H16[:, 32 * i:32 * i + 32]), n=far(512))
+            for s in (2 * i, 2 * i + 1):
+                pick2(["FL%d" % i], ["FP%d" % (s + 1)], T.FP[:, 256 * s + 256:256 * s + 512], T.FL[:, 256 * s:256 * s + 256])
+        ts(["HDa", "lb1"], ["FP7"], T.FP[:, 1807:2048:16], T.HD[:, 1:32:2], -1.0, OP.mult, PF["lb1"], OP.add)
+        cp(["LL%d" % t], ["LI0"], T.LI[:, 0:48], T.LL[:, 48 * t:48 * t + 48])
+        ts(["LI0"], ["LI1"], T.LI[:, 49:144:2], T.LI[:, 0:48], 255, OP.bitwise_and)
+        ts(["LI0"], ["LI2"], T.LI[:, 48:144:2], T.LI[:, 0:48], 8, OP.arith_shift_right)
+        cp(["LI1", "LI2"], ["YXe"], T.YX[:, 256:352], T.LI[:, 48:144], 96)
+        act(["YXz", "YXe", "NI16"], ["EW"], T.EW[:], T.YX[:].indirect(T.NI16[:]), n=far(256))
+        pick(["EW"], ["EQ"], T.EQ[:], T.EW[:])
+        ts(["EQ", "xq"], ["D8e"], T.D8[:, 7:128:8], T.EQ[:, E15], PF["xq"], OP.subtract)
+        ts(["FP%d" % s for s in range(8)] + ["G8L", "lb"], ["G8"], T.G8[:], T.FP[:].indirect(G8L), PF["lb"], OP.subtract, n=far(128))
+        scan(["G8", "D8", "D8e"], ["HL"], T.HL[:], T.G8[:], T.D8[:], 0.0, OP.mult, OP.add, 128)
+        cp(["HL"], ["L16"], T.L16[:], T.HL[:, 7:128:8])
+        if not last:
+            ts(["HL", "xq"], ["VT6"], VT6, T.HL[:, 7:128:8], 2.0 ** -8, OP.mult, PF["xq"], OP.add)
 
-        def chain(t=t):
-            src, k = T.Y0, "Y0"
-            for i in range(5):
-                dst, kd = ((T.YA, "YA"), (T.YB, "YB"))[i % 2] if i < 4 else (T.YX, "YX")
-                act([k, "M16"], [kd], dst[:, 0:256], src[:, 0:256].indirect(T.M16[:, 0:16]))
-                src, k = dst, kd
-            act(["YX", "YXe", "M16"], ["M1"], T.M1[:], T.YX[:].indirect(T.M16[:, 16:32]))
-
-        def unpack(t=t):
-            LL = "LL%d" % t
-            cp([LL], ["LI0"], T.LI[:, 0:48], T.LL[:, 48 * t:48 * t + 48])
-            ts(["LI0"], ["LI1"], T.LI[:, 48:96], T.LI[:, 0:48], 255, OP.bitwise_and)
-            ts(["LI0"], ["LI2"], T.LI[:, 96:144], T.LI[:, 0:48], 8, OP.arith_shift_right)
-            cp(["LI1", "LI2"], ["YXe"], T.YX[:, 256:352], T.LI[:, 48:144])
-
-        def relink():
-            scan(["EX", "M1"], ["NRx"], T.NR[:], T.EX[:], T.M1[:], 0.0, OP.add, OP.max)
-            r = T.SM[:, 144:160]
-            sm = [T.SM[:, 160 + 16 * i:176 + 16 * i] for i in range(3)]
-            act(["NRx", "nxq"], ["NR"], r, T.NR[:, E15], AF.Identity, T.PF[:, 14:15])
-            ts(["NR"], ["FL"], sm[0], r, 256.0, OP.is_ge)
-            tt(["CW", "NR"], ["G1"], sm[1], T.CW[:], r, OP.subtract)
-            tt(["FL", "G1"], ["G2"], sm[2], sm[0], sm[1], OP.mult)
-            tt(["G2", "NR"], ["LW"], T.CL[:, 16:32], sm[2], r, OP.add)
-            cp(["LW"], ["L16"], T.L16[:], T.CL[:, 16:32])
-        pending = [unpack, chain, relink]
-
-    mm(["V", "X3", "X3s"], "P7", 256, "V", 0, "X3", 0)
+    mm(["V", "X3", "X3s"], "PA", 256, "V", 0, "X3", 0)
     dma("S", "dOc", ["X3", "X3s"], ["oc"], [(T.oc[:, :], T.cX[:, 768:1024].bitcast(dt.uint8))] + [
         (T.osc[4 * k:4 * k + 4, :], T.sX[32 * k:32 * k + 4, 768:1024]) for k in range(4)])
-    pending[0]()
-    pending[1]()
-    cp(["P7"], ["YO"], T.YO[:], T.P7[:, 0:256])
+    act(["PA"], ["YO"], T.YO[:], ps("PA", 0, 256), n=256)
     dma("S", "dY", ["YO"], ["y"], [(T.y[:, :], T.YO[:])])
-    ts(["M1"], ["GS"], T.GS[:], T.M1[:], 256.0, OP.is_ge)
-    tt(["ID", "M1"], ["NRx"], T.NR[:], T.ID[:], T.M1[:], OP.subtract)
-    tt(["GS", "NRx"], ["Y0"], T.Y0[:], T.GS[:], T.NR[:], OP.mult)
-    tt(["Y0", "M1"], ["NSx", "NS"], T.NS[:], T.Y0[:], T.M1[:], OP.add)
-    dma("S", "dLk", ["NS"], ["lk"], [(T.lk[:, :], T.NS[0:128:16, :])])
+    cp(["ID", "L16"], ["LO"], T.LO[:], T.ID[:].indirect(T.L16[:]), far(256))
+    dma("S", "dLk", ["LO"], ["lk"], [(T.lk[:, :], T.LO[0:128:16, :])])
     schedule()
     for s in cnt:
         if known["S"].get(s, 0) < cnt[s]:

@@ -26,11 +26,11 @@ _sb(I, OL=16, PC=1, PI=8, OI=48, CI=24, LI=144, I0=112, I1=120)
 _q(W=512, U=128, UP=384, V=128, X=1024, L=320, P=384, E=384)
 _q(K=768)
 _q(C=256 + 2 * TILE_O[4])
-_sb(B, TK=3584, IR=256, I4=96, TI=128, BK=512, NB=256, RS=512, RC=256, EX=256, EB=256, E4=96, ET0=512, TR=128)
-_sb(B, C64=32, ZR=256, PD2=96)
-_sb(F, ID=256, PF=24, CY=368, CB=368, CW=32, NN=8, CP=16, C8=128, TMP=8)
+_sb(B, TK=1552, IR=256, I4=96, TI=128, BK=128, NB=256, RS=512, RC=256, EX=256, EB=256, E4=96, ET0=512, TR=128)
+_sb(B, C64=32, ZR=528, PD2=96, CB=368, SN=512)
+_sb(F, ID=256, PF=32, CW=32, NN=8, CP=16, TMP=8)
 _sb(U, OU=72)
-_sb(F, SG=512, SW=512, SB2=2, DL=2, TH0=128, TH1=128, AR=32, RW=32, EC=512, TE=16, EP=16)
+_sb(F, SR=512, SG=512, SW=512, SB2=2, DL=2, TH0=128, TH1=128, AR=32, RW=32, EC=512, TE=16, EP=16)
 _sb(B, BT=1024, CT=8 * TILE_O[4], AJ=1024, RD=512)
 _sb(F, LF=256, VH=1536, VT=1888, D7=112, CM=112, HR=112, D8=128, G8=128, HL=128)
 _sb(B, FT=1024, FU=1024, Z=1024, ET=512, RT=512)
@@ -50,10 +50,83 @@ for _i in range(4):
     PLACE["C0%d" % _i] = ("C", 256 + TILE_O[_i])
     PLACE["C1%d" % _i] = ("C", 256 + TILE_O[4] + TILE_O[_i])
     PLACE["E%d" % _i] = ("E", 128 * _i)
-CYCLE, WAKE, SLACK, FLIGHT, JUMP, STREW, SEND = 0.00088, 0.2, 0.15, 3.5, 1.5, 3.5, 0.7
+CYCLE, WAKE, FLIGHT, JUMP, STREW, SEND, FIRST = 0.00088, 0.2, 3.0, 1.5, 3.5, 0.7, 2.0
+PASSES, SPARE = 10, 0.3
+BY_SIGN = ((), (11, 10, 9))
 
 SEMAPHORES = ["sV", "sA", "sP", "sG", "dX", "dU", "dO", "dW", "dVV", "dPad", "dF", "dY", "dLk", "dOc", "ls",
               "aC0", "aC1", "aC2", "aL0", "aL1", "aL2"]
+
+
+ORDER, SPAN = [], []
+
+
+def plan(nodes):
+    n = len(nodes)
+    succ, pred = [{} for _ in range(n)], [{} for _ in range(n)]
+    wr, rd = {}, {}
+    only = [x[0][0][0] if len(x[0]) == 1 else None for x in nodes]
+
+    def edge(a, b):
+        if a != b:
+            succ[a][b] = pred[b][a] = nodes[a][3] + (0.0 if only[a] == only[b] == "P" else WAKE)
+    for i, (ways, r, w, late) in enumerate(nodes):
+        for k in r:
+            if k in wr:
+                edge(wr[k], i)
+            if k in BANK:
+                for j in rd.get(k, []):
+                    if only[j] is None or only[j] != only[i]:
+                        edge(j, i)
+        for k in w:
+            if k in wr:
+                edge(wr[k], i)
+            for j in rd.get(k, []):
+                edge(j, i)
+        for k in r:
+            rd.setdefault(k, []).append(i)
+        for k in w:
+            wr[k], rd[k] = i, []
+
+    def sweep(after, before, urgency, start):
+        left = [len(x) for x in before]
+        ready, busy, todo, end, order = list(start), {}, [i for i in range(n) if not left[i]], [0.0] * n, []
+        while todo:
+            i = max(todo, key=lambda j: urgency[j])
+            todo.remove(i)
+            offers = []
+            for k, (q, c) in enumerate(nodes[i][0]):
+                at, place, line = ready[i], 0, busy.setdefault(q, [])
+                place = len(line)
+                while place and line[place - 1][1] > at:
+                    place -= 1
+                while place < len(line) and line[place][0] < at + c:
+                    at = max(at, line[place][1])
+                    place += 1
+                offers.append((at + c + (SPARE if k else 0.0), at, k, place))
+            _, at, k, place = min(offers)
+            q, c = nodes[i][0][k]
+            busy[q].insert(place, (at, at + c))
+            order.append((at, len(order), i, k))
+            end[i] = at + c
+            for j in after[i]:
+                ready[j] = max(ready[j], end[i] + after[i][j])
+                left[j] -= 1
+                if not left[j]:
+                    todo.append(j)
+        return end, [x[2:] for x in sorted(order)]
+    rest = [0.0] * n
+    for i in range(n - 1, -1, -1):
+        rest[i] = nodes[i][0][0][1] + max([rest[j] + succ[i][j] for j in succ[i]] + [nodes[i][3]])
+    best = None
+    for _ in range(PASSES):
+        end, order = sweep(succ, pred, rest, [0.0] * n)
+        span = max(end[i] + nodes[i][3] for i in range(n))
+        if best is None or span < best[0]:
+            best = (span, order)
+        rest = sweep(pred, succ, [end[i] + nodes[i][3] for i in range(n)], [x[3] for x in nodes])[0]
+    SPAN.append(best[0])
+    return best[1]
 
 
 def rank_program(g, core, T, topo):
@@ -97,7 +170,7 @@ def rank_program(g, core, T, topo):
 
     nodes = []
 
-    def emit(q, r, w, fn, time, alone=False):
+    def way(q, r, w, fn, time, alone=False):
         def issue():
             deps(q, r, w)
             s = own[q]
@@ -108,70 +181,28 @@ def rank_program(g, core, T, topo):
             done((s, cnt[s], clk), r, w)
             if alone:
                 sync(q, [(s, cnt[s], clk)])
-        nodes.append((q, r, w, issue, time, -WAKE if alone else 0.0))
+        return (q, issue, time)
 
-    def dma(q, s, r, w, pairs):
+    def emit(q, r, w, fn, time, alone=False):
+        nodes.append(([way(q, r, w, fn, time, alone)], r, w, -WAKE if alone else 0.0))
+
+    def dma(q, s, r, w, pairs, late=2.5):
         def issue():
             deps(q, r, w)
             for o, i in pairs:
                 eng[q].dma_start(o, i).then_inc(T.sem[s], 16)
                 cnt[s] = cnt.get(s, 0) + 16
             done((s, cnt[s], dict(known[q])), r, w)
-        nodes.append((q, r, w, issue, 0.1, 2.5))
+        nodes.append(([(q, issue, 0.05 * len(pairs))], r, w, late))
 
     def arrival(key, r, tok):
-        nodes.append(("R", r, [key], lambda: done(tok, [], [key]), 0.0, FLIGHT))
+        nodes.append(([("R", lambda: done(tok, [], [key]), 0.0)], r, [key], FLIGHT))
 
     def schedule():
-        n = len(nodes)
-        succ, left = [[] for _ in range(n)], [0] * n
-        wr, rd = {}, {}
-
-        def edge(a, b, lag):
-            if a != b:
-                succ[a].append((b, lag))
-                left[b] += 1
-        for i, (q, r, w, fn, c, late) in enumerate(nodes):
-            for k in r:
-                if k in wr:
-                    edge(wr[k], i, 0.0 if q == "P" and nodes[wr[k]][0] == "P" else WAKE)
-                if k in BANK:
-                    for j in rd.get(k, []):
-                        if nodes[j][0] != q:
-                            edge(j, i, WAKE)
-            for k in w:
-                if k in wr:
-                    edge(wr[k], i, 0.0 if q == "P" and nodes[wr[k]][0] == "P" else WAKE)
-                for j in rd.get(k, []):
-                    edge(j, i, WAKE)
-            for k in r:
-                rd.setdefault(k, []).append(i)
-            for k in w:
-                wr[k], rd[k] = i, []
-        rest = [0.0] * n
-        for i in range(n - 1, -1, -1):
-            rest[i] = nodes[i][4] + nodes[i][5] + max([lag + rest[j] for j, lag in succ[i]] + [0.0])
-        ready, free, todo = [0.0] * n, {}, [i for i in range(n) if not left[i]]
-        while todo:
-            best = None
-            for i in todo:
-                at = max(ready[i], free.get(nodes[i][0], 0.0))
-                if best is None or (at, -rest[i]) < best[:2]:
-                    best = (at, -rest[i], i)
-            at, i = best[0], best[2]
-            for j in todo:
-                if nodes[j][0] == nodes[i][0] and max(ready[j], free.get(nodes[j][0], 0.0)) <= at + SLACK and rest[j] > rest[i]:
-                    i = j
-            at = max(ready[i], free.get(nodes[i][0], 0.0))
-            todo.remove(i)
-            nodes[i][3]()
-            end = at + nodes[i][4]
-            free[nodes[i][0]] = end
-            for j, lag in succ[i]:
-                ready[j] = max(ready[j], end + nodes[i][5] + lag)
-                left[j] -= 1
-                if not left[j]:
-                    todo.append(j)
+        if not ORDER:
+            ORDER.extend(plan([([(q, c) for q, fn, c in ways], r, w, late) for ways, r, w, late in nodes]))
+        for i, k in ORDER:
+            nodes[i][0][k][1]()
 
     def cyc(n):
         return CYCLE * max(64, n)
@@ -210,6 +241,22 @@ def rank_program(g, core, T, topo):
         else:
             emit("A", r, w, lambda e: e.activation(out, a, fn, bias, scale, accum_out=acc), cyc(n) + 0.02)
 
+    def lin(r, w, out, a, scale=1.0, bias=0.0, n=64, half=False):
+        plain = isinstance(scale, float) and isinstance(bias, float)
+        if plain and scale == 1.0 and bias == 0.0:
+            v = way("V", r, w, lambda e: e.tensor_copy(out, a), cyc(n // 2 if half else n))
+        else:
+            v = way("V", r, w, lambda e: e.tensor_scalar(out, a, scale, bias, OP.mult, OP.add), cyc(n // 2 if half else n))
+        if plain and scale == 1.0 and bias == 0.0:
+            s = way("A", r, w, lambda e: e.activation(out, a, AF.Copy), cyc(n))
+        else:
+            s = way("A", r, w, lambda e: e.activation(out, a, AF.Copy if plain and bias == 0.0 else AF.Identity, bias, scale), cyc(n))
+        nodes.append(([s, v], r, w, 0.0))
+
+    def zero(w, out, n):
+        nodes.append(([way("V", ["ZR"], w, lambda e: e.memset(out, 0.0), cyc(n // 2)),
+                       way("A", ["ZR"], w, lambda e: e.activation(out, T.ZR[:, 0:n], AF.Copy), cyc(n))], ["ZR"], w, 0.0))
+
     def far(n):
         return 70 + JUMP * n
 
@@ -237,12 +284,13 @@ def rank_program(g, core, T, topo):
     def pick2(r, w, out, row):
         scan(r + ["EB"], w, out, T.EB[:], row, 0.0, OP.add, OP.max, 128)
 
-    dma("S", "dX", [], ["XT"], [(T.XT[:], T.x[:])])
-    dma("A", "dU", [], ["UT"], [(T.UT[:], T.u[:])])
+    dma("S", "dX", [], ["XT"], [(T.XT[:], T.x[:])], 3.5)
+    dma("A", "dU", [], ["UT"], [(T.UT[:], T.u[:])], 2.8)
     dma("S", "dO", [], ["OL"], [(T.OL[:], T.ol[:])])
-    dma("A", "dW", [], ["W"], [(T.cW[:].bitcast(dt.uint8), T.wc[:]), (T.sW[:], T.ws[:])])
-    dma("S", "dVV", [], ["VTL"], [(T.VTL[:], T.v[:])])
+    dma("S", "dW", ["XT"], ["W"], [(T.cW[:].bitcast(dt.uint8), T.wc[:]), (T.sW[:], T.ws[:])], 4.0)
+    dma("S", "dVV", ["XT"], ["VTL"], [(T.VTL[:], T.v[:])])
 
+    fill(["ZR"], T.ZR[:], 0.0, 264)
     iota(["PC"], T.PC[:], [[0, 1]], 0, 1, 1, True)
     iota(["OI"], T.OI[:, 0:16], [[1, 2], [16, 8]], 0, 0, 16, True)
     iota(["OIb"], T.OI[:, 16:24], [[0, 8]], 8, 0, 8, True)
@@ -250,11 +298,10 @@ def rank_program(g, core, T, topo):
     iota(["IR"], T.IR[:], [[0, 16], [1, 16]], 0, 0, 256)
     iota(["TI"], T.TI[:], [[1, 128]], 0, -1, 128)
     iota(["ID"], T.ID[:], [[1, 256]], 0, 0, 256)
-    iota(["BK"], T.BK[:], [[1, 8], [0, 64]], 0, 0, 512)
+    iota(["BK"], T.BK[:], [[1, 8], [0, 16]], 0, 0, 128)
     iota(["C16"], T.CW[:, 16:32], [[16, 16]], 0, 0, 16)
     iota(["NN"], T.NN[:], [[1, 8]], 0, 0, 8)
     iota(["I4"], T.I4[:], [[0, 24], [1, 4]], 0, 0, 96)
-    iota(["CY"], T.CY[:], [[1, 368]], -112, 0, 368)
     cp(["OI", "OIb"], ["OU"], T.OU[:, 0:24], T.OI[:, 0:24])
     PF = {}
     names = ("q", "g", "m1", "q8", "r8", "q4", "r4")
@@ -270,17 +317,17 @@ def rank_program(g, core, T, topo):
 
     def affine(name, src, scale, bias):
         PF[name] = T.PF[:, len(PF):len(PF) + 1]
-        act([src], [name], PF[name], PF[src], AF.Identity, bias, scale)
+        lin([src], [name], PF[name], PF[src], scale, bias)
     affine("q1", "q", 1.0, 1.0)
     affine("qn", "q", -1.0, -0.5)
     number("xq", "q", 15.0, OP.is_lt, 512.0, OP.mult)
     affine("lb", "xq", 0.25, 0.0)
+    affine("nlb", "xq", -0.25, 0.0)
+    affine("nxq", "xq", -1.0, 0.0)
     affine("lb1", "xq", 0.25, 1.0)
     affine("lbc", "xq", 0.25, -223.0)
     affine("xq1", "xq", 1.0, 1.0)
     affine("q7", "q", 7.0, 1.0)
-    affine("nq", "q", -1.0, 0.0)
-    affine("nq128", "q", -1.0, -128.0)
     affine("q3", "q", 1.0, -3.0)
     affine("q16", "q", 1.0, -16.0)
     affine("q41", "q4", 1.0, 1.0)
@@ -299,28 +346,28 @@ def rank_program(g, core, T, topo):
     ts(["NN", "d8"], ["D8L"], T.OU[:, 64:72], T.NN[:], 14.0, OP.mult, T.SC[:, 7:8], OP.add)
     BC32, REP7, HOPS, G8L, D8L = T.OU[:, 24:40], T.OU[:, 40:47], T.OU[:, 48:54], T.OU[:, 56:64], T.OU[:, 64:72]
     ts(["IR", "q"], ["NB"], T.NB[:], T.IR[:], PF["q"], OP.not_equal, 2.0 ** 90, OP.mult, 128)
-    fill(["RS"], T.RS[:], 0.0, 256)
+    zero(["RS"], T.RS[:], 512)
     fill(["RS"], T.RS[:, 0:256:16], 2.0 ** 95)
     fill(["RS"], T.RS[:, 256:512:16], -2.0 ** 95)
     fill(["RC"], T.RC[:], 512.0, 128)
     ts(["C16", "q16"], ["RC"], T.RC[:, 0:256:16], T.CW[:, 16:32], -1.0, OP.mult, PF["q16"], OP.add)
     ts(["IR", "q"], ["e0"], T.ET0[:, 0:256], T.IR[:], PF["q"], OP.is_equal, -2.0 ** 20, OP.mult, 128)
-    ts(["IR", "q1"], ["e1"], T.ET0[:, 256:512], T.IR[:], PF["q1"], OP.is_equal, 512.0, OP.mult, 128)
-    tt(["e0", "e1"], ["EX"], T.EX[:], T.ET0[:, 0:256], T.ET0[:, 256:512], OP.add, 512)
-    act(["EX"], ["EB"], T.EB[:], T.EX[:], AF.Copy, 0.0, 0.25, n=256)
+    ts(["IR", "q1"], ["e1"], T.ET0[:, 256:512], T.IR[:], PF["q1"], OP.is_equal, -2.0 ** -11, OP.mult, 128)
+    scan(["e0", "e1"], ["EX"], T.EX[:], T.ET0[:, 256:512], T.ET0[:, 0:256], 0.0, OP.mult, OP.add, 128)
+    lin(["EX"], ["EB"], T.EB[:], T.EX[:], 0.25, n=256, half=True)
     ts(["I4", "q4", "EX"], ["e0"], T.ET0[:, 0:96], T.I4[:], PF["q4"], OP.is_equal, -2.0 ** 20, OP.mult)
-    ts(["I4", "q41", "EX"], ["e1"], T.ET0[:, 256:352], T.I4[:], PF["q41"], OP.is_equal, 512.0, OP.mult)
-    tt(["e0", "e1"], ["E4"], T.E4[:], T.ET0[:, 0:96], T.ET0[:, 256:352], OP.add, 192)
+    ts(["I4", "q41", "EX"], ["e1"], T.ET0[:, 256:352], T.I4[:], PF["q41"], OP.is_equal, -2.0 ** -11, OP.mult)
+    scan(["e0", "e1"], ["E4"], T.E4[:], T.ET0[:, 256:352], T.ET0[:, 0:96], 0.0, OP.mult, OP.add)
     ts(["TI"], ["TR"], T.TR[:], T.TI[:], 0.0, OP.is_le)
-    fill(["T128"], T.TK[:, 3072:3584], 128.0, 256)
-    fill(["TKB"], T.TK[:, 2560:3072], 1.0, 256)
-    ts(["BK", "g"], ["TKS"], T.TK[:, 2048:2560], T.BK[:], PF["g"], OP.is_equal, n=256)
-    quant(["TKB"], "KB", 128, T.TK[:, 2560:3072])
-    quant(["TKS"], "KS", 128, T.TK[:, 2048:2560])
+    fill(["TKB"], T.TK[:, 0:512], 1.0, 256)
+    for i in range(4):
+        ts(["BK", "g"], ["TKS%d" % i], T.TK[:, 512 + i:1024:4], T.BK[:], PF["g"], OP.is_equal)
+    zero(["TKR"], T.TK[:, 1024:1552], 528)
+    ts(["TI"], ["TKR"], T.TK[:, 1027:1539:4], T.TI[:], 0.0, OP.is_equal, 128.0, OP.mult)
+    quant(["TKB"], "KB", 128, T.TK[:, 0:512])
+    quant(["TKS%d" % i for i in range(4)], "KS", 128, T.TK[:, 512:1024])
     for b in range(4):
-        emit("G", ["T128"], ["TK%d" % b], lambda e, b=b: e.affine_select(
-            T.TK[:, 512 * b:512 * b + 512], T.TK[:, 3072:3584], [[-1, 128], [1000, 4]], OP.is_equal, 0.0, -1000 * b, 1), 1.1)
-        quant(["TK%d" % b], "KR%d" % b, 128, T.TK[:, 512 * b:512 * b + 512])
+        quant(["TKR"], "KR%d" % b, 128, T.TK[:, 1027 - b:1539 - b])
     quant(["UT"], "U", 128, T.UT[:])
     for i in (0, 2, 1):
         c = slice(128 * i, 128 * i + 128)
@@ -333,18 +380,16 @@ def rank_program(g, core, T, topo):
         for a in range(4):
             o = 4 * (TILE_O[4] * s + TILE_O[a])
             lo = 64 * (13 - 4 * a)
-            fill(["z%d%d" % (s, a)], T.CT[:, o + lo:o + 4 * TILE_N[a]], 0.0, 2 * TILE_N[a] - lo // 2)
-    fill(["zB"], T.BT[:], 0.0, 512)
+            zero(["z%d%d" % (s, a)], T.CT[:, o + lo:o + 4 * TILE_N[a]], 4 * TILE_N[a] - lo)
+    for i in (2, 3):
+        zero(["zB%d" % i], T.BT[:, i:1024:4], 256)
     fill(["AR"], T.AR[:], 0.0)
     dma("S", "dPad", ["X0"], ["pad"], [(T.cL[:, 288:320].bitcast(dt.uint8), T.cX[:, 0:32].bitcast(dt.uint8)),
                                        (T.sL[:, 288:320], T.sX[:, 0:32])])
-    act(["CY", "nq128"], ["CB"], T.CB[:], T.CY[:], AF.Abs, PF["nq128"], n=368)
-    act(["CB"], ["CB"], T.CB[:], T.CB[:], AF.Relu, 1024.0, -1024.0, n=368)
-    act(["CY", "nq"], ["CY"], T.CY[:], T.CY[:], AF.Abs, PF["nq"], n=368)
-    act(["CY"], ["CY"], T.CY[:], T.CY[:], AF.Relu, 1.0, -1.0, n=368)
-    tt(["CY", "CB"], ["CB"], T.CB[:], T.CB[:], T.CY[:], OP.add, 736)
+    zero(["CB"], T.CB[:], 368)
+    ts(["IR", "q"], ["CB"], T.CB[:, 112:128], T.IR[:, 0:16], PF["q"], OP.is_equal)
+    ts(["IR", "q"], ["CB"], T.CB[:, 240:256], T.IR[:, 0:16], PF["q"], OP.is_equal, 1024.0, OP.mult)
     fill(["C64"], T.C64[:], 64.0)
-    fill(["ZR"], T.ZR[:], 0.0, 128)
     fill(["PD2"], T.PD2[:], 0.0)
     fill(["PD2"], T.PD2[:, 1:96:2], 256.0)
     fill(["Q4z"], T.QQ[:, 0:32], 0.0)
@@ -352,19 +397,17 @@ def rank_program(g, core, T, topo):
     fill(["RTz"], T.RT[:, 384:512], 0.0)
     fill(["GS0"], T.GS[:, 0:16], 32.0)
     fill(["I1z"], T.I1[:, 112:120], 0)
-    fill(["YXz"], T.YX[:, 0:256], 0.0, 128)
-    fill(["C8"], T.C8[:], 0.0, 128)
+    zero(["YXz"], T.YX[:, 0:256], 256)
     fill(["HD"], T.HD[:], 0.0)
     quant(["VTL"], "V", 128, T.VTL[:])
     CW = T.CW[:, 0:16]
     ts(["C16", "q"], ["CW"], CW, T.CW[:, 16:32], PF["q"], OP.add)
     ts(["CW", "lbc"], ["CP"], T.CP[:], CW, PF["lbc"], OP.add)
-    cp(["CW"], ["C8"], T.C8[:, 0:128:8], CW)
-    cp(["CW"], ["HD"], T.HD[:, 33:64:2], CW)
+    lin(["CW"], ["HD"], T.HD[:, 33:64:2], CW)
     for s in (0, 7):
-        act(["ZR", "lb"], ["FP%d" % s], T.FP[:, 256 * s:256 * s + 256], T.ZR[:], AF.Identity, PF["lb"], n=256)
+        lin(["ZR", "lb"], ["FP%d" % s], T.FP[:, 256 * s:256 * s + 256], T.ZR[:, 0:256], 1.0, PF["lb"], 256, True)
     VV, VT0, VT6 = T.VT[:, 105:1888:16], T.VT[:, 105:1888:112], T.VT[:, 201:1888:112]
-    act(["ZR", "xq"], ["VT0"], VT0, T.ZR[:, 0:16], AF.Identity, PF["xq"])
+    lin(["ZR", "xq"], ["VT0"], VT0, T.ZR[:, 0:16], 1.0, PF["xq"])
     cp(["OL"], ["L16"], T.L16[:], T.OL[:])
     ts(["OL", "xq"], ["VT6"], VT6, T.OL[:], 2.0 ** -8, OP.mult, PF["xq"], OP.add)
 
@@ -373,14 +416,15 @@ def rank_program(g, core, T, topo):
     mask = topo.mask(core, nxt)
     n_eng = len(topo.engines(core, nxt))
     n_arr = len(topo.engines(prv, core))
-    sent = [0]
+    sent, first = [0], []
 
     def send(r, out, src, rsem):
         def issue():
             deps("G", r, [])
             g.remote_dma(out, src, T.sem[rsem], T.sem.ls, pid, rid, mask)
             sent[0] += n_eng
-        nodes.append(("G", r, ["snd" + rsem], issue, SEND, 0.0))
+        nodes.append(([("G", issue, SEND + (0.0 if first else FIRST))], r, ["snd" + rsem], 0.0))
+        first.append(rsem)
 
     for t in range(ROUNDS):
         X = "X%d" % t
@@ -394,19 +438,21 @@ def rank_program(g, core, T, topo):
         act(["PD0", "PD1"], ["SB"], T.SB2[:], T.PD[:, 8:1024:512])
         act(["PD0", "PD1"], ["DL"], T.DL[:], T.PD[:, 8:1024:512], AF.Abs, 2.0 ** -124, 1.25 * 2.0 ** -24)
         for h in range(2):
-            act(["TR", "DL", "SB"], ["TH%d" % h], T["TH%d" % h][:], T.TR[:], AF.Identity,
-                T.SB2[:, h:h + 1], T.DL[:, h:h + 1], n=128)
-        ts(["PC_", "SB", "zB"], ["BTa"], T.BT[:, 512:1024:4], ps("PC_", 128, 256), T.SB2[:, 0:1], OP.is_ge, n=128)
-        ts(["PC_", "SB", "zB"], ["BTb"], T.BT[:, 1:512:4], ps("PC_", 0, 128), T.SB2[:, 1:2], OP.is_gt, n=128)
-        tt(["PC_", "TH0", "zB"], ["BTc"], T.BT[:, 0:512:4], ps("PC_", 0, 128), T.TH0[:], OP.is_ge, 128)
-        tt(["PC_", "TH1", "zB"], ["BTd"], T.BT[:, 513:1024:4], ps("PC_", 128, 256), T.TH1[:], OP.is_ge, 128)
-        quant(["BTa", "BTb", "BTc", "BTd"], "B", 256, T.BT[:])
+            lin(["TR", "DL", "SB"], ["TH%d" % h], T["TH%d" % h][:], T.TR[:], T.DL[:, h:h + 1], T.SB2[:, h:h + 1], 128)
+        ts(["PC_", "SB"], ["BTa"], T.BT[:, 512:1024:4], ps("PC_", 128, 256), T.SB2[:, 0:1], OP.is_ge, n=128)
+        ts(["PC_", "SB"], ["BTb"], T.BT[:, 1:512:4], ps("PC_", 0, 128), T.SB2[:, 1:2], OP.is_gt, n=128)
+        tt(["PC_", "TH0"], ["BTc"], T.BT[:, 0:512:4], ps("PC_", 0, 128), T.TH0[:], OP.is_ge, 128)
+        tt(["PC_", "TH1"], ["BTd"], T.BT[:, 513:1024:4], ps("PC_", 128, 256), T.TH1[:], OP.is_ge, 128)
+        quant(["BTa", "BTb", "BTc", "BTd", "zB2", "zB3"], "B", 256, T.BT[:])
         mm(["B", "KB"], "PC_", 256, "KB", 0, "B", 0)
 
         def places(s):
             bank, sums = (("PA", "PD0"), ("PB", "PD1"))[s]
             c = slice(256 * s, 256 * s + 256)
             o = 4 * TILE_O[4] * s
+            if BY_SIGN[s]:
+                n = 16 * max(BY_SIGN[s])
+                act([bank], ["SR%d" % s], T.SR[:, 256 * s:256 * s + n], ps(bank, 0, n), n=n)
             tt([bank, "NB"], ["SG%d" % s], T.SG[:, c], ps(bank, 0, 256), T.NB[:], (OP.add, OP.subtract)[s], 256)
             scan(["RS", "SG%d" % s], ["SW%d" % s], T.SW[:, c], T.RS[:, c], T.SG[:, c], 0.0, OP.add, (OP.min, OP.max)[s], 256)
             run = T.CT[:, o:o + 1024:4]
@@ -417,6 +463,13 @@ def rank_program(g, core, T, topo):
                 for j, m in enumerate(ms):
                     if m < 16:
                         v = T.CT[:, o + 4 * TILE_O[a] + j:o + 4 * TILE_O[a] + 64 * m:4]
+                        if m in BY_SIGN[s]:
+                            k = 256 * (m % 2)
+                            act(["SR%d" % s, "SW%d" % s], ["SN%d" % (m % 2)], T.SN[:, k:k + 16 * m], T.SR[:, 256 * s:256 * s + 16 * m],
+                                AF.Sign, T.SW[:, 256 * s + 16 * m + 15:256 * s + 16 * m + 16], -1.0, n=16 * m)
+                            act(["SN%d" % (m % 2), "AR", "z%d%d" % (s, a)], ["AR%d.%d" % (s, m), "ct%d.%d" % (s, m)], v, T.SN[:, k:k + 16 * m],
+                                AF.Relu, 0.0, (-1.0, 1.0)[s], T.AR[:, 16 * s + m:16 * s + m + 1], n=16 * m)
+                            continue
                         ts([bank, "SW%d" % s, "z%d%d" % (s, a)], ["ct%d.%d" % (s, m)], v, ps(bank, 0, 16 * m),
                            T.SW[:, 256 * s + 16 * m + 15:256 * s + 16 * m + 16], (OP.is_gt, OP.is_lt)[s], n=16 * m)
                         act(["ct%d.%d" % (s, m), "AR"], ["AR%d.%d" % (s, m), "AJ%d" % j], T.AJ[:, 256 * j:256 * j + 16 * m], v,
@@ -434,12 +487,12 @@ def rank_program(g, core, T, topo):
         for b in range(4):
             k = ("Q0", "Q1", "Q2", "Q0")[b]
             mm(XK + ["KR%d" % b], k, 256, "KR%d" % b, 0, X, 0)
-            act([k], ["FT%d" % b], T.FT[:, 256 * b:256 * b + 256], ps(k, 0, 256), AF.Copy, 0.0, 2.0 ** -8, n=256)
+            lin([k], ["FT%d" % b], T.FT[:, 256 * b:256 * b + 256], ps(k, 0, 256), 2.0 ** -8, n=256)
         dma("S", "dF", ["FT0", "FT1", "FT2", "FT3"], ["FU"], [(T.FU[:], T.FT[:])])
-        act(["ID", "L16"], ["LF"], T.LF[:], T.ID[:].indirect(T.L16[:]), AF.Copy, 0.0, 2.0 ** -8, n=far(256))
+        lin(["ID", "L16"], ["LF"], T.LF[:], T.ID[:].indirect(T.L16[:]), 2.0 ** -8, n=far(256))
         tt(["PC_", "LF"], ["VH0"], T.VH[:, 0:256], ps("PC_", 0, 256), T.LF[:], OP.add, 256)
         for i in range(1, 6):
-            act(["VH%d" % (i - 1), "L16"], ["VH%d" % i], T.VH[:, 256 * i:256 * i + 256],
+            lin(["VH%d" % (i - 1), "L16"], ["VH%d" % i], T.VH[:, 256 * i:256 * i + 256],
                 T.VH[:, 256 * i - 256:256 * i].indirect(T.L16[:]), n=far(256))
             pick(["VH%d" % i], ["VT%d" % (6 - i)], T.VT[:, 96 - 16 * i:96 - 16 * i + 1786:7], T.VH[:, 256 * i:256 * i + 256])
         VK = ["VT%d" % k for k in range(7)]
@@ -461,19 +514,20 @@ def rank_program(g, core, T, topo):
         cp(["ID", "EP16"], ["EF"], T.EF[:].indirect(T.EP16[:]), T.ID[:], 60 + STREW * 256)
         scan(["E4", "EF"], ["ES"], T.ES[:], T.E4[:], T.EF[:, 0:96], 0.0, OP.add, OP.max, 96)
         ts(["ES", "eo"], ["EO"], T.EO[:], T.ES[:, 3:96:4], 4.0, OP.mult, PF["eo"], OP.add)
-        cp(ZK + ["EO"], ["ETa"], T.ET[:, 0:192], T.Z[:].indirect(T.EO[:, 0:12]), far(192))
-        cp(ZK + ["EO"], ["ETb"], T.ET[:, 192:384], T.Z[:].indirect(T.EO[:, 12:24]), far(192))
+        lin(ZK + ["EO"], ["ETa"], T.ET[:, 0:192], T.Z[:].indirect(T.EO[:, 0:12]), n=far(192))
+        lin(ZK + ["EO"], ["ETb"], T.ET[:, 192:384], T.Z[:].indirect(T.EO[:, 12:24]), n=far(192))
         scan(["PD2", "EF"], ["PK"], T.PK[:], T.PD2[:], T.EF[:, 0:96], 0.0, OP.mult, OP.add, 96)
         cp(["PK"], ["LS%d" % t], T.LS[:, 48 * t:48 * t + 48], T.PK[:, 1:96:2])
         lo = KEEP * (ROUNDS - 1 - t)
         quant(["ETa", "ETb", "ETz"], "E%d" % t, 128, T.ET[:])
         send(["LS%d" % t], T.LL[:, 48 * t:48 * t + 48], T.LS[:, 48 * t:48 * t + 48], "aL%d" % t)
-        send(["E%d" % t], T.cL[:, lo:lo + KEEP].bitcast(dt.uint8), T.cE[:, 128 * t:128 * t + KEEP].bitcast(dt.uint8), "aC%d" % t)
+        send(["E%d" % t, "sndaL0"], T.cL[:, lo:lo + KEEP].bitcast(dt.uint8), T.cE[:, 128 * t:128 * t + KEEP].bitcast(dt.uint8), "aC%d" % t)
         send(["E%d" % t], T.sL[:, lo:lo + KEEP], T.sE[:, 128 * t:128 * t + KEEP], "aC%d" % t)
         arrival("L%d" % t, ["sndaC%d" % t], ("aC%d" % t, 2 * n_arr, {}))
         arrival("LL%d" % t, ["sndaL%d" % t], ("aL%d" % t, n_arr, {}))
         cp(["I1", "I1z", "HOPS"], ["H16"], T.H16[:], T.I1[:].indirect(HOPS), far(96))
-        tt(["D7", "D8L", "C8"], ["D8", "D8e"], T.D8[:], T.D7[:].indirect(D8L), T.C8[:], OP.add, far(128))
+        lin(["D7", "D8L"], ["D8", "D8e"], T.D8[:], T.D7[:].indirect(D8L), n=far(128))
+        tt(["CW", "I1"], ["D8"], T.D8[:, 0:128:8], CW, T.I1[:, 1:112:7], OP.subtract)
         across(["CA%d" % z for z in range(8)], ["CI0"], T.CI[0:64, 0:8], T.CA[0:64, :], T.CA[64:128, :])
         ts(["CI0"], ["CI1"], T.CI[0:64, 8:16], T.CI[0:64, 0:8], 1023, OP.bitwise_and)
         ts(["CI0"], ["CI2"], T.CI[0:64, 16:24], T.CI[0:64, 0:8], 10, OP.arith_shift_right)
@@ -483,7 +537,7 @@ def rank_program(g, core, T, topo):
         tt(["Q5"], ["Q6b"], T.QQ[0:32, 80:96], T.QQ[0:32, 32:48], T.QQ[0:32, 48:64], OP.add)
         for a in range(4):
             turn(["Q6", "Q6b"], ["Q7%d" % a], T.QQ[32 * a:32 * a + 32, 96:128], T.QQ[0:32, 64:96])
-        act(["Q70", "Q71", "Q72", "Q73", "BC32"], ["RP"], T.RP[:], T.QQ[:, 96:128].indirect(BC32), n=far(256))
+        lin(["Q70", "Q71", "Q72", "Q73", "BC32"], ["RP"], T.RP[:], T.QQ[:, 96:128].indirect(BC32), n=far(256))
         turn(["RP"], ["TO"], T.TO[:], T.RP[:], 128)
         act(["TO", "qn"], ["AJ0", "AC"], T.AJ[:, 0:256], T.TO[:], AF.Sign, PF["qn"], 1.0, T.SC[:, 0:1], n=256)
         ts(["C64", "AC"], ["FBa"], T.FB[:, 0:32], T.C64[:], T.SC[:, 0:1], OP.is_ge)
@@ -493,7 +547,7 @@ def rank_program(g, core, T, topo):
         scan(["FX"], ["XS"], T.XS[:], T.FB[:, 64:80], T.FB[:, 96:112], 128.0, OP.mult, OP.max)
         ts(["TO", "SF"], ["LT"], T.LT[:], T.TO[:], T.SC[:, 1:2], OP.add, 16.0, OP.is_lt, 128)
         ts(["TO", "SF"], ["LE"], T.LE[:], T.TO[:], T.SC[:, 1:2], OP.add, 16.0, OP.is_le, 128)
-        scan(["LT", "ZR", "XS"], ["AA"], T.AA[:], T.LT[:], T.ZR[:], T.XS[:, 15:16], OP.add, OP.max, 128)
+        scan(["LT", "ZR", "XS"], ["AA"], T.AA[:], T.LT[:], T.ZR[:, 0:256], T.XS[:, 15:16], OP.add, OP.max, 128)
         scan(["LE", "AA", "GS0"], ["GS"], T.GS[:, 1:257], T.LE[:], T.AA[:], 32.0, OP.add, OP.min, 128)
         pick2(["GS"], ["P1"], T.P1[:], T.GS[:, 1:257])
         pick2(["GS"], ["P0"], T.P0[:], T.GS[:, 0:256])
@@ -506,41 +560,36 @@ def rank_program(g, core, T, topo):
             k = ("Q0", "Q1", "Q2", "PC_")[b]
             mm(["L%d" % t, "pad", "W"], k, 128, "W", 128 * b, "L", lo, True, False)
             mm(["L%d" % t, "pad", "KR%d" % b], k, 128, "KR%d" % b, 0, "L", lo, False, True)
-            if b < 3:
-                act([k, "RTz"], ["RT%d" % b], T.RT[:, b:384:4], ps(k, 0, 96), AF.Copy, 0.0, 2.0 ** -7, n=96)
-            else:
-                ts([k, "RTz"], ["RT%d" % b], T.RT[:, b:384:4], ps(k, 0, 96), 2.0 ** -7, OP.mult, n=96)
+            lin([k, "RTz"], ["RT%d" % b], T.RT[:, b:384:4], ps(k, 0, 96), 2.0 ** -7, n=96)
         quant(["RT0", "RT1", "RT2", "RT3"], "Pb", 128, T.RT[:])
         XN = "X%d" % (t + 1)
         emit("V", ["P", "Pb", "NI16"], [XN], lambda e, t=t: e.tensor_copy(
             T.cX[:, 256 * t + 256:256 * t + 512].bitcast(dt.uint32), T.cP[:, :].bitcast(dt.uint32).indirect(T.NI16[:])), cyc(far(256)))
-        emit("A", ["P", "Pb", "NI16"], [XN + "s"], lambda e, t=t: e.activation(
-            T.sX[:, 256 * t + 256:256 * t + 512], T.sP[:, :].indirect(T.NI16[:]), AF.Copy), cyc(far(256)))
-        for i in range(3):
-            c = slice(512 * i, 512 * i + 512)
-            (cp if last and i == 1 else act)(["GN", "H16"], ["FL%d" % i], T.FL[:, c], T.GN[:].indirect(T.H16[:, 32 * i:32 * i + 32]), n=far(512))
-            for s in (2 * i, 2 * i + 1):
-                pick2(["FL%d" % i], ["FP%d" % (s + 1)], T.FP[:, 256 * s + 256:256 * s + 512], T.FL[:, 256 * s:256 * s + 256])
-        ts(["HDa", "lb1"], ["FP7"], T.FP[:, 1807:2048:16], T.HD[:, 1:32:2], -1.0, OP.mult, PF["lb1"], OP.add)
+        lin(["P", "Pb", "NI16"], [XN + "s"], T.sX[:, 256 * t + 256:256 * t + 512], T.sP[:, :].indirect(T.NI16[:]), n=far(256))
+        for s in range(6):
+            c = slice(256 * s, 256 * s + 256)
+            lin(["GN", "H16"], ["FL%d" % s], T.FL[:, c], T.GN[:].indirect(T.H16[:, 16 * s:16 * s + 16]), n=far(256))
+            pick2(["FL%d" % s], ["FP%d" % (s + 1)], T.FP[:, 256 * s + 256:256 * s + 512], T.FL[:, c])
+        lin(["HDa", "lb1"], ["FP7"], T.FP[:, 1807:2048:16], T.HD[:, 1:32:2], -1.0, PF["lb1"])
         cp(["LL%d" % t], ["LI0"], T.LI[:, 0:48], T.LL[:, 48 * t:48 * t + 48])
         ts(["LI0"], ["LI1"], T.LI[:, 49:144:2], T.LI[:, 0:48], 255, OP.bitwise_and)
         ts(["LI0"], ["LI2"], T.LI[:, 48:144:2], T.LI[:, 0:48], 8, OP.arith_shift_right)
         cp(["LI1", "LI2"], ["YXe"], T.YX[:, 256:352], T.LI[:, 48:144], 96)
-        act(["YXz", "YXe", "NI16"], ["EW"], T.EW[:], T.YX[:].indirect(T.NI16[:]), n=far(256))
+        lin(["YXz", "YXe", "NI16"], ["EW"], T.EW[:], T.YX[:].indirect(T.NI16[:]), n=far(256))
         pick(["EW"], ["EQ"], T.EQ[:], T.EW[:])
-        ts(["EQ", "xq"], ["D8e"], T.D8[:, 7:128:8], T.EQ[:, E15], PF["xq"], OP.subtract)
-        ts(["FP%d" % s for s in range(8)] + ["G8L", "lb"], ["G8"], T.G8[:], T.FP[:].indirect(G8L), PF["lb"], OP.subtract, n=far(128))
+        lin(["EQ", "nxq"], ["D8e"], T.D8[:, 7:128:8], T.EQ[:, E15], 1.0, PF["nxq"])
+        lin(["FP%d" % s for s in range(8)] + ["G8L", "nlb"], ["G8"], T.G8[:], T.FP[:].indirect(G8L), 1.0, PF["nlb"], far(128))
         scan(["G8", "D8", "D8e"], ["HL"], T.HL[:], T.G8[:], T.D8[:], 0.0, OP.mult, OP.add, 128)
         cp(["HL"], ["L16"], T.L16[:], T.HL[:, 7:128:8])
         if not last:
-            ts(["HL", "xq"], ["VT6"], VT6, T.HL[:, 7:128:8], 2.0 ** -8, OP.mult, PF["xq"], OP.add)
+            lin(["HL", "xq"], ["VT6"], VT6, T.HL[:, 7:128:8], 2.0 ** -8, PF["xq"])
 
     mm(["V", "X3", "X3s"], "PA", 256, "V", 0, "X3", 0)
     dma("S", "dOc", ["X3", "X3s"], ["oc"], [(T.oc[:, :], T.cX[:, 768:1024].bitcast(dt.uint8))] + [
         (T.osc[4 * k:4 * k + 4, :], T.sX[32 * k:32 * k + 4, 768:1024]) for k in range(4)])
-    act(["PA"], ["YO"], T.YO[:], ps("PA", 0, 256), n=256)
-    dma("S", "dY", ["YO"], ["y"], [(T.y[:, :], T.YO[:])])
-    cp(["ID", "L16"], ["LO"], T.LO[:], T.ID[:].indirect(T.L16[:]), far(256))
+    lin(["PA"], ["YO"], T.YO[:], ps("PA", 0, 256), n=256)
+    dma("A", "dY", ["YO"], ["y"], [(T.y[:, :], T.YO[:])])
+    lin(["ID", "L16"], ["LO"], T.LO[:], T.ID[:].indirect(T.L16[:]), n=far(256))
     dma("S", "dLk", ["LO"], ["lk"], [(T.lk[:, :], T.LO[0:128:16, :])])
     schedule()
     for s in cnt:

@@ -28,16 +28,16 @@ _q(K=768)
 _q(C=256 + 2 * TILE_O[4])
 _sb(B, TK=1552, IR=256, I4=96, TI=128, BK=128, NB=256, RS=512, RC=256, EX=256, EB=256, E4=96, ET0=512, TR=128)
 _sb(B, C64=32, ZR=528, PD2=96, CB=368, SN=512)
-_sb(F, ID=256, PF=32, CW=32, NN=8, CP=16, TMP=8)
-_sb(U, OU=72)
-_sb(F, SR=512, SG=512, SW=512, SB2=2, DL=2, TH0=128, TH1=128, AR=32, RW=32, EC=512, TE=16, EP=16)
+_sb(F, ID=256, PF=32, CW=48, NN=8, CP=16, TMP=8)
+_sb(U, OU=80, SL=24)
+_sb(F, SR=512, SG=512, SW=512, SB2=2, DL=2, TH0=128, TH1=128, AR=32, RW=32, EC=512, EP=16)
 _sb(B, BT=1024, CT=8 * TILE_O[4], AJ=1024, RD=512)
 _sb(F, LF=256, VH=1536, VT=1888, D7=112, CM=112, HR=112, D8=128, G8=128, HL=128)
 _sb(B, FT=1024, FU=1024, Z=1024, ET=512, RT=512)
 _sb(F, EF=256, ES=96, PK=96)
 _sb(U, EP16=16, EO=24, LS=144, LL=144, R16=16, NI16=16, L16=16, H16=96)
-_sb(F, CA=8, CJ=512, QQ=128, SC=8, XS=16, HD=64, HO=32, EW=256, EQ=256, YO=256, LO=256)
-_sb(B, RP=256, TO=256, FB=128, LT=256, LE=256, AA=256, GS=272, GN=256, P1=256, P0=256, FL=1536, FP=2048, YX=352)
+_sb(F, CA=8, CJ=512, QQ=128, SC=8, HD=64, HO=32, YO=256, LO=256, VR=112)
+_sb(B, EW=256, EQ=256, RP=256, TO=256, FB=64, LT=256, LE=256, AA=256, GS=608, GN=256, TG=1088, FL=1536, FP=2048, YX=352)
 for _k in ("PA", "PB", "PC_", "Q0", "Q1", "Q2"):
     SCRATCH[_k] = ("psum", [128, 512], F)
 SCRATCH["PD"] = ("psum", [128, 1024], F)
@@ -50,8 +50,8 @@ for _i in range(4):
     PLACE["C0%d" % _i] = ("C", 256 + TILE_O[_i])
     PLACE["C1%d" % _i] = ("C", 256 + TILE_O[4] + TILE_O[_i])
     PLACE["E%d" % _i] = ("E", 128 * _i)
-CYCLE, WAKE, FLIGHT, JUMP, STREW, SEND, FIRST = 0.00088, 0.2, 3.0, 1.5, 3.5, 0.7, 2.0
-PASSES, SPARE = 10, 0.3
+CYCLE, WAKE, FLIGHT, JUMP, STREW, SEND, FIRST = 0.00085, 0.23, 2.5, 1.5, 3.5, 0.5, 1.0
+TRIES, SHAKE, SPARE = 3000, 1.5, 0.3
 BY_SIGN = ((), (11, 10, 9))
 
 SEMAPHORES = ["sV", "sA", "sP", "sG", "dX", "dU", "dO", "dW", "dVV", "dPad", "dF", "dY", "dLk", "dOc", "ls",
@@ -88,45 +88,79 @@ def plan(nodes):
         for k in w:
             wr[k], rd[k] = i, []
 
-    def sweep(after, before, urgency, start):
-        left = [len(x) for x in before]
-        ready, busy, todo, end, order = list(start), {}, [i for i in range(n) if not left[i]], [0.0] * n, []
-        while todo:
-            i = max(todo, key=lambda j: urgency[j])
-            todo.remove(i)
-            offers = []
+    succ, pred = [list(x.items()) for x in succ], [list(x.items()) for x in pred]
+    late = [x[3] for x in nodes]
+
+    def sweep(before, urgency, start, spare):
+        end, order, lines = [None] * n, [], {q: ([], []) for q in "VAPGSR"}
+
+        def put(i):
+            ready = start[i]
+            for j, lag in before[i]:
+                if end[j] is None:
+                    put(j)
+                if end[j] + lag > ready:
+                    ready = end[j] + lag
+            best = None
             for k, (q, c) in enumerate(nodes[i][0]):
-                at, place, line = ready[i], 0, busy.setdefault(q, [])
-                place = len(line)
-                while place and line[place - 1][1] > at:
-                    place -= 1
-                while place < len(line) and line[place][0] < at + c:
-                    at = max(at, line[place][1])
+                begins, ends = lines[q]
+                at, place, top = ready, 0, len(ends)
+                m = top
+                while place < top:
+                    mid = (place + top) // 2
+                    if ends[mid] > at:
+                        top = mid
+                    else:
+                        place = mid + 1
+                while place < m and begins[place] < at + c:
+                    at = ends[place]
                     place += 1
-                offers.append((at + c + (SPARE if k else 0.0), at, k, place))
-            _, at, k, place = min(offers)
+                offer = (at + c + (spare[i] if k else 0.0), at, k, place)
+                if best is None or offer < best:
+                    best = offer
+            _, at, k, place = best
             q, c = nodes[i][0][k]
-            busy[q].insert(place, (at, at + c))
+            lines[q][0].insert(place, at)
+            lines[q][1].insert(place, at + c)
             order.append((at, len(order), i, k))
             end[i] = at + c
-            for j in after[i]:
-                ready[j] = max(ready[j], end[i] + after[i][j])
-                left[j] -= 1
-                if not left[j]:
-                    todo.append(j)
-        return end, [x[2:] for x in sorted(order)]
+        for i in sorted(range(n), key=lambda j: -urgency[j]):
+            if end[i] is None:
+                put(i)
+        return end, order
+
+    def passes(urgency, spare, count):
+        best = None
+        for p in range(count):
+            end, order = sweep(pred, urgency, [0.0] * n, spare)
+            shown = [end[i] + late[i] for i in range(n)]
+            if best is None or max(shown) < best[0]:
+                best = (max(shown), order, urgency, spare)
+            if p < count - 1:
+                urgency = sweep(succ, shown, late, spare)[0]
+        return best
     rest = [0.0] * n
     for i in range(n - 1, -1, -1):
-        rest[i] = nodes[i][0][0][1] + max([rest[j] + succ[i][j] for j in succ[i]] + [nodes[i][3]])
-    best = None
-    for _ in range(PASSES):
-        end, order = sweep(succ, pred, rest, [0.0] * n)
-        span = max(end[i] + nodes[i][3] for i in range(n))
-        if best is None or span < best[0]:
-            best = (span, order)
-        rest = sweep(pred, succ, [end[i] + nodes[i][3] for i in range(n)], [x[3] for x in nodes])[0]
+        rest[i] = nodes[i][0][0][1] + max([rest[j] + lag for j, lag in succ[i]] + [late[i]])
+    best = passes(rest, [SPARE] * n, 6)
+    seed = [1]
+
+    def chance():
+        seed[0] = (seed[0] * 1103515245 + 12345) % 2147483648
+        return seed[0] / 2147483648.0
+    for _ in range(TRIES):
+        urgency, spare = list(best[2]), list(best[3])
+        mid, wide = chance() * best[0], 1.0 + 5.0 * chance()
+        for i in range(n):
+            if abs(urgency[i] - mid) < wide:
+                urgency[i] += SHAKE * (chance() + chance() - 1.0)
+                if len(nodes[i][0]) > 1 and chance() < 0.3:
+                    spare[i] = (-0.3, 0.0, 0.3, 1.0, 3.0)[int(5 * chance())]
+        other = passes(urgency, spare, 2)
+        if other[0] <= best[0] + 0.02:
+            best = other
     SPAN.append(best[0])
-    return best[1]
+    return [x[2:] for x in sorted(best[1])]
 
 
 def rank_program(g, core, T, topo):
@@ -263,12 +297,12 @@ def rank_program(g, core, T, topo):
     def ps(bank, a, b, step=1):
         return T[BANK[bank][0]][:, BANK[bank][1] + a:BANK[bank][1] + b:step]
 
-    def mm(r, bank, n, L, l0, R, r0, start=True, stop=True):
+    def mm(r, bank, n, L, l0, R, r0, start=True, stop=True, line=[]):
         L, lo_ = PLACE.get(L, (L, 0))
         R, ro_ = PLACE.get(R, (R, 0))
         l0, r0 = l0 + lo_, r0 + ro_
         o = BANK[bank][1]
-        emit("P", r, [bank], lambda e: e.matmul_mx(
+        emit("P", r, [bank] + line, lambda e: e.matmul_mx(
             T[BANK[bank][0]][:, o:o + n], T["c" + L][:, l0:l0 + 128], T["s" + L][:, l0:l0 + 128],
             T["c" + R][:, r0:r0 + n], T["s" + R][:, r0:r0 + n], start, stop), 0.00125 * (n + 16))
 
@@ -282,7 +316,7 @@ def rank_program(g, core, T, topo):
         scan(r + ["EX"], w, out, T.EX[:], row, 0.0, OP.add, OP.max, n)
 
     def pick2(r, w, out, row):
-        scan(r + ["EB"], w, out, T.EB[:], row, 0.0, OP.add, OP.max, 128)
+        scan(r + ["EB"], w, out, T.EB[:], row, 0.0, OP.add, OP.min, 128)
 
     dma("S", "dX", [], ["XT"], [(T.XT[:], T.x[:])], 3.5)
     dma("A", "dU", [], ["UT"], [(T.UT[:], T.u[:])], 2.8)
@@ -300,16 +334,17 @@ def rank_program(g, core, T, topo):
     iota(["ID"], T.ID[:], [[1, 256]], 0, 0, 256)
     iota(["BK"], T.BK[:], [[1, 8], [0, 16]], 0, 0, 128)
     iota(["C16"], T.CW[:, 16:32], [[16, 16]], 0, 0, 16)
+    iota(["C32"], T.CW[:, 32:48], [[32, 8], [0, 2]], -1, 0, 16)
     iota(["NN"], T.NN[:], [[1, 8]], 0, 0, 8)
     iota(["I4"], T.I4[:], [[0, 24], [1, 4]], 0, 0, 96)
     cp(["OI", "OIb"], ["OU"], T.OU[:, 0:24], T.OI[:, 0:24])
     PF = {}
-    names = ("q", "g", "m1", "q8", "r8", "q4", "r4")
-    for i, (sh, bits) in enumerate(((0, 15), (4, 7), (4, 1), (3, 1), (0, 7), (2, 3), (0, 3))):
+    names = ("q", "g", "m1", "q8", "r8", "q4", "r4", "r2")
+    for i, (sh, bits) in enumerate(((0, 15), (4, 7), (4, 1), (3, 1), (0, 7), (2, 3), (0, 3), (0, 1))):
         ts(["PC"], ["PI%d" % i], T.PI[:, i:i + 1], T.PC[:], sh, OP.arith_shift_right, bits, OP.bitwise_and)
         PF[names[i]] = T.PF[:, i:i + 1]
     cp(["PI0", "PI1"], ["q", "g"], T.PF[:, 0:2], T.PI[:, 0:2])
-    cp(["PI%d" % i for i in range(2, 7)], list(names[2:]), T.PF[:, 2:7], T.PI[:, 2:7])
+    cp(["PI%d" % i for i in range(2, 8)], list(names[2:]), T.PF[:, 2:8], T.PI[:, 2:8])
 
     def number(name, src, s1, o1, s2, o2, more=[]):
         PF[name] = T.PF[:, len(PF):len(PF) + 1]
@@ -319,13 +354,14 @@ def rank_program(g, core, T, topo):
         PF[name] = T.PF[:, len(PF):len(PF) + 1]
         lin([src], [name], PF[name], PF[src], scale, bias)
     affine("q1", "q", 1.0, 1.0)
-    affine("qn", "q", -1.0, -0.5)
+    affine("qn", "q", -1.0, 0.5)
     number("xq", "q", 15.0, OP.is_lt, 512.0, OP.mult)
-    affine("lb", "xq", 0.25, 0.0)
-    affine("nlb", "xq", -0.25, 0.0)
-    affine("nxq", "xq", -1.0, 0.0)
-    affine("lb1", "xq", 0.25, 1.0)
-    affine("lbc", "xq", 0.25, -223.0)
+    affine("lb", "xq", -0.5, 0.0)
+    affine("nlb", "xq", 0.5, 0.0)
+    affine("lb1", "xq", -0.5, 1.0)
+    number("t2", "r2", PF["m1"], OP.not_equal, 272.0, OP.mult, ["m1"])
+    number("t1", "q", PF["m1"], OP.subtract, 16.0, OP.mult, ["m1"])
+    number("tb", "t1", PF["t2"], OP.add, -1.0, OP.add, ["t2"])
     affine("xq1", "xq", 1.0, 1.0)
     affine("q7", "q", 7.0, 1.0)
     affine("q3", "q", 1.0, -3.0)
@@ -340,6 +376,7 @@ def rank_program(g, core, T, topo):
     ts(["C16", "q3"], ["r7a"], T.TMP[:], T.CW[:, 16:24], PF["q3"], OP.add, 1.0 / 7, OP.mult)
     cp(["r7a"], ["r7b"], T.OI[:, 40:48], T.TMP[:])
     cp(["r7b"], ["REP7"], T.OU[:, 40:48], T.OI[:, 40:48])
+    ts(["r7b"], ["REPE"], T.OU[:, 72:80], T.OI[:, 40:48], 16.0, OP.mult, 15.0, OP.add)
     ts(["NN", "q7"], ["HOPS"], T.OU[:, 48:54], T.NN[:, 0:6], PF["q7"], OP.add)
     ts(["NN", "g8"], ["G8L"], T.OU[:, 56:64], T.NN[:], 32.0, OP.mult, PF["g8"], OP.add)
     ts(["r8", "t7"], ["d8"], T.SC[:, 7:8], PF["r8"], 6.0, OP.min, PF["t7"], OP.add)
@@ -354,7 +391,7 @@ def rank_program(g, core, T, topo):
     ts(["IR", "q"], ["e0"], T.ET0[:, 0:256], T.IR[:], PF["q"], OP.is_equal, -2.0 ** 20, OP.mult, 128)
     ts(["IR", "q1"], ["e1"], T.ET0[:, 256:512], T.IR[:], PF["q1"], OP.is_equal, -2.0 ** -11, OP.mult, 128)
     scan(["e0", "e1"], ["EX"], T.EX[:], T.ET0[:, 256:512], T.ET0[:, 0:256], 0.0, OP.mult, OP.add, 128)
-    lin(["EX"], ["EB"], T.EB[:], T.EX[:], 0.25, n=256, half=True)
+    lin(["EX"], ["EB"], T.EB[:], T.EX[:], -0.5, n=256, half=True)
     ts(["I4", "q4", "EX"], ["e0"], T.ET0[:, 0:96], T.I4[:], PF["q4"], OP.is_equal, -2.0 ** 20, OP.mult)
     ts(["I4", "q41", "EX"], ["e1"], T.ET0[:, 256:352], T.I4[:], PF["q41"], OP.is_equal, -2.0 ** -11, OP.mult)
     scan(["e0", "e1"], ["E4"], T.E4[:], T.ET0[:, 256:352], T.ET0[:, 0:96], 0.0, OP.mult, OP.add)
@@ -395,14 +432,15 @@ def rank_program(g, core, T, topo):
     fill(["Q4z"], T.QQ[:, 0:32], 0.0)
     fill(["ETz"], T.ET[:, 384:512], 0.0)
     fill(["RTz"], T.RT[:, 384:512], 0.0)
-    fill(["GS0"], T.GS[:, 0:16], 32.0)
+    lin(["ZR"], ["GS0"], T.GS[:, 0:304], T.ZR[:, 0:304], 1.0, 64.0, 304, True)
+    zero(["GD"], T.GS[:, 304:608], 304)
     fill(["I1z"], T.I1[:, 112:120], 0)
     zero(["YXz"], T.YX[:, 0:256], 256)
     fill(["HD"], T.HD[:], 0.0)
     quant(["VTL"], "V", 128, T.VTL[:])
     CW = T.CW[:, 0:16]
     ts(["C16", "q"], ["CW"], CW, T.CW[:, 16:32], PF["q"], OP.add)
-    ts(["CW", "lbc"], ["CP"], T.CP[:], CW, PF["lbc"], OP.add)
+    lin(["CW"], ["CP"], T.CP[:], CW, 2.0, -446.0)
     lin(["CW"], ["HD"], T.HD[:, 33:64:2], CW)
     for s in (0, 7):
         lin(["ZR", "lb"], ["FP%d" % s], T.FP[:, 256 * s:256 * s + 256], T.ZR[:, 0:256], 1.0, PF["lb"], 256, True)
@@ -480,10 +518,9 @@ def rank_program(g, core, T, topo):
             tt(["RD%d" % s, "AR"] + ["AR%d.%d" % (s, m) for m in range(1, 16)], ["RW%d" % s], T.RW[:, 16 * s:16 * s + 16],
                T.RD[:, 256 * s + 15:256 * s + 256:16], T.AR[:, 16 * s:16 * s + 16], OP.add)
             pick([sums], ["EC%d" % s], T.EC[:, c], ps(sums, 0, 256))
-            tt(["EC%d" % s, "RW%d" % s], ["PL%d" % s], (T.TE, T.EP)[s][:], T.EC[:, 256 * s + 15:256 * s + 256:16],
-               T.RW[:, 16 * s:16 * s + 16], OP.subtract)
         places(0)
         places(1)
+        tt(["EC1", "RW1"], ["PL1"], T.EP[:], T.EC[:, 271:512:16], T.RW[:, 16:32], OP.subtract)
         for b in range(4):
             k = ("Q0", "Q1", "Q2", "Q0")[b]
             mm(XK + ["KR%d" % b], k, 256, "KR%d" % b, 0, X, 0)
@@ -499,7 +536,8 @@ def rank_program(g, core, T, topo):
         ts(VK + ["xq"], ["I0"], T.I0[:], VV, PF["xq"], OP.subtract, 256.0, OP.mult, 112)
         ts(["I0"], ["I1"], T.I1[:, 0:112], T.I0[:], 255, OP.bitwise_and, n=112)
         tt(["I1", "I1z"], ["D7"], T.D7[:], T.I1[:, 0:112], T.I1[:, 1:113], OP.subtract, 224)
-        tt(VK + ["PL0", "REP7"], ["CM"], T.CM[:], T.TE[:].indirect(REP7), VV, OP.is_le, far(112))
+        tt(VK + ["RW0", "REP7"], ["VR"], T.VR[:], T.RW[:, 0:16].indirect(REP7), VV, OP.add, far(112))
+        tt(["EC0", "VR", "REPE"], ["CM"], T.CM[:], T.EC[:, 0:256].indirect(T.OU[:, 72:79]), T.VR[:], OP.is_le, far(112))
         scan(["CM", "D7"], ["HR"], T.HR[:, 0:111], T.CM[:, 0:111], T.D7[:, 1:112], 0.0, OP.mult, OP.add, 111)
         cp(["HR"], ["R16"], T.R16[:], T.HR[:, 5:111:7])
         for z in range(8):
@@ -540,26 +578,29 @@ def rank_program(g, core, T, topo):
         lin(["Q70", "Q71", "Q72", "Q73", "BC32"], ["RP"], T.RP[:], T.QQ[:, 96:128].indirect(BC32), n=far(256))
         turn(["RP"], ["TO"], T.TO[:], T.RP[:], 128)
         act(["TO", "qn"], ["AJ0", "AC"], T.AJ[:, 0:256], T.TO[:], AF.Sign, PF["qn"], 1.0, T.SC[:, 0:1], n=256)
-        ts(["C64", "AC"], ["FBa"], T.FB[:, 0:32], T.C64[:], T.SC[:, 0:1], OP.is_ge)
-        ts(["C64", "AC"], ["FBb"], T.FB[:, 32:64], T.C64[:], T.SC[:, 0:1], OP.mult, 2.0 ** -7, OP.mult)
-        turn(["FBa", "FBb"], ["FX"], T.FB[:, 64:128], T.FB[:, 0:64])
-        emit("V", ["FX"], ["SF"], lambda e: e.tensor_reduce(T.SC[:, 1:2], T.FB[:, 64:80], AxisListType.X, OP.add), cyc(64))
-        scan(["FX"], ["XS"], T.XS[:], T.FB[:, 64:80], T.FB[:, 96:112], 128.0, OP.mult, OP.max)
-        ts(["TO", "SF"], ["LT"], T.LT[:], T.TO[:], T.SC[:, 1:2], OP.add, 16.0, OP.is_lt, 128)
-        ts(["TO", "SF"], ["LE"], T.LE[:], T.TO[:], T.SC[:, 1:2], OP.add, 16.0, OP.is_le, 128)
-        scan(["LT", "ZR", "XS"], ["AA"], T.AA[:], T.LT[:], T.ZR[:, 0:256], T.XS[:, 15:16], OP.add, OP.max, 128)
-        scan(["LE", "AA", "GS0"], ["GS"], T.GS[:, 1:257], T.LE[:], T.AA[:], 32.0, OP.add, OP.min, 128)
-        pick2(["GS"], ["P1"], T.P1[:], T.GS[:, 1:257])
-        pick2(["GS"], ["P0"], T.P0[:], T.GS[:, 0:256])
-        scan(["GS"], ["GN"], T.GN[:], T.GS[:, 1:257], T.GS[:, 0:256], 0.0, OP.max, OP.subtract, 128)
-        tt(["P1", "P0", "HD"], ["HDa"], T.HD[:, 1:32:2], T.P1[:, E15], T.P0[:, E15], OP.subtract)
-        tt(["P1", "CP", "HD"], ["HDb"], T.HD[:, 32:64:2], T.P1[:, E15], T.CP[:], OP.subtract)
+        ts(["C64", "AC"], ["FB"], T.FB[:, 0:32], T.C64[:], T.SC[:, 0:1], OP.is_lt)
+        turn(["FB"], ["FX"], T.FB[:, 32:64], T.FB[:, 0:32])
+        emit("V", ["FX"], ["SF"], lambda e: e.tensor_reduce(T.SC[:, 1:2], T.FB[:, 32:48], AxisListType.X, OP.add), cyc(64))
+        ts(["SF", "tb"], ["SL"], T.SL[:, 0:1], T.SC[:, 1:2], PF["tb"], OP.add)
+        ts(["SF", "C32"], ["SL2"], T.SL[:, 2:18], T.CW[:, 32:48], T.SC[:, 1:2], OP.add)
+        ts(["TO", "q"], ["LT"], T.LT[:], T.TO[:], PF["q"], OP.is_lt, 2.0, OP.mult, 128)
+        ts(["TO", "q"], ["LE"], T.LE[:], T.TO[:], PF["q"], OP.is_le, 2.0, OP.mult, 128)
+        scan(["LT", "ZR", "AC"], ["AA"], T.AA[:], T.LT[:], T.ZR[:, 0:256], T.SC[:, 0:1], OP.add, OP.max, 128)
+        scan(["LE", "AA", "GS0"], ["GS"], T.GS[:, 32:288], T.LE[:], T.AA[:], 64.0, OP.add, OP.min, 128)
+        scan(["GS", "GS0"], ["GD"], T.GS[:, 336:592], T.GS[:, 32:288], T.GS[:, 31:287], 0.0, OP.max, OP.subtract, 128)
+        for i, k in enumerate(("GS", "GD")):
+            turn([k], [k + "a"], T.TG[:, 544 * i:544 * i + 256], T.GS[:, 304 * i + 32:304 * i + 288], 128)
+            turn([k, "GS0"], [k + "b"], T.TG[:, 544 * i + 256:544 * i + 544], T.GS[:, 304 * i + 16:304 * i + 304], 144)
+        ts(["GDa", "GDb", "SL", "HD"], ["HDa"], T.HD[:, 1:32:2], T.TG[:, 544:1088].indirect(T.SL[:, 0:1]), 0.25, OP.mult, n=far(16))
+        tt(["GSa", "GSb", "SL", "CP", "HD"], ["HDb"], T.HD[:, 32:64:2], T.TG[:, 0:544].indirect(T.SL[:, 0:1]), T.CP[:], OP.subtract, far(16))
+        lin(["GDa", "SL2"], ["RP"], T.RP[:], T.TG[:, 544:800].indirect(T.SL[:, 2:18]), 0.5, n=far(256))
+        turn(["RP"], ["GN"], T.GN[:], T.RP[:], 128)
         scan(["HDa", "HDb"], ["HO"], T.HO[:], T.HD[:, 0:32], T.HD[:, 32:64], 0.0, OP.mult, OP.add)
         cp(["HO"], ["NI16"], T.NI16[:], T.HO[:, 1:32:2])
         for b in range(4):
             k = ("Q0", "Q1", "Q2", "PC_")[b]
-            mm(["L%d" % t, "pad", "W"], k, 128, "W", 128 * b, "L", lo, True, False)
-            mm(["L%d" % t, "pad", "KR%d" % b], k, 128, "KR%d" % b, 0, "L", lo, False, True)
+            mm(["L%d" % t, "pad", "W"], k, 128, "W", 128 * b, "L", lo, True, False, ["bank by bank"])
+            mm(["L%d" % t, "pad", "KR%d" % b], k, 128, "KR%d" % b, 0, "L", lo, False, True, ["bank by bank"])
             lin([k, "RTz"], ["RT%d" % b], T.RT[:, b:384:4], ps(k, 0, 96), 2.0 ** -7, n=96)
         quant(["RT0", "RT1", "RT2", "RT3"], "Pb", 128, T.RT[:])
         XN = "X%d" % (t + 1)
@@ -570,14 +611,14 @@ def rank_program(g, core, T, topo):
             c = slice(256 * s, 256 * s + 256)
             lin(["GN", "H16"], ["FL%d" % s], T.FL[:, c], T.GN[:].indirect(T.H16[:, 16 * s:16 * s + 16]), n=far(256))
             pick2(["FL%d" % s], ["FP%d" % (s + 1)], T.FP[:, 256 * s + 256:256 * s + 512], T.FL[:, c])
-        lin(["HDa", "lb1"], ["FP7"], T.FP[:, 1807:2048:16], T.HD[:, 1:32:2], -1.0, PF["lb1"])
+        lin(["HDa", "lb1"], ["FP7"], T.FP[:, 1807:2048:16], T.HD[:, 1:32:2], -2.0, PF["lb1"])
         cp(["LL%d" % t], ["LI0"], T.LI[:, 0:48], T.LL[:, 48 * t:48 * t + 48])
         ts(["LI0"], ["LI1"], T.LI[:, 49:144:2], T.LI[:, 0:48], 255, OP.bitwise_and)
         ts(["LI0"], ["LI2"], T.LI[:, 48:144:2], T.LI[:, 0:48], 8, OP.arith_shift_right)
         cp(["LI1", "LI2"], ["YXe"], T.YX[:, 256:352], T.LI[:, 48:144], 96)
         lin(["YXz", "YXe", "NI16"], ["EW"], T.EW[:], T.YX[:].indirect(T.NI16[:]), n=far(256))
-        pick(["EW"], ["EQ"], T.EQ[:], T.EW[:])
-        lin(["EQ", "nxq"], ["D8e"], T.D8[:, 7:128:8], T.EQ[:, E15], 1.0, PF["nxq"])
+        pick2(["EW"], ["EQ"], T.EQ[:], T.EW[:])
+        lin(["EQ", "nlb"], ["D8e"], T.D8[:, 7:128:8], T.EQ[:, E15], 1.0, PF["nlb"])
         lin(["FP%d" % s for s in range(8)] + ["G8L", "nlb"], ["G8"], T.G8[:], T.FP[:].indirect(G8L), 1.0, PF["nlb"], far(128))
         scan(["G8", "D8", "D8e"], ["HL"], T.HL[:], T.G8[:], T.D8[:], 0.0, OP.mult, OP.add, 128)
         cp(["HL"], ["L16"], T.L16[:], T.HL[:, 7:128:8])

@@ -27,17 +27,17 @@ _q(W=512, U=128, UP=384, V=128, X=1024, L=320, P=384, E=384)
 _q(K=768)
 _q(C=256 + 2 * TILE_O[4])
 _sb(B, TK=1552, IR=256, I4=96, TI=128, BK=128, NB=256, RS=512, RC=256, EX=256, EB=256, E4=96, ET0=512, TR=128)
-_sb(B, C64=32, ZR=528, PD2=96, CB=368, SN=512)
+_sb(B, C64=64, ZR=528, PD2=96, CB=368, SN=512)
 _sb(F, ID=256, PF=32, CW=48, NN=8, CP=16, TMP=8)
 _sb(U, OU=80, SL=24)
 _sb(F, SR=512, SG=512, SW=512, SB2=2, DL=2, TH0=128, TH1=128, AR=32, RW=32, EC=512, EP=16)
-_sb(B, BT=1024, CT=8 * TILE_O[4], AJ=1024, RD=512)
-_sb(F, LF=256, VH=1536, VT=1888, D7=112, CM=112, HR=112, D8=128, G8=128, HL=128)
+_sb(B, BT=1024, CT=8 * TILE_O[4], AJ=1024, RD=512, RV=2048)
+_sb(F, LF=256, VH=1536, VT=1888, D7=112, CM=112, HR=112, D8=128, G8=384, HL=128)
 _sb(B, FT=1024, FU=1024, Z=1024, ET=512, RT=512)
 _sb(F, EF=256, ES=96, PK=96)
 _sb(U, EP16=16, EO=24, LS=144, LL=144, R16=16, NI16=16, L16=16, H16=96)
-_sb(F, CA=8, CJ=512, QQ=128, SC=8, HD=64, HO=32, YO=256, LO=256, VR=112)
-_sb(B, EW=256, EQ=256, RP=256, TO=256, FB=64, LT=256, LE=256, AA=256, GS=608, GN=256, TG=1088, FL=1536, FP=2048, YX=352)
+_sb(F, CA=8, CJ=512, QQ=192, SC=8, HD=64, HO=32, YO=256, LO=256, VR=112)
+_sb(B, EW=256, EQ=256, RP=256, TO=256, FB=64, LT=512, LE=256, AA=256, GS=608, GN=256, TG=1088, FL=1536, FP=1792, YX=352)
 for _k in ("PA", "PB", "PC_", "Q0", "Q1", "Q2"):
     SCRATCH[_k] = ("psum", [128, 512], F)
 SCRATCH["PD"] = ("psum", [128, 1024], F)
@@ -50,8 +50,10 @@ for _i in range(4):
     PLACE["C0%d" % _i] = ("C", 256 + TILE_O[_i])
     PLACE["C1%d" % _i] = ("C", 256 + TILE_O[4] + TILE_O[_i])
     PLACE["E%d" % _i] = ("E", 128 * _i)
-CYCLE, WAKE, FLIGHT, JUMP, STREW, SEND, FIRST = 0.00085, 0.23, 2.5, 1.5, 3.5, 0.5, 1.0
+CYCLE, WAKE, FLIGHT, JUMP, STREW, SEND, FIRST = 0.00085, 0.23, 1.5, 1.5, 3.5, 0.35, 1.0
 TRIES, SHAKE, SPARE = 3000, 1.5, 0.3
+BY_SCAN = (16, 16)
+COUNT_V = 0
 BY_SIGN = ((), (11, 10, 9))
 
 SEMAPHORES = ["sV", "sA", "sP", "sG", "dX", "dU", "dO", "dW", "dVV", "dPad", "dF", "dY", "dLk", "dOc", "ls",
@@ -334,7 +336,6 @@ def rank_program(g, core, T, topo):
     iota(["ID"], T.ID[:], [[1, 256]], 0, 0, 256)
     iota(["BK"], T.BK[:], [[1, 8], [0, 16]], 0, 0, 128)
     iota(["C16"], T.CW[:, 16:32], [[16, 16]], 0, 0, 16)
-    iota(["C32"], T.CW[:, 32:48], [[32, 8], [0, 2]], -1, 0, 16)
     iota(["NN"], T.NN[:], [[1, 8]], 0, 0, 8)
     iota(["I4"], T.I4[:], [[0, 24], [1, 4]], 0, 0, 96)
     cp(["OI", "OIb"], ["OU"], T.OU[:, 0:24], T.OI[:, 0:24])
@@ -354,11 +355,11 @@ def rank_program(g, core, T, topo):
         PF[name] = T.PF[:, len(PF):len(PF) + 1]
         lin([src], [name], PF[name], PF[src], scale, bias)
     affine("q1", "q", 1.0, 1.0)
-    affine("qn", "q", -1.0, 0.5)
+    affine("qn", "q", -1.0, 255.5)
+    affine("q255", "q", -1.0, 255.0)
+    affine("q254", "q", -1.0, 254.5)
     number("xq", "q", 15.0, OP.is_lt, 512.0, OP.mult)
-    affine("lb", "xq", -0.5, 0.0)
     affine("nlb", "xq", 0.5, 0.0)
-    affine("lb1", "xq", -0.5, 1.0)
     number("t2", "r2", PF["m1"], OP.not_equal, 272.0, OP.mult, ["m1"])
     number("t1", "q", PF["m1"], OP.subtract, 16.0, OP.mult, ["m1"])
     number("tb", "t1", PF["t2"], OP.add, -1.0, OP.add, ["t2"])
@@ -370,7 +371,8 @@ def rank_program(g, core, T, topo):
     number("eo", "q4", 3.0, OP.is_lt, -2048.0, OP.mult)
     tt(["eo", "r4"], ["eo"], PF["eo"], PF["eo"], PF["r4"], OP.add)
     affine("t8", "q8", 16.0, 15.0)
-    number("g8", "r8", 256.0, OP.mult, PF["t8"], OP.add, ["t8"])
+    number("r7", "r8", 7.0, OP.is_lt, PF["r8"], OP.mult)
+    number("g8", "r7", 256.0, OP.mult, PF["t8"], OP.add, ["t8"])
     affine("t7", "q8", 7.0, 0.0)
     ts(["OI2", "m1"], ["BC32"], T.OU[:, 24:40], T.OI[:, 24:40], PF["m1"], OP.add)
     ts(["C16", "q3"], ["r7a"], T.TMP[:], T.CW[:, 16:24], PF["q3"], OP.add, 1.0 / 7, OP.mult)
@@ -426,7 +428,8 @@ def rank_program(g, core, T, topo):
     zero(["CB"], T.CB[:], 368)
     ts(["IR", "q"], ["CB"], T.CB[:, 112:128], T.IR[:, 0:16], PF["q"], OP.is_equal)
     ts(["IR", "q"], ["CB"], T.CB[:, 240:256], T.IR[:, 0:16], PF["q"], OP.is_equal, 1024.0, OP.mult)
-    fill(["C64"], T.C64[:], 64.0)
+    fill(["C64"], T.C64[:, 0:32], 64.0)
+    fill(["C64"], T.C64[:, 32:64], -2.0 ** -9)
     fill(["PD2"], T.PD2[:], 0.0)
     fill(["PD2"], T.PD2[:, 1:96:2], 256.0)
     fill(["Q4z"], T.QQ[:, 0:32], 0.0)
@@ -442,8 +445,7 @@ def rank_program(g, core, T, topo):
     ts(["C16", "q"], ["CW"], CW, T.CW[:, 16:32], PF["q"], OP.add)
     lin(["CW"], ["CP"], T.CP[:], CW, 2.0, -446.0)
     lin(["CW"], ["HD"], T.HD[:, 33:64:2], CW)
-    for s in (0, 7):
-        lin(["ZR", "lb"], ["FP%d" % s], T.FP[:, 256 * s:256 * s + 256], T.ZR[:, 0:256], 1.0, PF["lb"], 256, True)
+    lin(["ZR"], ["FP0"], T.FP[:, 0:256], T.ZR[:, 0:256], 1.0, -2048.0, 256, True)
     VV, VT0, VT6 = T.VT[:, 105:1888:16], T.VT[:, 105:1888:112], T.VT[:, 201:1888:112]
     lin(["ZR", "xq"], ["VT0"], VT0, T.ZR[:, 0:16], 1.0, PF["xq"])
     cp(["OL"], ["L16"], T.L16[:], T.OL[:])
@@ -510,17 +512,26 @@ def rank_program(g, core, T, topo):
                             continue
                         ts([bank, "SW%d" % s, "z%d%d" % (s, a)], ["ct%d.%d" % (s, m)], v, ps(bank, 0, 16 * m),
                            T.SW[:, 256 * s + 16 * m + 15:256 * s + 16 * m + 16], (OP.is_gt, OP.is_lt)[s], n=16 * m)
+                        if m >= BY_SCAN[s]:
+                            e = 1024 * s + 256 * (m - 11)
+                            scan(["ct%d.%d" % (s, m), "ZR"], ["AR%d.%d" % (s, m)], T.RV[:, e - 16 * m:e], T.ZR[:, 0:16 * m], v,
+                                 0.0, OP.add, OP.add, 8 * m)
+                            continue
                         act(["ct%d.%d" % (s, m), "AR"], ["AR%d.%d" % (s, m), "AJ%d" % j], T.AJ[:, 256 * j:256 * j + 16 * m], v,
                             AF.Copy, 0.0, 1.0, T.AR[:, 16 * s + m:16 * s + m + 1], n=16 * m)
                 k = "C%d%d" % (s, a)
                 quant(["ct%d.%d" % (s, m) for m in ms], k, TILE_N[a], T.CT[:, o + 4 * TILE_O[a]:o + 4 * TILE_O[a + 1]])
                 mm([k, "KS"], sums, TILE_N[a], "KS", 0, k, 0, a == 0, a == 3)
-            tt(["RD%d" % s, "AR"] + ["AR%d.%d" % (s, m) for m in range(1, 16)], ["RW%d" % s], T.RW[:, 16 * s:16 * s + 16],
-               T.RD[:, 256 * s + 15:256 * s + 256:16], T.AR[:, 16 * s:16 * s + 16], OP.add)
+            m = BY_SCAN[s]
+            tt(["RD%d" % s, "AR"] + ["AR%d.%d" % (s, i) for i in range(1, m)], ["RW%d" % s], T.RW[:, 16 * s:16 * s + m],
+               T.RD[:, 256 * s + 15:256 * s + 16 * m:16], T.AR[:, 16 * s:16 * s + m], OP.add)
+            if m < 16:
+                tt(["RD%d" % s] + ["AR%d.%d" % (s, i) for i in range(m, 16)], ["RV%d" % s], T.RW[:, 16 * s + m:16 * s + 16],
+                   T.RD[:, 256 * s + 16 * m + 15:256 * s + 256:16], T.RV[:, 1024 * s + 256 * (m - 11) - 1:1024 * s + 1024:256], OP.add)
             pick([sums], ["EC%d" % s], T.EC[:, c], ps(sums, 0, 256))
         places(0)
         places(1)
-        tt(["EC1", "RW1"], ["PL1"], T.EP[:], T.EC[:, 271:512:16], T.RW[:, 16:32], OP.subtract)
+        tt(["EC1", "RW1", "RV1"], ["PL1"], T.EP[:], T.EC[:, 271:512:16], T.RW[:, 16:32], OP.subtract)
         for b in range(4):
             k = ("Q0", "Q1", "Q2", "Q0")[b]
             mm(XK + ["KR%d" % b], k, 256, "KR%d" % b, 0, X, 0)
@@ -536,11 +547,15 @@ def rank_program(g, core, T, topo):
         ts(VK + ["xq"], ["I0"], T.I0[:], VV, PF["xq"], OP.subtract, 256.0, OP.mult, 112)
         ts(["I0"], ["I1"], T.I1[:, 0:112], T.I0[:], 255, OP.bitwise_and, n=112)
         tt(["I1", "I1z"], ["D7"], T.D7[:], T.I1[:, 0:112], T.I1[:, 1:113], OP.subtract, 224)
-        tt(VK + ["RW0", "REP7"], ["VR"], T.VR[:], T.RW[:, 0:16].indirect(REP7), VV, OP.add, far(112))
+        tt(VK + ["RW0", "RV0", "REP7"], ["VR"], T.VR[:], T.RW[:, 0:16].indirect(REP7), VV, OP.add, far(112))
         tt(["EC0", "VR", "REPE"], ["CM"], T.CM[:], T.EC[:, 0:256].indirect(T.OU[:, 72:79]), T.VR[:], OP.is_le, far(112))
         scan(["CM", "D7"], ["HR"], T.HR[:, 0:111], T.CM[:, 0:111], T.D7[:, 1:112], 0.0, OP.mult, OP.add, 111)
         cp(["HR"], ["R16"], T.R16[:], T.HR[:, 5:111:7])
         for z in range(8):
+            if z < COUNT_V:
+                cp(["CB", "R16"], ["EW"], T.EW[:], T.CB[:, 112 - 16 * z:368 - 16 * z].indirect(T.R16[:]), far(256))
+                emit("V", ["EW"], ["CA%d" % z], lambda e, z=z: e.tensor_reduce(T.CA[:, z:z + 1], T.EW[:], AxisListType.X, OP.add), cyc(256))
+                continue
             act(["CB", "R16"], ["CJ%d" % (z % 2), "CA%d" % z], T.CJ[:, 256 * (z % 2):256 * (z % 2) + 256],
                 T.CB[:, 112 - 16 * z:368 - 16 * z].indirect(T.R16[:]), AF.Copy, 0.0, 1.0, T.CA[:, z:z + 1], n=far(256))
         for b in range(4):
@@ -566,6 +581,7 @@ def rank_program(g, core, T, topo):
         cp(["I1", "I1z", "HOPS"], ["H16"], T.H16[:], T.I1[:].indirect(HOPS), far(96))
         lin(["D7", "D8L"], ["D8", "D8e"], T.D8[:], T.D7[:].indirect(D8L), n=far(128))
         tt(["CW", "I1"], ["D8"], T.D8[:, 0:128:8], CW, T.I1[:, 1:112:7], OP.subtract)
+        ts(["I1", "I1z", "D8L", "nlb"], ["I8"], T.G8[:, 256:384], T.I1[:].indirect(D8L), -2.0 ** -8, OP.mult, PF["nlb"], OP.add, far(128))
         across(["CA%d" % z for z in range(8)], ["CI0"], T.CI[0:64, 0:8], T.CA[0:64, :], T.CA[64:128, :])
         ts(["CI0"], ["CI1"], T.CI[0:64, 8:16], T.CI[0:64, 0:8], 1023, OP.bitwise_and)
         ts(["CI0"], ["CI2"], T.CI[0:64, 16:24], T.CI[0:64, 0:8], 10, OP.arith_shift_right)
@@ -575,17 +591,16 @@ def rank_program(g, core, T, topo):
         tt(["Q5"], ["Q6b"], T.QQ[0:32, 80:96], T.QQ[0:32, 32:48], T.QQ[0:32, 48:64], OP.add)
         for a in range(4):
             turn(["Q6", "Q6b"], ["Q7%d" % a], T.QQ[32 * a:32 * a + 32, 96:128], T.QQ[0:32, 64:96])
-        lin(["Q70", "Q71", "Q72", "Q73", "BC32"], ["RP"], T.RP[:], T.QQ[:, 96:128].indirect(BC32), n=far(256))
+        act(["Q70", "Q71", "Q72", "Q73", "BC32"], ["RP"], T.RP[:], T.QQ[:, 96:128].indirect(BC32), AF.Relu, 255.0, -1.0, n=far(256))
         turn(["RP"], ["TO"], T.TO[:], T.RP[:], 128)
-        act(["TO", "qn"], ["AJ0", "AC"], T.AJ[:, 0:256], T.TO[:], AF.Sign, PF["qn"], 1.0, T.SC[:, 0:1], n=256)
-        ts(["C64", "AC"], ["FB"], T.FB[:, 0:32], T.C64[:], T.SC[:, 0:1], OP.is_lt)
+        act(["TO", "qn"], ["AJ0", "AC"], T.AJ[:, 0:256], T.TO[:], AF.Sign, PF["qn"], -1.0, T.SC[:, 0:1], n=256)
+        ts(["C64", "AC"], ["FB"], T.FB[:, 0:32], T.C64[:, 0:32], T.SC[:, 0:1], OP.is_lt)
         turn(["FB"], ["FX"], T.FB[:, 32:64], T.FB[:, 0:32])
         emit("V", ["FX"], ["SF"], lambda e: e.tensor_reduce(T.SC[:, 1:2], T.FB[:, 32:48], AxisListType.X, OP.add), cyc(64))
         ts(["SF", "tb"], ["SL"], T.SL[:, 0:1], T.SC[:, 1:2], PF["tb"], OP.add)
-        ts(["SF", "C32"], ["SL2"], T.SL[:, 2:18], T.CW[:, 32:48], T.SC[:, 1:2], OP.add)
-        ts(["TO", "q"], ["LT"], T.LT[:], T.TO[:], PF["q"], OP.is_lt, 2.0, OP.mult, 128)
-        ts(["TO", "q"], ["LE"], T.LE[:], T.TO[:], PF["q"], OP.is_le, 2.0, OP.mult, 128)
-        scan(["LT", "ZR", "AC"], ["AA"], T.AA[:], T.LT[:], T.ZR[:, 0:256], T.SC[:, 0:1], OP.add, OP.max, 128)
+        ts(["TO", "q255"], ["LT"], T.LT[:, 0:256], T.TO[:], PF["q255"], OP.is_gt, 2.0, OP.mult, 128)
+        ts(["TO", "q255"], ["LE"], T.LE[:], T.TO[:], PF["q255"], OP.is_ge, 2.0, OP.mult, 128)
+        scan(["LT", "ZR", "AC"], ["AA"], T.AA[:], T.LT[:, 0:256], T.ZR[:, 0:256], T.SC[:, 0:1], OP.add, OP.max, 128)
         scan(["LE", "AA", "GS0"], ["GS"], T.GS[:, 32:288], T.LE[:], T.AA[:], 64.0, OP.add, OP.min, 128)
         scan(["GS", "GS0"], ["GD"], T.GS[:, 336:592], T.GS[:, 32:288], T.GS[:, 31:287], 0.0, OP.max, OP.subtract, 128)
         for i, k in enumerate(("GS", "GD")):
@@ -593,8 +608,14 @@ def rank_program(g, core, T, topo):
             turn([k, "GS0"], [k + "b"], T.TG[:, 544 * i + 256:544 * i + 544], T.GS[:, 304 * i + 16:304 * i + 304], 144)
         ts(["GDa", "GDb", "SL", "HD"], ["HDa"], T.HD[:, 1:32:2], T.TG[:, 544:1088].indirect(T.SL[:, 0:1]), 0.25, OP.mult, n=far(16))
         tt(["GSa", "GSb", "SL", "CP", "HD"], ["HDb"], T.HD[:, 32:64:2], T.TG[:, 0:544].indirect(T.SL[:, 0:1]), T.CP[:], OP.subtract, far(16))
-        lin(["GDa", "SL2"], ["RP"], T.RP[:], T.TG[:, 544:800].indirect(T.SL[:, 2:18]), 0.5, n=far(256))
-        turn(["RP"], ["GN"], T.GN[:], T.RP[:], 128)
+        ts(["TO", "q255"], ["LQ"], T.LT[:, 256:512], T.TO[:], PF["q255"], OP.is_equal, 2.0, OP.mult, 128)
+        scan(["LQ", "ZR"], ["CE"], T.GN[:], T.LT[:, 256:512], T.ZR[:, 0:256], 65.0, OP.add, OP.max, 128)
+        act(["CE", "AC"], ["AJ1", "JS"], T.AJ[:, 256:512], T.GN[:], AF.Sign, T.SC[:, 0:1], -1.0, T.SC[:, 2:3], n=256)
+        ts(["AC"], ["NV"], T.SC[:, 3:4], T.SC[:, 0:1], 64.0, OP.is_le, 1024.0, OP.mult)
+        lin(["NV", "q254"], ["NW"], T.SC[:, 4:5], T.SC[:, 3:4], 1.0, PF["q254"])
+        ts(["C64", "JS", "NW"], ["FK"], T.QQ[:, 128:160], T.C64[:, 32:64], T.SC[:, 2:3], OP.mult, T.SC[:, 4:5], OP.add)
+        turn(["FK"], ["FL_"], T.QQ[:, 160:192], T.QQ[:, 128:160])
+        emit("V", ["FL_"], ["TN"], lambda e: e.tensor_reduce(T.SC[:, 5:6], T.QQ[:, 160:176], AxisListType.X, OP.min), cyc(64))
         scan(["HDa", "HDb"], ["HO"], T.HO[:], T.HD[:, 0:32], T.HD[:, 32:64], 0.0, OP.mult, OP.add)
         cp(["HO"], ["NI16"], T.NI16[:], T.HO[:, 1:32:2])
         for b in range(4):
@@ -609,9 +630,11 @@ def rank_program(g, core, T, topo):
         lin(["P", "Pb", "NI16"], [XN + "s"], T.sX[:, 256 * t + 256:256 * t + 512], T.sP[:, :].indirect(T.NI16[:]), n=far(256))
         for s in range(6):
             c = slice(256 * s, 256 * s + 256)
-            lin(["GN", "H16"], ["FL%d" % s], T.FL[:, c], T.GN[:].indirect(T.H16[:, 16 * s:16 * s + 16]), n=far(256))
+            lin(["TO", "H16"], ["FL%d" % s], T.FL[:, c], T.TO[:].indirect(T.H16[:, 16 * s:16 * s + 16]), n=far(256))
             pick2(["FL%d" % s], ["FP%d" % (s + 1)], T.FP[:, 256 * s + 256:256 * s + 512], T.FL[:, c])
-        lin(["HDa", "lb1"], ["FP7"], T.FP[:, 1807:2048:16], T.HD[:, 1:32:2], -2.0, PF["lb1"])
+        tt(["FP%d" % s for s in range(7)] + ["G8L", "I8"], ["KY"], T.G8[:, 128:256], T.FP[:].indirect(G8L), T.G8[:, 256:384], OP.add, far(128))
+        ts(["KY", "TN"], ["G8", "G8k"], T.G8[:, 0:128], T.G8[:, 128:256], T.SC[:, 5:6], OP.is_ge, n=128)
+        lin(["HDa"], ["G8k"], T.G8[:, 7:128:8], T.HD[:, 1:32:2], -2.0, 1.0)
         cp(["LL%d" % t], ["LI0"], T.LI[:, 0:48], T.LL[:, 48 * t:48 * t + 48])
         ts(["LI0"], ["LI1"], T.LI[:, 49:144:2], T.LI[:, 0:48], 255, OP.bitwise_and)
         ts(["LI0"], ["LI2"], T.LI[:, 48:144:2], T.LI[:, 0:48], 8, OP.arith_shift_right)
@@ -619,8 +642,7 @@ def rank_program(g, core, T, topo):
         lin(["YXz", "YXe", "NI16"], ["EW"], T.EW[:], T.YX[:].indirect(T.NI16[:]), n=far(256))
         pick2(["EW"], ["EQ"], T.EQ[:], T.EW[:])
         lin(["EQ", "nlb"], ["D8e"], T.D8[:, 7:128:8], T.EQ[:, E15], 1.0, PF["nlb"])
-        lin(["FP%d" % s for s in range(8)] + ["G8L", "nlb"], ["G8"], T.G8[:], T.FP[:].indirect(G8L), 1.0, PF["nlb"], far(128))
-        scan(["G8", "D8", "D8e"], ["HL"], T.HL[:], T.G8[:], T.D8[:], 0.0, OP.mult, OP.add, 128)
+        scan(["G8", "G8k", "D8", "D8e"], ["HL"], T.HL[:], T.G8[:, 0:128], T.D8[:], 0.0, OP.mult, OP.add, 128)
         cp(["HL"], ["L16"], T.L16[:], T.HL[:, 7:128:8])
         if not last:
             lin(["HL", "xq"], ["VT6"], VT6, T.HL[:, 7:128:8], 2.0 ** -8, PF["xq"])

@@ -22,22 +22,22 @@ def _q(**widths):
 TILE_N = (256, 192, 128, 128)
 TILE_O = [sum(TILE_N[:a]) for a in range(5)]
 _sb(B, XT=1024, UT=512, VTL=512)
-_sb(I, OL=16, PC=1, PI=8, OI=48, CI=24, LI=144, I0=112, I1=120)
+_sb(I, OL=16, PC=1, PI=12, OI=48, CI=24, LI=144, I0=112, I1=120)
 _q(W=512, U=128, UP=384, V=128, X=1024, L=320, P=384, E=384)
 _q(K=768)
 _q(C=256 + 2 * TILE_O[4])
-_sb(B, TK=1552, IR=256, I4=96, TI=128, BK=128, NB=256, RS=512, RC=256, EX=256, EB=256, E4=96, ET0=512, TR=128)
-_sb(B, C64=64, ZR=528, PD2=96, CB=368, SN=512)
+_sb(B, TK=1552, IR=256, I4=96, TI=128, BK=128, NB=256, RS=512, RC=256, EX=256, E4=96, ET0=512, TR=128)
+_sb(B, C64=64, ZR=528, PD2=96, CB=448, SN=512)
 _sb(F, ID=256, PF=32, CW=48, NN=8, CP=16, TMP=8)
 _sb(U, OU=80, SL=24)
-_sb(F, SR=512, SG=512, SW=512, SB2=2, DL=2, TH0=128, TH1=128, AR=32, RW=32, EC=512, EP=16)
-_sb(B, BT=1024, CT=8 * TILE_O[4], AJ=1024, RD=512, RV=2048)
-_sb(F, LF=256, VH=1536, VT=1888, D7=112, CM=112, HR=112, D8=128, G8=384, HL=128)
+_sb(F, SR=512, SG=512, SW=512, SB2=4, DL=2, TH0=128, TH1=128, AR=32, RW=32, EC=512, EP=16)
+_sb(B, BT=1024, CT=8 * TILE_O[4], AJ=1024, RD=512, RV=8192)
+_sb(F, LF=256, VH=1536, VT=1888, D7=112, CM=112, HR=224, D8=128, G8=384, HL=128)
 _sb(B, FT=1024, FU=1024, Z=1024, ET=512, RT=512)
 _sb(F, EF=256, ES=96, PK=96)
-_sb(U, EP16=16, EO=24, LS=144, LL=144, R16=16, NI16=16, L16=16, H16=96)
-_sb(F, CA=8, CJ=512, QQ=192, SC=8, HD=64, HO=32, YO=256, LO=256, VR=112)
-_sb(B, EW=256, EQ=256, RP=256, TO=256, FB=64, LT=512, LE=256, AA=256, GS=608, GN=256, TG=1088, FL=1536, FP=1792, YX=352)
+_sb(U, EP16=16, EO=24, LS=144, LL=144, R16=16, R32=32, F16=16, NI16=16, L16=16, H16=96)
+_sb(F, CA=4, CJ=1024, QQ=192, SC=8, HD=64, HO=48, YC=352, YO=256, LO=256, VR=112)
+_sb(B, RP=256, TO=256, FB=64, LT=512, LE=256, AA=256, GS=608, GN=256, TG=1088, FL=1536, FP=1792, YX=352)
 for _k in ("PA", "PB", "PC_", "Q0", "Q1", "Q2"):
     SCRATCH[_k] = ("psum", [128, 512], F)
 SCRATCH["PD"] = ("psum", [128, 1024], F)
@@ -50,11 +50,12 @@ for _i in range(4):
     PLACE["C0%d" % _i] = ("C", 256 + TILE_O[_i])
     PLACE["C1%d" % _i] = ("C", 256 + TILE_O[4] + TILE_O[_i])
     PLACE["E%d" % _i] = ("E", 128 * _i)
-CYCLE, WAKE, FLIGHT, JUMP, STREW, SEND, FIRST = 0.00085, 0.23, 1.5, 1.5, 3.5, 0.35, 1.0
-TRIES, SHAKE, SPARE = 3000, 1.5, 0.3
+CYCLE, WAKE, FLIGHT, JUMP, STREW, SEND, FIRST = 0.00085, 0.25, 1.2, 1.5, 3.5, 0.3, 1.0
+TRIES, SHAKE, SPARE = 4000, 1.5, 0.3
 BY_SCAN = (16, 16)
-COUNT_V = 0
-BY_SIGN = ((), (11, 10, 9))
+EARLY, SPREAD, BIRTH_S = False, True, 1
+SLOW, SHARE = 1.4, 0.75
+BY_SIGN = ((11, 10, 9), (11, 10, 9))
 
 SEMAPHORES = ["sV", "sA", "sP", "sG", "dX", "dU", "dO", "dW", "dVV", "dPad", "dF", "dY", "dLk", "dOc", "ls",
               "aC0", "aC1", "aC2", "aL0", "aL1", "aL2"]
@@ -71,7 +72,7 @@ def plan(nodes):
 
     def edge(a, b):
         if a != b:
-            succ[a][b] = pred[b][a] = nodes[a][3] + (0.0 if only[a] == only[b] == "P" else WAKE)
+            succ[a][b] = pred[b][a] = nodes[a][3] + (0.0 if only[a] == only[b] and only[a] in ("P", "G") else WAKE)
     for i, (ways, r, w, late) in enumerate(nodes):
         for k in r:
             if k in wr:
@@ -131,13 +132,26 @@ def plan(nodes):
                 put(i)
         return end, order
 
-    def passes(urgency, spare, count):
+    def slower(order):
+        end, free = [0.0] * n, {q: 0.0 for q in "VAPGSR"}
+        for _, _, i, k in sorted(order):
+            q, c = nodes[i][0][k]
+            at = free[q]
+            for j, lag in pred[i]:
+                if end[j] + lag > at:
+                    at = end[j] + lag
+            end[i] = free[q] = at + (c * SLOW if q in "VA" else c)
+        return max(end[i] + late[i] for i in range(n))
+
+    def passes(urgency, spare, count, near=1e9):
         best = None
         for p in range(count):
             end, order = sweep(pred, urgency, [0.0] * n, spare)
             shown = [end[i] + late[i] for i in range(n)]
-            if best is None or max(shown) < best[0]:
-                best = (max(shown), order, urgency, spare)
+            mark = max(shown)
+            mark = (mark + SHARE * slower(order)) / 2 if mark < near else mark + near
+            if best is None or mark < best[0]:
+                best = (mark, order, urgency, spare)
             if p < count - 1:
                 urgency = sweep(succ, shown, late, spare)[0]
         return best
@@ -158,7 +172,7 @@ def plan(nodes):
                 urgency[i] += SHAKE * (chance() + chance() - 1.0)
                 if len(nodes[i][0]) > 1 and chance() < 0.3:
                     spare[i] = (-0.3, 0.0, 0.3, 1.0, 3.0)[int(5 * chance())]
-        other = passes(urgency, spare, 2)
+        other = passes(urgency, spare, 2, best[0] + 1.0)
         if other[0] <= best[0] + 0.02:
             best = other
     SPAN.append(best[0])
@@ -222,7 +236,7 @@ def rank_program(g, core, T, topo):
     def emit(q, r, w, fn, time, alone=False):
         nodes.append(([way(q, r, w, fn, time, alone)], r, w, -WAKE if alone else 0.0))
 
-    def dma(q, s, r, w, pairs, late=2.5):
+    def dma(q, s, r, w, pairs, late=2.0):
         def issue():
             deps(q, r, w)
             for o, i in pairs:
@@ -315,13 +329,13 @@ def rank_program(g, core, T, topo):
             emit("G", [], w, lambda e: e.iota(out, pattern, base, cm, allow_small_or_imprecise_dtypes=True), 0.13 + 2 * n * CYCLE)
 
     def pick(r, w, out, row, n=256):
-        scan(r + ["EX"], w, out, T.EX[:], row, 0.0, OP.add, OP.max, n)
+        scan(r + ["EX"], w, out, T.EX[:], row, 0.0, OP.add, OP.min, n)
 
     def pick2(r, w, out, row):
-        scan(r + ["EB"], w, out, T.EB[:], row, 0.0, OP.add, OP.min, 128)
+        pick(r, w, out, row, 128)
 
-    dma("S", "dX", [], ["XT"], [(T.XT[:], T.x[:])], 3.5)
-    dma("A", "dU", [], ["UT"], [(T.UT[:], T.u[:])], 2.8)
+    dma("S", "dX", [], ["XT"], [(T.XT[:], T.x[:])], 2.75)
+    dma("A", "dU", [], ["UT"], [(T.UT[:], T.u[:])], 1.9)
     dma("S", "dO", [], ["OL"], [(T.OL[:], T.ol[:])])
     dma("S", "dW", ["XT"], ["W"], [(T.cW[:].bitcast(dt.uint8), T.wc[:]), (T.sW[:], T.ws[:])], 4.0)
     dma("S", "dVV", ["XT"], ["VTL"], [(T.VTL[:], T.v[:])])
@@ -330,7 +344,7 @@ def rank_program(g, core, T, topo):
     iota(["PC"], T.PC[:], [[0, 1]], 0, 1, 1, True)
     iota(["OI"], T.OI[:, 0:16], [[1, 2], [16, 8]], 0, 0, 16, True)
     iota(["OIb"], T.OI[:, 16:24], [[0, 8]], 8, 0, 8, True)
-    iota(["OI2"], T.OI[:, 24:40], [[2, 8], [0, 2]], 0, 0, 16, True)
+    iota(["OI2"], T.OI[:, 24:40], [[1, 8], [0, 2]], 0, 0, 16, True)
     iota(["IR"], T.IR[:], [[0, 16], [1, 16]], 0, 0, 256)
     iota(["TI"], T.TI[:], [[1, 128]], 0, -1, 128)
     iota(["ID"], T.ID[:], [[1, 256]], 0, 0, 256)
@@ -340,12 +354,12 @@ def rank_program(g, core, T, topo):
     iota(["I4"], T.I4[:], [[0, 24], [1, 4]], 0, 0, 96)
     cp(["OI", "OIb"], ["OU"], T.OU[:, 0:24], T.OI[:, 0:24])
     PF = {}
-    names = ("q", "g", "m1", "q8", "r8", "q4", "r4", "r2")
-    for i, (sh, bits) in enumerate(((0, 15), (4, 7), (4, 1), (3, 1), (0, 7), (2, 3), (0, 3), (0, 1))):
+    names = ("q", "g", "m1", "q8", "r8", "q4", "r4", "r2", "r32")
+    for i, (sh, bits) in enumerate(((0, 15), (4, 7), (4, 1), (3, 1), (0, 7), (2, 3), (0, 3), (0, 1), (0, 31))):
         ts(["PC"], ["PI%d" % i], T.PI[:, i:i + 1], T.PC[:], sh, OP.arith_shift_right, bits, OP.bitwise_and)
         PF[names[i]] = T.PF[:, i:i + 1]
     cp(["PI0", "PI1"], ["q", "g"], T.PF[:, 0:2], T.PI[:, 0:2])
-    cp(["PI%d" % i for i in range(2, 8)], list(names[2:]), T.PF[:, 2:8], T.PI[:, 2:8])
+    cp(["PI%d" % i for i in range(2, 9)], list(names[2:]), T.PF[:, 2:9], T.PI[:, 2:9])
 
     def number(name, src, s1, o1, s2, o2, more=[]):
         PF[name] = T.PF[:, len(PF):len(PF) + 1]
@@ -358,8 +372,7 @@ def rank_program(g, core, T, topo):
     affine("qn", "q", -1.0, 255.5)
     affine("q255", "q", -1.0, 255.0)
     affine("q254", "q", -1.0, 254.5)
-    number("xq", "q", 15.0, OP.is_lt, 512.0, OP.mult)
-    affine("nlb", "xq", 0.5, 0.0)
+    number("xq", "q", 15.0, OP.is_lt, -256.0, OP.mult)
     number("t2", "r2", PF["m1"], OP.not_equal, 272.0, OP.mult, ["m1"])
     number("t1", "q", PF["m1"], OP.subtract, 16.0, OP.mult, ["m1"])
     number("tb", "t1", PF["t2"], OP.add, -1.0, OP.add, ["t2"])
@@ -374,7 +387,7 @@ def rank_program(g, core, T, topo):
     number("r7", "r8", 7.0, OP.is_lt, PF["r8"], OP.mult)
     number("g8", "r7", 256.0, OP.mult, PF["t8"], OP.add, ["t8"])
     affine("t7", "q8", 7.0, 0.0)
-    ts(["OI2", "m1"], ["BC32"], T.OU[:, 24:40], T.OI[:, 24:40], PF["m1"], OP.add)
+    cp(["OI2"], ["BC32"], T.OU[:, 24:40], T.OI[:, 24:40])
     ts(["C16", "q3"], ["r7a"], T.TMP[:], T.CW[:, 16:24], PF["q3"], OP.add, 1.0 / 7, OP.mult)
     cp(["r7a"], ["r7b"], T.OI[:, 40:48], T.TMP[:])
     cp(["r7b"], ["REP7"], T.OU[:, 40:48], T.OI[:, 40:48])
@@ -390,10 +403,9 @@ def rank_program(g, core, T, topo):
     fill(["RS"], T.RS[:, 256:512:16], -2.0 ** 95)
     fill(["RC"], T.RC[:], 512.0, 128)
     ts(["C16", "q16"], ["RC"], T.RC[:, 0:256:16], T.CW[:, 16:32], -1.0, OP.mult, PF["q16"], OP.add)
-    ts(["IR", "q"], ["e0"], T.ET0[:, 0:256], T.IR[:], PF["q"], OP.is_equal, -2.0 ** 20, OP.mult, 128)
+    ts(["IR", "q"], ["e0"], T.ET0[:, 0:256], T.IR[:], PF["q"], OP.is_equal, 2.0 ** 19, OP.mult, 128)
     ts(["IR", "q1"], ["e1"], T.ET0[:, 256:512], T.IR[:], PF["q1"], OP.is_equal, -2.0 ** -11, OP.mult, 128)
     scan(["e0", "e1"], ["EX"], T.EX[:], T.ET0[:, 256:512], T.ET0[:, 0:256], 0.0, OP.mult, OP.add, 128)
-    lin(["EX"], ["EB"], T.EB[:], T.EX[:], -0.5, n=256, half=True)
     ts(["I4", "q4", "EX"], ["e0"], T.ET0[:, 0:96], T.I4[:], PF["q4"], OP.is_equal, -2.0 ** 20, OP.mult)
     ts(["I4", "q41", "EX"], ["e1"], T.ET0[:, 256:352], T.I4[:], PF["q41"], OP.is_equal, -2.0 ** -11, OP.mult)
     scan(["e0", "e1"], ["E4"], T.E4[:], T.ET0[:, 256:352], T.ET0[:, 0:96], 0.0, OP.mult, OP.add)
@@ -425,9 +437,9 @@ def rank_program(g, core, T, topo):
     fill(["AR"], T.AR[:], 0.0)
     dma("S", "dPad", ["X0"], ["pad"], [(T.cL[:, 288:320].bitcast(dt.uint8), T.cX[:, 0:32].bitcast(dt.uint8)),
                                        (T.sL[:, 288:320], T.sX[:, 0:32])])
-    zero(["CB"], T.CB[:], 368)
-    ts(["IR", "q"], ["CB"], T.CB[:, 112:128], T.IR[:, 0:16], PF["q"], OP.is_equal)
-    ts(["IR", "q"], ["CB"], T.CB[:, 240:256], T.IR[:, 0:16], PF["q"], OP.is_equal, 1024.0, OP.mult)
+    zero(["CB"], T.CB[:], 448)
+    ts(["ID", "r32"], ["CB"], T.CB[:, 192:224], T.ID[:, 0:32], PF["r32"], OP.is_equal)
+    ts(["ID", "r32"], ["CB"], T.CB[:, 224:256], T.ID[:, 0:32], PF["r32"], OP.is_equal, 2048.0, OP.mult)
     fill(["C64"], T.C64[:, 0:32], 64.0)
     fill(["C64"], T.C64[:, 32:64], -2.0 ** -9)
     fill(["PD2"], T.PD2[:], 0.0)
@@ -438,7 +450,7 @@ def rank_program(g, core, T, topo):
     lin(["ZR"], ["GS0"], T.GS[:, 0:304], T.ZR[:, 0:304], 1.0, 64.0, 304, True)
     zero(["GD"], T.GS[:, 304:608], 304)
     fill(["I1z"], T.I1[:, 112:120], 0)
-    zero(["YXz"], T.YX[:, 0:256], 256)
+    lin(["ID"], ["YXz"], T.YX[:, 0:256], T.ID[:], n=256)
     fill(["HD"], T.HD[:], 0.0)
     quant(["VTL"], "V", 128, T.VTL[:])
     CW = T.CW[:, 0:16]
@@ -475,12 +487,21 @@ def rank_program(g, core, T, topo):
         mm(XK + ["U"], "PD1", 128, X, 128, "U", 0)
         mm(XK + ["UPc2", "UPs2"], "PC_", 256, "UP", 256, X, 0)
         mm(XK + ["UPc1", "UPs1"], "PB", 256, "UP", 128, X, 0)
-        act(["PD0", "PD1"], ["SB"], T.SB2[:], T.PD[:, 8:1024:512])
+        act(["PD0", "PD1"], ["SB"], T.SB2[:, 0:2], T.PD[:, 8:1024:512])
         act(["PD0", "PD1"], ["DL"], T.DL[:], T.PD[:, 8:1024:512], AF.Abs, 2.0 ** -124, 1.25 * 2.0 ** -24)
         for h in range(2):
             lin(["TR", "DL", "SB"], ["TH%d" % h], T["TH%d" % h][:], T.TR[:], T.DL[:, h:h + 1], T.SB2[:, h:h + 1], 128)
-        ts(["PC_", "SB"], ["BTa"], T.BT[:, 512:1024:4], ps("PC_", 128, 256), T.SB2[:, 0:1], OP.is_ge, n=128)
-        ts(["PC_", "SB"], ["BTb"], T.BT[:, 1:512:4], ps("PC_", 0, 128), T.SB2[:, 1:2], OP.is_gt, n=128)
+        if BIRTH_S > 1:
+            act(["SB", "DL"], ["SBm"], T.SB2[:, 2:3], T.DL[:, 0:1], AF.Identity, T.SB2[:, 0:1], -1.0)
+            act(["PC_", "SBm"], ["SN0"], T.SN[:, 0:128], ps("PC_", 128, 256), AF.Sign, T.SB2[:, 2:3], -1.0, n=128)
+            act(["SN0"], ["BTa"], T.BT[:, 512:1024:4], T.SN[:, 0:128], AF.Relu, 0.0, -1.0, n=128)
+        else:
+            ts(["PC_", "SB"], ["BTa"], T.BT[:, 512:1024:4], ps("PC_", 128, 256), T.SB2[:, 0:1], OP.is_ge, n=128)
+        if BIRTH_S:
+            act(["PC_", "SB"], ["SN1"], T.SN[:, 256:384], ps("PC_", 0, 128), AF.Sign, T.SB2[:, 1:2], -1.0, n=128)
+            act(["SN1"], ["BTb"], T.BT[:, 1:512:4], T.SN[:, 256:384], AF.Relu, 0.0, -1.0, n=128)
+        else:
+            ts(["PC_", "SB"], ["BTb"], T.BT[:, 1:512:4], ps("PC_", 0, 128), T.SB2[:, 1:2], OP.is_gt, n=128)
         tt(["PC_", "TH0"], ["BTc"], T.BT[:, 0:512:4], ps("PC_", 0, 128), T.TH0[:], OP.is_ge, 128)
         tt(["PC_", "TH1"], ["BTd"], T.BT[:, 513:1024:4], ps("PC_", 128, 256), T.TH1[:], OP.is_ge, 128)
         quant(["BTa", "BTb", "BTc", "BTd", "zB2", "zB3"], "B", 256, T.BT[:])
@@ -513,7 +534,7 @@ def rank_program(g, core, T, topo):
                         ts([bank, "SW%d" % s, "z%d%d" % (s, a)], ["ct%d.%d" % (s, m)], v, ps(bank, 0, 16 * m),
                            T.SW[:, 256 * s + 16 * m + 15:256 * s + 16 * m + 16], (OP.is_gt, OP.is_lt)[s], n=16 * m)
                         if m >= BY_SCAN[s]:
-                            e = 1024 * s + 256 * (m - 11)
+                            e = 4096 * s + 256 * m + 256
                             scan(["ct%d.%d" % (s, m), "ZR"], ["AR%d.%d" % (s, m)], T.RV[:, e - 16 * m:e], T.ZR[:, 0:16 * m], v,
                                  0.0, OP.add, OP.add, 8 * m)
                             continue
@@ -527,7 +548,7 @@ def rank_program(g, core, T, topo):
                T.RD[:, 256 * s + 15:256 * s + 16 * m:16], T.AR[:, 16 * s:16 * s + m], OP.add)
             if m < 16:
                 tt(["RD%d" % s] + ["AR%d.%d" % (s, i) for i in range(m, 16)], ["RV%d" % s], T.RW[:, 16 * s + m:16 * s + 16],
-                   T.RD[:, 256 * s + 16 * m + 15:256 * s + 256:16], T.RV[:, 1024 * s + 256 * (m - 11) - 1:1024 * s + 1024:256], OP.add)
+                   T.RD[:, 256 * s + 16 * m + 15:256 * s + 256:16], T.RV[:, 4096 * s + 256 * m + 255:4096 * s + 4096:256], OP.add)
             pick([sums], ["EC%d" % s], T.EC[:, c], ps(sums, 0, 256))
         places(0)
         places(1)
@@ -536,8 +557,9 @@ def rank_program(g, core, T, topo):
             k = ("Q0", "Q1", "Q2", "Q0")[b]
             mm(XK + ["KR%d" % b], k, 256, "KR%d" % b, 0, X, 0)
             lin([k], ["FT%d" % b], T.FT[:, 256 * b:256 * b + 256], ps(k, 0, 256), 2.0 ** -8, n=256)
-        dma("S", "dF", ["FT0", "FT1", "FT2", "FT3"], ["FU"], [(T.FU[:], T.FT[:])])
-        lin(["ID", "L16"], ["LF"], T.LF[:], T.ID[:].indirect(T.L16[:]), 2.0 ** -8, n=far(256))
+        dma("S", "dF", ["FT0", "FT1", "FT2", "FT3"], ["FU"], [(T.FU[:], T.FT[:])], 2.75)
+        if t == 0:
+            lin(["ID", "L16"], ["LF"], T.LF[:], T.ID[:].indirect(T.L16[:]), 2.0 ** -8, n=far(256))
         tt(["PC_", "LF"], ["VH0"], T.VH[:, 0:256], ps("PC_", 0, 256), T.LF[:], OP.add, 256)
         for i in range(1, 6):
             lin(["VH%d" % (i - 1), "L16"], ["VH%d" % i], T.VH[:, 256 * i:256 * i + 256],
@@ -547,17 +569,20 @@ def rank_program(g, core, T, topo):
         ts(VK + ["xq"], ["I0"], T.I0[:], VV, PF["xq"], OP.subtract, 256.0, OP.mult, 112)
         ts(["I0"], ["I1"], T.I1[:, 0:112], T.I0[:], 255, OP.bitwise_and, n=112)
         tt(["I1", "I1z"], ["D7"], T.D7[:], T.I1[:, 0:112], T.I1[:, 1:113], OP.subtract, 224)
-        tt(VK + ["RW0", "RV0", "REP7"], ["VR"], T.VR[:], T.RW[:, 0:16].indirect(REP7), VV, OP.add, far(112))
-        tt(["EC0", "VR", "REPE"], ["CM"], T.CM[:], T.EC[:, 0:256].indirect(T.OU[:, 72:79]), T.VR[:], OP.is_le, far(112))
-        scan(["CM", "D7"], ["HR"], T.HR[:, 0:111], T.CM[:, 0:111], T.D7[:, 1:112], 0.0, OP.mult, OP.add, 111)
-        cp(["HR"], ["R16"], T.R16[:], T.HR[:, 5:111:7])
-        for z in range(8):
-            if z < COUNT_V:
-                cp(["CB", "R16"], ["EW"], T.EW[:], T.CB[:, 112 - 16 * z:368 - 16 * z].indirect(T.R16[:]), far(256))
-                emit("V", ["EW"], ["CA%d" % z], lambda e, z=z: e.tensor_reduce(T.CA[:, z:z + 1], T.EW[:], AxisListType.X, OP.add), cyc(256))
-                continue
-            act(["CB", "R16"], ["CJ%d" % (z % 2), "CA%d" % z], T.CJ[:, 256 * (z % 2):256 * (z % 2) + 256],
-                T.CB[:, 112 - 16 * z:368 - 16 * z].indirect(T.R16[:]), AF.Copy, 0.0, 1.0, T.CA[:, z:z + 1], n=far(256))
+        if EARLY:
+            tt(VK + ["RW0", "RV0", "REP7"], ["VR"], T.VR[:], T.RW[:, 0:16].indirect(REP7), VV, OP.add, far(112))
+            tt(["EC0", "VR", "REPE"], ["CM"], T.CM[:], T.EC[:, 0:256].indirect(T.OU[:, 72:79]), T.VR[:], OP.is_le, far(112))
+        else:
+            tt(["EC0", "RW0", "RV0"], ["VR"], T.VR[:, 0:16], T.EC[:, 15:256:16], T.RW[:, 0:16], OP.subtract)
+            tt(VK + ["VR", "REP7"], ["CM"], T.CM[:], T.VR[:, 0:16].indirect(REP7), VV, OP.is_le, far(112))
+        for i in range(2):
+            scan(["CM", "D7"], ["HR%d" % i], T.HR[:, 112 * i:112 * i + 111], T.CM[:, 0:111], T.D7[:, 1:112], 0.0, OP.mult, OP.add, 111)
+        cp(["HR0"], ["R16"], T.R16[:], T.HR[:, 5:111:7])
+        turn(["HR0", "HR1"], ["RQ"], T.QQ[:, 32:64], T.HR[:, 5:223:7])
+        cp(["RQ"], ["R32"], T.R32[:], T.QQ[:, 32:64])
+        for z in range(4):
+            act(["CB", "R32"], ["CJ%d" % (z % 2), "CA%d" % z], T.CJ[:, 512 * (z % 2):512 * (z % 2) + 512],
+                T.CB[:, 192 - 64 * z:448 - 64 * z].indirect(T.R32[:]), AF.Copy, 0.0, 1.0, T.CA[:, z:z + 1], n=far(512))
         for b in range(4):
             tt(["FT%d" % b, "FU", "R16"], ["Z%d" % b], T.Z[:, b:1024:4], T.FT[:, 256 * b:256 * b + 256].indirect(T.R16[:]),
                T.FU[:, 256 * b:256 * b + 256], OP.add, far(256))
@@ -581,25 +606,28 @@ def rank_program(g, core, T, topo):
         cp(["I1", "I1z", "HOPS"], ["H16"], T.H16[:], T.I1[:].indirect(HOPS), far(96))
         lin(["D7", "D8L"], ["D8", "D8e"], T.D8[:], T.D7[:].indirect(D8L), n=far(128))
         tt(["CW", "I1"], ["D8"], T.D8[:, 0:128:8], CW, T.I1[:, 1:112:7], OP.subtract)
-        ts(["I1", "I1z", "D8L", "nlb"], ["I8"], T.G8[:, 256:384], T.I1[:].indirect(D8L), -2.0 ** -8, OP.mult, PF["nlb"], OP.add, far(128))
-        across(["CA%d" % z for z in range(8)], ["CI0"], T.CI[0:64, 0:8], T.CA[0:64, :], T.CA[64:128, :])
-        ts(["CI0"], ["CI1"], T.CI[0:64, 8:16], T.CI[0:64, 0:8], 1023, OP.bitwise_and)
-        ts(["CI0"], ["CI2"], T.CI[0:64, 16:24], T.CI[0:64, 0:8], 10, OP.arith_shift_right)
-        across(["CI1", "CI2", "Q4z"], ["Q4"], T.QQ[0:32, 0:16], T.CI[0:32, 8:24], T.CI[32:64, 8:24])
-        turn(["Q4"], ["Q5"], T.QQ[0:32, 32:64], T.QQ[0:32, 0:32])
-        tt(["Q5"], ["Q6"], T.QQ[0:32, 64:80], T.QQ[0:32, 32:48], T.QQ[0:32, 48:64], OP.add)
-        tt(["Q5"], ["Q6b"], T.QQ[0:32, 80:96], T.QQ[0:32, 32:48], T.QQ[0:32, 48:64], OP.add)
-        for a in range(4):
-            turn(["Q6", "Q6b"], ["Q7%d" % a], T.QQ[32 * a:32 * a + 32, 96:128], T.QQ[0:32, 64:96])
-        act(["Q70", "Q71", "Q72", "Q73", "BC32"], ["RP"], T.RP[:], T.QQ[:, 96:128].indirect(BC32), AF.Relu, 255.0, -1.0, n=far(256))
-        turn(["RP"], ["TO"], T.TO[:], T.RP[:], 128)
-        act(["TO", "qn"], ["AJ0", "AC"], T.AJ[:, 0:256], T.TO[:], AF.Sign, PF["qn"], -1.0, T.SC[:, 0:1], n=256)
+        ts(["I1", "I1z", "D8L", "xq"], ["I8"], T.G8[:, 256:384], T.I1[:].indirect(D8L), 2.0 ** -8, OP.mult, PF["xq"], OP.add, far(128))
+        across(["CA%d" % z for z in range(4)], ["CI0"], T.CI[0:64, 0:4], T.CA[0:64, :], T.CA[64:128, :])
+        ts(["CI0"], ["CI1"], T.CI[0:64, 8:16:2], T.CI[0:64, 0:4], 2047, OP.bitwise_and)
+        ts(["CI0"], ["CI2"], T.CI[0:64, 9:16:2], T.CI[0:64, 0:4], 11, OP.arith_shift_right)
+        across(["CI1", "CI2", "Q4z"], ["Q4"], T.QQ[0:32, 0:8], T.CI[0:32, 8:16], T.CI[32:64, 8:16])
+        if SPREAD:
+            for a in range(1, 4):
+                lin(["Q4"], ["Q4%d" % a], T.QQ[32 * a:32 * a + 32, 0:8], T.QQ[0:32, 0:8])
+            act(["Q4", "Q41", "Q42", "Q43", "BC32"], ["RP"], T.RP[:], T.QQ[:, 0:8].indirect(BC32), AF.Relu, 255.0, -1.0, n=far(256))
+            turn(["RP"], ["TO0"], T.TO[:], T.RP[:], 128)
+        else:
+            act(["Q4", "Q4z", "BC32"], ["RP"], T.RP[:], T.QQ[:, 0:8].indirect(BC32), AF.Relu, 255.0, -1.0, n=far(256))
+            for a in range(4):
+                turn(["RP"], ["TO%d" % a], T.TO[32 * a:32 * a + 32, :], T.RP[0:32, :], 128)
+        TO = ["TO0", "TO1", "TO2", "TO3"]
+        act(TO + ["qn"], ["AJ0", "AC"], T.AJ[:, 0:256], T.TO[:], AF.Sign, PF["qn"], -1.0, T.SC[:, 0:1], n=256)
         ts(["C64", "AC"], ["FB"], T.FB[:, 0:32], T.C64[:, 0:32], T.SC[:, 0:1], OP.is_lt)
         turn(["FB"], ["FX"], T.FB[:, 32:64], T.FB[:, 0:32])
         emit("V", ["FX"], ["SF"], lambda e: e.tensor_reduce(T.SC[:, 1:2], T.FB[:, 32:48], AxisListType.X, OP.add), cyc(64))
         ts(["SF", "tb"], ["SL"], T.SL[:, 0:1], T.SC[:, 1:2], PF["tb"], OP.add)
-        ts(["TO", "q255"], ["LT"], T.LT[:, 0:256], T.TO[:], PF["q255"], OP.is_gt, 2.0, OP.mult, 128)
-        ts(["TO", "q255"], ["LE"], T.LE[:], T.TO[:], PF["q255"], OP.is_ge, 2.0, OP.mult, 128)
+        ts(TO + ["q255"], ["LT"], T.LT[:, 0:256], T.TO[:], PF["q255"], OP.is_gt, 2.0, OP.mult, 128)
+        ts(TO + ["q255"], ["LE"], T.LE[:], T.TO[:], PF["q255"], OP.is_ge, 2.0, OP.mult, 128)
         scan(["LT", "ZR", "AC"], ["AA"], T.AA[:], T.LT[:, 0:256], T.ZR[:, 0:256], T.SC[:, 0:1], OP.add, OP.max, 128)
         scan(["LE", "AA", "GS0"], ["GS"], T.GS[:, 32:288], T.LE[:], T.AA[:], 64.0, OP.add, OP.min, 128)
         scan(["GS", "GS0"], ["GD"], T.GS[:, 336:592], T.GS[:, 32:288], T.GS[:, 31:287], 0.0, OP.max, OP.subtract, 128)
@@ -608,7 +636,7 @@ def rank_program(g, core, T, topo):
             turn([k, "GS0"], [k + "b"], T.TG[:, 544 * i + 256:544 * i + 544], T.GS[:, 304 * i + 16:304 * i + 304], 144)
         ts(["GDa", "GDb", "SL", "HD"], ["HDa"], T.HD[:, 1:32:2], T.TG[:, 544:1088].indirect(T.SL[:, 0:1]), 0.25, OP.mult, n=far(16))
         tt(["GSa", "GSb", "SL", "CP", "HD"], ["HDb"], T.HD[:, 32:64:2], T.TG[:, 0:544].indirect(T.SL[:, 0:1]), T.CP[:], OP.subtract, far(16))
-        ts(["TO", "q255"], ["LQ"], T.LT[:, 256:512], T.TO[:], PF["q255"], OP.is_equal, 2.0, OP.mult, 128)
+        ts(TO + ["q255"], ["LQ"], T.LT[:, 256:512], T.TO[:], PF["q255"], OP.is_equal, 2.0, OP.mult, 128)
         scan(["LQ", "ZR"], ["CE"], T.GN[:], T.LT[:, 256:512], T.ZR[:, 0:256], 65.0, OP.add, OP.max, 128)
         act(["CE", "AC"], ["AJ1", "JS"], T.AJ[:, 256:512], T.GN[:], AF.Sign, T.SC[:, 0:1], -1.0, T.SC[:, 2:3], n=256)
         ts(["AC"], ["NV"], T.SC[:, 3:4], T.SC[:, 0:1], 64.0, OP.is_le, 1024.0, OP.mult)
@@ -616,7 +644,7 @@ def rank_program(g, core, T, topo):
         ts(["C64", "JS", "NW"], ["FK"], T.QQ[:, 128:160], T.C64[:, 32:64], T.SC[:, 2:3], OP.mult, T.SC[:, 4:5], OP.add)
         turn(["FK"], ["FL_"], T.QQ[:, 160:192], T.QQ[:, 128:160])
         emit("V", ["FL_"], ["TN"], lambda e: e.tensor_reduce(T.SC[:, 5:6], T.QQ[:, 160:176], AxisListType.X, OP.min), cyc(64))
-        scan(["HDa", "HDb"], ["HO"], T.HO[:], T.HD[:, 0:32], T.HD[:, 32:64], 0.0, OP.mult, OP.add)
+        scan(["HDa", "HDb"], ["HO"], T.HO[:, 0:32], T.HD[:, 0:32], T.HD[:, 32:64], 0.0, OP.mult, OP.add)
         cp(["HO"], ["NI16"], T.NI16[:], T.HO[:, 1:32:2])
         for b in range(4):
             k = ("Q0", "Q1", "Q2", "PC_")[b]
@@ -630,30 +658,34 @@ def rank_program(g, core, T, topo):
         lin(["P", "Pb", "NI16"], [XN + "s"], T.sX[:, 256 * t + 256:256 * t + 512], T.sP[:, :].indirect(T.NI16[:]), n=far(256))
         for s in range(6):
             c = slice(256 * s, 256 * s + 256)
-            lin(["TO", "H16"], ["FL%d" % s], T.FL[:, c], T.TO[:].indirect(T.H16[:, 16 * s:16 * s + 16]), n=far(256))
+            lin(TO + ["H16"], ["FL%d" % s], T.FL[:, c], T.TO[:].indirect(T.H16[:, 16 * s:16 * s + 16]), n=far(256))
             pick2(["FL%d" % s], ["FP%d" % (s + 1)], T.FP[:, 256 * s + 256:256 * s + 512], T.FL[:, c])
-        tt(["FP%d" % s for s in range(7)] + ["G8L", "I8"], ["KY"], T.G8[:, 128:256], T.FP[:].indirect(G8L), T.G8[:, 256:384], OP.add, far(128))
-        ts(["KY", "TN"], ["G8", "G8k"], T.G8[:, 0:128], T.G8[:, 128:256], T.SC[:, 5:6], OP.is_ge, n=128)
+        lin(["I8", "TN"], ["KY"], T.G8[:, 128:256], T.G8[:, 256:384], 1.0, T.SC[:, 5:6], 128)
+        tt(["FP%d" % s for s in range(7)] + ["G8L", "KY"], ["G8", "G8k"], T.G8[:, 0:128], T.FP[:].indirect(G8L), T.G8[:, 128:256], OP.is_ge, far(128))
         lin(["HDa"], ["G8k"], T.G8[:, 7:128:8], T.HD[:, 1:32:2], -2.0, 1.0)
+        lin(["HDa"], ["G8g"], T.HO[:, 32:48], T.HD[:, 1:32:2], 2.0)
         cp(["LL%d" % t], ["LI0"], T.LI[:, 0:48], T.LL[:, 48 * t:48 * t + 48])
         ts(["LI0"], ["LI1"], T.LI[:, 49:144:2], T.LI[:, 0:48], 255, OP.bitwise_and)
         ts(["LI0"], ["LI2"], T.LI[:, 48:144:2], T.LI[:, 0:48], 8, OP.arith_shift_right)
         cp(["LI1", "LI2"], ["YXe"], T.YX[:, 256:352], T.LI[:, 48:144], 96)
-        lin(["YXz", "YXe", "NI16"], ["EW"], T.EW[:], T.YX[:].indirect(T.NI16[:]), n=far(256))
-        pick2(["EW"], ["EQ"], T.EQ[:], T.EW[:])
-        lin(["EQ", "nlb"], ["D8e"], T.D8[:, 7:128:8], T.EQ[:, E15], 1.0, PF["nlb"])
+        tt(["HO", "G8g"], ["D8e"], T.D8[:, 7:128:8], T.HO[:, 1:32:2], T.HO[:, 32:48], OP.mult)
         scan(["G8", "G8k", "D8", "D8e"], ["HL"], T.HL[:], T.G8[:, 0:128], T.D8[:], 0.0, OP.mult, OP.add, 128)
-        cp(["HL"], ["L16"], T.L16[:], T.HL[:, 7:128:8])
+        cp(["HL"], ["F16"], T.F16[:], T.HL[:, 7:128:8])
         if not last:
-            lin(["HL", "xq"], ["VT6"], VT6, T.HL[:, 7:128:8], 2.0 ** -8, PF["xq"])
+            lin(["YXz", "YXe", "F16"], ["LF"], T.LF[:], T.YX[:].indirect(T.F16[:]), 2.0 ** -8, n=far(256))
+            pick(["LF"], ["VT6"], T.VT[:, 96:96 + 1786:7], T.LF[:])
+            ts(["VT6", "xq"], ["L16"], T.L16[:], VT6, PF["xq"], OP.subtract, 256.0, OP.mult)
 
-    mm(["V", "X3", "X3s"], "PA", 256, "V", 0, "X3", 0)
+    mm(["V", "P"], "PA", 256, "V", 0, "P", 0)
+    mm(["V", "Pb"], "PB", 128, "V", 0, "Pb", 0)
+    lin(["PA"], ["YCa"], T.YC[:, 0:256], ps("PA", 0, 256), n=256)
+    lin(["PB"], ["YCb"], T.YC[:, 256:352], ps("PB", 0, 96), n=96)
     dma("S", "dOc", ["X3", "X3s"], ["oc"], [(T.oc[:, :], T.cX[:, 768:1024].bitcast(dt.uint8))] + [
         (T.osc[4 * k:4 * k + 4, :], T.sX[32 * k:32 * k + 4, 768:1024]) for k in range(4)])
-    lin(["PA"], ["YO"], T.YO[:], ps("PA", 0, 256), n=256)
+    lin(["YCa", "YCb", "NI16"], ["YO"], T.YO[:], T.YC[:].indirect(T.NI16[:]), n=far(256))
     dma("A", "dY", ["YO"], ["y"], [(T.y[:, :], T.YO[:])])
-    lin(["ID", "L16"], ["LO"], T.LO[:], T.ID[:].indirect(T.L16[:]), n=far(256))
-    dma("S", "dLk", ["LO"], ["lk"], [(T.lk[:, :], T.LO[0:128:16, :])])
+    lin(["YXz", "YXe", "F16"], ["LO"], T.LO[:], T.YX[:].indirect(T.F16[:]), n=far(256))
+    dma("S", "dLk", ["LO"], ["lk"], [(T.lk[:, :], T.LO[0:128:16, :])], 1.2)
     schedule()
     for s in cnt:
         if known["S"].get(s, 0) < cnt[s]:

@@ -27,7 +27,7 @@ _q(W=512, U=128, UP=384, V=128, X=1024, L=320, P=384, E=384)
 _q(K=768)
 _q(C=256 + 2 * TILE_O[4])
 _sb(B, TK=1552, IR=256, I4=96, TI=128, BK=128, NB=256, RS=512, RC=256, EX=256, E4=96, ET0=512, TR=128)
-_sb(B, C64=64, ZR=528, PD2=96, CB=448, SN=512)
+_sb(B, C64=64, ZR=528, PD2=96, CB=448, SN=1024)
 _sb(F, ID=256, PF=32, CW=48, NN=8, CP=16, TMP=8)
 _sb(U, OU=80, SL=24)
 _sb(F, SR=512, SG=512, SW=512, SB2=4, DL=2, TH0=128, TH1=128, AR=32, RW=32, EC=512, EP=16)
@@ -50,12 +50,13 @@ for _i in range(4):
     PLACE["C0%d" % _i] = ("C", 256 + TILE_O[_i])
     PLACE["C1%d" % _i] = ("C", 256 + TILE_O[4] + TILE_O[_i])
     PLACE["E%d" % _i] = ("E", 128 * _i)
-CYCLE, WAKE, FLIGHT, JUMP, STREW, SEND, FIRST = 0.00085, 0.25, 1.2, 1.5, 3.5, 0.3, 1.0
+CYCLE, WAKE, FLIGHT, JUMP, STREW, SEND, FIRST = 0.00085, 0.26, 1.2, 1.5, 3.5, 0.3, 1.0
+PE_CYCLE = 0.0007
 TRIES, SHAKE, SPARE = 4000, 1.5, 0.3
-BY_SCAN = (16, 16)
+BY_SCAN = (13, 13)
 EARLY, SPREAD, BIRTH_S = False, True, 1
 SLOW, SHARE = 1.4, 0.75
-BY_SIGN = ((11, 10, 9), (11, 10, 9))
+BY_SIGN = ((12, 11, 10, 9, 8), (12, 11, 10, 9, 8))
 
 SEMAPHORES = ["sV", "sA", "sP", "sG", "dX", "dU", "dO", "dW", "dVV", "dPad", "dF", "dY", "dLk", "dOc", "ls",
               "aC0", "aC1", "aC2", "aL0", "aL1", "aL2"]
@@ -303,9 +304,10 @@ def rank_program(g, core, T, topo):
             s = way("A", r, w, lambda e: e.activation(out, a, AF.Copy if plain and bias == 0.0 else AF.Identity, bias, scale), cyc(n))
         nodes.append(([s, v], r, w, 0.0))
 
-    def zero(w, out, n):
-        nodes.append(([way("V", ["ZR"], w, lambda e: e.memset(out, 0.0), cyc(n // 2)),
-                       way("A", ["ZR"], w, lambda e: e.activation(out, T.ZR[:, 0:n], AF.Copy), cyc(n))], ["ZR"], w, 0.0))
+    def zero(w, out, n, x=0):
+        nodes.append(([way("G", ["ZR"], w, lambda e: e.iota(out, [[0, n]], x, 0, allow_small_or_imprecise_dtypes=True), 0.13 + 2 * n * CYCLE),
+                       way("A", ["ZR"], w, lambda e: e.activation(out, T.ZR[:, 0:n], AF.Identity, float(x)), cyc(n)),
+                       way("V", ["ZR"], w, lambda e: e.memset(out, float(x)), cyc(n // 2))], ["ZR"], w, 0.0))
 
     def far(n):
         return 70 + JUMP * n
@@ -320,7 +322,7 @@ def rank_program(g, core, T, topo):
         o = BANK[bank][1]
         emit("P", r, [bank] + line, lambda e: e.matmul_mx(
             T[BANK[bank][0]][:, o:o + n], T["c" + L][:, l0:l0 + 128], T["s" + L][:, l0:l0 + 128],
-            T["c" + R][:, r0:r0 + n], T["s" + R][:, r0:r0 + n], start, stop), 0.00125 * (n + 16))
+            T["c" + R][:, r0:r0 + n], T["s" + R][:, r0:r0 + n], start, stop), PE_CYCLE * (n + 16))
 
     def iota(w, out, pattern, base, cm, n, whole=False):
         if whole:
@@ -401,7 +403,7 @@ def rank_program(g, core, T, topo):
     zero(["RS"], T.RS[:], 512)
     fill(["RS"], T.RS[:, 0:256:16], 2.0 ** 95)
     fill(["RS"], T.RS[:, 256:512:16], -2.0 ** 95)
-    fill(["RC"], T.RC[:], 512.0, 128)
+    zero(["RC"], T.RC[:], 256, 512)
     ts(["C16", "q16"], ["RC"], T.RC[:, 0:256:16], T.CW[:, 16:32], -1.0, OP.mult, PF["q16"], OP.add)
     ts(["IR", "q"], ["e0"], T.ET0[:, 0:256], T.IR[:], PF["q"], OP.is_equal, 2.0 ** 19, OP.mult, 128)
     ts(["IR", "q1"], ["e1"], T.ET0[:, 256:512], T.IR[:], PF["q1"], OP.is_equal, -2.0 ** -11, OP.mult, 128)
@@ -410,7 +412,7 @@ def rank_program(g, core, T, topo):
     ts(["I4", "q41", "EX"], ["e1"], T.ET0[:, 256:352], T.I4[:], PF["q41"], OP.is_equal, -2.0 ** -11, OP.mult)
     scan(["e0", "e1"], ["E4"], T.E4[:], T.ET0[:, 256:352], T.ET0[:, 0:96], 0.0, OP.mult, OP.add)
     ts(["TI"], ["TR"], T.TR[:], T.TI[:], 0.0, OP.is_le)
-    fill(["TKB"], T.TK[:, 0:512], 1.0, 256)
+    zero(["TKB"], T.TK[:, 0:512], 512, 1)
     for i in range(4):
         ts(["BK", "g"], ["TKS%d" % i], T.TK[:, 512 + i:1024:4], T.BK[:], PF["g"], OP.is_equal)
     zero(["TKR"], T.TK[:, 1024:1552], 528)
@@ -434,30 +436,28 @@ def rank_program(g, core, T, topo):
             zero(["z%d%d" % (s, a)], T.CT[:, o + lo:o + 4 * TILE_N[a]], 4 * TILE_N[a] - lo)
     for i in (2, 3):
         zero(["zB%d" % i], T.BT[:, i:1024:4], 256)
-    fill(["AR"], T.AR[:], 0.0)
+    zero(["AR"], T.AR[:], 32)
     dma("S", "dPad", ["X0"], ["pad"], [(T.cL[:, 288:320].bitcast(dt.uint8), T.cX[:, 0:32].bitcast(dt.uint8)),
                                        (T.sL[:, 288:320], T.sX[:, 0:32])])
     zero(["CB"], T.CB[:], 448)
     ts(["ID", "r32"], ["CB"], T.CB[:, 192:224], T.ID[:, 0:32], PF["r32"], OP.is_equal)
     ts(["ID", "r32"], ["CB"], T.CB[:, 224:256], T.ID[:, 0:32], PF["r32"], OP.is_equal, 2048.0, OP.mult)
-    fill(["C64"], T.C64[:, 0:32], 64.0)
-    fill(["C64"], T.C64[:, 32:64], -2.0 ** -9)
-    fill(["PD2"], T.PD2[:], 0.0)
-    fill(["PD2"], T.PD2[:, 1:96:2], 256.0)
-    fill(["Q4z"], T.QQ[:, 0:32], 0.0)
-    fill(["ETz"], T.ET[:, 384:512], 0.0)
-    fill(["RTz"], T.RT[:, 384:512], 0.0)
-    lin(["ZR"], ["GS0"], T.GS[:, 0:304], T.ZR[:, 0:304], 1.0, 64.0, 304, True)
+    zero(["C64"], T.C64[:, 0:32], 32, 64)
+    lin(["C64"], ["C64"], T.C64[:, 32:64], T.C64[:, 0:32], -2.0 ** -15)
+    iota(["PD2"], T.PD2[:], [[0, 48], [256, 2]], 0, 0, 96)
+    zero(["ETz"], T.ET[:, 384:512], 128)
+    zero(["RTz"], T.RT[:, 384:512], 128)
+    zero(["GS0"], T.GS[:, 0:304], 304, 64)
     zero(["GD"], T.GS[:, 304:608], 304)
-    fill(["I1z"], T.I1[:, 112:120], 0)
-    lin(["ID"], ["YXz"], T.YX[:, 0:256], T.ID[:], n=256)
-    fill(["HD"], T.HD[:], 0.0)
+    iota(["I1z"], T.I1[:, 112:120], [[0, 8]], 0, 0, 8, True)
+    iota(["YXz"], T.YX[:, 0:256], [[1, 256]], 0, 0, 256)
+    zero(["HD"], T.HD[:], 64)
     quant(["VTL"], "V", 128, T.VTL[:])
     CW = T.CW[:, 0:16]
     ts(["C16", "q"], ["CW"], CW, T.CW[:, 16:32], PF["q"], OP.add)
     lin(["CW"], ["CP"], T.CP[:], CW, 2.0, -446.0)
     lin(["CW"], ["HD"], T.HD[:, 33:64:2], CW)
-    lin(["ZR"], ["FP0"], T.FP[:, 0:256], T.ZR[:, 0:256], 1.0, -2048.0, 256, True)
+    zero(["FP0"], T.FP[:, 0:256], 256, -2048)
     VV, VT0, VT6 = T.VT[:, 105:1888:16], T.VT[:, 105:1888:112], T.VT[:, 201:1888:112]
     lin(["ZR", "xq"], ["VT0"], VT0, T.ZR[:, 0:16], 1.0, PF["xq"])
     cp(["OL"], ["L16"], T.L16[:], T.OL[:])
@@ -525,10 +525,10 @@ def rank_program(g, core, T, topo):
                     if m < 16:
                         v = T.CT[:, o + 4 * TILE_O[a] + j:o + 4 * TILE_O[a] + 64 * m:4]
                         if m in BY_SIGN[s]:
-                            k = 256 * (m % 2)
-                            act(["SR%d" % s, "SW%d" % s], ["SN%d" % (m % 2)], T.SN[:, k:k + 16 * m], T.SR[:, 256 * s:256 * s + 16 * m],
+                            k = 256 * (m % 4)
+                            act(["SR%d" % s, "SW%d" % s], ["SN%d" % (m % 4)], T.SN[:, k:k + 16 * m], T.SR[:, 256 * s:256 * s + 16 * m],
                                 AF.Sign, T.SW[:, 256 * s + 16 * m + 15:256 * s + 16 * m + 16], -1.0, n=16 * m)
-                            act(["SN%d" % (m % 2), "AR", "z%d%d" % (s, a)], ["AR%d.%d" % (s, m), "ct%d.%d" % (s, m)], v, T.SN[:, k:k + 16 * m],
+                            act(["SN%d" % (m % 4), "AR", "z%d%d" % (s, a)], ["AR%d.%d" % (s, m), "ct%d.%d" % (s, m)], v, T.SN[:, k:k + 16 * m],
                                 AF.Relu, 0.0, (-1.0, 1.0)[s], T.AR[:, 16 * s + m:16 * s + m + 1], n=16 * m)
                             continue
                         ts([bank, "SW%d" % s, "z%d%d" % (s, a)], ["ct%d.%d" % (s, m)], v, ps(bank, 0, 16 * m),
@@ -610,17 +610,12 @@ def rank_program(g, core, T, topo):
         across(["CA%d" % z for z in range(4)], ["CI0"], T.CI[0:64, 0:4], T.CA[0:64, :], T.CA[64:128, :])
         ts(["CI0"], ["CI1"], T.CI[0:64, 8:16:2], T.CI[0:64, 0:4], 2047, OP.bitwise_and)
         ts(["CI0"], ["CI2"], T.CI[0:64, 9:16:2], T.CI[0:64, 0:4], 11, OP.arith_shift_right)
-        across(["CI1", "CI2", "Q4z"], ["Q4"], T.QQ[0:32, 0:8], T.CI[0:32, 8:16], T.CI[32:64, 8:16])
-        if SPREAD:
-            for a in range(1, 4):
-                lin(["Q4"], ["Q4%d" % a], T.QQ[32 * a:32 * a + 32, 0:8], T.QQ[0:32, 0:8])
-            act(["Q4", "Q41", "Q42", "Q43", "BC32"], ["RP"], T.RP[:], T.QQ[:, 0:8].indirect(BC32), AF.Relu, 255.0, -1.0, n=far(256))
-            turn(["RP"], ["TO0"], T.TO[:], T.RP[:], 128)
-        else:
-            act(["Q4", "Q4z", "BC32"], ["RP"], T.RP[:], T.QQ[:, 0:8].indirect(BC32), AF.Relu, 255.0, -1.0, n=far(256))
-            for a in range(4):
-                turn(["RP"], ["TO%d" % a], T.TO[32 * a:32 * a + 32, :], T.RP[0:32, :], 128)
-        TO = ["TO0", "TO1", "TO2", "TO3"]
+        across(["CI1", "CI2"], ["Q4"], T.QQ[0:32, 0:8], T.CI[0:32, 8:16], T.CI[32:64, 8:16])
+        for a in range(1, 4):
+            lin(["Q4"], ["Q4%d" % a], T.QQ[32 * a:32 * a + 32, 0:8], T.QQ[0:32, 0:8])
+        act(["Q4", "Q41", "Q42", "Q43", "BC32"], ["RP"], T.RP[:], T.QQ[:, 0:8].indirect(BC32), AF.Relu, 255.0, -1.0, n=far(256))
+        turn(["RP"], ["TO"], T.TO[:], T.RP[:], 128)
+        TO = ["TO"]
         act(TO + ["qn"], ["AJ0", "AC"], T.AJ[:, 0:256], T.TO[:], AF.Sign, PF["qn"], -1.0, T.SC[:, 0:1], n=256)
         ts(["C64", "AC"], ["FB"], T.FB[:, 0:32], T.C64[:, 0:32], T.SC[:, 0:1], OP.is_lt)
         turn(["FB"], ["FX"], T.FB[:, 32:64], T.FB[:, 0:32])

@@ -1,3 +1,5 @@
+import math
+
 from concourse.mybir import dt, AluOpType, AxisListType, ActivationFunctionType
 
 OP = AluOpType
@@ -19,19 +21,19 @@ def _q(**widths):
         SCRATCH["s" + name] = ("sbuf", [128, widths[name]], U8)
 
 
-TILE_N = (256, 192, 128, 128)
-TILE_O = [sum(TILE_N[:a]) for a in range(5)]
+STRIP = 544
+ROOM = STRIP + 128
 _sb(B, XT=1024, UT=512, VTL=512)
 _sb(I, OL=16, PC=1, PI=12, OI=48, CI=24, LI=144, I0=112, I1=120)
 _q(W=512, U=128, UP=384, V=128, X=1024, L=320, P=384, E=384)
-_q(K=768)
-_q(C=256 + 2 * TILE_O[4])
-_sb(B, TK=1552, IR=256, I4=96, TI=128, BK=128, NB=256, RS=512, RC=256, EX=256, E4=96, ET0=512, TR=128)
+_q(K=896)
+_q(C=256 + 2 * ROOM)
+_sb(B, TK=2064, IR=256, I4=96, TI=128, BK=128, NB=256, RS=512, RC=256, EX=256, E4=96, ET0=512, TR=128, RM=480)
 _sb(B, C64=64, ZR=528, PD2=96, CB=448, SN=1024)
-_sb(F, ID=256, PF=32, CW=48, NN=8, CP=16, TMP=8)
-_sb(U, OU=80, SL=24)
-_sb(F, SR=512, SG=512, SW=512, SB2=4, DL=2, TH0=128, TH1=128, AR=32, RW=32, EC=512, EP=16)
-_sb(B, BT=1024, CT=8 * TILE_O[4], AJ=1024, RD=512, RV=8192)
+_sb(F, ID=256, PF=40, CW=48, NN=8, CP=16, TMP=8)
+_sb(U, OU=88, SL=24)
+_sb(F, SR=512, SG=512, SW=512, SB2=4, DL=2, TH0=128, TH1=128, RW=32, EC=128, EP=16, RV=960)
+_sb(B, BT=1024, CT=8 * STRIP, AJ=1024, RD=512)
 _sb(F, LF=256, VH=1536, VT=1888, D7=112, CM=112, HR=224, D8=128, G8=384, HL=128)
 _sb(B, FT=1024, FU=1024, Z=1024, ET=512, RT=512)
 _sb(F, EF=256, ES=96, PK=96)
@@ -43,22 +45,43 @@ for _k in ("PA", "PB", "PC_", "Q0", "Q1", "Q2"):
 SCRATCH["PD"] = ("psum", [128, 1024], F)
 BANK = {"PA": ("PA", 0), "PB": ("PB", 0), "PC_": ("PC_", 0), "Q0": ("Q0", 0), "Q1": ("Q1", 0), "Q2": ("Q2", 0),
         "PD0": ("PD", 0), "PD1": ("PD", 512)}
-PLACE = {"B": ("C", 0), "KS": ("K", 512), "KB": ("K", 640), "Pb": ("P", 256)}
+PLACE = {"B": ("C", 0), "KS": ("K", 512), "KB": ("K", 640), "KI": ("K", 768), "Pb": ("P", 256),
+         "C0": ("C", 256), "C1": ("C", 256 + ROOM)}
 for _i in range(4):
     PLACE["X%d" % _i] = ("X", 256 * _i)
     PLACE["KR%d" % _i] = ("K", 128 * _i)
-    PLACE["C0%d" % _i] = ("C", 256 + TILE_O[_i])
-    PLACE["C1%d" % _i] = ("C", 256 + TILE_O[4] + TILE_O[_i])
     PLACE["E%d" % _i] = ("E", 128 * _i)
+PARTS = []
+for _i in range(8):
+    PARTS.append((7 - _i, 64 + 60 * _i, (16 - _i, 16), (0, 7 - _i)))
+    PARTS.append((15 - _i, 92 + 60 * _i, (16, 16), (7 - _i, 15 - _i)))
+SIGNED = (8, 10)
+CUTS = ((0, 136, 272, 408, 544), (0, 136, 272, 408, 544))
+FRAMES = (8, 7, 6, 5, 4, 0, 3, 1, 2)
+TWINS, F_BANKS, ROWS = ("PD1", "Q1"), ("Q0", "Q2", "Q0", "Q0"), ("Q2", "Q2")
+COUNT_V, RP_SPLIT, OWN, F_CUT = 0, True, 1, (4, 4)
+TWICE, STEP = (), (0, 1, 1, 2, 2, 2)
+_sb(B, L2=512)
+_sb(I, LH=152)
+_sb(B, FQ=800, FP=1888)
+_sb(F, TMP=24)
+PAIRS = (0, 1)
+LOW = (True, True)
+_sb(F, LW=32, TH=256)
+_sb(B, D0=256, C64=128, CK=512)
+_sb(U, M16=16)
+for _k, _gone in (("NN", True), ("LT", True), ("SR", all(TWINS)), ("TH1", True), ("TH0", True), ("L2", not TWICE), ("M16", not TWICE),
+                  ("CK", not COUNT_V)):
+    if _gone:
+        SCRATCH.pop(_k)
 CYCLE, WAKE, FLIGHT, JUMP, STREW, SEND, FIRST = 0.00085, 0.26, 1.2, 1.5, 3.5, 0.3, 1.0
 PE_CYCLE = 0.0007
-TRIES, SHAKE, SPARE = 4000, 1.5, 0.3
-BY_SCAN = (13, 13)
-EARLY, SPREAD, BIRTH_S = False, True, 1
+FIRST_TRIES, SHAKE, SPARE = 200, 1.5, 0.3
+TRIES, PACE, NEAR, REACH, HEAT, SEEK, SORT, AIM = 500000, 1.15, 0.15, 20, 0.02, 6, 50, 0.7
+BIRTH_S = 2
 SLOW, SHARE = 1.4, 0.75
-BY_SIGN = ((12, 11, 10, 9, 8), (12, 11, 10, 9, 8))
 
-SEMAPHORES = ["sV", "sA", "sP", "sG", "dX", "dU", "dO", "dW", "dVV", "dPad", "dF", "dY", "dLk", "dOc", "ls",
+SEMAPHORES = ["sV", "sA", "sP", "sG", "dX", "dU", "dO", "dW", "dVV", "dPad", "dF0", "dF1", "dF2", "dF3", "dY", "dLk", "dOc", "ls",
               "aC0", "aC1", "aC2", "aL0", "aL1", "aL2"]
 
 
@@ -165,7 +188,7 @@ def plan(nodes):
     def chance():
         seed[0] = (seed[0] * 1103515245 + 12345) % 2147483648
         return seed[0] / 2147483648.0
-    for _ in range(TRIES):
+    for _ in range(FIRST_TRIES):
         urgency, spare = list(best[2]), list(best[3])
         mid, wide = chance() * best[0], 1.0 + 5.0 * chance()
         for i in range(n):
@@ -174,10 +197,167 @@ def plan(nodes):
                 if len(nodes[i][0]) > 1 and chance() < 0.3:
                     spare[i] = (-0.3, 0.0, 0.3, 1.0, 3.0)[int(5 * chance())]
         other = passes(urgency, spare, 2, best[0] + 1.0)
-        if other[0] <= best[0] + 0.02:
+        if other[0] <= best[0]:
             best = other
-    SPAN.append(best[0])
-    return [x[2:] for x in sorted(best[1])]
+    ways = [[(q, c * PACE if q in "VA" else c) for q, c in x[0]] for x in nodes]
+    order = [x[2] for x in sorted(best[1])]
+    took = [0] * n
+    for x in best[1]:
+        took[x[2]] = x[3]
+    end, rest, at, before, after = [0.0] * n, [0.0] * n, [0] * n, [-1] * n, [-1] * n
+
+    def times(lo, hi):
+        last = dict(head)
+        for p in range(lo, hi + 1):
+            i = order[p]
+            at[i] = p
+            q, cost[i] = ways[i][took[i]]
+            j = before[i] = last[q]
+            if j >= 0:
+                after[j] = i
+            last[q] = i
+        p, reach, stale = lo, hi, set()
+        for q in last:
+            i, j = last[q], tail[q]
+            if i >= 0:
+                after[i] = j
+            if j >= 0:
+                before[j] = i
+                stale.add(j)
+                reach = max(reach, at[j])
+        while p <= reach:
+            i = order[p]
+            if p <= hi or i in stale:
+                j = before[i]
+                t = end[j] if j >= 0 else 0.0
+                for j, lag in pred[i]:
+                    if end[j] + lag > t:
+                        t = end[j] + lag
+                t += cost[i]
+                if t != end[i]:
+                    end[i] = t
+                    for j, lag in succ[i]:
+                        stale.add(j)
+                        if at[j] > reach:
+                            reach = at[j]
+                    j = after[i]
+                    if j >= 0:
+                        stale.add(j)
+                        if at[j] > reach:
+                            reach = at[j]
+            p += 1
+        p, reach, stale = hi, lo, set()
+        for q in head:
+            if head[q] >= 0:
+                stale.add(head[q])
+                reach = min(reach, at[head[q]])
+        while p >= reach:
+            i = order[p]
+            if p >= lo or i in stale:
+                j = after[i]
+                t = late[i]
+                if j >= 0 and rest[j] > t:
+                    t = rest[j]
+                for j, lag in succ[i]:
+                    if rest[j] + lag > t:
+                        t = rest[j] + lag
+                t += cost[i]
+                if t != rest[i]:
+                    rest[i] = t
+                    for j, lag in pred[i]:
+                        stale.add(j)
+                        if at[j] < reach:
+                            reach = at[j]
+                    j = before[i]
+                    if j >= 0:
+                        stale.add(j)
+                        if at[j] < reach:
+                            reach = at[j]
+            p -= 1
+        return max([rest[i] for i in roots])
+
+    def through(lo, hi, part):
+        new, free = {}, {}
+        head.clear()
+        tail.clear()
+        for p in range(lo, hi + 1):
+            i = order[p]
+            q = ways[i][was[1] if i == was[0] else took[i]][0]
+            if q not in head:
+                head[q] = before[i]
+            tail[q] = after[i]
+        most = 0.0
+        for i in part:
+            q, c = ways[i][took[i]]
+            if q not in head:
+                p = lo - 1
+                while p >= 0 and ways[order[p]][took[order[p]]][0] != q:
+                    p -= 1
+                head[q] = order[p] if p >= 0 else -1
+                p = hi + 1
+                while p < n and ways[order[p]][took[order[p]]][0] != q:
+                    p += 1
+                tail[q] = order[p] if p < n else -1
+            t = free[q] if q in free else (end[head[q]] if head[q] >= 0 else 0.0)
+            for j, lag in pred[i]:
+                e = new[j] if j in new else end[j]
+                if e + lag > t:
+                    t = e + lag
+            t += c
+            new[i] = free[q] = t
+            e = late[i]
+            for j, lag in succ[i]:
+                if at[j] > hi and rest[j] + lag > e:
+                    e = rest[j] + lag
+            if t + e > most:
+                most = t + e
+        for q in free:
+            if tail[q] >= 0 and free[q] + rest[tail[q]] > most:
+                most = free[q] + rest[tail[q]]
+        return most
+    cost, roots = [0.0] * n, [i for i in range(n) if not pred[i]]
+    head, tail = {q: -1 for q in "VAPGSR"}, {q: -1 for q in "VAPGSR"}
+    span = times(0, n - 1)
+    kept, was = (span, list(order), list(took)), [-1, 0]
+    for step in range(TRIES):
+        for _ in range(SEEK):
+            i = int(chance() * n)
+            if end[i] - cost[i] + rest[i] > span - NEAR:
+                break
+        if chance() < 0.3 and before[i] >= 0:
+            i = before[i]
+        was[0], was[1] = i, took[i]
+        p, far_, back = at[i], 1 + int(REACH * chance() ** 2), chance() < 0.5
+        if len(ways[i]) > 1 and chance() < 0.3:
+            took[i] = (took[i] + 1 + int(chance() * (len(ways[i]) - 1))) % len(ways[i])
+        elif chance() < AIM:
+            j = i
+            for _ in range(1 + int(3 * chance() ** 2)):
+                k = before[j] if back else after[j]
+                j = k if k >= 0 else j
+            far_ = abs(at[j] - p)
+        if back:
+            to = max([p - far_, 0] + [at[j] + 1 for j, lag in pred[i]])
+            lo, hi, part = to, p, [i] + order[to:p]
+        else:
+            to = min([p + far_, n - 1] + [at[j] - 1 for j, lag in succ[i]])
+            lo, hi, part = p, to, order[p + 1:to + 1] + [i]
+        if (lo < hi or took[i] != was[1]) and through(lo, hi, part) <= span - HEAT * (1.0 - step / TRIES) * math.log(chance() + 1e-9):
+            order[lo:hi + 1] = part
+            span = times(lo, hi)
+            if span < kept[0] - 1e-9:
+                kept = (span, list(order), list(took))
+        else:
+            took[i] = was[1]
+        if step % SORT == 0:
+            if step % (2 * SORT):
+                order.sort(key=lambda j: end[j] - cost[j])
+            else:
+                order.sort(key=lambda j: -rest[j])
+            for p in range(n):
+                at[order[p]] = p
+    SPAN.append(kept[0])
+    return [(i, kept[2][i]) for i in kept[1]]
 
 
 def rank_program(g, core, T, topo):
@@ -282,9 +462,10 @@ def rank_program(g, core, T, topo):
     def fill(w, ap, x, n=64):
         emit("V", [], w, lambda e: e.memset(ap, x), cyc(n))
 
-    def quant(r, name, n, tile):
+    def quant(r, name, n, tile, first=0):
         k, o = PLACE.get(name, (name, 0))
-        emit("V", r, [name], lambda e: e.quantize_mx(T["c" + k][:, o:o + n], T["s" + k][:, o:o + n], tile), CYCLE * (16 + 1.06 * n))
+        o += first
+        emit("V", r, [name + (".%d" % first if name in ("C0", "C1") else "")], lambda e: e.quantize_mx(T["c" + k][:, o:o + n], T["s" + k][:, o:o + n], tile), CYCLE * (16 + 1.06 * n))
 
     def act(r, w, out, a, fn=AF.Copy, bias=0.0, scale=1.0, acc=None, n=64):
         if acc is None:
@@ -352,7 +533,6 @@ def rank_program(g, core, T, topo):
     iota(["ID"], T.ID[:], [[1, 256]], 0, 0, 256)
     iota(["BK"], T.BK[:], [[1, 8], [0, 16]], 0, 0, 128)
     iota(["C16"], T.CW[:, 16:32], [[16, 16]], 0, 0, 16)
-    iota(["NN"], T.NN[:], [[1, 8]], 0, 0, 8)
     iota(["I4"], T.I4[:], [[0, 24], [1, 4]], 0, 0, 96)
     cp(["OI", "OIb"], ["OU"], T.OU[:, 0:24], T.OI[:, 0:24])
     PF = {}
@@ -371,40 +551,55 @@ def rank_program(g, core, T, topo):
         PF[name] = T.PF[:, len(PF):len(PF) + 1]
         lin([src], [name], PF[name], PF[src], scale, bias)
     affine("q1", "q", 1.0, 1.0)
-    affine("qn", "q", -1.0, 255.5)
-    affine("q255", "q", -1.0, 255.0)
-    affine("q254", "q", -1.0, 254.5)
+    affine("qn", "q", -1.0, 15.5)
+    affine("q255", "q", 1.0, -14.5)
+    affine("q254", "q", -2.0, 29.0)
     number("xq", "q", 15.0, OP.is_lt, -256.0, OP.mult)
     number("t2", "r2", PF["m1"], OP.not_equal, 272.0, OP.mult, ["m1"])
     number("t1", "q", PF["m1"], OP.subtract, 16.0, OP.mult, ["m1"])
     number("tb", "t1", PF["t2"], OP.add, -1.0, OP.add, ["t2"])
-    affine("xq1", "xq", 1.0, 1.0)
-    affine("q7", "q", 7.0, 1.0)
+    number("lv", "q4", 3.0, OP.is_lt, 512.0, OP.mult)
+    affine("lv1", "lv", 1.0, 1.0)
+    number("dl", "lv", PF["xq"], OP.subtract, 1.0, OP.mult, ["xq"])
+    affine("dm", "dl", -256.0, 0.0)
     affine("q3", "q", 1.0, -3.0)
-    affine("q16", "q", 1.0, -16.0)
+    affine("q16", "q", 1.0, -128.0)
     affine("q41", "q4", 1.0, 1.0)
+    affine("e8", "q8", 32.0, 447.0)
     number("eo", "q4", 3.0, OP.is_lt, -2048.0, OP.mult)
     tt(["eo", "r4"], ["eo"], PF["eo"], PF["eo"], PF["r4"], OP.add)
-    affine("t8", "q8", 16.0, 15.0)
-    number("r7", "r8", 7.0, OP.is_lt, PF["r8"], OP.mult)
-    number("g8", "r7", 256.0, OP.mult, PF["t8"], OP.add, ["t8"])
-    affine("t7", "q8", 7.0, 0.0)
     cp(["OI2"], ["BC32"], T.OU[:, 24:40], T.OI[:, 24:40])
-    ts(["C16", "q3"], ["r7a"], T.TMP[:], T.CW[:, 16:24], PF["q3"], OP.add, 1.0 / 7, OP.mult)
-    cp(["r7a"], ["r7b"], T.OI[:, 40:48], T.TMP[:])
+    ts(["C16", "q3"], ["r7a"], T.TMP[:, 0:8], T.CW[:, 16:24], PF["q3"], OP.add, 1.0 / 7, OP.mult)
+    cp(["r7a"], ["r7b"], T.OI[:, 40:48], T.TMP[:, 0:8])
     cp(["r7b"], ["REP7"], T.OU[:, 40:48], T.OI[:, 40:48])
-    ts(["r7b"], ["REPE"], T.OU[:, 72:80], T.OI[:, 40:48], 16.0, OP.mult, 15.0, OP.add)
-    ts(["NN", "q7"], ["HOPS"], T.OU[:, 48:54], T.NN[:, 0:6], PF["q7"], OP.add)
-    ts(["NN", "g8"], ["G8L"], T.OU[:, 56:64], T.NN[:], 32.0, OP.mult, PF["g8"], OP.add)
-    ts(["r8", "t7"], ["d8"], T.SC[:, 7:8], PF["r8"], 6.0, OP.min, PF["t7"], OP.add)
-    ts(["NN", "d8"], ["D8L"], T.OU[:, 64:72], T.NN[:], 14.0, OP.mult, T.SC[:, 7:8], OP.add)
-    BC32, REP7, HOPS, G8L, D8L = T.OU[:, 24:40], T.OU[:, 40:47], T.OU[:, 48:54], T.OU[:, 56:64], T.OU[:, 64:72]
+    CW = T.CW[:, 0:16]
+    ts(["C16", "q"], ["CW"], CW, T.CW[:, 16:32], PF["q"], OP.add)
+    if PAIRS:
+        tt(["CW", "r7b"], ["r7a"], T.TMP[:, 0:8], T.CW[:, 0:8], T.OI[:, 40:48], OP.subtract)
+        ts(["r7b"], ["r7c"], T.TMP[:, 8:16], T.OI[:, 40:48], 6.0, OP.mult)
+        tt(["r7a", "r7c"], ["r7d"], T.TMP[:, 16:24], T.TMP[:, 0:8], T.TMP[:, 8:16], OP.is_gt)
+        tt(["r7a", "r7d"], ["r7c"], T.TMP[:, 8:16], T.TMP[:, 0:8], T.TMP[:, 16:24], OP.mult)
+        cp(["r7c"], ["SIX"], T.OU[:, 48:56], T.TMP[:, 8:16])
+        iota(["LHz"], T.LH[:, 0:1], [[0, 1]], -1024, 0, 1, True)
+    if len(PAIRS) < ROUNDS:
+        affine("q7", "q", 7.0, 1.0)
+        affine("xn", "xq", -1.0, 0.0)
+        ts(["ID", "q7"], ["HOPS"], T.OU[:, 56:62], T.ID[:, 0:6], PF["q7"], OP.add)
+        zero(["FPz"], T.FP[:, 105:1888:112], 16, -1024)
+    ts(["r8", "e8"], ["ENDS"], T.OU[:, 80:81], PF["r8"], -60.0, OP.mult, PF["e8"], OP.add)
+    BC32, REP7, SIX = T.OU[:, 24:40], T.OU[:, 40:47], T.OU[:, 48:55]
     ts(["IR", "q"], ["NB"], T.NB[:], T.IR[:], PF["q"], OP.not_equal, 2.0 ** 90, OP.mult, 128)
     zero(["RS"], T.RS[:], 512)
     fill(["RS"], T.RS[:, 0:256:16], 2.0 ** 95)
     fill(["RS"], T.RS[:, 256:512:16], -2.0 ** 95)
     zero(["RC"], T.RC[:], 256, 512)
-    ts(["C16", "q16"], ["RC"], T.RC[:, 0:256:16], T.CW[:, 16:32], -1.0, OP.mult, PF["q16"], OP.add)
+    for h in range(2):
+        ts(["ZR", "q16"], ["RC"], T.RC[:, 128 * h:128 * h + 128:16], T.ZR[:, 0:8], PF["q16"], OP.add, -16.0 * h, OP.add)
+    zero(["RM"], T.RM[:], 480, 1)
+    fill(["RM"], T.RM[:, 0:480:60], 0.0)
+    fill(["RM"], T.RM[:, 28:480:60], 0.0)
+    for s in range(2):
+        iota(["RVz%d" % s], T.RV[:, 480 * s:480 * s + 30 * SIGNED[s]], [[0, 30 * SIGNED[s]]], 0, 0, 30 * SIGNED[s])
     ts(["IR", "q"], ["e0"], T.ET0[:, 0:256], T.IR[:], PF["q"], OP.is_equal, 2.0 ** 19, OP.mult, 128)
     ts(["IR", "q1"], ["e1"], T.ET0[:, 256:512], T.IR[:], PF["q1"], OP.is_equal, -2.0 ** -11, OP.mult, 128)
     scan(["e0", "e1"], ["EX"], T.EX[:], T.ET0[:, 256:512], T.ET0[:, 0:256], 0.0, OP.mult, OP.add, 128)
@@ -413,8 +608,12 @@ def rank_program(g, core, T, topo):
     scan(["e0", "e1"], ["E4"], T.E4[:], T.ET0[:, 256:352], T.ET0[:, 0:96], 0.0, OP.mult, OP.add)
     ts(["TI"], ["TR"], T.TR[:], T.TI[:], 0.0, OP.is_le)
     zero(["TKB"], T.TK[:, 0:512], 512, 1)
+    zero(["TKS"], T.TK[:, 512:1024], 512)
     for i in range(4):
-        ts(["BK", "g"], ["TKS%d" % i], T.TK[:, 512 + i:1024:4], T.BK[:], PF["g"], OP.is_equal)
+        ts(["BK", "g", "TKS"], ["TKS%d" % i], T.TK[:, 512 + 5 * i:1024:16], T.BK[:, 0:128:4], PF["g"], OP.is_equal)
+    emit("G", ["TKB"], ["TKI"], lambda e: e.affine_select(T.TK[:, 1552:2064], T.TK[:, 0:512], [[1, 128], [0, 4]], OP.is_equal, 0.0, 0, -1),
+         0.17 + 1024 * CYCLE)
+    quant(["TKI"], "KI", 128, T.TK[:, 1552:2064])
     zero(["TKR"], T.TK[:, 1024:1552], 528)
     ts(["TI"], ["TKR"], T.TK[:, 1027:1539:4], T.TI[:], 0.0, OP.is_equal, 128.0, OP.mult)
     quant(["TKB"], "KB", 128, T.TK[:, 0:512])
@@ -430,38 +629,35 @@ def rank_program(g, core, T, topo):
             T.sUP[:, c], T.sU[:, 0:128].indirect(T.OU[:, 8 * i:8 * i + 8]), AF.Copy), cyc(far(128)))
     quant(["XT"], "X0", 256, T.XT[:])
     for s in range(2):
-        for a in range(4):
-            o = 4 * (TILE_O[4] * s + TILE_O[a])
-            lo = 64 * (13 - 4 * a)
-            zero(["z%d%d" % (s, a)], T.CT[:, o + lo:o + 4 * TILE_N[a]], 4 * TILE_N[a] - lo)
+        quant(["ZR"], "C%d" % s, 128, T.ZR[:, 0:512], STRIP)
     for i in (2, 3):
         zero(["zB%d" % i], T.BT[:, i:1024:4], 256)
-    zero(["AR"], T.AR[:], 32)
     dma("S", "dPad", ["X0"], ["pad"], [(T.cL[:, 288:320].bitcast(dt.uint8), T.cX[:, 0:32].bitcast(dt.uint8)),
                                        (T.sL[:, 288:320], T.sX[:, 0:32])])
     zero(["CB"], T.CB[:], 448)
     ts(["ID", "r32"], ["CB"], T.CB[:, 192:224], T.ID[:, 0:32], PF["r32"], OP.is_equal)
     ts(["ID", "r32"], ["CB"], T.CB[:, 224:256], T.ID[:, 0:32], PF["r32"], OP.is_equal, 2048.0, OP.mult)
     zero(["C64"], T.C64[:, 0:32], 32, 64)
-    lin(["C64"], ["C64"], T.C64[:, 32:64], T.C64[:, 0:32], -2.0 ** -15)
+    if RP_SPLIT:
+        iota(["C15"], T.C64[:, 64:128], [[16, 2], [0, 32]], -1, 0, 64)
+    lin(["C64"], ["C64"], T.C64[:, 32:64], T.C64[:, 0:32], -2.0 ** -14)
     iota(["PD2"], T.PD2[:], [[0, 48], [256, 2]], 0, 0, 96)
     zero(["ETz"], T.ET[:, 384:512], 128)
     zero(["RTz"], T.RT[:, 384:512], 128)
-    zero(["GS0"], T.GS[:, 0:304], 304, 64)
+    zero(["GS0"], T.GS[:, 0:304], 304, 160)
     zero(["GD"], T.GS[:, 304:608], 304)
     iota(["I1z"], T.I1[:, 112:120], [[0, 8]], 0, 0, 8, True)
     iota(["YXz"], T.YX[:, 0:256], [[1, 256]], 0, 0, 256)
     zero(["HD"], T.HD[:], 64)
     quant(["VTL"], "V", 128, T.VTL[:])
-    CW = T.CW[:, 0:16]
-    ts(["C16", "q"], ["CW"], CW, T.CW[:, 16:32], PF["q"], OP.add)
-    lin(["CW"], ["CP"], T.CP[:], CW, 2.0, -446.0)
+    lin(["CW"], ["CP"], T.CP[:], CW, 1.0, -351.0)
+    zero(["D0"], T.D0[:], 256)
+    zero(["D0"], T.D0[:, 0:1], 1, 96)
     lin(["CW"], ["HD"], T.HD[:, 33:64:2], CW)
-    zero(["FP0"], T.FP[:, 0:256], 256, -2048)
     VV, VT0, VT6 = T.VT[:, 105:1888:16], T.VT[:, 105:1888:112], T.VT[:, 201:1888:112]
-    lin(["ZR", "xq"], ["VT0"], VT0, T.ZR[:, 0:16], 1.0, PF["xq"])
+    lin(["ZR", "lv"], ["VT0"], VT0, T.ZR[:, 0:16], 1.0, PF["lv"])
     cp(["OL"], ["L16"], T.L16[:], T.OL[:])
-    ts(["OL", "xq"], ["VT6"], VT6, T.OL[:], 2.0 ** -8, OP.mult, PF["xq"], OP.add)
+    ts(["OL", "lv"], ["VT6"], VT6, T.OL[:], 2.0 ** -8, OP.mult, PF["lv"], OP.add)
 
     E15 = slice(15, 256, 16)
     rid, pid = topo.addr(nxt)[0], topo.addr(nxt)[1]
@@ -490,105 +686,135 @@ def rank_program(g, core, T, topo):
         act(["PD0", "PD1"], ["SB"], T.SB2[:, 0:2], T.PD[:, 8:1024:512])
         act(["PD0", "PD1"], ["DL"], T.DL[:], T.PD[:, 8:1024:512], AF.Abs, 2.0 ** -124, 1.25 * 2.0 ** -24)
         for h in range(2):
-            lin(["TR", "DL", "SB"], ["TH%d" % h], T["TH%d" % h][:], T.TR[:], T.DL[:, h:h + 1], T.SB2[:, h:h + 1], 128)
+            lin(["TR", "DL", "SB"], ["TH%d" % h], T.TH[:, 128 * h:128 * h + 128], T.TR[:], T.DL[:, h:h + 1], T.SB2[:, h:h + 1], 128)
         if BIRTH_S > 1:
             act(["SB", "DL"], ["SBm"], T.SB2[:, 2:3], T.DL[:, 0:1], AF.Identity, T.SB2[:, 0:1], -1.0)
-            act(["PC_", "SBm"], ["SN0"], T.SN[:, 0:128], ps("PC_", 128, 256), AF.Sign, T.SB2[:, 2:3], -1.0, n=128)
-            act(["SN0"], ["BTa"], T.BT[:, 512:1024:4], T.SN[:, 0:128], AF.Relu, 0.0, -1.0, n=128)
+            act(["PC_", "SBm"], ["AJ3"], T.AJ[:, 768:896], ps("PC_", 128, 256), AF.Sign, T.SB2[:, 2:3], -1.0, n=128)
+            act(["AJ3"], ["BTa"], T.BT[:, 512:1024:4], T.AJ[:, 768:896], AF.Relu, 0.0, -1.0, n=128)
         else:
             ts(["PC_", "SB"], ["BTa"], T.BT[:, 512:1024:4], ps("PC_", 128, 256), T.SB2[:, 0:1], OP.is_ge, n=128)
         if BIRTH_S:
-            act(["PC_", "SB"], ["SN1"], T.SN[:, 256:384], ps("PC_", 0, 128), AF.Sign, T.SB2[:, 1:2], -1.0, n=128)
-            act(["SN1"], ["BTb"], T.BT[:, 1:512:4], T.SN[:, 256:384], AF.Relu, 0.0, -1.0, n=128)
+            act(["PC_", "SB"], ["AJ2"], T.AJ[:, 512:640], ps("PC_", 0, 128), AF.Sign, T.SB2[:, 1:2], -1.0, n=128)
+            act(["AJ2"], ["BTb"], T.BT[:, 1:512:4], T.AJ[:, 512:640], AF.Relu, 0.0, -1.0, n=128)
         else:
             ts(["PC_", "SB"], ["BTb"], T.BT[:, 1:512:4], ps("PC_", 0, 128), T.SB2[:, 1:2], OP.is_gt, n=128)
-        tt(["PC_", "TH0"], ["BTc"], T.BT[:, 0:512:4], ps("PC_", 0, 128), T.TH0[:], OP.is_ge, 128)
-        tt(["PC_", "TH1"], ["BTd"], T.BT[:, 513:1024:4], ps("PC_", 128, 256), T.TH1[:], OP.is_ge, 128)
+        tt(["PC_", "TH0"], ["BTc"], T.BT[:, 0:512:4], ps("PC_", 0, 128), T.TH[:, 0:128], OP.is_ge, 128)
+        tt(["PC_", "TH1"], ["BTd"], T.BT[:, 513:1024:4], ps("PC_", 128, 256), T.TH[:, 128:256], OP.is_ge, 128)
         quant(["BTa", "BTb", "BTc", "BTd", "zB2", "zB3"], "B", 256, T.BT[:])
         mm(["B", "KB"], "PC_", 256, "KB", 0, "B", 0)
 
         def places(s):
             bank, sums = (("PA", "PD0"), ("PB", "PD1"))[s]
             c = slice(256 * s, 256 * s + 256)
-            o = 4 * TILE_O[4] * s
-            if BY_SIGN[s]:
-                n = 16 * max(BY_SIGN[s])
-                act([bank], ["SR%d" % s], T.SR[:, 256 * s:256 * s + n], ps(bank, 0, n), n=n)
+            o, k = 4 * STRIP * s, "C%d" % s
+            TWIN = TWINS[s]
+            if TWIN:
+                twin = TWIN
+                mm(XK + ["UPc%d" % s, "UPs%d" % s], twin, 256, "UP", 128 * s, X, 0)
+            else:
+                twin = "SR%d" % s
+                act([bank], [twin], T.SR[:, c], ps(bank, 0, 256), n=256)
             tt([bank, "NB"], ["SG%d" % s], T.SG[:, c], ps(bank, 0, 256), T.NB[:], (OP.add, OP.subtract)[s], 256)
             scan(["RS", "SG%d" % s], ["SW%d" % s], T.SW[:, c], T.RS[:, c], T.SG[:, c], 0.0, OP.add, (OP.min, OP.max)[s], 256)
-            run = T.CT[:, o:o + 1024:4]
-            tt([bank, "SW%d" % s, "z%d0" % s], ["ct%d.16" % s], run, ps(bank, 0, 256), T.SW[:, c], (OP.is_ge, OP.is_le)[s], 256)
-            scan(["RC", "ct%d.16" % s], ["RD%d" % s], T.RD[:, c], T.RC[:], run, 0.0, OP.min, OP.add, 128)
-            for a in range(4):
-                ms = [m for m in range(16 - 4 * a, 12 - 4 * a, -1)]
-                for j, m in enumerate(ms):
-                    if m < 16:
-                        v = T.CT[:, o + 4 * TILE_O[a] + j:o + 4 * TILE_O[a] + 64 * m:4]
-                        if m in BY_SIGN[s]:
-                            k = 256 * (m % 4)
-                            act(["SR%d" % s, "SW%d" % s], ["SN%d" % (m % 4)], T.SN[:, k:k + 16 * m], T.SR[:, 256 * s:256 * s + 16 * m],
-                                AF.Sign, T.SW[:, 256 * s + 16 * m + 15:256 * s + 16 * m + 16], -1.0, n=16 * m)
-                            act(["SN%d" % (m % 4), "AR", "z%d%d" % (s, a)], ["AR%d.%d" % (s, m), "ct%d.%d" % (s, m)], v, T.SN[:, k:k + 16 * m],
-                                AF.Relu, 0.0, (-1.0, 1.0)[s], T.AR[:, 16 * s + m:16 * s + m + 1], n=16 * m)
-                            continue
-                        ts([bank, "SW%d" % s, "z%d%d" % (s, a)], ["ct%d.%d" % (s, m)], v, ps(bank, 0, 16 * m),
-                           T.SW[:, 256 * s + 16 * m + 15:256 * s + 16 * m + 16], (OP.is_gt, OP.is_lt)[s], n=16 * m)
-                        if m >= BY_SCAN[s]:
-                            e = 4096 * s + 256 * m + 256
-                            scan(["ct%d.%d" % (s, m), "ZR"], ["AR%d.%d" % (s, m)], T.RV[:, e - 16 * m:e], T.ZR[:, 0:16 * m], v,
-                                 0.0, OP.add, OP.add, 8 * m)
-                            continue
-                        act(["ct%d.%d" % (s, m), "AR"], ["AR%d.%d" % (s, m), "AJ%d" % j], T.AJ[:, 256 * j:256 * j + 16 * m], v,
-                            AF.Copy, 0.0, 1.0, T.AR[:, 16 * s + m:16 * s + m + 1], n=16 * m)
-                k = "C%d%d" % (s, a)
-                quant(["ct%d.%d" % (s, m) for m in ms], k, TILE_N[a], T.CT[:, o + 4 * TILE_O[a]:o + 4 * TILE_O[a + 1]])
-                mm([k, "KS"], sums, TILE_N[a], "KS", 0, k, 0, a == 0, a == 3)
-            m = BY_SCAN[s]
-            tt(["RD%d" % s, "AR"] + ["AR%d.%d" % (s, i) for i in range(1, m)], ["RW%d" % s], T.RW[:, 16 * s:16 * s + m],
-               T.RD[:, 256 * s + 15:256 * s + 16 * m:16], T.AR[:, 16 * s:16 * s + m], OP.add)
-            if m < 16:
-                tt(["RD%d" % s] + ["AR%d.%d" % (s, i) for i in range(m, 16)], ["RV%d" % s], T.RW[:, 16 * s + m:16 * s + 16],
-                   T.RD[:, 256 * s + 16 * m + 15:256 * s + 256:16], T.RV[:, 4096 * s + 256 * m + 255:4096 * s + 4096:256], OP.add)
-            pick([sums], ["EC%d" % s], T.EC[:, c], ps(sums, 0, 256))
+            run = T.CT[:, o:o + 256]
+            tt([bank, "SW%d" % s], ["ct%d.0" % s], run, ps(bank, 0, 256), T.SW[:, c], (OP.is_ge, OP.is_le)[s], 256)
+            scan(["RC", "ct%d.0" % s], ["RD%d" % s], T.RD[:, c], T.RC[:], run, 0.0, OP.min, OP.add, 128)
+            if LOW[s]:
+                low = T.SW[:, 256 * s + 15:256 * s + 128:16]
+                act(["SW%d" % s], ["LD%d" % s], T.LW[:, 16 * s:16 * s + 8], low, AF.Abs, 2.0 ** -124, 1.25 * 2.0 ** -24)
+                tt(["SW%d" % s, "LD%d" % s], ["LW%d" % s], T.LW[:, 16 * s + 8:16 * s + 16], low, T.LW[:, 16 * s:16 * s + 8], (OP.subtract, OP.add)[s])
+            made, ones = [(0, 64, "ct%d.0" % s)], []
+            for i, (m, w, (a0, a1), (b0, b1)) in enumerate(PARTS):
+                mine = T.SW[:, 256 * s + 16 * m + 15:256 * s + 16 * m + 16]
+                na, nb = 16 * (a1 - a0), 16 * (b1 - b0)
+                e = o + 4 * w
+                if i < SIGNED[s]:
+                    j, name = 128 * (i % 8), "SN%d" % (i % 8)
+                    if na and LOW[s]:
+                        act([twin, "LW%d" % s], [name + "a"], T.SN[:, j:j + na],
+                            ps(twin, 16 * a0, 16 * a1) if TWIN else T.SR[:, 256 * s + 16 * a0:256 * s + 16 * a1], AF.Sign,
+                            T.LW[:, 16 * s + 8 + m:16 * s + 9 + m], -1.0, n=na)
+                    elif na:
+                        ts([bank, "SW%d" % s], [name + "a"], T.SN[:, j:j + na], ps(bank, 16 * a0, 16 * a1), mine, (OP.is_ge, OP.is_le)[s],
+                           (-1.0, 1.0)[s], OP.mult, n=na)
+                    act([twin, "SW%d" % s], [name], T.SN[:, j + na:j + na + nb],
+                        ps(twin, 16 * b0, 16 * b1) if TWIN else T.SR[:, 256 * s + 16 * b0:256 * s + 16 * b1], AF.Sign, mine, -1.0, n=nb)
+                    end = 480 * s + w - 65 + (na + nb) // 4
+                    act([name, name + "a", "RVz%d" % s], ["AR%d.%d" % (s, m), "ct%d.%d" % (s, w)], T.CT[:, e:e + na + nb], T.SN[:, j:j + na + nb],
+                        AF.Relu, 0.0, (-1.0, 1.0)[s], T.RV[:, end:end + 1], n=na + nb)
+                    made.append((w, w + (na + nb) // 4, "ct%d.%d" % (s, w)))
+                    ones.append("AR%d.%d" % (s, m))
+                    continue
+                for c0, n, at, op in ((a0, na, 0, (OP.is_ge, OP.is_le)), (b0, nb, na, (OP.is_gt, OP.is_lt))):
+                    if n:
+                        name = "ct%d.%d" % (s, w + at // 4)
+                        ts([bank, "SW%d" % s], [name], T.CT[:, e + at:e + at + n], ps(bank, 16 * c0, 16 * c0 + n), mine, op[s], n=n)
+                        made.append((w + at // 4, w + (at + n) // 4, name))
+            cuts = list(zip(CUTS[s], CUTS[s][1:] + (ROOM,)))
+            for lo, hi in cuts[:-1]:
+                quant([x[2] for x in made if x[0] < hi and lo < x[1]], k, hi - lo, T.CT[:, o + 4 * lo:o + 4 * hi], lo)
+
+            def words(lo, hi):
+                return ["%s.%d" % (k, a) for a, b in cuts if a < hi and lo < b]
+            for f in FRAMES:
+                mm(words(64 * f, 64 * f + 128) + ["KS"], sums, 128, "KS", 0, k, 64 * f, f == FRAMES[0], f == FRAMES[-1])
+            w = PARTS[SIGNED[s]][1]
+            mm(words(w, STRIP) + ["KI"], ROWS[s], STRIP - w, "KI", 0, k, w)
+            scan([ROWS[s], "RM"], ["RV%d" % s], T.RV[:, 480 * s + w - 64:480 * s + 480], T.RM[:, w - 64:480], ps(ROWS[s], 0, STRIP - w),
+                 0.0, OP.mult, OP.add, STRIP - w)
+            tt(["RD%d" % s, "RV%d" % s, "ENDS"] + ones, ["RW%d" % s], T.RW[:, 16 * s:16 * s + 16],
+               T.RV[:, 480 * s:480 * s + 480].indirect(T.OU[:, 80:81]), T.RD[:, 256 * s + 15:256 * s + 256:16], OP.add, far(16))
+            scan([sums, "E4"], ["EC%d" % s], T.EC[:, 64 * s:64 * s + 64], T.E4[:, 0:64], ps(sums, 0, 64), 0.0, OP.add, OP.max)
+        def halves(bs):
+            for b in bs:
+                k = F_BANKS[b]
+                mm(XK + ["KR%d" % b], k, 256, "KR%d" % b, 0, X, 0)
+                lin([k], ["FT%d" % b], T.FT[:, 256 * b:256 * b + 256], ps(k, 0, 256), 2.0 ** -8, n=256)
+        halves(range(F_CUT[0]))
         places(0)
+        halves(range(F_CUT[0], F_CUT[1]))
         places(1)
-        tt(["EC1", "RW1", "RV1"], ["PL1"], T.EP[:], T.EC[:, 271:512:16], T.RW[:, 16:32], OP.subtract)
-        for b in range(4):
-            k = ("Q0", "Q1", "Q2", "Q0")[b]
-            mm(XK + ["KR%d" % b], k, 256, "KR%d" % b, 0, X, 0)
-            lin([k], ["FT%d" % b], T.FT[:, 256 * b:256 * b + 256], ps(k, 0, 256), 2.0 ** -8, n=256)
-        dma("S", "dF", ["FT0", "FT1", "FT2", "FT3"], ["FU"], [(T.FU[:], T.FT[:])], 2.75)
+        halves(range(F_CUT[1], 4))
+        tt(["EC1", "RW1"], ["PL1"], T.EP[:], T.EC[:, 67:128:4], T.RW[:, 16:32], OP.subtract)
+        for b in range(0, 4, OWN):
+            c = slice(256 * b, 256 * (b + OWN))
+            dma("S", "dF%d" % b, ["FT%d" % i for i in range(b, b + OWN)], ["FU%d" % i for i in range(b, b + OWN)],
+                [(T.FU[:, c], T.FT[:, c])], 1.75 + 0.25 * OWN)
         if t == 0:
-            lin(["ID", "L16"], ["LF"], T.LF[:], T.ID[:].indirect(T.L16[:]), 2.0 ** -8, n=far(256))
+            lin(["ID", "L16", "dl"], ["LF"], T.LF[:], T.ID[:].indirect(T.L16[:]), 2.0 ** -8, PF["dl"], n=far(256))
         tt(["PC_", "LF"], ["VH0"], T.VH[:, 0:256], ps("PC_", 0, 256), T.LF[:], OP.add, 256)
+        if t in TWICE:
+            lin(["LF", "L16", "dm"], ["L2"], T.L2[:, 0:256], T.LF[:].indirect(T.L16[:]), 256.0, PF["dm"], n=far(256))
+            pick2(["L2"], ["L2p"], T.L2[:, 256:512], T.L2[:, 0:256])
+            ts(["L2p", "xq"], ["M16"], T.M16[:], T.L2[:, 271:512:16], PF["xq"], OP.subtract)
         for i in range(1, 6):
-            lin(["VH%d" % (i - 1), "L16"], ["VH%d" % i], T.VH[:, 256 * i:256 * i + 256],
-                T.VH[:, 256 * i - 256:256 * i].indirect(T.L16[:]), n=far(256))
+            j, by = (i - 2, "M16") if i > 1 and t in TWICE and STEP[i] == 2 else (i - 1, "L16")
+            lin(["VH%d" % j, by], ["VH%d" % i], T.VH[:, 256 * i:256 * i + 256],
+                T.VH[:, 256 * j:256 * j + 256].indirect(T[by][:]), n=far(256))
             pick(["VH%d" % i], ["VT%d" % (6 - i)], T.VT[:, 96 - 16 * i:96 - 16 * i + 1786:7], T.VH[:, 256 * i:256 * i + 256])
         VK = ["VT%d" % k for k in range(7)]
-        ts(VK + ["xq"], ["I0"], T.I0[:], VV, PF["xq"], OP.subtract, 256.0, OP.mult, 112)
+        ts(VK + ["lv"], ["I0"], T.I0[:], VV, PF["lv"], OP.subtract, 256.0, OP.mult, 112)
         ts(["I0"], ["I1"], T.I1[:, 0:112], T.I0[:], 255, OP.bitwise_and, n=112)
         tt(["I1", "I1z"], ["D7"], T.D7[:], T.I1[:, 0:112], T.I1[:, 1:113], OP.subtract, 224)
-        if EARLY:
-            tt(VK + ["RW0", "RV0", "REP7"], ["VR"], T.VR[:], T.RW[:, 0:16].indirect(REP7), VV, OP.add, far(112))
-            tt(["EC0", "VR", "REPE"], ["CM"], T.CM[:], T.EC[:, 0:256].indirect(T.OU[:, 72:79]), T.VR[:], OP.is_le, far(112))
-        else:
-            tt(["EC0", "RW0", "RV0"], ["VR"], T.VR[:, 0:16], T.EC[:, 15:256:16], T.RW[:, 0:16], OP.subtract)
-            tt(VK + ["VR", "REP7"], ["CM"], T.CM[:], T.VR[:, 0:16].indirect(REP7), VV, OP.is_le, far(112))
+        tt(["EC0", "RW0"], ["VR"], T.VR[:, 0:16], T.EC[:, 3:64:4], T.RW[:, 0:16], OP.subtract)
+        tt(VK + ["VR", "REP7"], ["CM"], T.CM[:], T.VR[:, 0:16].indirect(REP7), VV, OP.is_le, far(112))
         for i in range(2):
             scan(["CM", "D7"], ["HR%d" % i], T.HR[:, 112 * i:112 * i + 111], T.CM[:, 0:111], T.D7[:, 1:112], 0.0, OP.mult, OP.add, 111)
         cp(["HR0"], ["R16"], T.R16[:], T.HR[:, 5:111:7])
         turn(["HR0", "HR1"], ["RQ"], T.QQ[:, 32:64], T.HR[:, 5:223:7])
         cp(["RQ"], ["R32"], T.R32[:], T.QQ[:, 32:64])
-        for z in range(4):
+        for z in range(4 - COUNT_V, 4):
+            cp(["CB", "R32"], ["CK"], T.CK[:], T.CB[:, 192 - 64 * z:448 - 64 * z].indirect(T.R32[:]), far(512))
+            emit("V", ["CK"], ["CA%d" % z], lambda e, z=z: e.tensor_reduce(T.CA[:, z:z + 1], T.CK[:], AxisListType.X, OP.add), cyc(512))
+        for z in range(4 - COUNT_V):
             act(["CB", "R32"], ["CJ%d" % (z % 2), "CA%d" % z], T.CJ[:, 512 * (z % 2):512 * (z % 2) + 512],
                 T.CB[:, 192 - 64 * z:448 - 64 * z].indirect(T.R32[:]), AF.Copy, 0.0, 1.0, T.CA[:, z:z + 1], n=far(512))
         for b in range(4):
-            tt(["FT%d" % b, "FU", "R16"], ["Z%d" % b], T.Z[:, b:1024:4], T.FT[:, 256 * b:256 * b + 256].indirect(T.R16[:]),
+            tt(["FT%d" % b, "FU%d" % b, "R16"], ["Z%d" % b], T.Z[:, b:1024:4], T.FT[:, 256 * b:256 * b + 256].indirect(T.R16[:]),
                T.FU[:, 256 * b:256 * b + 256], OP.add, far(256))
         ZK = ["Z0", "Z1", "Z2", "Z3"]
         quant(ZK, "P", 256, T.Z[:])
-        ts(["PL1", "xq1"], ["EP16"], T.EP16[:], T.EP[:], PF["xq1"], OP.subtract)
+        ts(["PL1", "lv1"], ["EP16"], T.EP16[:], T.EP[:], PF["lv1"], OP.subtract)
         cp(["ID", "EP16"], ["EF"], T.EF[:].indirect(T.EP16[:]), T.ID[:], 60 + STREW * 256)
         scan(["E4", "EF"], ["ES"], T.ES[:], T.E4[:], T.EF[:, 0:96], 0.0, OP.add, OP.max, 96)
         ts(["ES", "eo"], ["EO"], T.EO[:], T.ES[:, 3:96:4], 4.0, OP.mult, PF["eo"], OP.add)
@@ -603,36 +829,43 @@ def rank_program(g, core, T, topo):
         send(["E%d" % t], T.sL[:, lo:lo + KEEP], T.sE[:, 128 * t:128 * t + KEEP], "aC%d" % t)
         arrival("L%d" % t, ["sndaC%d" % t], ("aC%d" % t, 2 * n_arr, {}))
         arrival("LL%d" % t, ["sndaL%d" % t], ("aL%d" % t, n_arr, {}))
-        cp(["I1", "I1z", "HOPS"], ["H16"], T.H16[:], T.I1[:].indirect(HOPS), far(96))
-        lin(["D7", "D8L"], ["D8", "D8e"], T.D8[:], T.D7[:].indirect(D8L), n=far(128))
-        tt(["CW", "I1"], ["D8"], T.D8[:, 0:128:8], CW, T.I1[:, 1:112:7], OP.subtract)
-        ts(["I1", "I1z", "D8L", "xq"], ["I8"], T.G8[:, 256:384], T.I1[:].indirect(D8L), 2.0 ** -8, OP.mult, PF["xq"], OP.add, far(128))
+        if t in PAIRS:
+            cp(["I1"], ["H5", "H16"], T.H16[:, 0:16], T.I1[:, 2:112:7])
+            cp(["I1"], ["H3", "H16"], T.H16[:, 16:32], T.I1[:, 4:112:7])
+        else:
+            cp(["I1", "HOPS"], ["H16", "H5", "H3"], T.H16[:, 0:80], T.I1[:, 0:112].indirect(T.OU[:, 56:61]), far(80))
+        tt(["CW", "I1"], ["D7", "D8"], T.D7[:, 0:112:7], CW, T.I1[:, 1:112:7], OP.subtract)
         across(["CA%d" % z for z in range(4)], ["CI0"], T.CI[0:64, 0:4], T.CA[0:64, :], T.CA[64:128, :])
         ts(["CI0"], ["CI1"], T.CI[0:64, 8:16:2], T.CI[0:64, 0:4], 2047, OP.bitwise_and)
         ts(["CI0"], ["CI2"], T.CI[0:64, 9:16:2], T.CI[0:64, 0:4], 11, OP.arith_shift_right)
         across(["CI1", "CI2"], ["Q4"], T.QQ[0:32, 0:8], T.CI[0:32, 8:16], T.CI[32:64, 8:16])
         for a in range(1, 4):
             lin(["Q4"], ["Q4%d" % a], T.QQ[32 * a:32 * a + 32, 0:8], T.QQ[0:32, 0:8])
-        act(["Q4", "Q41", "Q42", "Q43", "BC32"], ["RP"], T.RP[:], T.QQ[:, 0:8].indirect(BC32), AF.Relu, 255.0, -1.0, n=far(256))
-        turn(["RP"], ["TO"], T.TO[:], T.RP[:], 128)
+        if RP_SPLIT:
+            for b in range(8):
+                r, w, out, x = ["Q4", "Q41", "Q42", "Q43", "C15"], ["RP%d" % b], T.RP[:, 32 * b:32 * b + 32], T.QQ[:, b:b + 1]
+                nodes.append(([way("A", r, w, lambda e, out=out, x=x: e.activation(out, T.C64[:, 64:96], AF.Relu, 15.0, x), cyc(64)),
+                               way("V", r, w, lambda e, out=out, x=x: e.tensor_scalar(out, T.C64[:, 96:128], x, 0.0, OP.subtract, OP.max), cyc(64))],
+                              r, w, 0.0))
+        else:
+            act(["Q4", "Q41", "Q42", "Q43", "BC32"], ["RP0"], T.RP[:], T.QQ[:, 0:8].indirect(BC32), AF.Relu, 15.0, -1.0, n=far(256))
+        turn(["RP%d" % b for b in range(8)], ["TO"], T.TO[:], T.RP[:], 128)
         TO = ["TO"]
         act(TO + ["qn"], ["AJ0", "AC"], T.AJ[:, 0:256], T.TO[:], AF.Sign, PF["qn"], -1.0, T.SC[:, 0:1], n=256)
         ts(["C64", "AC"], ["FB"], T.FB[:, 0:32], T.C64[:, 0:32], T.SC[:, 0:1], OP.is_lt)
         turn(["FB"], ["FX"], T.FB[:, 32:64], T.FB[:, 0:32])
         emit("V", ["FX"], ["SF"], lambda e: e.tensor_reduce(T.SC[:, 1:2], T.FB[:, 32:48], AxisListType.X, OP.add), cyc(64))
         ts(["SF", "tb"], ["SL"], T.SL[:, 0:1], T.SC[:, 1:2], PF["tb"], OP.add)
-        ts(TO + ["q255"], ["LT"], T.LT[:, 0:256], T.TO[:], PF["q255"], OP.is_gt, 2.0, OP.mult, 128)
-        ts(TO + ["q255"], ["LE"], T.LE[:], T.TO[:], PF["q255"], OP.is_ge, 2.0, OP.mult, 128)
-        scan(["LT", "ZR", "AC"], ["AA"], T.AA[:], T.LT[:, 0:256], T.ZR[:, 0:256], T.SC[:, 0:1], OP.add, OP.max, 128)
-        scan(["LE", "AA", "GS0"], ["GS"], T.GS[:, 32:288], T.LE[:], T.AA[:], 64.0, OP.add, OP.min, 128)
+        act(TO + ["q255"], ["LE"], T.LE[:], T.TO[:], AF.Sign, PF["q255"], 1.0, n=256)
+        scan(["AJ0", "D0", "AC"], ["AA"], T.AA[:], T.D0[:], T.AJ[:, 0:256], T.SC[:, 0:1], OP.add, OP.subtract, 128)
+        scan(["LE", "AA", "GS0"], ["GS"], T.GS[:, 32:288], T.LE[:], T.AA[:], 160.0, OP.add, OP.min, 128)
         scan(["GS", "GS0"], ["GD"], T.GS[:, 336:592], T.GS[:, 32:288], T.GS[:, 31:287], 0.0, OP.max, OP.subtract, 128)
         for i, k in enumerate(("GS", "GD")):
             turn([k], [k + "a"], T.TG[:, 544 * i:544 * i + 256], T.GS[:, 304 * i + 32:304 * i + 288], 128)
             turn([k, "GS0"], [k + "b"], T.TG[:, 544 * i + 256:544 * i + 544], T.GS[:, 304 * i + 16:304 * i + 304], 144)
-        ts(["GDa", "GDb", "SL", "HD"], ["HDa"], T.HD[:, 1:32:2], T.TG[:, 544:1088].indirect(T.SL[:, 0:1]), 0.25, OP.mult, n=far(16))
+        ts(["GDa", "GDb", "SL", "HD"], ["HDa"], T.HD[:, 1:32:2], T.TG[:, 544:1088].indirect(T.SL[:, 0:1]), 0.25, OP.mult, 0.25, OP.add, n=far(16))
         tt(["GSa", "GSb", "SL", "CP", "HD"], ["HDb"], T.HD[:, 32:64:2], T.TG[:, 0:544].indirect(T.SL[:, 0:1]), T.CP[:], OP.subtract, far(16))
-        ts(TO + ["q255"], ["LQ"], T.LT[:, 256:512], T.TO[:], PF["q255"], OP.is_equal, 2.0, OP.mult, 128)
-        scan(["LQ", "ZR"], ["CE"], T.GN[:], T.LT[:, 256:512], T.ZR[:, 0:256], 65.0, OP.add, OP.max, 128)
+        scan(["LE", "AJ0"], ["CE"], T.GN[:], T.LE[:], T.AJ[:, 0:256], 65.0, OP.add, OP.add, 128)
         act(["CE", "AC"], ["AJ1", "JS"], T.AJ[:, 256:512], T.GN[:], AF.Sign, T.SC[:, 0:1], -1.0, T.SC[:, 2:3], n=256)
         ts(["AC"], ["NV"], T.SC[:, 3:4], T.SC[:, 0:1], 64.0, OP.is_le, 1024.0, OP.mult)
         lin(["NV", "q254"], ["NW"], T.SC[:, 4:5], T.SC[:, 3:4], 1.0, PF["q254"])
@@ -651,25 +884,38 @@ def rank_program(g, core, T, topo):
         emit("V", ["P", "Pb", "NI16"], [XN], lambda e, t=t: e.tensor_copy(
             T.cX[:, 256 * t + 256:256 * t + 512].bitcast(dt.uint32), T.cP[:, :].bitcast(dt.uint32).indirect(T.NI16[:])), cyc(far(256)))
         lin(["P", "Pb", "NI16"], [XN + "s"], T.sX[:, 256 * t + 256:256 * t + 512], T.sP[:, :].indirect(T.NI16[:]), n=far(256))
-        for s in range(6):
-            c = slice(256 * s, 256 * s + 256)
-            lin(TO + ["H16"], ["FL%d" % s], T.FL[:, c], T.TO[:].indirect(T.H16[:, 16 * s:16 * s + 16]), n=far(256))
-            pick2(["FL%d" % s], ["FP%d" % (s + 1)], T.FP[:, 256 * s + 256:256 * s + 512], T.FL[:, c])
-        lin(["I8", "TN"], ["KY"], T.G8[:, 128:256], T.G8[:, 256:384], 1.0, T.SC[:, 5:6], 128)
-        tt(["FP%d" % s for s in range(7)] + ["G8L", "KY"], ["G8", "G8k"], T.G8[:, 0:128], T.FP[:].indirect(G8L), T.G8[:, 128:256], OP.is_ge, far(128))
-        lin(["HDa"], ["G8k"], T.G8[:, 7:128:8], T.HD[:, 1:32:2], -2.0, 1.0)
+        ts(["I1", "TN"], ["KY"], T.G8[:, 0:112], T.I1[:, 0:112], 2.0 ** -7, OP.mult, T.SC[:, 5:6], OP.add, 112)
+        if t in PAIRS:
+            lin(TO + ["L16"], ["FL3"], T.FL[:, 768:1024], T.TO[:].indirect(T.L16[:]), -16.0, 256.0, n=far(256))
+            scan(TO + ["FL3"], ["FL4"], T.FL[:, 1024:1280], T.TO[:], T.FL[:, 768:1024], 0.0, OP.max, OP.subtract, 128)
+            for s, (name, by) in enumerate((("H5", T.H16[:, 0:16]), ("H3", T.H16[:, 16:32]), ("L16", T.L16[:]))):
+                c = slice(256 * s, 256 * s + 256)
+                lin(["FL4", name], ["FL%d" % s], T.FL[:, c], T.FL[:, 1024:1280].indirect(by), 1.0, 256.0, n=far(256))
+                pick2(["FL%d" % s], ["FQ%d" % s], T.FQ[:, 16 * s:16 * s + 766:3], T.FL[:, c])
+            ts(["FQ0", "FQ1", "FQ2"], ["LH0"], T.LH[:, 104:152], T.FQ[:, 45:800:16], 2.0, OP.mult)
+            ts(["LH0"], ["LH1"], T.LH[:, 1:97:2], T.LH[:, 104:152], 4, OP.arith_shift_right, 30, OP.bitwise_and)
+            ts(["LH0"], ["LH2"], T.LH[:, 2:98:2], T.LH[:, 104:152], 30, OP.bitwise_and)
+            tt(["LH1", "LH2", "LHz", "SIX", "KY"], ["G8"], T.G8[:, 112:224], T.LH[:, 0:97].indirect(SIX), T.G8[:, 0:112], OP.is_ge, far(112))
+        else:
+            for s in range(6):
+                c = slice(256 * s, 256 * s + 256)
+                lin(TO + ["H16", "L16", "xn"], ["FL%d" % s], T.FL[:, c], T.TO[:].indirect(T.H16[:, 16 * s:16 * s + 16] if s < 5 else T.L16[:]),
+                    2.0, PF["xn"], n=far(256))
+                pick2(["FL%d" % s], ["FP%d" % s], T.FP[:, 16 * s + 16:16 * s + 16 + 1786:7], T.FL[:, c])
+            tt(["FP%d" % s for s in range(6)] + ["FPz", "KY"], ["G8"], T.G8[:, 112:224], T.FP[:, 105:1888:16], T.G8[:, 0:112], OP.is_ge, 224)
         lin(["HDa"], ["G8g"], T.HO[:, 32:48], T.HD[:, 1:32:2], 2.0)
         cp(["LL%d" % t], ["LI0"], T.LI[:, 0:48], T.LL[:, 48 * t:48 * t + 48])
         ts(["LI0"], ["LI1"], T.LI[:, 49:144:2], T.LI[:, 0:48], 255, OP.bitwise_and)
         ts(["LI0"], ["LI2"], T.LI[:, 48:144:2], T.LI[:, 0:48], 8, OP.arith_shift_right)
         cp(["LI1", "LI2"], ["YXe"], T.YX[:, 256:352], T.LI[:, 48:144], 96)
-        tt(["HO", "G8g"], ["D8e"], T.D8[:, 7:128:8], T.HO[:, 1:32:2], T.HO[:, 32:48], OP.mult)
-        scan(["G8", "G8k", "D8", "D8e"], ["HL"], T.HL[:], T.G8[:, 0:128], T.D8[:], 0.0, OP.mult, OP.add, 128)
-        cp(["HL"], ["F16"], T.F16[:], T.HL[:, 7:128:8])
+        tt(["HO", "G8g"], ["D8e"], T.D8[:, 0:16], T.HO[:, 1:32:2], T.HO[:, 32:48], OP.mult)
+        scan(["G8", "D7", "D8"], ["HL"], T.HL[:, 0:112], T.G8[:, 112:224], T.D7[:], 0.0, OP.mult, OP.add, 112)
+        tt(["HL", "D8e"], ["HM"], T.D8[:, 16:32], T.HL[:, 6:112:7], T.D8[:, 0:16], OP.max)
+        cp(["HM"], ["F16"], T.F16[:], T.D8[:, 16:32])
         if not last:
-            lin(["YXz", "YXe", "F16"], ["LF"], T.LF[:], T.YX[:].indirect(T.F16[:]), 2.0 ** -8, n=far(256))
+            lin(["YXz", "YXe", "F16"], ["LF"], T.LF[:], T.YX[:].indirect(T.F16[:]), 2.0 ** -8, PF["dl"], n=far(256))
             pick(["LF"], ["VT6"], T.VT[:, 96:96 + 1786:7], T.LF[:])
-            ts(["VT6", "xq"], ["L16"], T.L16[:], VT6, PF["xq"], OP.subtract, 256.0, OP.mult)
+            ts(["VT6", "lv"], ["L16"], T.L16[:], VT6, PF["lv"], OP.subtract, 256.0, OP.mult)
 
     mm(["V", "P"], "PA", 256, "V", 0, "P", 0)
     mm(["V", "Pb"], "PB", 128, "V", 0, "Pb", 0)

import math

from concourse.mybir import dt, AluOpType, AxisListType, ActivationFunctionType

OP = AluOpType
AF = ActivationFunctionType
ROUNDS, KEEP = 3, 96
F, B, I, U, X4, U8 = "float32", "bfloat16", "int32", "uint16", "float8_e4m3fn_x4", "uint8"

SCRATCH = {}


def _sb(dtype, **widths):
    for name in widths:
        SCRATCH[name] = ("sbuf", [128, widths[name]], dtype)


def _q(**widths):
    for name in widths:
        SCRATCH["c" + name] = ("sbuf", [128, widths[name]], X4)
        SCRATCH["s" + name] = ("sbuf", [128, widths[name]], U8)


STRIP = 544
ROOM = STRIP + 128
_sb(B, XT=1024, UT=512, VTL=512)
_sb(I, OL=16, PC=1, PI=12, OI=48, CI=24, LI=144, I0=112, I1=120)
_q(W=512, U=128, UP=384, V=128, X=1024, L=320, P=384, E=384)
_q(K=896)
_q(C=256 + 2 * ROOM)
_sb(B, TK=2064, IR=256, I4=96, TI=128, BK=128, NB=256, RS=512, RC=256, EX=256, E4=96, ET0=512, TR=128, RM=480)
_sb(B, C64=64, ZR=528, PD2=96, CB=448, SN=1024)
_sb(F, ID=256, PF=40, CW=48, NN=8, CP=16, TMP=8)
_sb(U, OU=88, SL=24)
_sb(F, SR=512, SG=512, SW=512, SB2=4, DL=2, TH0=128, TH1=128, RW=32, EC=128, EP=16, RV=960)
_sb(B, BT=1024, CT=8 * STRIP, AJ=1024, RD=512)
_sb(F, LF=256, VH=1536, VT=1888, D7=112, CM=112, HR=224, D8=128, G8=384, HL=128)
_sb(B, FT=1024, FU=1024, Z=1024, ET=512, RT=512)
_sb(F, EF=256, ES=96, PK=96)
_sb(U, EP16=16, EO=24, LS=144, LL=144, R16=16, R32=32, F16=16, NI16=16, L16=16, H16=96)
_sb(F, CA=4, CJ=1024, QQ=192, SC=8, HD=64, HO=48, YC=352, YO=256, LO=256, VR=112)
_sb(B, RP=256, TO=256, FB=64, LT=512, LE=256, AA=256, GS=608, GN=256, TG=1088, FL=1536, FP=1792, YX=352)
for _k in ("PA", "PB", "PC_", "Q0", "Q1", "Q2"):
    SCRATCH[_k] = ("psum", [128, 512], F)
SCRATCH["PD"] = ("psum", [128, 1024], F)
BANK = {"PA": ("PA", 0), "PB": ("PB", 0), "PC_": ("PC_", 0), "Q0": ("Q0", 0), "Q1": ("Q1", 0), "Q2": ("Q2", 0),
        "PD0": ("PD", 0), "PD1": ("PD", 512)}
PLACE = {"B": ("C", 0), "KS": ("K", 512), "KB": ("K", 640), "KI": ("K", 768), "Pb": ("P", 256),
         "C0": ("C", 256), "C1": ("C", 256 + ROOM)}
for _i in range(4):
    PLACE["X%d" % _i] = ("X", 256 * _i)
    PLACE["KR%d" % _i] = ("K", 128 * _i)
    PLACE["E%d" % _i] = ("E", 128 * _i)
PARTS = []
for _i in range(8):
    PARTS.append((7 - _i, 64 + 60 * _i, (16 - _i, 16), (0, 7 - _i)))
    PARTS.append((15 - _i, 92 + 60 * _i, (16, 16), (7 - _i, 15 - _i)))
SIGNED = (8, 10)
CUTS = ((0, 136, 272, 408, 544), (0, 136, 272, 408, 544))
FRAMES = (8, 7, 6, 5, 4, 0, 3, 1, 2)
TWINS, F_BANKS, ROWS = ("PD1", "Q1"), ("Q0", "Q2", "Q0", "Q0"), ("Q2", "Q2")
COUNT_V, RP_SPLIT, OWN, F_CUT = 0, True, 1, (4, 4)
TWICE, STEP = (), (0, 1, 1, 2, 2, 2)
_sb(B, L2=512)
_sb(I, LH=152)
_sb(B, FQ=800, FP=1888)
_sb(F, TMP=24)
PAIRS = (0, 1)
LOW = (True, True)
_sb(F, LW=32, TH=256)
_sb(B, D0=256, C64=128, CK=512)
_sb(U, M16=16)
for _k, _gone in (("NN", True), ("LT", True), ("SR", all(TWINS)), ("TH1", True), ("TH0", True), ("L2", not TWICE), ("M16", not TWICE),
                  ("CK", not COUNT_V)):
    if _gone:
        SCRATCH.pop(_k)
CYCLE, WAKE, FLIGHT, JUMP, STREW, SEND, FIRST = 0.00085, 0.26, 1.2, 1.5, 3.5, 0.3, 1.0
PE_CYCLE = 0.0007
FIRST_TRIES, SHAKE, SPARE = 200, 1.5, 0.3
TRIES, PACE, NEAR, REACH, HEAT, SEEK, SORT, AIM = 500000, 1.15, 0.15, 20, 0.02, 6, 50, 0.7
BIRTH_S = 2
SLOW, SHARE = 1.4, 0.75

SEMAPHORES = ["sV", "sA", "sP", "sG", "dX", "dU", "dO", "dW", "dVV", "dPad", "dF0", "dF1", "dF2", "dF3", "dY", "dLk", "dOc", "ls",
              "aC0", "aC1", "aC2", "aL0", "aL1", "aL2"]


ORDER, SPAN = [], []


def plan(nodes):
    n = len(nodes)
    succ, pred = [{} for _ in range(n)], [{} for _ in range(n)]
    wr, rd = {}, {}
    only = [x[0][0][0] if len(x[0]) == 1 else None for x in nodes]

    def edge(a, b):
        if a != b:
            succ[a][b] = pred[b][a] = nodes[a][3] + (0.0 if only[a] == only[b] and only[a] in ("P", "G") else WAKE)
    for i, (ways, r, w, late) in enumerate(nodes):
        for k in r:
            if k in wr:
                edge(wr[k], i)
            if k in BANK:
                for j in rd.get(k, []):
                    if only[j] is None or only[j] != only[i]:
                        edge(j, i)
        for k in w:
            if k in wr:
                edge(wr[k], i)
            for j in rd.get(k, []):
                edge(j, i)
        for k in r:
            rd.setdefault(k, []).append(i)
        for k in w:
            wr[k], rd[k] = i, []

    succ, pred = [list(x.items()) for x in succ], [list(x.items()) for x in pred]
    late = [x[3] for x in nodes]

    def sweep(before, urgency, start, spare):
        end, order, lines = [None] * n, [], {q: ([], []) for q in "VAPGSR"}

        def put(i):
            ready = start[i]
            for j, lag in before[i]:
                if end[j] is None:
                    put(j)
                if end[j] + lag > ready:
                    ready = end[j] + lag
            best = None
            for k, (q, c) in enumerate(nodes[i][0]):
                begins, ends = lines[q]
                at, place, top = ready, 0, len(ends)
                m = top
                while place < top:
                    mid = (place + top) // 2
                    if ends[mid] > at:
                        top = mid
                    else:
                        place = mid + 1
                while place < m and begins[place] < at + c:
                    at = ends[place]
                    place += 1
                offer = (at + c + (spare[i] if k else 0.0), at, k, place)
                if best is None or offer < best:
                    best = offer
            _, at, k, place = best
            q, c = nodes[i][0][k]
            lines[q][0].insert(place, at)
            lines[q][1].insert(place, at + c)
            order.append((at, len(order), i, k))
            end[i] = at + c
        for i in sorted(range(n), key=lambda j: -urgency[j]):
            if end[i] is None:
                put(i)
        return end, order

    def slower(order):
        end, free = [0.0] * n, {q: 0.0 for q in "VAPGSR"}
        for _, _, i, k in sorted(order):
            q, c = nodes[i][0][k]
            at = free[q]
            for j, lag in pred[i]:
                if end[j] + lag > at:
                    at = end[j] + lag
            end[i] = free[q] = at + (c * SLOW if q in "VA" else c)
        return max(end[i] + late[i] for i in range(n))

    def passes(urgency, spare, count, near=1e9):
        best = None
        for p in range(count):
            end, order = sweep(pred, urgency, [0.0] * n, spare)
            shown = [end[i] + late[i] for i in range(n)]
            mark = max(shown)
            mark = (mark + SHARE * slower(order)) / 2 if mark < near else mark + near
            if best is None or mark < best[0]:
                best = (mark, order, urgency, spare)
            if p < count - 1:
                urgency = sweep(succ, shown, late, spare)[0]
        return best
    rest = [0.0] * n
    for i in range(n - 1, -1, -1):
        rest[i] = nodes[i][0][0][1] + max([rest[j] + lag for j, lag in succ[i]] + [late[i]])
    best = passes(rest, [SPARE] * n, 6)
    seed = [1]

    def chance():
        seed[0] = (seed[0] * 1103515245 + 12345) % 2147483648
        return seed[0] / 2147483648.0
    for _ in range(FIRST_TRIES):
        urgency, spare = list(best[2]), list(best[3])
        mid, wide = chance() * best[0], 1.0 + 5.0 * chance()
        for i in range(n):
            if abs(urgency[i] - mid) < wide:
                urgency[i] += SHAKE * (chance() + chance() - 1.0)
                if len(nodes[i][0]) > 1 and chance() < 0.3:
                    spare[i] = (-0.3, 0.0, 0.3, 1.0, 3.0)[int(5 * chance())]
        other = passes(urgency, spare, 2, best[0] + 1.0)
        if other[0] <= best[0]:
            best = other
    ways = [[(q, c * PACE if q in "VA" else c) for q, c in x[0]] for x in nodes]
    order = [x[2] for x in sorted(best[1])]
    took = [0] * n
    for x in best[1]:
        took[x[2]] = x[3]
    end, rest, at, before, after = [0.0] * n, [0.0] * n, [0] * n, [-1] * n, [-1] * n

    def times(lo, hi):
        last = dict(head)
        for p in range(lo, hi + 1):
            i = order[p]
            at[i] = p
            q, cost[i] = ways[i][took[i]]
            j = before[i] = last[q]
            if j >= 0:
                after[j] = i
            last[q] = i
        p, reach, stale = lo, hi, set()
        for q in last:
            i, j = last[q], tail[q]
            if i >= 0:
                after[i] = j
            if j >= 0:
                before[j] = i
                stale.add(j)
                reach = max(reach, at[j])
        while p <= reach:
            i = order[p]
            if p <= hi or i in stale:
                j = before[i]
                t = end[j] if j >= 0 else 0.0
                for j, lag in pred[i]:
                    if end[j] + lag > t:
                        t = end[j] + lag
                t += cost[i]
                if t != end[i]:
                    end[i] = t
                    for j, lag in succ[i]:
                        stale.add(j)
                        if at[j] > reach:
                            reach = at[j]
                    j = after[i]
                    if j >= 0:
                        stale.add(j)
                        if at[j] > reach:
                            reach = at[j]
            p += 1
        p, reach, stale = hi, lo, set()
        for q in head:
            if head[q] >= 0:
                stale.add(head[q])
                reach = min(reach, at[head[q]])
        while p >= reach:
            i = order[p]
            if p >= lo or i in stale:
                j = after[i]
                t = late[i]
                if j >= 0 and rest[j] > t:
                    t = rest[j]
                for j, lag in succ[i]:
                    if rest[j] + lag > t:
                        t = rest[j] + lag
                t += cost[i]
                if t != rest[i]:
                    rest[i] = t
                    for j, lag in pred[i]:
                        stale.add(j)
                        if at[j] < reach:
                            reach = at[j]
                    j = before[i]
                    if j >= 0:
                        stale.add(j)
                        if at[j] < reach:
                            reach = at[j]
            p -= 1
        return max([rest[i] for i in roots])

    def through(lo, hi, part):
        new, free = {}, {}
        head.clear()
        tail.clear()
        for p in range(lo, hi + 1):
            i = order[p]
            q = ways[i][was[1] if i == was[0] else took[i]][0]
            if q not in head:
                head[q] = before[i]
            tail[q] = after[i]
        most = 0.0
        for i in part:
            q, c = ways[i][took[i]]
            if q not in head:
                p = lo - 1
                while p >= 0 and ways[order[p]][took[order[p]]][0] != q:
                    p -= 1
                head[q] = order[p] if p >= 0 else -1
                p = hi + 1
                while p < n and ways[order[p]][took[order[p]]][0] != q:
                    p += 1
                tail[q] = order[p] if p < n else -1
            t = free[q] if q in free else (end[head[q]] if head[q] >= 0 else 0.0)
            for j, lag in pred[i]:
                e = new[j] if j in new else end[j]
                if e + lag > t:
                    t = e + lag
            t += c
            new[i] = free[q] = t
            e = late[i]
            for j, lag in succ[i]:
                if at[j] > hi and rest[j] + lag > e:
                    e = rest[j] + lag
            if t + e > most:
                most = t + e
        for q in free:
            if tail[q] >= 0 and free[q] + rest[tail[q]] > most:
                most = free[q] + rest[tail[q]]
        return most
    cost, roots = [0.0] * n, [i for i in range(n) if not pred[i]]
    head, tail = {q: -1 for q in "VAPGSR"}, {q: -1 for q in "VAPGSR"}
    span = times(0, n - 1)
    kept, was = (span, list(order), list(took)), [-1, 0]
    for step in range(TRIES):
        for _ in range(SEEK):
            i = int(chance() * n)
            if end[i] - cost[i] + rest[i] > span - NEAR:
                break
        if chance() < 0.3 and before[i] >= 0:
            i = before[i]
        was[0], was[1] = i, took[i]
        p, far_, back = at[i], 1 + int(REACH * chance() ** 2), chance() < 0.5
        if len(ways[i]) > 1 and chance() < 0.3:
            took[i] = (took[i] + 1 + int(chance() * (len(ways[i]) - 1))) % len(ways[i])
        elif chance() < AIM:
            j = i
            for _ in range(1 + int(3 * chance() ** 2)):
                k = before[j] if back else after[j]
                j = k if k >= 0 else j
            far_ = abs(at[j] - p)
        if back:
            to = max([p - far_, 0] + [at[j] + 1 for j, lag in pred[i]])
            lo, hi, part = to, p, [i] + order[to:p]
        else:
            to = min([p + far_, n - 1] + [at[j] - 1 for j, lag in succ[i]])
            lo, hi, part = p, to, order[p + 1:to + 1] + [i]
        if (lo < hi or took[i] != was[1]) and through(lo, hi, part) <= span - HEAT * (1.0 - step / TRIES) * math.log(chance() + 1e-9):
            order[lo:hi + 1] = part
            span = times(lo, hi)
            if span < kept[0] - 1e-9:
                kept = (span, list(order), list(took))
        else:
            took[i] = was[1]
        if step % SORT == 0:
            if step % (2 * SORT):
                order.sort(key=lambda j: end[j] - cost[j])
            else:
                order.sort(key=lambda j: -rest[j])
            for p in range(n):
                at[order[p]] = p
    SPAN.append(kept[0])
    return [(i, kept[2][i]) for i in kept[1]]


def rank_program(g, core, T, topo):
    rank = T.rank_of(core)
    if rank is None:
        return
    cores = T.cores
    n_ranks = len(cores)
    nxt, prv = cores[(rank + 1) % n_ranks], cores[(rank - 1) % n_ranks]
    eng = {"V": g.vector, "A": g.scalar, "P": g.tensor, "G": g, "S": g.sync}
    own = {"V": "sV", "A": "sA", "P": "sP", "G": "sG"}
    cnt, known, lastw, readers = {}, {q: {} for q in eng}, {}, {}

    def sync(q, toks):
        for s, n, clk in sorted(toks, key=lambda t: -sum(t[2].values())):
            if known[q].get(s, 0) < n:
                eng[q].wait_ge(T.sem[s], n)
                for k in clk:
                    known[q][k] = max(known[q].get(k, 0), clk[k])
                known[q][s] = max(known[q].get(s, 0), n)

    def deps(q, r, w):
        toks, me = [], own.get(q)
        for k in r:
            if k in lastw and not (q == "P" and lastw[k][0] == "sP"):
                toks.append(lastw[k])
            if k in BANK:
                toks += [t for s, t in readers.get(k, {}).items() if s != me]
        for k in w:
            if k in lastw and not (q == "P" and lastw[k][0] == "sP"):
                toks.append(lastw[k])
            toks += [t for s, t in readers.get(k, {}).items()]
        sync(q, toks)

    def done(tok, r, w):
        for k in r:
            readers.setdefault(k, {})[tok[0]] = tok
        for k in w:
            lastw[k] = tok
            readers[k] = {}

    nodes = []

    def way(q, r, w, fn, time, alone=False):
        def issue():
            deps(q, r, w)
            s = own[q]
            fn(eng[q]).then_inc(T.sem[s], 1)
            cnt[s] = cnt.get(s, 0) + 1
            clk = dict(known[q])
            clk[s] = cnt[s]
            done((s, cnt[s], clk), r, w)
            if alone:
                sync(q, [(s, cnt[s], clk)])
        return (q, issue, time)

    def emit(q, r, w, fn, time, alone=False):
        nodes.append(([way(q, r, w, fn, time, alone)], r, w, -WAKE if alone else 0.0))

    def dma(q, s, r, w, pairs, late=2.0):
        def issue():
            deps(q, r, w)
            for o, i in pairs:
                eng[q].dma_start(o, i).then_inc(T.sem[s], 16)
                cnt[s] = cnt.get(s, 0) + 16
            done((s, cnt[s], dict(known[q])), r, w)
        nodes.append(([(q, issue, 0.05 * len(pairs))], r, w, late))

    def arrival(key, r, tok):
        nodes.append(([("R", lambda: done(tok, [], [key]), 0.0)], r, [key], FLIGHT))

    def schedule():
        if not ORDER:
            ORDER.extend(plan([([(q, c) for q, fn, c in ways], r, w, late) for ways, r, w, late in nodes]))
        for i, k in ORDER:
            nodes[i][0][k][1]()

    def cyc(n):
        return CYCLE * max(64, n)

    def tt(r, w, out, a, b, op, n=64):
        emit("V", r, w, lambda e: e.tensor_tensor(out, a, b, op), cyc(n))

    def across(r, w, out, a, b):
        emit("V", r, w, lambda e: e.tensor_tensor(out, a, b, OP.add), cyc(64) + WAKE, True)

    def ts(r, w, out, a, s1, o1, s2=None, o2=None, n=64):
        if o2 is None:
            emit("V", r, w, lambda e: e.tensor_scalar(out, a, s1, None, o1), cyc(n))
        else:
            emit("V", r, w, lambda e: e.tensor_scalar(out, a, s1, s2, o1, o2), cyc(n))

    def cp(r, w, out, a, n=64):
        emit("V", r, w, lambda e: e.tensor_copy(out, a), cyc(n))

    def scan(r, w, out, d0, d1, init, o0, o1, n=64):
        emit("V", r, w, lambda e: e.tensor_tensor_scan(out, d0, d1, init, o0, o1), cyc(n))

    def turn(r, w, out, a, n=64):
        emit("V", r, w, lambda e: e.transpose(out, a), cyc(n))

    def fill(w, ap, x, n=64):
        emit("V", [], w, lambda e: e.memset(ap, x), cyc(n))

    def quant(r, name, n, tile, first=0):
        k, o = PLACE.get(name, (name, 0))
        o += first
        emit("V", r, [name + (".%d" % first if name in ("C0", "C1") else "")], lambda e: e.quantize_mx(T["c" + k][:, o:o + n], T["s" + k][:, o:o + n], tile), CYCLE * (16 + 1.06 * n))

    def act(r, w, out, a, fn=AF.Copy, bias=0.0, scale=1.0, acc=None, n=64):
        if acc is None:
            emit("A", r, w, lambda e: e.activation(out, a, fn, bias, scale), cyc(n))
        else:
            emit("A", r, w, lambda e: e.activation(out, a, fn, bias, scale, accum_out=acc), cyc(n) + 0.02)

    def lin(r, w, out, a, scale=1.0, bias=0.0, n=64, half=False):
        plain = isinstance(scale, float) and isinstance(bias, float)
        if plain and scale == 1.0 and bias == 0.0:
            v = way("V", r, w, lambda e: e.tensor_copy(out, a), cyc(n // 2 if half else n))
        else:
            v = way("V", r, w, lambda e: e.tensor_scalar(out, a, scale, bias, OP.mult, OP.add), cyc(n // 2 if half else n))
        if plain and scale == 1.0 and bias == 0.0:
            s = way("A", r, w, lambda e: e.activation(out, a, AF.Copy), cyc(n))
        else:
            s = way("A", r, w, lambda e: e.activation(out, a, AF.Copy if plain and bias == 0.0 else AF.Identity, bias, scale), cyc(n))
        nodes.append(([s, v], r, w, 0.0))

    def zero(w, out, n, x=0):
        nodes.append(([way("G", ["ZR"], w, lambda e: e.iota(out, [[0, n]], x, 0, allow_small_or_imprecise_dtypes=True), 0.13 + 2 * n * CYCLE),
                       way("A", ["ZR"], w, lambda e: e.activation(out, T.ZR[:, 0:n], AF.Identity, float(x)), cyc(n)),
                       way("V", ["ZR"], w, lambda e: e.memset(out, float(x)), cyc(n // 2))], ["ZR"], w, 0.0))

    def far(n):
        return 70 + JUMP * n

    def ps(bank, a, b, step=1):
        return T[BANK[bank][0]][:, BANK[bank][1] + a:BANK[bank][1] + b:step]

    def mm(r, bank, n, L, l0, R, r0, start=True, stop=True, line=[]):
        L, lo_ = PLACE.get(L, (L, 0))
        R, ro_ = PLACE.get(R, (R, 0))
        l0, r0 = l0 + lo_, r0 + ro_
        o = BANK[bank][1]
        emit("P", r, [bank] + line, lambda e: e.matmul_mx(
            T[BANK[bank][0]][:, o:o + n], T["c" + L][:, l0:l0 + 128], T["s" + L][:, l0:l0 + 128],
            T["c" + R][:, r0:r0 + n], T["s" + R][:, r0:r0 + n], start, stop), PE_CYCLE * (n + 16))

    def iota(w, out, pattern, base, cm, n, whole=False):
        if whole:
            emit("G", [], w, lambda e: e.iota(out, pattern, base, cm), 0.13 + 2 * n * CYCLE)
        else:
            emit("G", [], w, lambda e: e.iota(out, pattern, base, cm, allow_small_or_imprecise_dtypes=True), 0.13 + 2 * n * CYCLE)

    def pick(r, w, out, row, n=256):
        scan(r + ["EX"], w, out, T.EX[:], row, 0.0, OP.add, OP.min, n)

    def pick2(r, w, out, row):
        pick(r, w, out, row, 128)

    dma("S", "dX", [], ["XT"], [(T.XT[:], T.x[:])], 2.75)
    dma("A", "dU", [], ["UT"], [(T.UT[:], T.u[:])], 1.9)
    dma("S", "dO", [], ["OL"], [(T.OL[:], T.ol[:])])
    dma("S", "dW", ["XT"], ["W"], [(T.cW[:].bitcast(dt.uint8), T.wc[:]), (T.sW[:], T.ws[:])], 4.0)
    dma("S", "dVV", ["XT"], ["VTL"], [(T.VTL[:], T.v[:])])

    fill(["ZR"], T.ZR[:], 0.0, 264)
    iota(["PC"], T.PC[:], [[0, 1]], 0, 1, 1, True)
    iota(["OI"], T.OI[:, 0:16], [[1, 2], [16, 8]], 0, 0, 16, True)
    iota(["OIb"], T.OI[:, 16:24], [[0, 8]], 8, 0, 8, True)
    iota(["OI2"], T.OI[:, 24:40], [[1, 8], [0, 2]], 0, 0, 16, True)
    iota(["IR"], T.IR[:], [[0, 16], [1, 16]], 0, 0, 256)
    iota(["TI"], T.TI[:], [[1, 128]], 0, -1, 128)
    iota(["ID"], T.ID[:], [[1, 256]], 0, 0, 256)
    iota(["BK"], T.BK[:], [[1, 8], [0, 16]], 0, 0, 128)
    iota(["C16"], T.CW[:, 16:32], [[16, 16]], 0, 0, 16)
    iota(["I4"], T.I4[:], [[0, 24], [1, 4]], 0, 0, 96)
    cp(["OI", "OIb"], ["OU"], T.OU[:, 0:24], T.OI[:, 0:24])
    PF = {}
    names = ("q", "g", "m1", "q8", "r8", "q4", "r4", "r2", "r32")
    for i, (sh, bits) in enumerate(((0, 15), (4, 7), (4, 1), (3, 1), (0, 7), (2, 3), (0, 3), (0, 1), (0, 31))):
        ts(["PC"], ["PI%d" % i], T.PI[:, i:i + 1], T.PC[:], sh, OP.arith_shift_right, bits, OP.bitwise_and)
        PF[names[i]] = T.PF[:, i:i + 1]
    cp(["PI0", "PI1"], ["q", "g"], T.PF[:, 0:2], T.PI[:, 0:2])
    cp(["PI%d" % i for i in range(2, 9)], list(names[2:]), T.PF[:, 2:9], T.PI[:, 2:9])

    def number(name, src, s1, o1, s2, o2, more=[]):
        PF[name] = T.PF[:, len(PF):len(PF) + 1]
        ts([src] + more, [name], PF[name], PF[src], s1, o1, s2, o2)

    def affine(name, src, scale, bias):
        PF[name] = T.PF[:, len(PF):len(PF) + 1]
        lin([src], [name], PF[name], PF[src], scale, bias)
    affine("q1", "q", 1.0, 1.0)
    affine("qn", "q", -1.0, 15.5)
    affine("q255", "q", 1.0, -14.5)
    affine("q254", "q", -2.0, 29.0)
    number("xq", "q", 15.0, OP.is_lt, -256.0, OP.mult)
    number("t2", "r2", PF["m1"], OP.not_equal, 272.0, OP.mult, ["m1"])
    number("t1", "q", PF["m1"], OP.subtract, 16.0, OP.mult, ["m1"])
    number("tb", "t1", PF["t2"], OP.add, -1.0, OP.add, ["t2"])
    number("lv", "q4", 3.0, OP.is_lt, 512.0, OP.mult)
    affine("lv1", "lv", 1.0, 1.0)
    number("dl", "lv", PF["xq"], OP.subtract, 1.0, OP.mult, ["xq"])
    affine("dm", "dl", -256.0, 0.0)
    affine("q3", "q", 1.0, -3.0)
    affine("q16", "q", 1.0, -128.0)
    affine("q41", "q4", 1.0, 1.0)
    affine("e8", "q8", 32.0, 447.0)
    number("eo", "q4", 3.0, OP.is_lt, -2048.0, OP.mult)
    tt(["eo", "r4"], ["eo"], PF["eo"], PF["eo"], PF["r4"], OP.add)
    cp(["OI2"], ["BC32"], T.OU[:, 24:40], T.OI[:, 24:40])
    ts(["C16", "q3"], ["r7a"], T.TMP[:, 0:8], T.CW[:, 16:24], PF["q3"], OP.add, 1.0 / 7, OP.mult)
    cp(["r7a"], ["r7b"], T.OI[:, 40:48], T.TMP[:, 0:8])
    cp(["r7b"], ["REP7"], T.OU[:, 40:48], T.OI[:, 40:48])
    CW = T.CW[:, 0:16]
    ts(["C16", "q"], ["CW"], CW, T.CW[:, 16:32], PF["q"], OP.add)
    if PAIRS:
        tt(["CW", "r7b"], ["r7a"], T.TMP[:, 0:8], T.CW[:, 0:8], T.OI[:, 40:48], OP.subtract)
        ts(["r7b"], ["r7c"], T.TMP[:, 8:16], T.OI[:, 40:48], 6.0, OP.mult)
        tt(["r7a", "r7c"], ["r7d"], T.TMP[:, 16:24], T.TMP[:, 0:8], T.TMP[:, 8:16], OP.is_gt)
        tt(["r7a", "r7d"], ["r7c"], T.TMP[:, 8:16], T.TMP[:, 0:8], T.TMP[:, 16:24], OP.mult)
        cp(["r7c"], ["SIX"], T.OU[:, 48:56], T.TMP[:, 8:16])
        iota(["LHz"], T.LH[:, 0:1], [[0, 1]], -1024, 0, 1, True)
    if len(PAIRS) < ROUNDS:
        affine("q7", "q", 7.0, 1.0)
        affine("xn", "xq", -1.0, 0.0)
        ts(["ID", "q7"], ["HOPS"], T.OU[:, 56:62], T.ID[:, 0:6], PF["q7"], OP.add)
        zero(["FPz"], T.FP[:, 105:1888:112], 16, -1024)
    ts(["r8", "e8"], ["ENDS"], T.OU[:, 80:81], PF["r8"], -60.0, OP.mult, PF["e8"], OP.add)
    BC32, REP7, SIX = T.OU[:, 24:40], T.OU[:, 40:47], T.OU[:, 48:55]
    ts(["IR", "q"], ["NB"], T.NB[:], T.IR[:], PF["q"], OP.not_equal, 2.0 ** 90, OP.mult, 128)
    zero(["RS"], T.RS[:], 512)
    fill(["RS"], T.RS[:, 0:256:16], 2.0 ** 95)
    fill(["RS"], T.RS[:, 256:512:16], -2.0 ** 95)
    zero(["RC"], T.RC[:], 256, 512)
    for h in range(2):
        ts(["ZR", "q16"], ["RC"], T.RC[:, 128 * h:128 * h + 128:16], T.ZR[:, 0:8], PF["q16"], OP.add, -16.0 * h, OP.add)
    zero(["RM"], T.RM[:], 480, 1)
    fill(["RM"], T.RM[:, 0:480:60], 0.0)
    fill(["RM"], T.RM[:, 28:480:60], 0.0)
    for s in range(2):
        iota(["RVz%d" % s], T.RV[:, 480 * s:480 * s + 30 * SIGNED[s]], [[0, 30 * SIGNED[s]]], 0, 0, 30 * SIGNED[s])
    ts(["IR", "q"], ["e0"], T.ET0[:, 0:256], T.IR[:], PF["q"], OP.is_equal, 2.0 ** 19, OP.mult, 128)
    ts(["IR", "q1"], ["e1"], T.ET0[:, 256:512], T.IR[:], PF["q1"], OP.is_equal, -2.0 ** -11, OP.mult, 128)
    scan(["e0", "e1"], ["EX"], T.EX[:], T.ET0[:, 256:512], T.ET0[:, 0:256], 0.0, OP.mult, OP.add, 128)
    ts(["I4", "q4", "EX"], ["e0"], T.ET0[:, 0:96], T.I4[:], PF["q4"], OP.is_equal, -2.0 ** 20, OP.mult)
    ts(["I4", "q41", "EX"], ["e1"], T.ET0[:, 256:352], T.I4[:], PF["q41"], OP.is_equal, -2.0 ** -11, OP.mult)
    scan(["e0", "e1"], ["E4"], T.E4[:], T.ET0[:, 256:352], T.ET0[:, 0:96], 0.0, OP.mult, OP.add)
    ts(["TI"], ["TR"], T.TR[:], T.TI[:], 0.0, OP.is_le)
    zero(["TKB"], T.TK[:, 0:512], 512, 1)
    zero(["TKS"], T.TK[:, 512:1024], 512)
    for i in range(4):
        ts(["BK", "g", "TKS"], ["TKS%d" % i], T.TK[:, 512 + 5 * i:1024:16], T.BK[:, 0:128:4], PF["g"], OP.is_equal)
    emit("G", ["TKB"], ["TKI"], lambda e: e.affine_select(T.TK[:, 1552:2064], T.TK[:, 0:512], [[1, 128], [0, 4]], OP.is_equal, 0.0, 0, -1),
         0.17 + 1024 * CYCLE)
    quant(["TKI"], "KI", 128, T.TK[:, 1552:2064])
    zero(["TKR"], T.TK[:, 1024:1552], 528)
    ts(["TI"], ["TKR"], T.TK[:, 1027:1539:4], T.TI[:], 0.0, OP.is_equal, 128.0, OP.mult)
    quant(["TKB"], "KB", 128, T.TK[:, 0:512])
    quant(["TKS%d" % i for i in range(4)], "KS", 128, T.TK[:, 512:1024])
    for b in range(4):
        quant(["TKR"], "KR%d" % b, 128, T.TK[:, 1027 - b:1539 - b])
    quant(["UT"], "U", 128, T.UT[:])
    for i in (0, 2, 1):
        c = slice(128 * i, 128 * i + 128)
        emit("V", ["U", "OU"], ["UPc%d" % i], lambda e, i=i, c=c: e.tensor_copy(
            T.cUP[:, c].bitcast(dt.uint32), T.cU[:, 0:128].bitcast(dt.uint32).indirect(T.OU[:, 8 * i:8 * i + 8])), cyc(far(128)))
        emit("A", ["U", "OU"], ["UPs%d" % i], lambda e, i=i, c=c: e.activation(
            T.sUP[:, c], T.sU[:, 0:128].indirect(T.OU[:, 8 * i:8 * i + 8]), AF.Copy), cyc(far(128)))
    quant(["XT"], "X0", 256, T.XT[:])
    for s in range(2):
        quant(["ZR"], "C%d" % s, 128, T.ZR[:, 0:512], STRIP)
    for i in (2, 3):
        zero(["zB%d" % i], T.BT[:, i:1024:4], 256)
    dma("S", "dPad", ["X0"], ["pad"], [(T.cL[:, 288:320].bitcast(dt.uint8), T.cX[:, 0:32].bitcast(dt.uint8)),
                                       (T.sL[:, 288:320], T.sX[:, 0:32])])
    zero(["CB"], T.CB[:], 448)
    ts(["ID", "r32"], ["CB"], T.CB[:, 192:224], T.ID[:, 0:32], PF["r32"], OP.is_equal)
    ts(["ID", "r32"], ["CB"], T.CB[:, 224:256], T.ID[:, 0:32], PF["r32"], OP.is_equal, 2048.0, OP.mult)
    zero(["C64"], T.C64[:, 0:32], 32, 64)
    if RP_SPLIT:
        iota(["C15"], T.C64[:, 64:128], [[16, 2], [0, 32]], -1, 0, 64)
    lin(["C64"], ["C64"], T.C64[:, 32:64], T.C64[:, 0:32], -2.0 ** -14)
    iota(["PD2"], T.PD2[:], [[0, 48], [256, 2]], 0, 0, 96)
    zero(["ETz"], T.ET[:, 384:512], 128)
    zero(["RTz"], T.RT[:, 384:512], 128)
    zero(["GS0"], T.GS[:, 0:304], 304, 160)
    zero(["GD"], T.GS[:, 304:608], 304)
    iota(["I1z"], T.I1[:, 112:120], [[0, 8]], 0, 0, 8, True)
    iota(["YXz"], T.YX[:, 0:256], [[1, 256]], 0, 0, 256)
    zero(["HD"], T.HD[:], 64)
    quant(["VTL"], "V", 128, T.VTL[:])
    lin(["CW"], ["CP"], T.CP[:], CW, 1.0, -351.0)
    zero(["D0"], T.D0[:], 256)
    zero(["D0"], T.D0[:, 0:1], 1, 96)
    lin(["CW"], ["HD"], T.HD[:, 33:64:2], CW)
    VV, VT0, VT6 = T.VT[:, 105:1888:16], T.VT[:, 105:1888:112], T.VT[:, 201:1888:112]
    lin(["ZR", "lv"], ["VT0"], VT0, T.ZR[:, 0:16], 1.0, PF["lv"])
    cp(["OL"], ["L16"], T.L16[:], T.OL[:])
    ts(["OL", "lv"], ["VT6"], VT6, T.OL[:], 2.0 ** -8, OP.mult, PF["lv"], OP.add)

    E15 = slice(15, 256, 16)
    rid, pid = topo.addr(nxt)[0], topo.addr(nxt)[1]
    mask = topo.mask(core, nxt)
    n_eng = len(topo.engines(core, nxt))
    n_arr = len(topo.engines(prv, core))
    sent, first = [0], []

    def send(r, out, src, rsem):
        def issue():
            deps("G", r, [])
            g.remote_dma(out, src, T.sem[rsem], T.sem.ls, pid, rid, mask)
            sent[0] += n_eng
        nodes.append(([("G", issue, SEND + (0.0 if first else FIRST))], r, ["snd" + rsem], 0.0))
        first.append(rsem)

    for t in range(ROUNDS):
        X = "X%d" % t
        XK = [X, X + "s"]
        last = t == ROUNDS - 1
        mm(XK + ["UPc0", "UPs0"], "PA", 256, "UP", 0, X, 0)
        mm(XK + ["U"], "PD0", 128, X, 0, "U", 0)
        mm(XK + ["U"], "PD1", 128, X, 128, "U", 0)
        mm(XK + ["UPc2", "UPs2"], "PC_", 256, "UP", 256, X, 0)
        mm(XK + ["UPc1", "UPs1"], "PB", 256, "UP", 128, X, 0)
        act(["PD0", "PD1"], ["SB"], T.SB2[:, 0:2], T.PD[:, 8:1024:512])
        act(["PD0", "PD1"], ["DL"], T.DL[:], T.PD[:, 8:1024:512], AF.Abs, 2.0 ** -124, 1.25 * 2.0 ** -24)
        for h in range(2):
            lin(["TR", "DL", "SB"], ["TH%d" % h], T.TH[:, 128 * h:128 * h + 128], T.TR[:], T.DL[:, h:h + 1], T.SB2[:, h:h + 1], 128)
        if BIRTH_S > 1:
            act(["SB", "DL"], ["SBm"], T.SB2[:, 2:3], T.DL[:, 0:1], AF.Identity, T.SB2[:, 0:1], -1.0)
            act(["PC_", "SBm"], ["AJ3"], T.AJ[:, 768:896], ps("PC_", 128, 256), AF.Sign, T.SB2[:, 2:3], -1.0, n=128)
            act(["AJ3"], ["BTa"], T.BT[:, 512:1024:4], T.AJ[:, 768:896], AF.Relu, 0.0, -1.0, n=128)
        else:
            ts(["PC_", "SB"], ["BTa"], T.BT[:, 512:1024:4], ps("PC_", 128, 256), T.SB2[:, 0:1], OP.is_ge, n=128)
        if BIRTH_S:
            act(["PC_", "SB"], ["AJ2"], T.AJ[:, 512:640], ps("PC_", 0, 128), AF.Sign, T.SB2[:, 1:2], -1.0, n=128)
            act(["AJ2"], ["BTb"], T.BT[:, 1:512:4], T.AJ[:, 512:640], AF.Relu, 0.0, -1.0, n=128)
        else:
            ts(["PC_", "SB"], ["BTb"], T.BT[:, 1:512:4], ps("PC_", 0, 128), T.SB2[:, 1:2], OP.is_gt, n=128)
        tt(["PC_", "TH0"], ["BTc"], T.BT[:, 0:512:4], ps("PC_", 0, 128), T.TH[:, 0:128], OP.is_ge, 128)
        tt(["PC_", "TH1"], ["BTd"], T.BT[:, 513:1024:4], ps("PC_", 128, 256), T.TH[:, 128:256], OP.is_ge, 128)
        quant(["BTa", "BTb", "BTc", "BTd", "zB2", "zB3"], "B", 256, T.BT[:])
        mm(["B", "KB"], "PC_", 256, "KB", 0, "B", 0)

        def places(s):
            bank, sums = (("PA", "PD0"), ("PB", "PD1"))[s]
            c = slice(256 * s, 256 * s + 256)
            o, k = 4 * STRIP * s, "C%d" % s
            TWIN = TWINS[s]
            if TWIN:
                twin = TWIN
                mm(XK + ["UPc%d" % s, "UPs%d" % s], twin, 256, "UP", 128 * s, X, 0)
            else:
                twin = "SR%d" % s
                act([bank], [twin], T.SR[:, c], ps(bank, 0, 256), n=256)
            tt([bank, "NB"], ["SG%d" % s], T.SG[:, c], ps(bank, 0, 256), T.NB[:], (OP.add, OP.subtract)[s], 256)
            scan(["RS", "SG%d" % s], ["SW%d" % s], T.SW[:, c], T.RS[:, c], T.SG[:, c], 0.0, OP.add, (OP.min, OP.max)[s], 256)
            run = T.CT[:, o:o + 256]
            tt([bank, "SW%d" % s], ["ct%d.0" % s], run, ps(bank, 0, 256), T.SW[:, c], (OP.is_ge, OP.is_le)[s], 256)
            scan(["RC", "ct%d.0" % s], ["RD%d" % s], T.RD[:, c], T.RC[:], run, 0.0, OP.min, OP.add, 128)
            if LOW[s]:
                low = T.SW[:, 256 * s + 15:256 * s + 128:16]
                act(["SW%d" % s], ["LD%d" % s], T.LW[:, 16 * s:16 * s + 8], low, AF.Abs, 2.0 ** -124, 1.25 * 2.0 ** -24)
                tt(["SW%d" % s, "LD%d" % s], ["LW%d" % s], T.LW[:, 16 * s + 8:16 * s + 16], low, T.LW[:, 16 * s:16 * s + 8], (OP.subtract, OP.add)[s])
            made, ones = [(0, 64, "ct%d.0" % s)], []
            for i, (m, w, (a0, a1), (b0, b1)) in enumerate(PARTS):
                mine = T.SW[:, 256 * s + 16 * m + 15:256 * s + 16 * m + 16]
                na, nb = 16 * (a1 - a0), 16 * (b1 - b0)
                e = o + 4 * w
                if i < SIGNED[s]:
                    j, name = 128 * (i % 8), "SN%d" % (i % 8)
                    if na and LOW[s]:
                        act([twin, "LW%d" % s], [name + "a"], T.SN[:, j:j + na],
                            ps(twin, 16 * a0, 16 * a1) if TWIN else T.SR[:, 256 * s + 16 * a0:256 * s + 16 * a1], AF.Sign,
                            T.LW[:, 16 * s + 8 + m:16 * s + 9 + m], -1.0, n=na)
                    elif na:
                        ts([bank, "SW%d" % s], [name + "a"], T.SN[:, j:j + na], ps(bank, 16 * a0, 16 * a1), mine, (OP.is_ge, OP.is_le)[s],
                           (-1.0, 1.0)[s], OP.mult, n=na)
                    act([twin, "SW%d" % s], [name], T.SN[:, j + na:j + na + nb],
                        ps(twin, 16 * b0, 16 * b1) if TWIN else T.SR[:, 256 * s + 16 * b0:256 * s + 16 * b1], AF.Sign, mine, -1.0, n=nb)
                    end = 480 * s + w - 65 + (na + nb) // 4
                    act([name, name + "a", "RVz%d" % s], ["AR%d.%d" % (s, m), "ct%d.%d" % (s, w)], T.CT[:, e:e + na + nb], T.SN[:, j:j + na + nb],
                        AF.Relu, 0.0, (-1.0, 1.0)[s], T.RV[:, end:end + 1], n=na + nb)
                    made.append((w, w + (na + nb) // 4, "ct%d.%d" % (s, w)))
                    ones.append("AR%d.%d" % (s, m))
                    continue
                for c0, n, at, op in ((a0, na, 0, (OP.is_ge, OP.is_le)), (b0, nb, na, (OP.is_gt, OP.is_lt))):
                    if n:
                        name = "ct%d.%d" % (s, w + at // 4)
                        ts([bank, "SW%d" % s], [name], T.CT[:, e + at:e + at + n], ps(bank, 16 * c0, 16 * c0 + n), mine, op[s], n=n)
                        made.append((w + at // 4, w + (at + n) // 4, name))
            cuts = list(zip(CUTS[s], CUTS[s][1:] + (ROOM,)))
            for lo, hi in cuts[:-1]:
                quant([x[2] for x in made if x[0] < hi and lo < x[1]], k, hi - lo, T.CT[:, o + 4 * lo:o + 4 * hi], lo)

            def words(lo, hi):
                return ["%s.%d" % (k, a) for a, b in cuts if a < hi and lo < b]
            for f in FRAMES:
                mm(words(64 * f, 64 * f + 128) + ["KS"], sums, 128, "KS", 0, k, 64 * f, f == FRAMES[0], f == FRAMES[-1])
            w = PARTS[SIGNED[s]][1]
            mm(words(w, STRIP) + ["KI"], ROWS[s], STRIP - w, "KI", 0, k, w)
            scan([ROWS[s], "RM"], ["RV%d" % s], T.RV[:, 480 * s + w - 64:480 * s + 480], T.RM[:, w - 64:480], ps(ROWS[s], 0, STRIP - w),
                 0.0, OP.mult, OP.add, STRIP - w)
            tt(["RD%d" % s, "RV%d" % s, "ENDS"] + ones, ["RW%d" % s], T.RW[:, 16 * s:16 * s + 16],
               T.RV[:, 480 * s:480 * s + 480].indirect(T.OU[:, 80:81]), T.RD[:, 256 * s + 15:256 * s + 256:16], OP.add, far(16))
            scan([sums, "E4"], ["EC%d" % s], T.EC[:, 64 * s:64 * s + 64], T.E4[:, 0:64], ps(sums, 0, 64), 0.0, OP.add, OP.max)
        def halves(bs):
            for b in bs:
                k = F_BANKS[b]
                mm(XK + ["KR%d" % b], k, 256, "KR%d" % b, 0, X, 0)
                lin([k], ["FT%d" % b], T.FT[:, 256 * b:256 * b + 256], ps(k, 0, 256), 2.0 ** -8, n=256)
        halves(range(F_CUT[0]))
        places(0)
        halves(range(F_CUT[0], F_CUT[1]))
        places(1)
        halves(range(F_CUT[1], 4))
        tt(["EC1", "RW1"], ["PL1"], T.EP[:], T.EC[:, 67:128:4], T.RW[:, 16:32], OP.subtract)
        for b in range(0, 4, OWN):
            c = slice(256 * b, 256 * (b + OWN))
            dma("S", "dF%d" % b, ["FT%d" % i for i in range(b, b + OWN)], ["FU%d" % i for i in range(b, b + OWN)],
                [(T.FU[:, c], T.FT[:, c])], 1.75 + 0.25 * OWN)
        if t == 0:
            lin(["ID", "L16", "dl"], ["LF"], T.LF[:], T.ID[:].indirect(T.L16[:]), 2.0 ** -8, PF["dl"], n=far(256))
        tt(["PC_", "LF"], ["VH0"], T.VH[:, 0:256], ps("PC_", 0, 256), T.LF[:], OP.add, 256)
        if t in TWICE:
            lin(["LF", "L16", "dm"], ["L2"], T.L2[:, 0:256], T.LF[:].indirect(T.L16[:]), 256.0, PF["dm"], n=far(256))
            pick2(["L2"], ["L2p"], T.L2[:, 256:512], T.L2[:, 0:256])
            ts(["L2p", "xq"], ["M16"], T.M16[:], T.L2[:, 271:512:16], PF["xq"], OP.subtract)
        for i in range(1, 6):
            j, by = (i - 2, "M16") if i > 1 and t in TWICE and STEP[i] == 2 else (i - 1, "L16")
            lin(["VH%d" % j, by], ["VH%d" % i], T.VH[:, 256 * i:256 * i + 256],
                T.VH[:, 256 * j:256 * j + 256].indirect(T[by][:]), n=far(256))
            pick(["VH%d" % i], ["VT%d" % (6 - i)], T.VT[:, 96 - 16 * i:96 - 16 * i + 1786:7], T.VH[:, 256 * i:256 * i + 256])
        VK = ["VT%d" % k for k in range(7)]
        ts(VK + ["lv"], ["I0"], T.I0[:], VV, PF["lv"], OP.subtract, 256.0, OP.mult, 112)
        ts(["I0"], ["I1"], T.I1[:, 0:112], T.I0[:], 255, OP.bitwise_and, n=112)
        tt(["I1", "I1z"], ["D7"], T.D7[:], T.I1[:, 0:112], T.I1[:, 1:113], OP.subtract, 224)
        tt(["EC0", "RW0"], ["VR"], T.VR[:, 0:16], T.EC[:, 3:64:4], T.RW[:, 0:16], OP.subtract)
        tt(VK + ["VR", "REP7"], ["CM"], T.CM[:], T.VR[:, 0:16].indirect(REP7), VV, OP.is_le, far(112))
        for i in range(2):
            scan(["CM", "D7"], ["HR%d" % i], T.HR[:, 112 * i:112 * i + 111], T.CM[:, 0:111], T.D7[:, 1:112], 0.0, OP.mult, OP.add, 111)
        cp(["HR0"], ["R16"], T.R16[:], T.HR[:, 5:111:7])
        turn(["HR0", "HR1"], ["RQ"], T.QQ[:, 32:64], T.HR[:, 5:223:7])
        cp(["RQ"], ["R32"], T.R32[:], T.QQ[:, 32:64])
        for z in range(4 - COUNT_V, 4):
            cp(["CB", "R32"], ["CK"], T.CK[:], T.CB[:, 192 - 64 * z:448 - 64 * z].indirect(T.R32[:]), far(512))
            emit("V", ["CK"], ["CA%d" % z], lambda e, z=z: e.tensor_reduce(T.CA[:, z:z + 1], T.CK[:], AxisListType.X, OP.add), cyc(512))
        for z in range(4 - COUNT_V):
            act(["CB", "R32"], ["CJ%d" % (z % 2), "CA%d" % z], T.CJ[:, 512 * (z % 2):512 * (z % 2) + 512],
                T.CB[:, 192 - 64 * z:448 - 64 * z].indirect(T.R32[:]), AF.Copy, 0.0, 1.0, T.CA[:, z:z + 1], n=far(512))
        for b in range(4):
            tt(["FT%d" % b, "FU%d" % b, "R16"], ["Z%d" % b], T.Z[:, b:1024:4], T.FT[:, 256 * b:256 * b + 256].indirect(T.R16[:]),
               T.FU[:, 256 * b:256 * b + 256], OP.add, far(256))
        ZK = ["Z0", "Z1", "Z2", "Z3"]
        quant(ZK, "P", 256, T.Z[:])
        ts(["PL1", "lv1"], ["EP16"], T.EP16[:], T.EP[:], PF["lv1"], OP.subtract)
        cp(["ID", "EP16"], ["EF"], T.EF[:].indirect(T.EP16[:]), T.ID[:], 60 + STREW * 256)
        scan(["E4", "EF"], ["ES"], T.ES[:], T.E4[:], T.EF[:, 0:96], 0.0, OP.add, OP.max, 96)
        ts(["ES", "eo"], ["EO"], T.EO[:], T.ES[:, 3:96:4], 4.0, OP.mult, PF["eo"], OP.add)
        lin(ZK + ["EO"], ["ETa"], T.ET[:, 0:192], T.Z[:].indirect(T.EO[:, 0:12]), n=far(192))
        lin(ZK + ["EO"], ["ETb"], T.ET[:, 192:384], T.Z[:].indirect(T.EO[:, 12:24]), n=far(192))
        scan(["PD2", "EF"], ["PK"], T.PK[:], T.PD2[:], T.EF[:, 0:96], 0.0, OP.mult, OP.add, 96)
        cp(["PK"], ["LS%d" % t], T.LS[:, 48 * t:48 * t + 48], T.PK[:, 1:96:2])
        lo = KEEP * (ROUNDS - 1 - t)
        quant(["ETa", "ETb", "ETz"], "E%d" % t, 128, T.ET[:])
        send(["LS%d" % t], T.LL[:, 48 * t:48 * t + 48], T.LS[:, 48 * t:48 * t + 48], "aL%d" % t)
        send(["E%d" % t, "sndaL0"], T.cL[:, lo:lo + KEEP].bitcast(dt.uint8), T.cE[:, 128 * t:128 * t + KEEP].bitcast(dt.uint8), "aC%d" % t)
        send(["E%d" % t], T.sL[:, lo:lo + KEEP], T.sE[:, 128 * t:128 * t + KEEP], "aC%d" % t)
        arrival("L%d" % t, ["sndaC%d" % t], ("aC%d" % t, 2 * n_arr, {}))
        arrival("LL%d" % t, ["sndaL%d" % t], ("aL%d" % t, n_arr, {}))
        if t in PAIRS:
            cp(["I1"], ["H5", "H16"], T.H16[:, 0:16], T.I1[:, 2:112:7])
            cp(["I1"], ["H3", "H16"], T.H16[:, 16:32], T.I1[:, 4:112:7])
        else:
            cp(["I1", "HOPS"], ["H16", "H5", "H3"], T.H16[:, 0:80], T.I1[:, 0:112].indirect(T.OU[:, 56:61]), far(80))
        tt(["CW", "I1"], ["D7", "D8"], T.D7[:, 0:112:7], CW, T.I1[:, 1:112:7], OP.subtract)
        across(["CA%d" % z for z in range(4)], ["CI0"], T.CI[0:64, 0:4], T.CA[0:64, :], T.CA[64:128, :])
        ts(["CI0"], ["CI1"], T.CI[0:64, 8:16:2], T.CI[0:64, 0:4], 2047, OP.bitwise_and)
        ts(["CI0"], ["CI2"], T.CI[0:64, 9:16:2], T.CI[0:64, 0:4], 11, OP.arith_shift_right)
        across(["CI1", "CI2"], ["Q4"], T.QQ[0:32, 0:8], T.CI[0:32, 8:16], T.CI[32:64, 8:16])
        for a in range(1, 4):
            lin(["Q4"], ["Q4%d" % a], T.QQ[32 * a:32 * a + 32, 0:8], T.QQ[0:32, 0:8])
        if RP_SPLIT:
            for b in range(8):
                r, w, out, x = ["Q4", "Q41", "Q42", "Q43", "C15"], ["RP%d" % b], T.RP[:, 32 * b:32 * b + 32], T.QQ[:, b:b + 1]
                nodes.append(([way("A", r, w, lambda e, out=out, x=x: e.activation(out, T.C64[:, 64:96], AF.Relu, 15.0, x), cyc(64)),
                               way("V", r, w, lambda e, out=out, x=x: e.tensor_scalar(out, T.C64[:, 96:128], x, 0.0, OP.subtract, OP.max), cyc(64))],
                              r, w, 0.0))
        else:
            act(["Q4", "Q41", "Q42", "Q43", "BC32"], ["RP0"], T.RP[:], T.QQ[:, 0:8].indirect(BC32), AF.Relu, 15.0, -1.0, n=far(256))
        turn(["RP%d" % b for b in range(8)], ["TO"], T.TO[:], T.RP[:], 128)
        TO = ["TO"]
        act(TO + ["qn"], ["AJ0", "AC"], T.AJ[:, 0:256], T.TO[:], AF.Sign, PF["qn"], -1.0, T.SC[:, 0:1], n=256)
        ts(["C64", "AC"], ["FB"], T.FB[:, 0:32], T.C64[:, 0:32], T.SC[:, 0:1], OP.is_lt)
        turn(["FB"], ["FX"], T.FB[:, 32:64], T.FB[:, 0:32])
        emit("V", ["FX"], ["SF"], lambda e: e.tensor_reduce(T.SC[:, 1:2], T.FB[:, 32:48], AxisListType.X, OP.add), cyc(64))
        ts(["SF", "tb"], ["SL"], T.SL[:, 0:1], T.SC[:, 1:2], PF["tb"], OP.add)
        act(TO + ["q255"], ["LE"], T.LE[:], T.TO[:], AF.Sign, PF["q255"], 1.0, n=256)
        scan(["AJ0", "D0", "AC"], ["AA"], T.AA[:], T.D0[:], T.AJ[:, 0:256], T.SC[:, 0:1], OP.add, OP.subtract, 128)
        scan(["LE", "AA", "GS0"], ["GS"], T.GS[:, 32:288], T.LE[:], T.AA[:], 160.0, OP.add, OP.min, 128)
        scan(["GS", "GS0"], ["GD"], T.GS[:, 336:592], T.GS[:, 32:288], T.GS[:, 31:287], 0.0, OP.max, OP.subtract, 128)
        for i, k in enumerate(("GS", "GD")):
            turn([k], [k + "a"], T.TG[:, 544 * i:544 * i + 256], T.GS[:, 304 * i + 32:304 * i + 288], 128)
            turn([k, "GS0"], [k + "b"], T.TG[:, 544 * i + 256:544 * i + 544], T.GS[:, 304 * i + 16:304 * i + 304], 144)
        ts(["GDa", "GDb", "SL", "HD"], ["HDa"], T.HD[:, 1:32:2], T.TG[:, 544:1088].indirect(T.SL[:, 0:1]), 0.25, OP.mult, 0.25, OP.add, n=far(16))
        tt(["GSa", "GSb", "SL", "CP", "HD"], ["HDb"], T.HD[:, 32:64:2], T.TG[:, 0:544].indirect(T.SL[:, 0:1]), T.CP[:], OP.subtract, far(16))
        scan(["LE", "AJ0"], ["CE"], T.GN[:], T.LE[:], T.AJ[:, 0:256], 65.0, OP.add, OP.add, 128)
        act(["CE", "AC"], ["AJ1", "JS"], T.AJ[:, 256:512], T.GN[:], AF.Sign, T.SC[:, 0:1], -1.0, T.SC[:, 2:3], n=256)
        ts(["AC"], ["NV"], T.SC[:, 3:4], T.SC[:, 0:1], 64.0, OP.is_le, 1024.0, OP.mult)
        lin(["NV", "q254"], ["NW"], T.SC[:, 4:5], T.SC[:, 3:4], 1.0, PF["q254"])
        ts(["C64", "JS", "NW"], ["FK"], T.QQ[:, 128:160], T.C64[:, 32:64], T.SC[:, 2:3], OP.mult, T.SC[:, 4:5], OP.add)
        turn(["FK"], ["FL_"], T.QQ[:, 160:192], T.QQ[:, 128:160])
        emit("V", ["FL_"], ["TN"], lambda e: e.tensor_reduce(T.SC[:, 5:6], T.QQ[:, 160:176], AxisListType.X, OP.min), cyc(64))
        scan(["HDa", "HDb"], ["HO"], T.HO[:, 0:32], T.HD[:, 0:32], T.HD[:, 32:64], 0.0, OP.mult, OP.add)
        cp(["HO"], ["NI16"], T.NI16[:], T.HO[:, 1:32:2])
        for b in range(4):
            k = ("Q0", "Q1", "Q2", "PC_")[b]
            mm(["L%d" % t, "pad", "W"], k, 128, "W", 128 * b, "L", lo, True, False, ["bank by bank"])
            mm(["L%d" % t, "pad", "KR%d" % b], k, 128, "KR%d" % b, 0, "L", lo, False, True, ["bank by bank"])
            lin([k, "RTz"], ["RT%d" % b], T.RT[:, b:384:4], ps(k, 0, 96), 2.0 ** -7, n=96)
        quant(["RT0", "RT1", "RT2", "RT3"], "Pb", 128, T.RT[:])
        XN = "X%d" % (t + 1)
        emit("V", ["P", "Pb", "NI16"], [XN], lambda e, t=t: e.tensor_copy(
            T.cX[:, 256 * t + 256:256 * t + 512].bitcast(dt.uint32), T.cP[:, :].bitcast(dt.uint32).indirect(T.NI16[:])), cyc(far(256)))
        lin(["P", "Pb", "NI16"], [XN + "s"], T.sX[:, 256 * t + 256:256 * t + 512], T.sP[:, :].indirect(T.NI16[:]), n=far(256))
        ts(["I1", "TN"], ["KY"], T.G8[:, 0:112], T.I1[:, 0:112], 2.0 ** -7, OP.mult, T.SC[:, 5:6], OP.add, 112)
        if t in PAIRS:
            lin(TO + ["L16"], ["FL3"], T.FL[:, 768:1024], T.TO[:].indirect(T.L16[:]), -16.0, 256.0, n=far(256))
            scan(TO + ["FL3"], ["FL4"], T.FL[:, 1024:1280], T.TO[:], T.FL[:, 768:1024], 0.0, OP.max, OP.subtract, 128)
            for s, (name, by) in enumerate((("H5", T.H16[:, 0:16]), ("H3", T.H16[:, 16:32]), ("L16", T.L16[:]))):
                c = slice(256 * s, 256 * s + 256)
                lin(["FL4", name], ["FL%d" % s], T.FL[:, c], T.FL[:, 1024:1280].indirect(by), 1.0, 256.0, n=far(256))
                pick2(["FL%d" % s], ["FQ%d" % s], T.FQ[:, 16 * s:16 * s + 766:3], T.FL[:, c])
            ts(["FQ0", "FQ1", "FQ2"], ["LH0"], T.LH[:, 104:152], T.FQ[:, 45:800:16], 2.0, OP.mult)
            ts(["LH0"], ["LH1"], T.LH[:, 1:97:2], T.LH[:, 104:152], 4, OP.arith_shift_right, 30, OP.bitwise_and)
            ts(["LH0"], ["LH2"], T.LH[:, 2:98:2], T.LH[:, 104:152], 30, OP.bitwise_and)
            tt(["LH1", "LH2", "LHz", "SIX", "KY"], ["G8"], T.G8[:, 112:224], T.LH[:, 0:97].indirect(SIX), T.G8[:, 0:112], OP.is_ge, far(112))
        else:
            for s in range(6):
                c = slice(256 * s, 256 * s + 256)
                lin(TO + ["H16", "L16", "xn"], ["FL%d" % s], T.FL[:, c], T.TO[:].indirect(T.H16[:, 16 * s:16 * s + 16] if s < 5 else T.L16[:]),
                    2.0, PF["xn"], n=far(256))
                pick2(["FL%d" % s], ["FP%d" % s], T.FP[:, 16 * s + 16:16 * s + 16 + 1786:7], T.FL[:, c])
            tt(["FP%d" % s for s in range(6)] + ["FPz", "KY"], ["G8"], T.G8[:, 112:224], T.FP[:, 105:1888:16], T.G8[:, 0:112], OP.is_ge, 224)
        lin(["HDa"], ["G8g"], T.HO[:, 32:48], T.HD[:, 1:32:2], 2.0)
        cp(["LL%d" % t], ["LI0"], T.LI[:, 0:48], T.LL[:, 48 * t:48 * t + 48])
        ts(["LI0"], ["LI1"], T.LI[:, 49:144:2], T.LI[:, 0:48], 255, OP.bitwise_and)
        ts(["LI0"], ["LI2"], T.LI[:, 48:144:2], T.LI[:, 0:48], 8, OP.arith_shift_right)
        cp(["LI1", "LI2"], ["YXe"], T.YX[:, 256:352], T.LI[:, 48:144], 96)
        tt(["HO", "G8g"], ["D8e"], T.D8[:, 0:16], T.HO[:, 1:32:2], T.HO[:, 32:48], OP.mult)
        scan(["G8", "D7", "D8"], ["HL"], T.HL[:, 0:112], T.G8[:, 112:224], T.D7[:], 0.0, OP.mult, OP.add, 112)
        tt(["HL", "D8e"], ["HM"], T.D8[:, 16:32], T.HL[:, 6:112:7], T.D8[:, 0:16], OP.max)
        cp(["HM"], ["F16"], T.F16[:], T.D8[:, 16:32])
        if not last:
            lin(["YXz", "YXe", "F16"], ["LF"], T.LF[:], T.YX[:].indirect(T.F16[:]), 2.0 ** -8, PF["dl"], n=far(256))
            pick(["LF"], ["VT6"], T.VT[:, 96:96 + 1786:7], T.LF[:])
            ts(["VT6", "lv"], ["L16"], T.L16[:], VT6, PF["lv"], OP.subtract, 256.0, OP.mult)

    mm(["V", "P"], "PA", 256, "V", 0, "P", 0)
    mm(["V", "Pb"], "PB", 128, "V", 0, "Pb", 0)
    lin(["PA"], ["YCa"], T.YC[:, 0:256], ps("PA", 0, 256), n=256)
    lin(["PB"], ["YCb"], T.YC[:, 256:352], ps("PB", 0, 96), n=96)
    dma("S", "dOc", ["X3", "X3s"], ["oc"], [(T.oc[:, :], T.cX[:, 768:1024].bitcast(dt.uint8))] + [
        (T.osc[4 * k:4 * k + 4, :], T.sX[32 * k:32 * k + 4, 768:1024]) for k in range(4)])
    lin(["YCa", "YCb", "NI16"], ["YO"], T.YO[:], T.YC[:].indirect(T.NI16[:]), n=far(256))
    dma("A", "dY", ["YO"], ["y"], [(T.y[:, :], T.YO[:])])
    lin(["YXz", "YXe", "F16"], ["LO"], T.LO[:], T.YX[:].indirect(T.F16[:]), n=far(256))
    dma("S", "dLk", ["LO"], ["lk"], [(T.lk[:, :], T.LO[0:128:16, :])], 1.2)
    schedule()
    for s in cnt:
        if known["S"].get(s, 0) < cnt[s]:
            g.sync.wait_ge(T.sem[s], cnt[s])
    g.wait_ge(T.sem.ls, sent[0])
